import numpy as np, ml_dtypes
CORES = [9,25,41,57]
N = 4
BF = ml_dtypes.bfloat16
V, HV, LV, K, T, S, EPS, LK = 4096, 2048, 12, 256, 5, 1, 72, 9
def pick(tab, ix):
    return np.take_along_axis(tab, ix[:, :, None, :], 3)
def parts(rng):
    px = np.clip(rng.integers(0, 256, (1, 8, 16, V)) + rng.integers(-48, 49, (N, 8, 16, V)), 0, 255)
    vi = rng.integers(0, V, (N, 8, 16, V))
    few = rng.integers(0, V, (N, 8, 16))
    v = np.where(rng.random((N, 8, K)) < 0.25, np.take_along_axis(few, rng.integers(0, 16, (N, 8, K)), 2), rng.integers(0, V, (N, 8, K)))
    near = np.clip(pick(px, v) + rng.integers(-120, 121, (N, 8, 16, K)), 0, 255)
    z = np.where(rng.random((N, 8, 1, K)) < 0.4, near, rng.integers(0, 256, (N, 8, 16, K)))
    f = rng.integers(0, V, (N, 8, 16, K)); d = rng.integers(0, 4, (N, 8, K))
    return px, vi, z, f, v, d, rng.integers(0, 256, (N, 8, 16)), rng.integers(0, 4096, (N, 8, 16))
def pack(px, vi, z, f, v, d, w, k):
    return {"px": np.ascontiguousarray(px.reshape(N, 128, V)).astype(np.float32).astype(BF), "vw": (vi[..., :HV] + V * vi[..., HV:]).reshape(N, 128, HV).astype(np.int32),
            "z0": z.reshape(N, 128, K).astype(np.float32).astype(BF), "f0": f.reshape(N, 128, K).astype(np.int32), "v0": v.astype(np.int32), "d0": d.astype(np.int32),
            "wt": w.reshape(N, 128, 1).astype(np.int32), "kap": k.reshape(N, 128, 1).astype(np.int32)}
def setup_inputs(rng):
    return pack(*parts(rng))
def setup_inputs_corners(rng):
    px, vi, z, f, v, d, w, k = parts(rng); own = np.arange(V)[None, :]; lane = np.arange(16); i = np.arange(K); one = 0 * i
    for r in range(N):
        for g in range(8):
            m = r + g
            d[r, g] = (one, one + 1, one + 3, 3 * (i & 1))[m & 3]
            v[r, g] = (one + (0, V - 1, HV)[m % 3], rng.permutation(V)[:K], (V - 1) * (i & 1), V - K + i)[(r + (g >> 1)) & 3]
            vi[r, g] = (own + 0 * lane[:, None], V - 1 - own + 0 * lane[:, None], (own + 1 + lane[:, None]) & (V - 1), (V - 1) * rng.integers(0, 2, (16, V)))[g & 3]
            f[r, g] = vi[r, g][:, v[r, g]] if m & 1 else (V - 1) * rng.integers(0, 2, (16, K))
            w[r, g] = (0 * lane, 0 * lane + 255, 255 * (lane == 15), w[r, g])[(m >> 1) & 3]
            k[r, g] = (0 * lane, 0 * lane + 4095, 4095 * (lane == 15), k[r, g])[(r + 3 * g) & 3]
            likes = (i >= 0, i < 0, (i & 1) == 0, (i & 1) == 1, rng.random(K) < 0.5)[(r + 2 * g) % 5]
            x = px[r, g][:, v[r, g]]; z[r, g] = np.where(likes[None, :], x, (x + 128) & 255)
    return pack(px, vi, z, f, v, d, w, k)
def setup_inputs_ends(rng):
    def bits(*shape):
        return rng.integers(0, 2, shape)
    pat = 255 * bits(N, 8, 16, 6); pat[..., 0] = 0; pat[..., 1] = 255; pat[..., 3] = 255 - pat[..., 2]
    px = np.take_along_axis(pat, rng.integers(0, 6, (N, 8, 1, V)), 3)
    px[..., 0] = 0; px[..., V - 1] = 255; px[..., V - 613] = 255
    vi = (V - 1) * bits(N, 8, 16, HV); vi = np.concatenate([vi, vi], axis=3)
    z = 255 * bits(N, 8, 16, K); f = (V - 1) * bits(N, 8, 16, K); v = (V - 1) * bits(N, 8, K); d = 3 * bits(N, 8, K)
    w = 255 * bits(N, 8, 16); w[:, 1::2] = 255; k = 4095 * bits(N, 8, 16); k[..., 15] = 4095
    for h in (0, K - 4):
        z[..., h] = 255; v[..., h] = V - 1
        z[..., h + 1] = 255; v[..., h + 1] = 0; d[..., h + 1] = 3
        z[..., h + 2] = 0; z[:, :, 0, h + 2] = 255; z[:, :, 1, h + 2] = 2; v[..., h + 2] = V - 1
        z[..., h + 3] = 0; v[..., h + 3] = V - 1
    return pack(px, vi, z, f, v, d, w, k)
def setup_inputs_spread(rng):
    px = np.minimum((np.exp2(8 * rng.random((N, 8, 1, V))) * rng.random((N, 8, 16, V))).astype(np.int64), 255)
    z = np.minimum((np.exp2(8 * rng.random((N, 8, 1, K))) * rng.random((N, 8, 16, K))).astype(np.int64), 255)
    vi = np.minimum((V * rng.random((N, 8, 16, V)) ** 3).astype(np.int64), V - 1)
    f = np.minimum((V * rng.random((N, 8, 16, K)) ** 4).astype(np.int64), V - 1)
    v = np.minimum((V * rng.random((N, 8, K)) ** 2).astype(np.int64), V - 1)
    d = np.minimum((4 * rng.random((N, 8, K)) ** 2).astype(np.int64), 3)
    w = np.minimum(np.exp2(8 * rng.random((N, 8, 16))).astype(np.int64), 255); k = np.minimum(np.exp2(12 * rng.random((N, 8, 16))).astype(np.int64), 4095)
    return pack(px, vi, z, f, v, d, w, k)
def setup_inputs_ties(rng):
    px, vi, z, f, v, d, w, k = parts(rng)
    pat = np.broadcast_to(rng.integers(0, 256, (1, 8, 16, 8)), (N, 8, 16, 8))
    px = np.take_along_axis(pat, rng.integers(0, 8, (N, 8, 1, V)), 3)
    v = np.take_along_axis(rng.integers(0, V, (N, 8, 24)), rng.integers(0, 24, (N, 8, K)), 2)
    x = pick(px, v); n = LK - rng.integers(0, 2, (N, 8, 1, K)); o = np.argsort(rng.random((N, 8, 16, K)), axis=2)
    far = EPS + (o >= n).astype(np.int64); z = np.where(x + far <= 255, x + far, x - far)
    vi = np.where(rng.random((N, 8, 16, V)) < 0.2, np.arange(V), vi)
    return pack(px, vi, z, f, v, d, w, k)
def check_inputs(d):
    bad = []
    for a, lo, hi in (("px", 0, 255), ("vw", 0, V * V - 1), ("z0", 0, 255), ("f0", 0, V - 1), ("v0", 0, V - 1), ("d0", 0, 3), ("wt", 0, 255), ("kap", 0, 4095)):
        x = np.asarray(d[a]).astype(np.float64)
        if not (np.min(x) >= lo and np.max(x) <= hi): bad.append("range of " + a)
        if not np.all(x == np.rint(x)): bad.append("whole numbers of " + a)
    return bad
def distances(X, ix, q):
    flat = ix.reshape(N, 8, 16 * K); out = np.zeros((N, 8, 16, K), np.int64)
    for i in range(16):
        out += np.abs(np.take_along_axis(X[:, :, i], flat, 2).reshape(N, 8, 16, K) - q[:, :, i][:, :, None, :])
    return out
def place(view, k):
    return np.take_along_axis(view, k[:, :, None, :], 2)[:, :, 0]
def reference(px, vw, z0, f0, v0, d0, wt, kap):
    X = px.astype(np.int64).reshape(N, 8, 16, V); packed = vw.astype(np.int64).reshape(N, 8, 16, HV)
    vi = np.concatenate([packed & (V - 1), packed >> LV], axis=3)
    z = z0.astype(np.int64).reshape(N, 8, 16, K); f = f0.astype(np.int64).reshape(N, 8, 16, K); v = v0.astype(np.int64); dl = d0.astype(np.int64); A = np.zeros((N, 8, K), np.int64)
    wl = wt.astype(np.int64).reshape(N, 8, 16, 1); kl = kap.astype(np.int64).reshape(N, 8, 16, 1); other = np.arange(K) ^ 1
    for t in range(T):
        x = pick(X, v); e = pick(vi, v)
        like = np.add.reduce((np.abs(x - z) <= EPS).astype(np.int64), axis=2) >= LK + (A & 1); L = like[:, :, None, :]
        u = np.add.reduce(wl * z, axis=2) & (V - 1)
        h = np.where(L, f, (((u[:, :, None, :] * kl) >> 5) + 613 * v[:, :, None, :]) & (V - 1))
        de = distances(X, e, x); dh = distances(X, h, np.where(L, x, z))
        e = np.where(L & (dh < de), h, e)
        for r in range(N):
            for g in range(8):
                j = np.flatnonzero(like[r, g]); users, first = np.unique(v[r, g, j], return_index=True)
                vi[r, g][:, users] = e[r, g][:, j[first]]
        z = np.where(L, (z + x) >> 1, z); A = A + like.astype(np.int64); dl = np.where(like, 0, dl + 1)
        s = np.add.reduce(z, axis=2)
        v = np.where(like, place(e, (s + t) & 15), place(h, np.argmin(dh, axis=2)))
        f = e; second = place(e, (s + t + 8) & 15)
        over = like[:, :, other] & (dl >= 2); O = over[:, :, None, :]
        z = np.where(O, z[..., other], z); f = np.where(O, f[..., other], f); A = np.where(over, A[..., other], A)
        v = np.where(over, second[..., other], v); dl = np.where(over, 0, dl)
        if t < T - 1: z, f, v, A, dl = [np.roll(a, S, axis=0) for a in (z, f, v, A, dl)]
    return {"yw": (vi[..., :HV] + V * vi[..., HV:]).reshape(N, 128, HV).astype(np.float32), "yz": z.reshape(N, 128, K).astype(np.float32), "yf": f.reshape(N, 128, K).astype(np.float32),
            "yv": v.astype(np.float32), "yc": (16 * A + dl).astype(np.float32)}

@@ -1,0 +1,803 @@
+import numpy as np
+from concourse.bass import DstId, RemoteDMATransfer
+from concourse.mybir import dt, AluOpType, AxisListType, ActivationFunctionType
+
+A = AluOpType
+F = ActivationFunctionType
+n = 128
+NT = 5
+XW = 32 + 3 * n
+WW = 4 * n
+MAGIC = 12582912.0
+PRI = {'fr0': 3.4, 'fr1': 10.5, 'qx0': -12.4, 'qx1': -8.0, 'ha0': 6.0, 'ha1': -1.7, 'dd0': -0.6, 'dd1': 4.5, 'h0': -4.1, 'h1': 0.6, 'e0': -9.4, 'e1': 3.2, 'ea0': -3.8, 'ea1': 1.7, 'kk0': -2.7,
+       'kk1': 11.4, 'hb0': -6.6, 'hb1': -5.1, 'hm0': 5.8, 'hm1': -7.9, 'km0': -5.6, 'km1': -1.7, 'eb0': 12.0, 'eb1': -5.3, 'cc0': 3.1, 'cc1': 13.2, 'ff0': 1.5, 'ff1': 11.6, 'sc0': -18.1, 'sc1': -12.0}
+NE = 64
+f4, b2, h2, i4, u2 = "float32", "bfloat16", "float16", "int32", "uint16"
+
+SCRATCH = {
+    "PX": ("sbuf", [128, 4096], b2), "VI": ("sbuf", [128, 4096 + 2 * n], f4), "VW": ("sbuf", [128, 2048], i4),
+    "IT": ("sbuf", [128, 2048], i4), "YT": ("sbuf", [128, 2048], f4), "YU": ("sbuf", [128, 2048], f4),
+    "XZ": ("sbuf", [128, 10 * XW], b2), "W": ("sbuf", [128, 10 * WW], f4), "VH": ("sbuf", [128, 10 * 8], h2),
+    "ZB": ("sbuf", [128, 10 * (32 + n)], b2), "FB": ("sbuf", [128, 10 * n], f4), "VB": ("sbuf", [128, 10 * 8], h2),
+    "HE": ("sbuf", [128, 4 * n], f4), "HEL": ("sbuf", [128, 4 * n], u2), "QS": ("sbuf", [128, 16 * n], h2), "QX": ("sbuf", [128, 32 * n], h2),
+    "GH": ("sbuf", [128, 32 * n], b2), "GE": ("sbuf", [128, 32 * n], b2), "DH": ("sbuf", [128, 32 * n], h2), "DE": ("sbuf", [128, 32 * n], h2),
+    "RH": ("sbuf", [128, 32 * n], h2), "RE": ("sbuf", [128, 32 * n], h2),
+    "OTL": ("sbuf", [128, 16], u2), "AB": ("sbuf", [128, 2 * n], b2), "IND": ("sbuf", [128, 2 * n], h2), "LK": ("sbuf", [128, 16], b2),
+    "LSL": ("sbuf", [128, 32], u2), "HI1": ("sbuf", [128, 2 * n], i4), "HI2": ("sbuf", [128, 2 * n], i4), "T1": ("sbuf", [128, 2 * n], f4),
+    "D1": ("sbuf", [128, 16], b2), "OV": ("sbuf", [128, 16], b2), "TLL": ("sbuf", [128, 48], u2), "P1": ("sbuf", [128, 32], b2), "RA": ("sbuf", [128, 80], b2),
+    "KT": ("sbuf", [128, 2 * n], f4), "KU": ("sbuf", [128, 2 * n], f4), "SP": ("sbuf", [128, 2 * n], f4), "BP": ("sbuf", [128, 8], b2), "CB": ("sbuf", [128, 16], b2), "SJb": ("sbuf", [128, 2048], b2), "OK": ("sbuf", [128, 16], f4), "CLB": ("sbuf", [128, 8], f4),
+    "WBs": ("sbuf", [128, 128], b2), "I4kn": ("sbuf", [128, 128], b2), "CH": ("sbuf", [128, 128], b2), "T2": ("sbuf", [128, 2 * n], f4), "FL": ("sbuf", [128, 2 * n], b2), "EQ2": ("sbuf", [128, 2 * n], h2), "OHL": ("sbuf", [128, 2 * n], b2),
+    "VS": ("sbuf", [128, 2 * n], f4), "VR": ("sbuf", [128, 2 * n], f4), "EQ": ("sbuf", [128, 2 * n], b2),
+    "W0": ("sbuf", [128, 16], b2), "O2": ("sbuf", [128, 16], f4), "OFF": ("sbuf", [128, 32], u2),
+    "HME": ("sbuf", [128, 2 * n], f4), "KEY": ("sbuf", [128, 2 * n], f4), "MT": ("sbuf", [128, 2 * n], b2), "MM": ("sbuf", [128, 2 * n], f4),
+    "PM": ("sbuf", [128, 2 * n], f4), "MN": ("sbuf", [128, 2 * n], f4), "OHT": ("sbuf", [128, 2 * n], b2), "CF": ("sbuf", [128, 2 * n], f4), "PP": ("sbuf", [128, 2 * n], h2),
+    "I16b": ("sbuf", [128, 128], b2), "I8k": ("sbuf", [128, 128], b2), "I8kn": ("sbuf", [128, 128], b2), "BO613": ("sbuf", [128, 128], h2), "C256": ("sbuf", [128, n], h2),
+    "If": ("sbuf", [128, 128], f4), "Ib": ("sbuf", [128, 128], b2), "Ih": ("sbuf", [128, 128], h2), "Inb": ("sbuf", [128, 128], b2), "Ihalf": ("sbuf", [128, 128], b2),
+    "Sb": ("sbuf", [128, 128], b2), "Sb100": ("sbuf", [128, 128], b2), "In": ("sbuf", [128, 128], b2), "I2n": ("sbuf", [128, 128], b2),
+    "Imh": ("sbuf", [128, 128], b2), "I7h": ("sbuf", [128, 128], b2), "I4k": ("sbuf", [128, 128], f4),
+    "Ip100": ("sbuf", [128, 128], b2), "Im100": ("sbuf", [128, 128], b2),
+    "Gn": ("sbuf", [128, 128], b2), "G0": ("sbuf", [128, 128], b2),
+    "ONE": ("sbuf", [128, 128], f4), "G8": ("sbuf", [128, 128], f4), "BO": ("sbuf", [128, 128], b2), "BOh": ("sbuf", [128, 128], h2), "BOg": ("sbuf", [128, 128], b2), "WB": ("sbuf", [128, 128], b2),
+    "Bh": ("sbuf", [128, 144], h2), "B32": ("sbuf", [128, 8], h2), "Bm16": ("sbuf", [128, 8], h2),
+    "SJ": ("sbuf", [128, 2048], h2), "LTJ": ("sbuf", [128, 2048], b2), "PI": ("sbuf", [128, 32], i4), "PC": ("sbuf", [128, 16], f4),
+    "OJ": ("sbuf", [128, 16], f4),  "IJ": ("sbuf", [128, 16], f4), "CMI": ("sbuf", [128, 8], f4), "CM": ("sbuf", [128, 32], h2), "CMm": ("sbuf", [128, 16], h2),
+    "CON": ("sbuf", [128, 80], b2), "O2V": ("sbuf", [128, 32], b2), "KC": ("sbuf", [128, 128], b2), "MK": ("sbuf", [128, 16 * n], b2), "MF": ("sbuf", [128, n], f4), "RST": ("sbuf", [128, 128], f4),
+    "CQ": ("sbuf", [128, 128], b2), "ON": ("sbuf", [128, 128], b2), "WT": ("sbuf", [128, 2], i4), "WTf": ("sbuf", [128, 8], f4),
+    "VZ": ("sbuf", [128, 512], i4), "VZi": ("sbuf", [128, 512], i4), "VZh": ("sbuf", [128, 768], h2), "FI": ("sbuf", [128, 256], i4), "YC": ("sbuf", [128, 16], b2),
+}
+for _b in range(8):
+    SCRATCH["b%d" % _b] = ("psum", [128, 512], f4)
+LOADS = ["px0", "px1", "vw0", "vw1", "z0", "z1", "f0", "v0", "d0", "wt", "kap"]
+SEMAPHORES = ["V", "S", "P", "G", "out", "ls"] + ["ld_" + x for x in LOADS] + ["r%s_%d_%d" % (k, t, h) for k in "zfv" for t in range(1, NT) for h in range(2)]
+
+
+def ref(name, c0, c1, step=1, p0=0, p1=128, pstep=1):
+    return (name, c0, c1, step, p0, p1, pstep)
+
+
+def new_prog():
+    return {"ops": [], "acc": {}, "rr": [0], "st": "", "bmap": {}}
+
+
+def touch(pg, o, r, wr):
+    name, c0, c1 = r[0], r[1], r[2]
+    lst = pg["acc"].setdefault(name, [])
+    psum = name[0] == "b" and name[1:].isdigit()
+    ops = pg["ops"]
+    keep = []
+    for a in lst:
+        p, a0, a1, aw = a
+        over = a0 < c1 and c0 < a1
+        if p != o["i"]:
+            if psum:
+                if ops[p]["q"] != o["q"]:
+                    o["dep"].add(p)
+                elif o["q"] == "P":
+                    o["ord"].add(p)
+            elif over and (wr or aw):
+                o["dep"].add(p)
+        if wr and a0 >= c0 and a1 <= c1 and p != o["i"] and not psum and r[3] == 1 and r[6] == 1:
+            continue
+        keep.append(a)
+    if psum and len(keep) > 24:
+        keep = keep[-24:]
+    keep.append((o["i"], c0, c1, wr))
+    pg["acc"][name] = keep
+
+
+def add(pg, q, cost, fn, rd, wr, sem=None, val=1, after=(), lat=0.0, tag=""):
+    o = {"i": len(pg["ops"]), "q": q, "cost": cost, "fn": fn, "dep": set(after), "ord": set(), "sem": sem, "val": val, "lat": lat, "send": None, "tag": tag, "st": pg["st"], "wake": WAKE}
+    pg["ops"].append(o)
+    for r in rd:
+        touch(pg, o, r, False)
+    for r in wr:
+        touch(pg, o, r, True)
+    o["tiles"] = sorted(set(r[0] for r in list(rd) + list(wr) if r[0][0] == "b" and r[0][1:].isdigit()))
+    o["dyn"] = set()
+    return o["i"]
+
+
+WAKE = 0.10
+GC = 1.5
+PEC = 0.00055
+CY = 0.00083
+LNK = 1.6
+FIX = {"V": 0.03, "S": 0.04, "P": 0.03, "G": 0.05, "Y": 0.05}
+
+
+def schedule(pg):
+    ops = pg["ops"]
+    N_ = len(ops)
+    succ = [[] for _ in ops]
+    cnt = [0] * N_
+    for o in ops:
+        ps = set(o["dep"]) | o["ord"]
+        if o["send"] is not None:
+            ps.add(o["send"])
+        cnt[o["i"]] = len(ps)
+        for p in ps:
+            succ[p].append(o["i"])
+    pri = [0.0] * N_
+    for o in reversed(ops):
+        i = o["i"]
+        pri[i] = max([pri[s] for s in succ[i]] + [0.0]) + o["cost"] + o["lat"] + WAKE
+    for o in ops:
+        pri[o["i"]] += PRI.get(o["st"], 0.0)
+    uses, first = {}, {}
+    for o in ops:
+        for tname in o["tiles"]:
+            if tname not in uses:
+                uses[tname] = 0
+                first.setdefault(o["i"], []).append(tname)
+            uses[tname] += 1
+    bfree = {b: (0.0, []) for b in range(8)}
+    bmap, held, late = {}, {}, {}
+    ready = {}
+    avail = [0.0] * N_
+    free = {}
+    order = {}
+    fin = [0.0] * N_
+    for o in ops:
+        if cnt[o["i"]] == 0:
+            ready.setdefault(o["q"], []).append(o["i"])
+    left = N_
+    while left:
+        best = None
+        for q, lst in ready.items():
+            if not lst:
+                continue
+            if q[0] == "R":
+                cand = (avail[lst[0]], q, lst[0])
+            else:
+                fr = free.get(q, 0.0)
+                full_ = lst
+                if q == "P":
+                    if not bfree:
+                        lst = [i for i in lst if i not in first]
+                        if not lst:
+                            continue
+                    else:
+                        bt = min(v[0] for v in bfree.values())
+                        for i in lst:
+                            if i in first and avail[i] < bt:
+                                late[i] = bt
+                st = min(max(fr, avail[i], late.get(i, 0.0)) for i in lst)
+                c = [i for i in lst if max(fr, avail[i], late.get(i, 0.0)) <= st + 0.02]
+                cand = (st, q, max(c, key=lambda i: pri[i]))
+            if best is None or cand[0] < best[0]:
+                best = cand
+        if best is None:
+            pg["fin"] = 1e6
+            return
+        st, q, i = best
+        ready[q].remove(i)
+        late.clear()
+        o = ops[i]
+        o["dyn"] = set()
+        for tname in first.get(i, ()):
+            b = min(bfree, key=lambda b: bfree[b][0])
+            o["dyn"] |= set(bfree.pop(b)[1])
+            bmap[tname] = b
+            held[tname] = [0.0, []]
+        end = st + o["cost"]
+        free[q] = end
+        fin[i] = end + o["lat"]
+        order.setdefault(q, []).append(i)
+        left -= 1
+        for tname in o["tiles"]:
+            hd = held[tname]
+            hd[0] = max(hd[0], end + WAKE)
+            if q != "P":
+                hd[1].append(i)
+            uses[tname] -= 1
+            if uses[tname] == 0:
+                bfree[bmap[tname]] = (hd[0], hd[1])
+        for s in succ[i]:
+            cnt[s] -= 1
+            w = 0.0 if i in ops[s]["ord"] else WAKE
+            avail[s] = max(avail[s], fin[i] + w)
+            if cnt[s] == 0:
+                ready.setdefault(ops[s]["q"], []).append(s)
+        o["t0"], o["t1"] = st, end
+    pg["order"] = order
+    pg["bmap"].clear()
+    pg["bmap"].update(bmap)
+    pg["fin"] = max(fin)
+    pg["seq"] = sorted(range(N_), key=lambda i: (ops[i]["t0"], ops[i]["q"][0] != "R", i))
+
+
+def emit(pg, g, T):
+    ops = pg["ops"]
+    eng = {"V": g.vector, "S": g.scalar, "P": g.tensor, "G": g, "Y": g.sync}
+    pos, key, know = {}, {}, {}
+    for q, lst in pg["order"].items():
+        c = 0
+        for i in lst:
+            if ops[i]["sem"] is None:
+                c += 1
+                key[i], pos[i] = q, c
+            else:
+                key[i], pos[i] = ops[i]["sem"], ops[i]["val"]
+    qk = {}
+    done = {}
+    queues = {q: list(l) for q, l in pg["order"].items()}
+    state = {q: 0 for q in queues}
+    prog = True
+    tot = sum(len(l) for l in queues.values())
+    k = 0
+    while k < tot:
+        prog = False
+        for q in queues:
+            while state[q] < len(queues[q]):
+                i = queues[q][state[q]]
+                o = ops[i]
+                if o["dyn"]:
+                    o["dep"] |= o["dyn"]
+                if any(d not in done for d in o["dep"]) or (o["send"] is not None and o["send"] not in done):
+                    break
+                kn = qk.setdefault(q, {})
+                if q[0] != "R":
+                    need = {}
+                    for d in sorted(o["dep"], key=lambda d: -ops[d]["t1"]):
+                        if kn.get(key[d], 0) >= pos[d]:
+                            continue
+                        if need.get(key[d], 0) < pos[d]:
+                            need[key[d]] = pos[d]
+                    ds = [d for d in o["dep"] if need.get(key[d], 0) == pos[d]]
+                    for d in ds:
+                        for d2 in ds:
+                            if d2 != d and key[d] in need and key[d2] in need and key[d] != key[d2] and know[d2].get(key[d], 0) >= pos[d]:
+                                need.pop(key[d])
+                    for kk in sorted(need):
+                        eng[q].wait_ge(T.sem[kk], int(need[kk]))
+                    for d in o["dep"]:
+                        for kk, v in know[d].items():
+                            if kn.get(kk, 0) < v:
+                                kn[kk] = v
+                    ins = o["fn"](eng[q])
+                    if o["sem"] is None:
+                        ins.then_inc(T.sem[q], 1)
+                me = dict(kn)
+                if o["send"] is not None:
+                    me = dict(know[o["send"]])
+                    for kk in list(me):
+                        me.pop(kk)
+                me[key[i]] = max(me.get(key[i], 0), pos[i])
+                know[i] = me
+                done[i] = 1
+                state[q] += 1
+                k += 1
+                prog = True
+        if not prog:
+            raise ValueError("no order")
+    for q in "VSPG":
+        if pg["order"].get(q):
+            c = sum(1 for i in pg["order"][q] if ops[i]["sem"] is None)
+            if c:
+                g.wait_ge(T.sem[q], int(c))
+
+
+def build(T, topo, core, rank):
+    pg = new_prog()
+    def ap(r):
+        name, c0, c1, step, p0, p1, ps = r
+        t = T["b%d" % pg["bmap"][name]] if name in pg["bmap"] else T[name]
+        rows = slice(p0, p1) if ps == 1 else slice(p0, p1, ps)
+        cols = slice(c0, c1) if step == 1 else slice(c0, c1, step)
+        return t[rows, cols]
+
+    def cnt(r):
+        return (r[2] - r[1] + r[3] - 1) // r[3]
+
+    def two(*rs):
+        return all(r[0] in SCRATCH and SCRATCH[r[0]][2] in (b2, h2, u2) for r in rs)
+
+    def inap(x):
+        if x[0] == "ind":
+            return ap(x[1]).indirect(ap(x[2]))
+        return ap(x)
+
+    def regs(x):
+        return [x[1], x[2]] if x[0] == "ind" else [x]
+
+    def dcol(s):
+        return ap(s) if isinstance(s, tuple) else s
+
+    def vcost(e, c, ind):
+        return FIX["V"] + CY * max(64, e * (GC if ind else c)) + (0.03 if ind else 0)
+
+    def ts(out, in0, s1, op0, s2=None, op1=None):
+        ind = in0[0] == "ind"
+        sc = [s for s in (s1, s2) if isinstance(s, tuple)]
+        c = 0.5 if (not ind and two(out, in0)) else 1
+        if op1 is None:
+            fn = lambda e: e.tensor_scalar(ap(out), inap(in0), dcol(s1), None, op0)
+        else:
+            fn = lambda e: e.tensor_scalar(ap(out), inap(in0), dcol(s1), dcol(s2), op0, op1)
+        return add(pg, "V", vcost(cnt(out), c, ind), fn, regs(in0) + sc, [out], tag="ts " + out[0])
+
+    def tt(out, a, b, op):
+        ind = a[0] == "ind"
+        ps = any(r[0][0] == "b" and r[0][1:].isdigit() for r in (a, b) if r[0] != "ind")
+        return add(pg, "V", vcost(cnt(out), 1 if ps else 2, ind), lambda e: e.tensor_tensor(ap(out), inap(a), ap(b), op), regs(a) + [b], [out], tag="tt " + out[0])
+
+    def cp(out, a):
+        ind = a[0] == "ind"
+        return add(pg, "V", vcost(cnt(out), 0.5 if (not ind and two(out, a)) else 1, ind), lambda e: e.tensor_copy(ap(out), inap(a)), regs(a), [out], tag="cp " + out[0])
+
+    def scan(out, d0, d1, init, op0, op1):
+        return add(pg, "V", vcost(cnt(out), 0.5 if two(out, d0, d1) else 1, False), lambda e: e.tensor_tensor_scan(ap(out), ap(d0), ap(d1), init, op0, op1), [d0, d1], [out], tag="scan " + out[0])
+
+    def fill(out, c):
+        return add(pg, "V", vcost(cnt(out), 0.5 if two(out) else 1, False), lambda e: e.memset(ap(out), c), [], [out], tag="fill " + out[0])
+
+    def act(out, in_, func, bias=0.0, scale=1.0):
+        ind = in_[0] == "ind"
+        sc = [s for s in (bias, scale) if isinstance(s, tuple)]
+        return add(pg, "S", FIX["S"] + CY * max(64, cnt(out) * (GC if ind else 1)) + (0.04 if ind else 0),
+                   lambda e: e.activation(ap(out), inap(in_), func, bias=dcol(bias), scale=dcol(scale)), regs(in_) + sc, [out], tag="act " + out[0])
+
+    def pe(mms):
+        cost = 0.0
+        rd, wr = {}, {}
+        for out, l, r, s, e_ in mms:
+            k = 4 if SCRATCH[l[0]][2] == f4 else 1
+            cost += PEC * k * max(min(64, cnt(l)), cnt(r)) + 0.006
+            for x in (l, r):
+                y = rd.get(x[0])
+                rd[x[0]] = (x[0], min(x[1], y[1]) if y else x[1], max(x[2], y[2]) if y else x[2], 1, 0, 128, 1)
+            y = wr.get(out[0])
+            wr[out[0]] = (out[0], min(out[1], y[1]) if y else out[1], max(out[2], y[2]) if y else out[2], 1, 0, 128, 1)
+
+        def fn(e):
+            ins = None
+            for out, l, r, s, e_ in mms:
+                ins = e.matmul(ap(out), ap(l), ap(r), s, e_)
+            return ins
+        return add(pg, "P", cost + FIX["P"], fn, list(rd.values()), list(wr.values()), tag="pe " + mms[0][0][0])
+
+    def acc(out, *pairs):
+        return [(out, l, r, i == 0, i == len(pairs) - 1) for i, (l, r) in enumerate(pairs)]
+
+    def bank(h, w=n):
+        pg["rr"][0] += 1
+        return "b%d" % (99 + pg["rr"][0])
+
+    def load(name, out, src, q="Y"):
+        s = "ld_" + name
+        return add(pg, q, 0.1, lambda e: e.dma_start(ap(out), src).then_inc(T.sem[s], 16), [], [out], sem=s, val=16, lat=3.0, tag="load " + name)
+
+    nout = [0]
+
+    def store(dst, in_, q="Y"):
+        nout[0] += 16
+        return add(pg, q, 0.1, lambda e: e.dma_start(dst, ap(in_)).then_inc(T.sem["out"], 16), [in_], [], sem="out", val=nout[0], lat=2.5, tag="store")
+
+    dst = T.cores[(rank + 1) % 4]
+    rid, pid, _se = topo.addr(dst)
+    mask = sum(1 << e for e in topo.engines(core, dst))
+    neng = len(topo.engines(core, dst))
+    nls = [0]
+
+    def send(kind, t, h, out, in_):
+        s = "r%s_%d_%d" % (kind, t, h)
+        nls[0] += neng
+        i = add(pg, "G", 0.4, lambda e: e.remote_dma(ap(out), ap(in_), T.sem[s], T.sem["ls"], pid, rid, mask), [in_], [], sem="ls", val=nls[0], lat=LNK, tag="send " + s)
+        j = add(pg, "R" + s, 0.0, None, [], [out], sem=s, val=neng)
+        pg["ops"][j]["send"] = i
+
+    sm = lambda name, h, w=8, x=0, k=8: ref(name, h * w + x, h * w + x + k)
+    tl = lambda name, h: ref(name, h * n, h * n + n)
+    full = lambda name: ref(name, 0, SCRATCH[name][1][1])
+
+    load("wt", ref("WT", 0, 1), T.wt[:, :])
+    load("kap", ref("WT", 1, 2), T.kap[:, :])
+    fill(full("VZ"), 0)
+    load("v0", ref("VZ", 0, 256, 1, 0, 128, 16), T.v0[:, :])
+    load("d0", ref("VZ", 256, 512, 1, 0, 128, 16), T.d0[:, :])
+    load("px0", ref("PX", 0, 2048), T.px[:, 0:2048])
+    load("px1", ref("PX", 2048, 4096), T.px[:, 2048:4096])
+    for h in (1, 0):
+        load("z%d" % h, ref("XZ", h * XW + 32, h * XW + 32 + n), T.z0[:, h * n:h * n + n])
+    load("f0", full("FI"), T.f0[:, :])
+    load("vw0", ref("VW", 0, 1024), T.vw[:, 0:1024])
+    load("vw1", ref("VW", 1024, 2048), T.vw[:, 1024:2048])
+
+    def sel(out, in_, pat, cmp, fillv, base, cm):
+        return add(pg, "G", 0.2 + 2 * CY * cnt(out), lambda e: e.affine_select(ap(out), ap(in_), pat, cmp, fillv, base, cm), [in_], [out], tag="sel")
+
+    def iota(out, pat, base, cm, small=False):
+        if small:
+            fn = lambda e: e.iota(ap(out), pat, base, cm, allow_small_or_imprecise_dtypes=True)
+        else:
+            fn = lambda e: e.iota(ap(out), pat, base, cm)
+        return add(pg, "G", 0.2 + 2 * CY * cnt(out), fn, [], [out], tag="iota")
+
+    iota0 = lambda out: iota(out, [[0, cnt(out)]], 0, 0, True)
+    fill(full("ONE"), 1.0)
+    sel(full("G8"), full("ONE"), [[1, 128]], A.is_ge, 0.0, 0, -16)
+    sel(full("G8"), full("G8"), [[-1, 128]], A.is_ge, 0.0, 15, 16)
+    sel(full("If"), full("ONE"), [[-1, 128]], A.is_equal, 0.0, 0, 1)
+    iota(ref("PI", 0, 1), [[0, 1]], 0, 1)
+    iota(full("IJ"), [[1, 16]], 0, 0, True)
+    iota(full("CMI"), [[16, 8]], 0, 0, True)
+    iota(full("KC"), [[0, 8], [1, 16]], 0, 0, True)
+    g8 = ref("G8", 0, 128, 1, 0, 8)
+    bk = bank(0)
+    pe([(ref(bk, 0, 128), g8, g8, True, True)])
+    cp(full("BO"), ref(bk, 0, 128))
+    cp(full("BOh"), full("BO"))
+    cp(full("Ib"), full("If"))
+    cp(full("Ih"), full("If"))
+    act(full("Inb"), full("If"), F.Copy, 0.0, -1.0)
+    act(full("Ihalf"), full("If"), F.Copy, 0.0, 0.5)
+    act(full("I16b"), full("If"), F.Copy, 0.0, 16.0)
+    ts(ref("PI", 16, 17), ref("PI", 0, 1), 15, A.bitwise_and)
+    ts(ref("PI", 24, 25), ref("PI", 0, 1), 1, A.bitwise_and)
+    pm, sg, sgn, pmh = ref("PC", 0, 1), ref("PC", 4, 5), ref("PC", 8, 9), ref("PC", 12, 13)
+    ts(sgn, ref("PI", 24, 25), -2.0, A.mult, 1.0 + n, A.add)
+    ts(pmh, ref("PI", 16, 17), -7.5, A.add)
+    cp(pm, ref("PI", 16, 17))
+    ts(sg, ref("PI", 24, 25), -2.0, A.mult, 1.0, A.add)
+    cp(ref("WTf", 0, 2), full("WT"))
+    wcol, kcol = ref("WTf", 0, 1), ref("WTf", 1, 2)
+    act(full("WB"), full("BO"), F.Copy, 0.0, wcol)
+    fill(full("Bh"), 0.0)
+    cp(ref("Bh", 15, 143, 16), ref("BO", 0, 128, 16))
+    fill(full("CLB"), -65536.0)
+    HB = ref("CLB", 0, 1)
+    act(full("WBs"), full("WB"), F.Copy, 0.0, 1.0 / 4096)
+    act(full("I4kn"), full("If"), F.Copy, 0.0, -4096.0)
+    fill(ref("CH", 0, 128, 1, 0, 64), -0.5 / 64)
+    fill(ref("CH", 0, 128, 1, 64, 128), 2.0 ** -19)
+    ts(full("B32"), ref("BO", 0, 128, 16), 32.0, A.mult)
+    ts(full("Bm16"), ref("BO", 0, 128, 16), -16.0, A.mult)
+    ts(full("OJ"), full("IJ"), pm, A.is_equal, 613.0, A.mult)
+    ts(full("OK"), full("IJ"), pm, A.is_equal)
+    for j in range(16):
+        ts(ref("SJ", 128 * j, 128 * j + 128), full("BOh"), ref("OJ", j, j + 1), A.mult)
+    for j in range(16):
+        act(ref("SJb", 128 * j, 128 * j + 128), full("BO"), F.Copy, 0.0, ref("OK", j, j + 1))
+    ts(ref("CM", 0, 8), full("CMI"), pm, A.add)
+    ts(ref("CM", 8, 16), full("CMI"), pm, A.add)
+    ts(ref("CM", 16, 24), ref("CM", 0, 8), float(2 * n), A.add)
+    ts(ref("CM", 24, 32), ref("CM", 0, 8), float(3 * n), A.add)
+    iota(ref("CON", 56, 72), [[0, 16]], -100, 0, True)
+    for h in range(2):
+        ts(sm("CMm", h), ref("CM", 0, 8), float(n * h), A.add)
+    consts = (-9, -4096, 2048, -100, 1, 100)
+    for i, c in enumerate(consts):
+        iota(ref("CON", 8 * i, 8 * i + 8), [[0, 8]], c, 0, True)
+    con = lambda c: ref("CON", 8 * consts.index(int(c)), 8 * consts.index(int(c)) + 8)
+    ts(full("BO613"), full("BOh"), 613.0, A.mult)
+    for nm, c in (("In", float(n)), ("I2n", float(2 * n)), ("I8k", 8192.0), ("Im100", -100.0), ("Ip100", 100.0), ("I8kn", -8192.0), ("Imh", -0.5), ("I7h", 7.5)):
+        act(full(nm), full("If"), F.Copy, 0.0, c)
+    act(full("G0"), full("If"), F.Copy, 0.0, sg)
+    act(full("Gn"), full("If"), F.Copy, 0.0, sgn)
+    act(full("BP"), ref("BO", 0, 128, 16), F.Copy, 0.0, -1048576.0)
+    act(ref("Sb", 0, 128, 2), ref("If", 1, 128, 2), F.Copy)
+    act(ref("Sb", 1, 128, 2), ref("If", 0, 128, 2), F.Copy)
+    act(full("Sb100"), full("Sb"), F.Copy, 0.0, 100.0)
+    act(full("I4k"), full("If"), F.Copy, 0.0, 4096.0)
+    fill(full("ON"), 1.0)
+    fill(full("CQ"), -0.25 / 128)
+    iota(full("MK"), [[0, 16 * n]], 1, 0, True)
+    sel(full("MK"), full("MK"), [[0, n], [1, 16]], A.not_equal, 0.0, 0, 0)
+    iota(full("MF"), [[0, n]], 1, 0, True)
+    sel(full("MF"), full("MF"), [[0, n // 16], [1, 16]], A.not_equal, 0.0, 0, 0)
+    iota(full("RST"), [[0, 128]], 0, 0, True)
+    sel(full("RST"), full("RST"), [[0, 8], [1, 16]], A.not_equal, 1048576.0, 0, 0)
+    fill(full("QS"), 0.0)
+    fill(full("C256"), 256.0)
+    iota(full("VS"), [[0, 2 * n]], 0, 0, True)
+    iota(full("SP"), [[0, 2 * n]], 0, 0, True)
+    for k in range(8):
+        iota0(ref("ZB", k * (32 + n) + 24, k * (32 + n) + 32))
+
+    def ots(out, tile, base="Bh", first=(), last=()):
+        prs = list(first)
+        for j in range(16):
+            prs.append((ref(base, 15 - j, 143 - j), ref(tile[0], tile[1] + j, tile[2], 16)))
+        return acc(out, *(prs + list(last)))
+
+    def spread(out, src):
+        return [(ref(out[0], out[1] + j, out[2], 16), ref("SJ", 128 * j, 128 * j + 128), src, True, True) for j in range(16)]
+
+    ts(ref("VZi", 0, 256), ref("VZ", 0, 256), 4032, A.bitwise_and)
+    cp(ref("VZh", 0, 256), ref("VZi", 0, 256))
+    ts(ref("VZi", 256, 512), ref("VZ", 0, 256), 63, A.bitwise_and)
+    cp(ref("VZh", 256, 512), ref("VZi", 256, 512))
+    cp(ref("VZh", 512, 768), ref("VZ", 256, 512))
+
+    def s16(c0):
+        return [(ref("Bh", 15 - j, 143 - j), ref("VZh", c0 + j, c0 + 256, 16)) for j in range(16)]
+    b6, b5 = bank(0), bank(0)
+    pe(acc(ref(b6, 0, 16), *(s16(0) + s16(256))))
+    pe(acc(ref(b5, 0, 16), *s16(512)))
+    for h in (1, 0):
+        ts(ref("VH", 8 * h, 8 * h + 8), ref(b6, 8 * h, 8 * h + 8), -2048.0, A.add)
+        fill(ref("XZ", h * XW, h * XW + 16), 0.0)
+        ts(ref("XZ", h * XW + 16, h * XW + 24), ref(b5, 8 * h, 8 * h + 8), 1.0, A.add)
+        cp(ref("W", h * WW + n, h * WW + 2 * n), ref("FI", h * n, h * n + n))
+    for c in range(2):
+        x = ref("VW", 1024 * c, 1024 * c + 1024)
+        it = ref("IT", 1024 * c, 1024 * c + 1024)
+        ts(it, x, 4095, A.bitwise_and)
+        cp(ref("VI", 1024 * c, 1024 * c + 1024), it)
+        ts(x, x, 12, A.arith_shift_right)
+        cp(ref("VI", 2048 + 1024 * c, 3072 + 1024 * c), x)
+
+    def tiles(t, h):
+        k = 2 * t + h
+        x0, w0 = k * XW, k * WW
+        return {"cnt": lambda j: ref("XZ", x0 + 8 * j, x0 + 8 * j + 8), "z": ref("XZ", x0 + 32, x0 + 32 + n), "x": ref("XZ", x0 + 32 + n, x0 + 32 + 2 * n),
+                "hz": ref("XZ", x0 + 32 + 2 * n, x0 + 32 + 3 * n), "xz": ref("XZ", x0 + 32, x0 + 32 + 2 * n), "xzh": ref("XZ", x0 + 32, x0 + 32 + 3 * n),
+                "hd": ref("W", w0, w0 + n), "f": ref("W", w0 + n, w0 + 2 * n), "e": ref("W", w0 + 2 * n, w0 + 3 * n), "c": ref("W", w0 + 3 * n, w0 + 4 * n),
+                "w2": ref("W", w0, w0 + 2 * n), "w3": ref("W", w0, w0 + 3 * n), "w4": ref("W", w0, w0 + 4 * n), "vh": ref("VH", 8 * k, 8 * k + 8),
+                "land": ref("XZ", x0, x0 + 32 + n), "zb": ref("ZB", k * (32 + n), (k + 1) * (32 + n)), "zf": ref("ZB", k * (32 + n) + 32, (k + 1) * (32 + n)),
+                "zc": ref("ZB", k * (32 + n), k * (32 + n) + 24), "fb": ref("FB", k * n, k * n + n), "vb": ref("VB", 8 * k, 8 * k + 8)}
+
+    px, views = full("PX"), ref("VI", 0, 4096)
+    vks = {}
+
+    def mark(name, h):
+        pg["st"] = name + str(h)
+
+    def front(t, h):
+        mark("fr", h)
+        L = tiles(t, h)
+        otl = sm("OTL", h)
+        ts(otl, L["vh"], 2048.0, A.add)
+        act(L["x"], ("ind", px, otl), F.Copy)
+        act(L["e"], ("ind", views, otl), F.Copy)
+        bk = bank(h)
+        vk = ref(bank(h), 0, n)
+        vks[h] = vk
+        dx = ref(bk, 0, n)
+        pe(acc(dx, (full("Ib"), L["x"]), (full("Inb"), L["z"])))
+        y = ref(bank(h), 0, n)
+        pe(acc(y, (full("WBs"), L["z"]), (full("CH"), full("ON"))))
+        act(tl("AB", h), dx, F.Abs)
+        ts(tl("IND", h), tl("AB", h), 72.0, A.is_le)
+        pe([(vk, full("BO613"), full("C256"), True, False)]
+           + [(ref(vk[0], j, n, 16), ref("SJ", 128 * j, 128 * j + 128), L["vh"], False, j == 15) for j in range(16)])
+        ct = ref(bank(h), 0, 8)
+        pe(ots(ct, tl("IND", h), "Bh", [(full("Ib"), con(-9.0))], [(full("Inb"), L["cnt"](1))]))
+        lk = sm("LK", h)
+        ts(lk, ct, -0.5, A.is_ge)
+        b = bank(h)
+        pe([(ref(b, 0, 16), full("Ih"), ref("CM", 0, 16), True, False), (ref(b, 0, 8), full("In"), lk, False, False), (ref(b, 8, 16), full("I2n"), lk, False, True)]
+           + acc(ref(b, 16, 24), (full("Ih"), L["vh"]), (full("Ib"), con(-4096.0)), (full("I8k"), lk)))
+        cp(sm("LSL", h, 16, 0, 16), ref(b, 0, 16))
+        act(ref("VS", h * n, h * n + n, 16), ref(b, 16, 24), F.Relu, 0.0, 613.0)
+        q0 = h * 16 * n
+        mark("qx", h)
+        ts(ref("QS", 0, 16 * n, 16), ("ind", L["xz"], sm("LSL", h, 16)), -512.0, A.add)
+        scan(ref("QX", q0, q0 + 16 * n), full("MK"), full("QS"), 0.0, A.mult, A.add)
+        a, c = tl("HI1", h), tl("HI2", h)
+        mark("ha", h)
+        act(tl("T2", h), y, F.Identity, MAGIC)
+        act(tl("FL", h), tl("T2", h), F.Identity, -MAGIC)
+        um = ref(y[0], n, 2 * n)
+        pe(acc(um, (full("WB"), L["z"]), (full("I4kn"), tl("FL", h))))
+        act(tl("T2", h), um, F.Identity, HB, kcol)
+        cp(a, tl("T2", h))
+        ts(c, a, 5, A.arith_shift_right)
+        tt(a, c, vk, A.add)
+        ts(c, a, 4095, A.bitwise_and)
+        cp(L["hd"], c)
+        mark("dd", h)
+        scan(tl("VR", h), full("MF"), tl("VS", h), 0.0, A.mult, A.add)
+        tt(tl("EQ", h), tl("VR", h), vk, A.is_equal)
+        tt(ref("EQ2", h * n + 16, h * n + n), ref("VR", h * n, h * n + n - 16), ref(vk[0], 16, n), A.is_equal)
+        for i in range(2):
+            mark("he"[i], h)
+            he = ref("HE", (2 * h + i) * n, (2 * h + i + 1) * n)
+            act(he, ("ind", L["w2"] if i == 0 else L["w3"], sm("LSL", h, 16, 8 * i)), F.Copy)
+            cp(ref("HEL", (2 * h + i) * n, (2 * h + i + 1) * n), he)
+
+    def dedupe(t, h):
+        mark("dd", h)
+        L = tiles(t, h)
+        lk = sm("LK", h)
+        du = ref(bank(h), 0, 8)
+        m3 = acc(du, *([(full("Ib"), con(100.0)), (full("Im100"), lk)] + [(ref("LTJ", 128 * j, 128 * j + 128), ref("EQ", h * n + j, h * n + n, 16)) for j in range(16)]))
+        m3[-1] = m3[-1][:4] + (False,)
+        pe(m3 + [(ref(du[0], 1, 8, 2), ref("Bh", 15 - j, 143 - j), ref("EQ2", h * n + 16 + j, h * n + n, 32), False, j == 15) for j in range(16)])
+        ts(sm("W0", h), du, 0.5, A.is_lt)
+        vd = ref(bank(h), 0, 8)
+        pe(acc(vd, (full("Ib"), con(2048.0)), (full("Ih"), sm("CMm", h)), (full("I8kn"), sm("W0", h))))
+        tt(sm("O2", h), L["vh"], vd, A.max)
+        ts(sm("OFF", h), sm("O2", h), 2048.0, A.add)
+
+    def early(t, h):
+        mark("ea", h)
+        L = tiles(t, h)
+        lk, d1, ov = sm("LK", h), sm("D1", h), sm("OV", h)
+        Ih, Ib, Sb, Ip, Im = full("Ih"), full("Ib"), full("Sb"), full("Ip100"), full("Im100")
+        hz = ref(bank(h), 0, n)
+        pe(acc(hz, (full("Ihalf"), L["x"]), (full("Ihalf"), L["z"]), (full("CQ"), full("ON"))))
+        act(tl("T1", h), hz, F.Identity, MAGIC)
+        act(L["hz"], tl("T1", h), F.Identity, -MAGIC)
+        dp = ref(bank(h), 0, 8)
+        pe(acc(dp, (Ib, L["cnt"](2)), (Im, lk)))
+        act(d1, dp, F.Relu)
+        po = ref(bank(h), 0, 8)
+        pe(acc(po, (Ib, d1), (full("Sb100"), lk)))
+        ts(ov, po, 101.5, A.is_ge)
+        b = bank(h)
+        pe([(ref(b, 0, 24), Ih, ref("CM", 8, 32), True, False)]
+           + [(ref(b, c, c + 8), full(m), v, False, c == 16) for c, m, v in ((0, "I2n", lk), (0, "I2n", ov), (0, "G0", ov), (8, "In", lk), (8, "Gn", ov), (16, "G0", ov))])
+        cp(sm("TLL", h, 24, 0, 24), ref(b, 0, 24))
+        act(L["zf"], ("ind", L["xzh"], sm("TLL", h, 24)), F.Copy)
+        b = bank(h)
+        pe([(ref(b, 0, 16), Ib, ref(L["cnt"](0)[0], L["cnt"](0)[1], L["cnt"](1)[2]), True, False), (ref(b, 0, 8), Ib, lk, False, False), (ref(b, 8, 16), full("Inb"), lk, False, True)])
+        ap_ = sm("P1", h, 16, 0, 16)
+        act(ap_, ref(b, 0, 16), F.Abs)
+        act(sm("O2V", h, 16), ov, F.Copy)
+        act(sm("O2V", h, 16, 8), ov, F.Copy)
+        oo = sm("O2V", h, 16, 0, 16)
+        b = bank(h)
+        pe(acc(ref(b, 0, 16), (Ib, ap_), (Im, oo)) + acc(ref(b, 16, 32), (Sb, ap_), (Ip, oo), (Ib, ref("CON", 56, 72))) + acc(ref(b, 32, 40), (Ib, d1), (Im, ov)))
+        ra = lambda j: sm("RA", h, 40, 8 * j)
+        ra2 = lambda j: sm("RA", h, 40, 16 * j, 16)
+        act(sm("RA", h, 40, 0, 40), ref(b, 0, 40), F.Relu)
+        b = bank(h)
+        if t < NT - 1:
+            pe(acc(ref(b, 0, 16), (Ib, ra2(0)), (Ib, ra2(1))) + acc(ref(b, 16, 24), (Ib, ra(4)), (Ib, con(1.0))))
+            act(L["zc"], ref(b, 0, 24), F.Copy)
+            send("z", t + 1, h, tiles(t + 1, h)["land"], L["zb"])
+        else:
+            i16 = full("I16b")
+            pe(acc(ref(b, 0, 8), (i16, ra(0)), (i16, ra(2)), (Ib, ra(4))))
+            act(sm("YC", h), ref(b, 0, 8), F.Copy)
+            b = ref(bank(h), 0, n)
+            pe([(ref(b[0], j, n, 16), ref("SJb", 128 * j, 128 * j + 128), sm("YC", h), True, True) for j in range(16)])
+            act(ref("YU", h * n, h * n + n), b, F.Copy)
+            store(T.yc[:, h * n:h * n + n], ref("YU", h * n, h * n + n, 1, 0, 128, 16))
+            act(ref("YU", 1024 + h * n, 1024 + h * n + n), L["zf"], F.Copy)
+            store(T.yz[:, h * n:h * n + n], ref("YU", 1024 + h * n, 1024 + h * n + n))
+        mark("kk", h)
+        cb = ref(bank(h), 0, 8)
+        pe(acc(cb, (full("Imh"), lk), (full("I7h"), ov)))
+        act(sm("CB", h), cb, F.Identity, t - 7.0)
+        y = ref(bank(h), 0, n)
+        pe([(y, full("BO"), L["zf"], True, False)]
+           + [(ref(y[0], j, n, 16), ref("SJb", 128 * j, 128 * j + 128), sm("CB", h), False, j == 15) for j in range(16)])
+        act(tl("KT", h), y, F.Identity, MAGIC, 1.0 / 16)
+        act(tl("KU", h), tl("KT", h), F.Identity, -MAGIC)
+        act(tl("KT", h), tl("KU", h), F.Identity, pmh, 16.0)
+        tt(tl("OHL", h), tl("KT", h), y, A.is_equal)
+
+    def bulk(t, h):
+        mark("hb", h)
+        L = tiles(t, h)
+        q0, e0 = h * 16 * n, h * 2 * n
+        key = tl("KEY", h)
+        bh_, be_ = bank(h), bank(h)
+
+        def part(G, D, R, l0, a, b, fused):
+            g_, d_, r_ = ref(G, q0 + 16 * a, q0 + 16 * b), ref(D, q0 + 16 * a, q0 + 16 * b), ref(R, q0 + 16 * a, q0 + 16 * b)
+            off = ref("HEL", l0 + a, l0 + b)
+            qx = ref("QX", q0 + 16 * a, q0 + 16 * b)
+            if fused:
+                tt(d_, ("ind", px, off), qx, A.subtract)
+            else:
+                act(g_, ("ind", px, off), F.Copy)
+                scan(d_, g_, qx, 600.0, A.min, A.subtract)
+            ts(r_, d_, 512.0, A.max)
+
+        def sums(out, D, R, first):
+            mm = []
+            if first:
+                mm.append((out, full("Ib"), full("KC"), True, False))
+            for k in range(16):
+                o = ref(out[0], out[1] + k, out[2], 16)
+                mm.append((o, ref(R, q0 + k, q0 + 16 * n, 16), full("B32"), not first, False))
+                mm.append((o, ref(D, q0 + k, q0 + 16 * n, 16), full("Bm16"), False, (not first) or k == 15))
+            if len(mm) > 30:
+                pe(mm[:17])
+                pe(mm[17:])
+            else:
+                pe(mm)
+        ph, pd = ref(bh_, 0, n), ref(be_, 0, n)
+        part("GH", "DH", "RH", e0, 0, n // 2, False)
+        part("GH", "DH", "RH", e0, n // 2, n, False)
+        sums(ph, "DH", "RH", True)
+        act(key, ph, F.Copy)
+        he1, he2 = ref("HE", e0, e0 + n), ref("HE", e0 + n, e0 + 2 * n)
+        mark("hm", h)
+        tt(tl("HME", h), he1, he2, A.subtract)
+        mark("km", h)
+        scan(tl("PM", h), full("RST"), key, 0.0, A.add, A.min)
+        mx = ref(bank(h), 0, 8)
+        pe([(mx, tl("OHL", h), full("BP"), True, True)])
+        tt(ref("SP", h * n, h * n + n, 16), ref("PM", h * n + 15, h * n + n, 16), mx, A.add)
+        scan(tl("MN", h), full("MF"), tl("SP", h), 0.0, A.mult, A.add)
+        tt(tl("OHT", h), tl("MN", h), ph, A.is_equal)
+        mark("eb", h)
+        if NE > 0:
+            part("GE", "DE", "RE", e0 + n, 0, NE, False)
+        if NE < n:
+            part("GE", "DE", "RE", e0 + n, NE, n, True)
+        sums(pd, "DE", "RE", False)
+        mark("cc", h)
+        tt(tl("MT", h), key, pd, A.is_lt)
+        mk = ref(bank(h), 0, n)
+        pe([(mk, tl("MT", h), full("Ib"), True, True)])
+        tt(tl("MM", h), tl("HME", h), mk, A.mult)
+        tt(L["c"], tl("MM", h), he2, A.add)
+        act(tl("CF", h), ("ind", L["w4"], sm("TLL", h, 24, 16)), F.Identity, -2048.0)
+        oc = ref(bank(h), 0, n)
+        pe([(oc, tl("OHT", h), full("Ib"), True, False), (oc, full("Ib"), tl("OHL", h), False, True)])
+        tt(tl("PP", h), tl("CF", h), oc, A.mult)
+        vo = ref(bank(h), 0, n)
+        if t < NT - 1:
+            vo = ref(vo[0], 0, 8)
+            pe(ots(vo, tl("PP", h)))
+            cp(L["vb"], vo)
+            send("v", t + 1, h, tiles(t + 1, h)["vh"], L["vb"])
+        else:
+            pe(acc(vo, (full("BOh"), tl("PP", h))))
+            act(ref("YU", 512 + h * n, 512 + h * n + n), vo, F.Identity, 2048.0)
+            store(T.yv[:, h * n:h * n + n], ref("YU", 512 + h * n, 512 + h * n + n, 1, 0, 128, 16))
+        mark("ff", h)
+        act(L["fb"], ("ind", L["w4"], sm("TLL", h, 24, 8)), F.Copy)
+        if t < NT - 1:
+            send("f", t + 1, h, tiles(t + 1, h)["f"], L["fb"])
+        else:
+            store(T.yf[:, h * n:h * n + n], L["fb"])
+
+    def scatter(t, h):
+        mark("sc", h)
+        L = tiles(t, h)
+        c0 = L["c"][1]
+        for c in range(3, -1, -1):
+            add(pg, "V", 0.18, lambda e, c=c: e.tensor_copy(ap(full("VI")).indirect(ap(ref("OFF", h * 8 + 2 * c, h * 8 + 2 * c + 2))), ap(ref("W", c0 + 32 * c, c0 + 32 * c + 32))),
+                [ref("OFF", h * 8 + 2 * c, h * 8 + 2 * c + 2), ref("W", c0 + 32 * c, c0 + 32 * c + 32)], [full("VI")], tag="scatter")
+
+    front(0, 1)
+    sel(full("BOg"), full("BO"), [[1, 128]], A.is_gt, 0.0, 0, -1)
+    iota(full("LTJ"), [[0, 2048]], 0, 0, True)
+    for j in range(16):
+        act(ref("LTJ", 128 * j + j, 128 * j + 128, 16), ref("BOg", j, 128, 16), F.Copy)
+    fill(ref("VI", 4096, 4096 + 2 * n), 0.0)
+    front(0, 0)
+    for t in range(NT):
+        for h in (1, 0):
+            if t > 0 and h == 1:
+                pass
+            early(t, h)
+            dedupe(t, h)
+            bulk(t, h)
+            scatter(t, h)
+            if t < NT - 1 and h == 1:
+                pass
+        if t < NT - 1:
+            front(t + 1, 1)
+            front(t + 1, 0)
+    pg["st"] = ""
+    for c in (3, 0, 1, 2):
+        a, b = 512 * c, 512 * c + 512
+        if c == 3:
+            yb = ref(bank(0), 0, 512)
+            pe(acc(yb, (full("If"), ref("VI", a, b)), (full("I4k"), ref("VI", 2048 + a, 2048 + b))))
+            act(ref("YT", a, b), yb, F.Copy)
+            store(T.yw[:, a:b], ref("YT", a, b))
+            continue
+        act(ref("YT", a, b), ref("VI", 2048 + a, 2048 + b), F.Copy, 0.0, 4096.0)
+        tt(ref("YT", a, b), ref("YT", a, b), ref("VI", a, b), A.add)
+        store(T.yw[:, a:b], ref("YT", a, b))
+    pg["nls"], pg["nout"] = nls[0], nout[0]
+    return pg
+
+
+def rank_program(g, core, T, topo):
+    rank = T.rank_of(core)
+    if rank is None:
+        return
+    pg = build(T, topo, core, rank)
+    schedule(pg)
+    emit(pg, g, T)
+    g.wait_ge(T.sem["ls"], int(pg["nls"]))
+    g.wait_ge(T.sem["out"], int(pg["nout"]))

@@ -7,67 +7,76 @@ F = ActivationFunctionType
 n = 128
 NT = 5
 XW = 32 + 3 * n
-WW = 4 * n
+WW = 3 * n
 MAGIC = 12582912.0
-PRI = {'fr0': 3.4, 'fr1': 10.5, 'qx0': -12.4, 'qx1': -8.0, 'ha0': 6.0, 'ha1': -1.7, 'dd0': -0.6, 'dd1': 4.5, 'h0': -4.1, 'h1': 0.6, 'e0': -9.4, 'e1': 3.2, 'ea0': -3.8, 'ea1': 1.7, 'kk0': -2.7,
-       'kk1': 11.4, 'hb0': -6.6, 'hb1': -5.1, 'hm0': 5.8, 'hm1': -7.9, 'km0': -5.6, 'km1': -1.7, 'eb0': 12.0, 'eb1': -5.3, 'cc0': 3.1, 'cc1': 13.2, 'ff0': 1.5, 'ff1': 11.6, 'sc0': -18.1, 'sc1': -12.0}
-NE = 64
+OFS = 8192.0
+HC = 262000
+NOH = 4112
+PARTS = (((0, 64, "S"), (64, 128, "S")), ((0, 64, "S"), (64, 128, "S")))
+CHUNKS = (((0, 64), (64, 128)), ((0, 64), (64, 128)))
+ONV = ("cf", "key")
+SPLIT = 8
 f4, b2, h2, i4, u2 = "float32", "bfloat16", "float16", "int32", "uint16"
 
 SCRATCH = {
-    "PX": ("sbuf", [128, 4096], b2), "VI": ("sbuf", [128, 4096 + 2 * n], f4), "VW": ("sbuf", [128, 2048], i4),
+    "PX": ("sbuf", [128, 4096], b2), "VI": ("sbuf", [128, 4096 + 32], f4), "VW": ("sbuf", [128, 2048], i4),
     "IT": ("sbuf", [128, 2048], i4), "YT": ("sbuf", [128, 2048], f4), "YU": ("sbuf", [128, 2048], f4),
-    "XZ": ("sbuf", [128, 10 * XW], b2), "W": ("sbuf", [128, 10 * WW], f4), "VH": ("sbuf", [128, 10 * 8], h2),
-    "ZB": ("sbuf", [128, 10 * (32 + n)], b2), "FB": ("sbuf", [128, 10 * n], f4), "VB": ("sbuf", [128, 10 * 8], h2),
-    "HE": ("sbuf", [128, 4 * n], f4), "HEL": ("sbuf", [128, 4 * n], u2), "QS": ("sbuf", [128, 16 * n], h2), "QX": ("sbuf", [128, 32 * n], h2),
-    "GH": ("sbuf", [128, 32 * n], b2), "GE": ("sbuf", [128, 32 * n], b2), "DH": ("sbuf", [128, 32 * n], h2), "DE": ("sbuf", [128, 32 * n], h2),
-    "RH": ("sbuf", [128, 32 * n], h2), "RE": ("sbuf", [128, 32 * n], h2),
-    "OTL": ("sbuf", [128, 16], u2), "AB": ("sbuf", [128, 2 * n], b2), "IND": ("sbuf", [128, 2 * n], h2), "LK": ("sbuf", [128, 16], b2),
-    "LSL": ("sbuf", [128, 32], u2), "HI1": ("sbuf", [128, 2 * n], i4), "HI2": ("sbuf", [128, 2 * n], i4), "T1": ("sbuf", [128, 2 * n], f4),
-    "D1": ("sbuf", [128, 16], b2), "OV": ("sbuf", [128, 16], b2), "TLL": ("sbuf", [128, 48], u2), "P1": ("sbuf", [128, 32], b2), "RA": ("sbuf", [128, 80], b2),
-    "KT": ("sbuf", [128, 2 * n], f4), "KU": ("sbuf", [128, 2 * n], f4), "SP": ("sbuf", [128, 2 * n], f4), "BP": ("sbuf", [128, 8], b2), "CB": ("sbuf", [128, 16], b2), "SJb": ("sbuf", [128, 2048], b2), "OK": ("sbuf", [128, 16], f4), "CLB": ("sbuf", [128, 8], f4),
-    "WBs": ("sbuf", [128, 128], b2), "I4kn": ("sbuf", [128, 128], b2), "CH": ("sbuf", [128, 128], b2), "T2": ("sbuf", [128, 2 * n], f4), "FL": ("sbuf", [128, 2 * n], b2), "EQ2": ("sbuf", [128, 2 * n], h2), "OHL": ("sbuf", [128, 2 * n], b2),
-    "VS": ("sbuf", [128, 2 * n], f4), "VR": ("sbuf", [128, 2 * n], f4), "EQ": ("sbuf", [128, 2 * n], b2),
-    "W0": ("sbuf", [128, 16], b2), "O2": ("sbuf", [128, 16], f4), "OFF": ("sbuf", [128, 32], u2),
+    "W613": ("sbuf", [128, 4096 + 8], f4), "OHW": ("sbuf", [128, NOH], b2),
+    "XZ": ("sbuf", [128, 10 * XW], b2), "W": ("sbuf", [128, 10 * WW], f4), "VH": ("sbuf", [128, 10 * 8], u2),
+    "ZB": ("sbuf", [128, 8 * (32 + n)], b2), "FB": ("sbuf", [128, 10 * n], f4), "VB": ("sbuf", [128, 10 * 8], u2), "ZL": ("sbuf", [128, 2 * n], b2),
+    "E": ("sbuf", [128, 2 * n], f4), "HEL": ("sbuf", [128, 4 * n], u2), "QS": ("sbuf", [128, 16 * n], b2), "QX": ("sbuf", [128, 32 * n], b2),
+    "GH": ("sbuf", [128, 32 * n], b2), "GE": ("sbuf", [128, 32 * n], b2), "MH": ("sbuf", [128, 32 * n], b2), "ME": ("sbuf", [128, 32 * n], b2),
+    "IND": ("sbuf", [128, 2 * n], b2), "LK": ("sbuf", [128, 16], b2), "LSL": ("sbuf", [128, 16], u2),
+    "HI1": ("sbuf", [128, 2 * n], i4), "HI2": ("sbuf", [128, 2 * n], i4), "FL": ("sbuf", [128, 2 * n], h2),
+    "OV": ("sbuf", [128, 16], b2), "TLL": ("sbuf", [128, 32], u2), "RA": ("sbuf", [128, 48], b2), "KL": ("sbuf", [128, 16], u2), "OHL": ("sbuf", [128, 2 * n], b2),
+    "VF": ("sbuf", [128, 16], h2), "VN": ("sbuf", [128, 16], f4), "DL": ("sbuf", [128, 24], u2), "G1": ("sbuf", [128, 384], f4), "EQ": ("sbuf", [128, 384], b2),
+    "DS": ("sbuf", [128, 384], b2), "OFF": ("sbuf", [128, 16], u2),
     "HME": ("sbuf", [128, 2 * n], f4), "KEY": ("sbuf", [128, 2 * n], f4), "MT": ("sbuf", [128, 2 * n], b2), "MM": ("sbuf", [128, 2 * n], f4),
-    "PM": ("sbuf", [128, 2 * n], f4), "MN": ("sbuf", [128, 2 * n], f4), "OHT": ("sbuf", [128, 2 * n], b2), "CF": ("sbuf", [128, 2 * n], f4), "PP": ("sbuf", [128, 2 * n], h2),
-    "I16b": ("sbuf", [128, 128], b2), "I8k": ("sbuf", [128, 128], b2), "I8kn": ("sbuf", [128, 128], b2), "BO613": ("sbuf", [128, 128], h2), "C256": ("sbuf", [128, n], h2),
-    "If": ("sbuf", [128, 128], f4), "Ib": ("sbuf", [128, 128], b2), "Ih": ("sbuf", [128, 128], h2), "Inb": ("sbuf", [128, 128], b2), "Ihalf": ("sbuf", [128, 128], b2),
-    "Sb": ("sbuf", [128, 128], b2), "Sb100": ("sbuf", [128, 128], b2), "In": ("sbuf", [128, 128], b2), "I2n": ("sbuf", [128, 128], b2),
-    "Imh": ("sbuf", [128, 128], b2), "I7h": ("sbuf", [128, 128], b2), "I4k": ("sbuf", [128, 128], f4),
-    "Ip100": ("sbuf", [128, 128], b2), "Im100": ("sbuf", [128, 128], b2),
-    "Gn": ("sbuf", [128, 128], b2), "G0": ("sbuf", [128, 128], b2),
-    "ONE": ("sbuf", [128, 128], f4), "G8": ("sbuf", [128, 128], f4), "BO": ("sbuf", [128, 128], b2), "BOh": ("sbuf", [128, 128], h2), "BOg": ("sbuf", [128, 128], b2), "WB": ("sbuf", [128, 128], b2),
-    "Bh": ("sbuf", [128, 144], h2), "B32": ("sbuf", [128, 8], h2), "Bm16": ("sbuf", [128, 8], h2),
-    "SJ": ("sbuf", [128, 2048], h2), "LTJ": ("sbuf", [128, 2048], b2), "PI": ("sbuf", [128, 32], i4), "PC": ("sbuf", [128, 16], f4),
-    "OJ": ("sbuf", [128, 16], f4),  "IJ": ("sbuf", [128, 16], f4), "CMI": ("sbuf", [128, 8], f4), "CM": ("sbuf", [128, 32], h2), "CMm": ("sbuf", [128, 16], h2),
-    "CON": ("sbuf", [128, 80], b2), "O2V": ("sbuf", [128, 32], b2), "KC": ("sbuf", [128, 128], b2), "MK": ("sbuf", [128, 16 * n], b2), "MF": ("sbuf", [128, n], f4), "RST": ("sbuf", [128, 128], f4),
-    "CQ": ("sbuf", [128, 128], b2), "ON": ("sbuf", [128, 128], b2), "WT": ("sbuf", [128, 2], i4), "WTf": ("sbuf", [128, 8], f4),
-    "VZ": ("sbuf", [128, 512], i4), "VZi": ("sbuf", [128, 512], i4), "VZh": ("sbuf", [128, 768], h2), "FI": ("sbuf", [128, 256], i4), "YC": ("sbuf", [128, 16], b2),
+    "PM": ("sbuf", [128, 2 * n], f4), "OHT": ("sbuf", [128, 2 * n], b2), "CF": ("sbuf", [128, 2 * n], f4), "PP": ("sbuf", [128, 2 * n], h2),
+    "YC": ("sbuf", [128, 16], b2), "VZ": ("sbuf", [128, 512], i4), "VZh": ("sbuf", [128, 512], h2), "FI": ("sbuf", [128, 256], i4),
+    "ON": ("sbuf", [128, 144], b2), "BO": ("sbuf", [128, 128], b2), "B8": ("sbuf", [128, 144], b2), "Bh": ("sbuf", [128, 144], b2),
+    "B32": ("sbuf", [128, 8], b2), "Bm16": ("sbuf", [128, 8], b2), "WB": ("sbuf", [128, 128], b2), "CH": ("sbuf", [128, 128], b2), "CP": ("sbuf", [128, 128], b2),
+    "Sb": ("sbuf", [128, 128], b2), "Sb100": ("sbuf", [128, 128], b2), "MP": ("sbuf", [128, 128], b2), "DG": ("sbuf", [128, 128], b2), "G0": ("sbuf", [128, 128], b2),
+    "G256": ("sbuf", [128, 128], h2), "ZE": ("sbuf", [128, 128], b2),
+    "KC": ("sbuf", [128, 128], b2), "RST": ("sbuf", [128, 128], f4), "MK": ("sbuf", [128, 16 * n], b2), "D0": ("sbuf", [128, 384], b2),
+    "PI": ("sbuf", [128, 32], i4), "PC": ("sbuf", [128, 32], f4), "IJ": ("sbuf", [128, 16], f4), "CMI": ("sbuf", [128, 32], f4), "CM": ("sbuf", [128, 16], b2),
+    "CS": ("sbuf", [128, 24], b2), "CL": ("sbuf", [128, 32], u2), "WT": ("sbuf", [128, 2], i4), "WTf": ("sbuf", [128, 8], f4),
 }
+DIAG = {"Ib": (1.0, b2), "In": (-1.0, b2), "I2": (2.0, b2), "Ic": (0.00689697265625, b2), "Icn": (-0.00689697265625, b2), "Ihz": (0.5 - 2.0 ** -11, h2),
+        "I128": (128.0, b2), "I256": (256.0, b2), "Ip100": (100.0, b2), "Im100": (-100.0, b2), "I8k": (8192.0, b2), "I8kn": (-8192.0, b2), "I8200": (8200.0, h2),
+        "I4kn": (-4096.0, b2), "Ibig": (-262144.0, b2), "Ifl": (0.4375, b2), "I16": (16.0, b2)}
+for _k in DIAG:
+    SCRATCH[_k] = ("sbuf", [128, 128], DIAG[_k][1])
 for _b in range(8):
     SCRATCH["b%d" % _b] = ("psum", [128, 512], f4)
 LOADS = ["px0", "px1", "vw0", "vw1", "z0", "z1", "f0", "v0", "d0", "wt", "kap"]
 SEMAPHORES = ["V", "S", "P", "G", "out", "ls"] + ["ld_" + x for x in LOADS] + ["r%s_%d_%d" % (k, t, h) for k in "zfv" for t in range(1, NT) for h in range(2)]
+
+COSTS = ({"cy": 0.00083, "gather": 1.56, "wake": 0.10, "pe": 0.00055, "link": 1.9, "scat": 0.18},
+         {"cy": 0.00083, "gather": 1.1, "wake": 0.08, "pe": 0.00045, "link": 1.6, "scat": 0.12},
+         {"cy": 0.00108, "gather": 1.8, "wake": 0.15, "pe": 0.0006, "link": 2.5, "scat": 0.25})
+FIX = {"V": 0.03, "S": 0.04, "P": 0.03, "G": 0.05, "Y": 0.05}
+ROUNDS = 3000
+STAGGER = 7.0
 
 
 def ref(name, c0, c1, step=1, p0=0, p1=128, pstep=1):
     return (name, c0, c1, step, p0, p1, pstep)
 
 
-def new_prog():
-    return {"ops": [], "acc": {}, "rr": [0], "st": "", "bmap": {}}
+def is_psum(name):
+    return name[0] == "b" and name[1:].isdigit()
 
 
 def touch(pg, o, r, wr):
     name, c0, c1 = r[0], r[1], r[2]
     lst = pg["acc"].setdefault(name, [])
-    psum = name[0] == "b" and name[1:].isdigit()
+    psum = is_psum(name)
     ops = pg["ops"]
     keep = []
     for a in lst:
-        p, a0, a1, aw = a
-        over = a0 < c1 and c0 < a1
+        p, a0, a1, aw, st = a
+        over = a0 < c1 and c0 < a1 and not (st == r[3] and (a0 - c0) % st)
         if p != o["i"]:
             if psum:
                 if ops[p]["q"] != o["q"]:
@@ -76,209 +85,235 @@ def touch(pg, o, r, wr):
                     o["ord"].add(p)
             elif over and (wr or aw):
                 o["dep"].add(p)
-        if wr and a0 >= c0 and a1 <= c1 and p != o["i"] and not psum and r[3] == 1 and r[6] == 1:
+        if wr and a0 >= c0 and a1 <= c1 and p != o["i"] and not psum and r[3] == 1 and r[6] == 1 and r[4] == 0 and r[5] == 128:
             continue
         keep.append(a)
-    if psum and len(keep) > 24:
-        keep = keep[-24:]
-    keep.append((o["i"], c0, c1, wr))
+    keep.append((o["i"], c0, c1, wr, r[3]))
     pg["acc"][name] = keep
 
 
-def add(pg, q, cost, fn, rd, wr, sem=None, val=1, after=(), lat=0.0, tag=""):
-    o = {"i": len(pg["ops"]), "q": q, "cost": cost, "fn": fn, "dep": set(after), "ord": set(), "sem": sem, "val": val, "lat": lat, "send": None, "tag": tag, "st": pg["st"], "wake": WAKE}
+def add(pg, q, cost, fn, rd, wr, sem=None, val=1, lat=0.0, tag=""):
+    o = {"i": len(pg["ops"]), "q": q, "cost": cost, "fn": fn, "dep": set(), "ord": set(), "sem": sem, "val": val, "lat": lat, "send": None, "tag": tag, "st": pg["st"], "hop": pg["hop"]}
     pg["ops"].append(o)
     for r in rd:
         touch(pg, o, r, False)
     for r in wr:
         touch(pg, o, r, True)
-    o["tiles"] = sorted(set(r[0] for r in list(rd) + list(wr) if r[0][0] == "b" and r[0][1:].isdigit()))
-    o["dyn"] = set()
+    o["tiles"] = sorted(set(r[0] for r in list(rd) + list(wr) if is_psum(r[0])))
     return o["i"]
 
 
-WAKE = 0.10
-GC = 1.5
-PEC = 0.00055
-CY = 0.00083
-LNK = 1.6
-FIX = {"V": 0.03, "S": 0.04, "P": 0.03, "G": 0.05, "Y": 0.05}
+def place(key, pred, succ, q, cost, head):
+    cnt = [len(p) for p in pred]
+    ready = [(key[i], i) for i in range(len(key)) if cnt[i] == 0]
+    st = [0.0] * len(key)
+    S, E = {}, {}
+    while ready:
+        x = min(ready)
+        ready.remove(x)
+        i = x[1]
+        t = head[i]
+        for d, w in pred[i]:
+            x = st[d] + cost[d] + w
+            if x > t:
+                t = x
+        c = cost[i]
+        if c > 0:
+            s, e = S.setdefault(q[i], []), E.setdefault(q[i], [])
+            m = k = len(s)
+            while k > 0 and e[k - 1] > t:
+                k -= 1
+            while k < m and s[k] < t + c - 1e-9:
+                t = e[k]
+                k += 1
+            s.insert(k, t)
+            e.insert(k, t + c)
+        st[i] = t
+        for j, w in succ[i]:
+            cnt[j] -= 1
+            if cnt[j] == 0:
+                ready.append((key[j], j))
+    return st
 
 
-def schedule(pg):
+def replay(ops, seq, c, dyn, uses=None):
+    cost, lat, wake = c
+    fin = [0.0] * len(ops)
+    free, bmap, held = {}, {}, {}
+    bfree = {b: (0.0, []) for b in range(8)}
+    for i in seq:
+        o = ops[i]
+        q = o["q"]
+        st = free.get(q, 0.0)
+        for d in o["dep"]:
+            if fin[d] + wake > st:
+                st = fin[d] + wake
+        if o["send"] is not None:
+            st = max(st, fin[o["send"]])
+        if uses is None:
+            for d in dyn.get(i, ()):
+                if fin[d] + wake > st:
+                    st = fin[d] + wake
+        else:
+            for t in o["tiles"]:
+                if t not in bmap:
+                    if not bfree:
+                        return None, None
+                    bmap[t] = min(bfree, key=lambda b: bfree[b][0])
+                    x, l = bfree.pop(bmap[t])
+                    st = max(st, x)
+                    dyn.setdefault(i, []).extend(l)
+                    held[t] = [0.0, []]
+        free[q] = st + cost[i]
+        fin[i] = free[q] + lat[i]
+        if uses is not None:
+            for t in o["tiles"]:
+                if q != "P":
+                    held[t][0] = max(held[t][0], free[q] + wake)
+                    held[t][1].append(i)
+                uses[t] -= 1
+                if uses[t] == 0:
+                    bfree[bmap[t]] = held[t]
+    return max(fin), bmap
+
+
+def schedule(pg, cs, rounds, seed):
     ops = pg["ops"]
     N_ = len(ops)
-    succ = [[] for _ in ops]
-    cnt = [0] * N_
+    cost, lat, wake = cs[0]
+    pred, succ = [[] for _ in ops], [[] for _ in ops]
+    uses, phase, seen, slot = {}, {}, {}, {}
     for o in ops:
-        ps = set(o["dep"]) | o["ord"]
-        if o["send"] is not None:
-            ps.add(o["send"])
-        cnt[o["i"]] = len(ps)
-        for p in ps:
-            succ[p].append(o["i"])
-    pri = [0.0] * N_
-    for o in reversed(ops):
         i = o["i"]
-        pri[i] = max([pri[s] for s in succ[i]] + [0.0]) + o["cost"] + o["lat"] + WAKE
-    for o in ops:
-        pri[o["i"]] += PRI.get(o["st"], 0.0)
-    uses, first = {}, {}
-    for o in ops:
-        for tname in o["tiles"]:
-            if tname not in uses:
-                uses[tname] = 0
-                first.setdefault(o["i"], []).append(tname)
-            uses[tname] += 1
-    bfree = {b: (0.0, []) for b in range(8)}
-    bmap, held, late = {}, {}, {}
-    ready = {}
-    avail = [0.0] * N_
-    free = {}
-    order = {}
-    fin = [0.0] * N_
-    for o in ops:
-        if cnt[o["i"]] == 0:
-            ready.setdefault(o["q"], []).append(o["i"])
-    left = N_
-    while left:
-        best = None
-        for q, lst in ready.items():
-            if not lst:
-                continue
-            if q[0] == "R":
-                cand = (avail[lst[0]], q, lst[0])
-            else:
-                fr = free.get(q, 0.0)
-                full_ = lst
-                if q == "P":
-                    if not bfree:
-                        lst = [i for i in lst if i not in first]
-                        if not lst:
-                            continue
-                    else:
-                        bt = min(v[0] for v in bfree.values())
-                        for i in lst:
-                            if i in first and avail[i] < bt:
-                                late[i] = bt
-                st = min(max(fr, avail[i], late.get(i, 0.0)) for i in lst)
-                c = [i for i in lst if max(fr, avail[i], late.get(i, 0.0)) <= st + 0.02]
-                cand = (st, q, max(c, key=lambda i: pri[i]))
-            if best is None or cand[0] < best[0]:
-                best = cand
-        if best is None:
-            pg["fin"] = 1e6
-            return
-        st, q, i = best
-        ready[q].remove(i)
-        late.clear()
-        o = ops[i]
-        o["dyn"] = set()
-        for tname in first.get(i, ()):
-            b = min(bfree, key=lambda b: bfree[b][0])
-            o["dyn"] |= set(bfree.pop(b)[1])
-            bmap[tname] = b
-            held[tname] = [0.0, []]
-        end = st + o["cost"]
-        free[q] = end
-        fin[i] = end + o["lat"]
-        order.setdefault(q, []).append(i)
-        left -= 1
-        for tname in o["tiles"]:
-            hd = held[tname]
-            hd[0] = max(hd[0], end + WAKE)
-            if q != "P":
-                hd[1].append(i)
-            uses[tname] -= 1
-            if uses[tname] == 0:
-                bfree[bmap[tname]] = (hd[0], hd[1])
-        for s in succ[i]:
-            cnt[s] -= 1
-            w = 0.0 if i in ops[s]["ord"] else WAKE
-            avail[s] = max(avail[s], fin[i] + w)
-            if cnt[s] == 0:
-                ready.setdefault(ops[s]["q"], []).append(s)
-        o["t0"], o["t1"] = st, end
-    pg["order"] = order
-    pg["bmap"].clear()
-    pg["bmap"].update(bmap)
-    pg["fin"] = max(fin)
-    pg["seq"] = sorted(range(N_), key=lambda i: (ops[i]["t0"], ops[i]["q"][0] != "R", i))
+        e = {d: wake + lat[d] for d in o["dep"]}
+        for d in o["ord"]:
+            e.setdefault(d, 0.0)
+        if o["send"] is not None:
+            e[o["send"]] = lat[o["send"]]
+        for d in sorted(e):
+            pred[i].append((d, e[d]))
+            succ[d].append((i, e[d]))
+        for t in o["tiles"]:
+            uses[t] = uses.get(t, 0) + 1
+        phase.setdefault(o["st"], []).append(i)
+        if o["st"]:
+            k = (o["hop"], o["st"], o["tag"])
+            seen[k] = seen.get(k, 0) + 1
+            slot.setdefault((o["st"], o["tag"], seen[k]), []).append(i)
+    phases, slots = list(phase.values()), list(slot.values())
+    q = [o["q"] for o in ops]
+    zero = [0.0] * N_
+    way = [0.0] * N_
+    for i in range(N_ - 1, -1, -1):
+        way[i] = max([way[j] + w for j, w in succ[i]] + [lat[i]]) + cost[i]
+    first = []
+
+    def judge(st):
+        seq = sorted(range(N_), key=lambda i: (st[i], i))
+        dyn = {}
+        f, bmap = replay(ops, seq, cs[0], dyn, dict(uses))
+        if f is None:
+            return 1e9, None
+        r = [f] + [replay(ops, seq, c, dyn)[0] for c in cs[1:]]
+        if not first:
+            first.extend(r)
+        return sum(x / y for x, y in zip(r, first)) / len(r), (seq, dyn, bmap, r, st)
+
+    rng = np.random.default_rng(seed)
+    cur = [-way[o["i"]] + (STAGGER if o["st"][-1:] == "0" else 0.0) for o in ops]
+    now, best, keep = 1e9, 1e9, None
+    for it in range(rounds):
+        key = list(cur)
+        mode, d, a = int(rng.integers(5)), float(rng.normal()), float(rng.uniform(min(cur), max(cur)))
+        if it == 0:
+            pass
+        elif mode == 0:
+            for t in rng.integers(len(phases), size=int(rng.integers(1, 4))):
+                d = float(rng.normal(0, rng.choice([0.5, 1.5, 4.0])))
+                for i in phases[t]:
+                    key[i] += d
+        elif mode == 1:
+            wd, sg = float(rng.uniform(2, 15)), float(rng.choice([0.2, 0.6, 1.5]))
+            for i in range(N_):
+                if a <= key[i] <= a + wd:
+                    key[i] += float(rng.normal(0, sg))
+        elif mode == 2:
+            for i in phases[int(rng.integers(len(phases)))]:
+                if a <= key[i] <= a + 18:
+                    key[i] += 3 * d
+        else:
+            s0 = slots[int(rng.integers(len(slots)))]
+            at = lambda sl: cur[sl[min(1, len(sl) - 1)]]
+            wd, d = float(rng.choice([0.0, 0.5, 2.0])), d * float(rng.choice([0.3, 1.0, 3.0]))
+            for sl in slots:
+                if at(s0) <= at(sl) <= at(s0) + wd and (mode == 3 or q[sl[0]] == q[s0[0]]):
+                    if mode == 4:
+                        d = float(rng.normal(0, 0.7))
+                    for i in sl:
+                        key[i] += d
+        st = place(key, pred, succ, q, cost, zero)
+        back = place([-(st[i] + cost[i]) for i in range(N_)], succ, pred, q, cost, lat)
+        for x in (st, place([-(back[i] + cost[i]) for i in range(N_)], pred, succ, q, cost, zero)):
+            f, info = judge(x)
+            if f <= now + 0.002 * (1 - it / rounds) * float(rng.exponential()):
+                now, cur = f, x
+            if f < best:
+                best, keep = f, info
+    return keep
 
 
-def emit(pg, g, T):
+def plan(T, topo, core, rank, rounds=None, seed=1):
+    pgs = [build(T, topo, core, rank, c) for c in COSTS]
+    cs = [([o["cost"] for o in p["ops"]], [o["lat"] for o in p["ops"]], c["wake"]) for p, c in zip(pgs, COSTS)]
+    return schedule(pgs[0], cs, rounds or ROUNDS, seed)
+
+
+def emit(pg, keep, g, T):
     ops = pg["ops"]
+    seq, dyn, bmap = keep[:3]
+    pg["bmap"].update(bmap)
     eng = {"V": g.vector, "S": g.scalar, "P": g.tensor, "G": g, "Y": g.sync}
-    pos, key, know = {}, {}, {}
-    for q, lst in pg["order"].items():
-        c = 0
-        for i in lst:
-            if ops[i]["sem"] is None:
-                c += 1
-                key[i], pos[i] = q, c
-            else:
-                key[i], pos[i] = ops[i]["sem"], ops[i]["val"]
-    qk = {}
-    done = {}
-    queues = {q: list(l) for q, l in pg["order"].items()}
-    state = {q: 0 for q in queues}
-    prog = True
-    tot = sum(len(l) for l in queues.values())
-    k = 0
-    while k < tot:
-        prog = False
-        for q in queues:
-            while state[q] < len(queues[q]):
-                i = queues[q][state[q]]
-                o = ops[i]
-                if o["dyn"]:
-                    o["dep"] |= o["dyn"]
-                if any(d not in done for d in o["dep"]) or (o["send"] is not None and o["send"] not in done):
-                    break
-                kn = qk.setdefault(q, {})
-                if q[0] != "R":
-                    need = {}
-                    for d in sorted(o["dep"], key=lambda d: -ops[d]["t1"]):
-                        if kn.get(key[d], 0) >= pos[d]:
-                            continue
-                        if need.get(key[d], 0) < pos[d]:
-                            need[key[d]] = pos[d]
-                    ds = [d for d in o["dep"] if need.get(key[d], 0) == pos[d]]
-                    for d in ds:
-                        for d2 in ds:
-                            if d2 != d and key[d] in need and key[d2] in need and key[d] != key[d2] and know[d2].get(key[d], 0) >= pos[d]:
-                                need.pop(key[d])
-                    for kk in sorted(need):
-                        eng[q].wait_ge(T.sem[kk], int(need[kk]))
-                    for d in o["dep"]:
-                        for kk, v in know[d].items():
-                            if kn.get(kk, 0) < v:
-                                kn[kk] = v
-                    ins = o["fn"](eng[q])
-                    if o["sem"] is None:
-                        ins.then_inc(T.sem[q], 1)
-                me = dict(kn)
-                if o["send"] is not None:
-                    me = dict(know[o["send"]])
-                    for kk in list(me):
-                        me.pop(kk)
-                me[key[i]] = max(me.get(key[i], 0), pos[i])
-                know[i] = me
-                done[i] = 1
-                state[q] += 1
-                k += 1
-                prog = True
-        if not prog:
-            raise ValueError("no order")
+    pos, key, know, count, qk = {}, {}, {}, {}, {}
+    for i in seq:
+        o = ops[i]
+        q = o["q"]
+        if o["sem"] is None:
+            count[q] = count.get(q, 0) + 1
+            key[i], pos[i] = q, count[q]
+        else:
+            key[i], pos[i] = o["sem"], o["val"]
+        dep = sorted(o["dep"] | set(dyn.get(i, ())))
+        kn = qk.setdefault(q, {})
+        if q[0] != "R":
+            need = {}
+            for d in dep:
+                if kn.get(key[d], 0) < pos[d] and need.get(key[d], 0) < pos[d]:
+                    need[key[d]] = pos[d]
+            ds = [d for d in dep if need.get(key[d], 0) == pos[d]]
+            for d in ds:
+                for d2 in ds:
+                    if key[d] != key[d2] and key[d] in need and key[d2] in need and know[d2].get(key[d], 0) >= pos[d]:
+                        need.pop(key[d])
+            for kk in sorted(need):
+                eng[q].wait_ge(T.sem[kk], int(need[kk]))
+            for d in dep:
+                for kk, v in know[d].items():
+                    if kn.get(kk, 0) < v:
+                        kn[kk] = v
+            ins = o["fn"](eng[q])
+            if o["sem"] is None:
+                ins.then_inc(T.sem[q], 1)
+        me = dict(kn) if o["send"] is None else {}
+        me[key[i]] = max(me.get(key[i], 0), pos[i])
+        know[i] = me
     for q in "VSPG":
-        if pg["order"].get(q):
-            c = sum(1 for i in pg["order"][q] if ops[i]["sem"] is None)
-            if c:
-                g.wait_ge(T.sem[q], int(c))
+        g.wait_ge(T.sem[q], int(count[q]))
 
 
-def build(T, topo, core, rank):
-    pg = new_prog()
+def build(T, topo, core, rank, CO=COSTS[0]):
+    pg = {"ops": [], "acc": {}, "rr": [0], "st": "", "hop": 0, "bmap": {}}
+    CY, GC, PEC = CO["cy"], CO["gather"], CO["pe"]
+
     def ap(r):
         name, c0, c1, step, p0, p1, ps = r
         t = T["b%d" % pg["bmap"][name]] if name in pg["bmap"] else T[name]
@@ -318,7 +353,7 @@ def build(T, topo, core, rank):
 
     def tt(out, a, b, op):
         ind = a[0] == "ind"
-        ps = any(r[0][0] == "b" and r[0][1:].isdigit() for r in (a, b) if r[0] != "ind")
+        ps = any(is_psum(r[0]) for r in (a, b) if r[0] != "ind")
         return add(pg, "V", vcost(cnt(out), 1 if ps else 2, ind), lambda e: e.tensor_tensor(ap(out), inap(a), ap(b), op), regs(a) + [b], [out], tag="tt " + out[0])
 
     def cp(out, a):
@@ -337,13 +372,21 @@ def build(T, topo, core, rank):
         return add(pg, "S", FIX["S"] + CY * max(64, cnt(out) * (GC if ind else 1)) + (0.04 if ind else 0),
                    lambda e: e.activation(ap(out), inap(in_), func, bias=dcol(bias), scale=dcol(scale)), regs(in_) + sc, [out], tag="act " + out[0])
 
-    def pe(mms):
+    def flex(name, out, in_, bias=0.0):
+        if name in ONV:
+            return ts(out, in_, bias, A.add) if bias else cp(out, in_)
+        return act(out, in_, F.Identity if bias else F.Copy, bias)
+
+    def pe(mms, sub=False):
         cost = 0.0
         rd, wr = {}, {}
         for out, l, r, s, e_ in mms:
             k = 4 if SCRATCH[l[0]][2] == f4 else 1
             cost += PEC * k * max(min(64, cnt(l)), cnt(r)) + 0.006
             for x in (l, r):
+                if sub:
+                    rd[x] = x
+                    continue
                 y = rd.get(x[0])
                 rd[x[0]] = (x[0], min(x[1], y[1]) if y else x[1], max(x[2], y[2]) if y else x[2], 1, 0, 128, 1)
             y = wr.get(out[0])
@@ -354,18 +397,21 @@ def build(T, topo, core, rank):
             for out, l, r, s, e_ in mms:
                 ins = e.matmul(ap(out), ap(l), ap(r), s, e_)
             return ins
-        return add(pg, "P", cost + FIX["P"], fn, list(rd.values()), list(wr.values()), tag="pe " + mms[0][0][0])
+        return add(pg, "P", cost + FIX["P"], fn, list(rd.values()), list(wr.values()), tag="pe " + mms[0][1][0] + " " + mms[0][2][0])
 
     def acc(out, *pairs):
         return [(out, l, r, i == 0, i == len(pairs) - 1) for i, (l, r) in enumerate(pairs)]
 
-    def bank(h, w=n):
+    def grp(*mms):
+        return [(o, l, r, i == 0, i == len(mms) - 1) for i, (o, l, r) in enumerate(mms)]
+
+    def bank():
         pg["rr"][0] += 1
         return "b%d" % (99 + pg["rr"][0])
 
-    def load(name, out, src, q="Y"):
+    def load(name, out, src, lat, q="Y"):
         s = "ld_" + name
-        return add(pg, q, 0.1, lambda e: e.dma_start(ap(out), src).then_inc(T.sem[s], 16), [], [out], sem=s, val=16, lat=3.0, tag="load " + name)
+        return add(pg, q, 0.1, lambda e: e.dma_start(ap(out), src).then_inc(T.sem[s], 16), [], [out], sem=s, val=16, lat=lat, tag="load " + name)
 
     nout = [0]
 
@@ -382,7 +428,7 @@ def build(T, topo, core, rank):
     def send(kind, t, h, out, in_):
         s = "r%s_%d_%d" % (kind, t, h)
         nls[0] += neng
-        i = add(pg, "G", 0.4, lambda e: e.remote_dma(ap(out), ap(in_), T.sem[s], T.sem["ls"], pid, rid, mask), [in_], [], sem="ls", val=nls[0], lat=LNK, tag="send " + s)
+        i = add(pg, "G", 0.4, lambda e: e.remote_dma(ap(out), ap(in_), T.sem[s], T.sem["ls"], pid, rid, mask), [in_], [], sem="ls", val=nls[0], lat=CO["link"], tag="send " + kind)
         j = add(pg, "R" + s, 0.0, None, [], [out], sem=s, val=neng)
         pg["ops"][j]["send"] = i
 
@@ -390,414 +436,359 @@ def build(T, topo, core, rank):
     tl = lambda name, h: ref(name, h * n, h * n + n)
     full = lambda name: ref(name, 0, SCRATCH[name][1][1])
 
-    load("wt", ref("WT", 0, 1), T.wt[:, :])
-    load("kap", ref("WT", 1, 2), T.kap[:, :])
-    fill(full("VZ"), 0)
-    load("v0", ref("VZ", 0, 256, 1, 0, 128, 16), T.v0[:, :])
-    load("d0", ref("VZ", 256, 512, 1, 0, 128, 16), T.d0[:, :])
-    load("px0", ref("PX", 0, 2048), T.px[:, 0:2048])
-    load("px1", ref("PX", 2048, 4096), T.px[:, 2048:4096])
+    loads = [load("v0", ref("VZ", 0, 256, 1, 0, 8), T.v0[:, :], 2.2),
+             load("d0", ref("VZ", 256, 512, 1, 0, 8), T.d0[:, :], 2.2),
+             load("px0", ref("PX", 0, 2048), T.px[:, 0:2048], 3.8),
+             load("px1", ref("PX", 2048, 4096), T.px[:, 2048:4096], 5.3)]
     for h in (1, 0):
-        load("z%d" % h, ref("XZ", h * XW + 32, h * XW + 32 + n), T.z0[:, h * n:h * n + n])
-    load("f0", full("FI"), T.f0[:, :])
-    load("vw0", ref("VW", 0, 1024), T.vw[:, 0:1024])
-    load("vw1", ref("VW", 1024, 2048), T.vw[:, 1024:2048])
+        loads.append(load("z%d" % h, ref("XZ", h * XW + 32, h * XW + 32 + n), T.z0[:, h * n:h * n + n], 5.3))
+    loads += [load("wt", ref("WT", 0, 1), T.wt[:, :], 5.3),
+              load("kap", ref("WT", 1, 2), T.kap[:, :], 5.3),
+              load("f0", full("FI"), T.f0[:, :], 5.6),
+              load("vw0", ref("VW", 0, 1024), T.vw[:, 0:1024], 7.0),
+              load("vw1", ref("VW", 1024, 2048), T.vw[:, 1024:2048], 8.5)]
+    for a, b in zip(loads, loads[1:]):
+        pg["ops"][b]["ord"].add(a)
 
     def sel(out, in_, pat, cmp, fillv, base, cm):
-        return add(pg, "G", 0.2 + 2 * CY * cnt(out), lambda e: e.affine_select(ap(out), ap(in_), pat, cmp, fillv, base, cm), [in_], [out], tag="sel")
+        return add(pg, "G", 0.2 + 2 * CY * cnt(out), lambda e: e.affine_select(ap(out), ap(in_), pat, cmp, fillv, base, cm), [in_], [out], tag="sel " + out[0])
 
-    def iota(out, pat, base, cm, small=False):
+    def iota(out, pat, base, cm, small=True):
         if small:
             fn = lambda e: e.iota(ap(out), pat, base, cm, allow_small_or_imprecise_dtypes=True)
         else:
             fn = lambda e: e.iota(ap(out), pat, base, cm)
-        return add(pg, "G", 0.2 + 2 * CY * cnt(out), fn, [], [out], tag="iota")
+        return add(pg, "G", 0.15 + 2 * CY * cnt(out), fn, [], [out], tag="iota " + out[0])
 
-    iota0 = lambda out: iota(out, [[0, cnt(out)]], 0, 0, True)
-    fill(full("ONE"), 1.0)
-    sel(full("G8"), full("ONE"), [[1, 128]], A.is_ge, 0.0, 0, -16)
-    sel(full("G8"), full("G8"), [[-1, 128]], A.is_ge, 0.0, 15, 16)
-    sel(full("If"), full("ONE"), [[-1, 128]], A.is_equal, 0.0, 0, 1)
-    iota(ref("PI", 0, 1), [[0, 1]], 0, 1)
-    iota(full("IJ"), [[1, 16]], 0, 0, True)
-    iota(full("CMI"), [[16, 8]], 0, 0, True)
-    iota(full("KC"), [[0, 8], [1, 16]], 0, 0, True)
-    g8 = ref("G8", 0, 128, 1, 0, 8)
-    bk = bank(0)
-    pe([(ref(bk, 0, 128), g8, g8, True, True)])
-    cp(full("BO"), ref(bk, 0, 128))
-    cp(full("BOh"), full("BO"))
-    cp(full("Ib"), full("If"))
-    cp(full("Ih"), full("If"))
-    act(full("Inb"), full("If"), F.Copy, 0.0, -1.0)
-    act(full("Ihalf"), full("If"), F.Copy, 0.0, 0.5)
-    act(full("I16b"), full("If"), F.Copy, 0.0, 16.0)
+    Ib, on = full("Ib"), ref("ON", 0, 128)
+    fill(full("ON"), 1.0)
+    sel(Ib, on, [[-1, 128]], A.is_equal, 0.0, 0, 1)
+    sel(ref("B8", 0, 144, 1, 0, 8), ref("ON", 0, 144, 1, 0, 8), [[1, 144]], A.is_equal, 0.0, -15, -16)
+    sel(full("BO"), on, [[-16, 8], [0, 16]], A.is_ge, 0.0, 0, 1)
+    sel(full("BO"), full("BO"), [[16, 8], [0, 16]], A.is_ge, 0.0, 15, -1)
+    iota(ref("PI", 0, 1), [[0, 1]], 0, 1, False)
+    iota(full("IJ"), [[1, 16]], 0, 0)
+    iota(ref("CMI", 0, 8), [[16, 8]], 0, 0)
+    iota(ref("W613", 0, 1024), [[613, 1024]], HC, 0)
+    act(ref("W613", 1024, 2048), ref("W613", 0, 1024), F.Identity, 613.0 * 1024)
+    act(ref("W613", 2048, 4096), ref("W613", 0, 2048), F.Identity, 613.0 * 2048)
+    fill(ref("W613", 4096, 4104), -1.0)
+    iota(full("MK"), [[0, n], [256, 16]], 0, 0)
+    iota(full("KC"), [[0, 8], [1, 16]], 0, 0)
+    for j, b in enumerate((0, 1, 1)):
+        iota(ref("CMI", 8 + j, 32, 3), [[2, 8]], b, 0)
+    ts(ref("CL", 0, 8), ref("CMI", 0, 8), 15.0, A.add)
+    cp(ref("CL", 8, 32), ref("CMI", 8, 32))
+    iota(full("RST"), [[0, 128]], 0, 0)
+    sel(full("RST"), full("RST"), [[0, 8], [1, 16]], A.not_equal, 1048576.0, 0, 0)
+    for i, c in enumerate((1, 0, -99)):
+        iota(ref("CS", 8 * i, 8 * i + 8), [[0, 8]], c, 0)
+    for k in range(8):
+        iota(ref("ZB", k * (32 + n) + 24, k * (32 + n) + 32), [[0, 8]], 0, 0)
+    iota(full("ZE"), [[0, 128]], 0, 0)
+    for nm in DIAG:
+        if nm in ("Ibig", "Ifl", "I16", "I8k", "I256", "Ip100", "I8kn"):
+            sel(full(nm), full("ZE"), [[-1, 128]], A.not_equal, DIAG[nm][0], 0, 1)
+        elif DIAG[nm][1] == h2:
+            ts(full(nm), Ib, DIAG[nm][0], A.mult)
+        elif nm != "Ib":
+            act(full(nm), Ib, F.Copy, 0.0, DIAG[nm][0])
     ts(ref("PI", 16, 17), ref("PI", 0, 1), 15, A.bitwise_and)
     ts(ref("PI", 24, 25), ref("PI", 0, 1), 1, A.bitwise_and)
-    pm, sg, sgn, pmh = ref("PC", 0, 1), ref("PC", 4, 5), ref("PC", 8, 9), ref("PC", 12, 13)
-    ts(sgn, ref("PI", 24, 25), -2.0, A.mult, 1.0 + n, A.add)
-    ts(pmh, ref("PI", 16, 17), -7.5, A.add)
+    pm, sg, sg256, dg, sp0, sp1 = [ref("PC", 4 * i, 4 * i + 1) for i in range(6)]
     cp(pm, ref("PI", 16, 17))
     ts(sg, ref("PI", 24, 25), -2.0, A.mult, 1.0, A.add)
+    ts(sg256, ref("PI", 24, 25), -2.0, A.mult, 257.0, A.add)
+    ts(dg, pm, 15.0, A.is_equal, 8192.0 - 2.0 ** -5, A.mult)
+    ts(dg, dg, 2.0 ** -5, A.add)
+    ts(sp0, pm, 4096.0, A.add)
+    ts(sp1, pm, 4112.0, A.add)
+    ts(full("G0"), Ib, sg, A.mult)
+    ts(full("G256"), Ib, sg256, A.mult)
+    ts(full("DG"), Ib, dg, A.mult)
     cp(ref("WTf", 0, 2), full("WT"))
-    wcol, kcol = ref("WTf", 0, 1), ref("WTf", 1, 2)
-    act(full("WB"), full("BO"), F.Copy, 0.0, wcol)
+    ts(ref("WTf", 4, 5), ref("WTf", 1, 2), 1.0 / 32, A.mult)
+    wcol, kcol = ref("WTf", 0, 1), ref("WTf", 4, 5)
+    ts(full("WB"), full("BO"), wcol, A.mult)
     fill(full("Bh"), 0.0)
     cp(ref("Bh", 15, 143, 16), ref("BO", 0, 128, 16))
-    fill(full("CLB"), -65536.0)
-    HB = ref("CLB", 0, 1)
-    act(full("WBs"), full("WB"), F.Copy, 0.0, 1.0 / 4096)
-    act(full("I4kn"), full("If"), F.Copy, 0.0, -4096.0)
-    fill(ref("CH", 0, 128, 1, 0, 64), -0.5 / 64)
-    fill(ref("CH", 0, 128, 1, 64, 128), 2.0 ** -19)
+    fill(full("CH"), 49152.0)
+    fill(full("CP"), -4096.0)
     ts(full("B32"), ref("BO", 0, 128, 16), 32.0, A.mult)
     ts(full("Bm16"), ref("BO", 0, 128, 16), -16.0, A.mult)
-    ts(full("OJ"), full("IJ"), pm, A.is_equal, 613.0, A.mult)
-    ts(full("OK"), full("IJ"), pm, A.is_equal)
-    for j in range(16):
-        ts(ref("SJ", 128 * j, 128 * j + 128), full("BOh"), ref("OJ", j, j + 1), A.mult)
-    for j in range(16):
-        act(ref("SJb", 128 * j, 128 * j + 128), full("BO"), F.Copy, 0.0, ref("OK", j, j + 1))
-    ts(ref("CM", 0, 8), full("CMI"), pm, A.add)
-    ts(ref("CM", 8, 16), full("CMI"), pm, A.add)
-    ts(ref("CM", 16, 24), ref("CM", 0, 8), float(2 * n), A.add)
-    ts(ref("CM", 24, 32), ref("CM", 0, 8), float(3 * n), A.add)
-    iota(ref("CON", 56, 72), [[0, 16]], -100, 0, True)
-    for h in range(2):
-        ts(sm("CMm", h), ref("CM", 0, 8), float(n * h), A.add)
-    consts = (-9, -4096, 2048, -100, 1, 100)
-    for i, c in enumerate(consts):
-        iota(ref("CON", 8 * i, 8 * i + 8), [[0, 8]], c, 0, True)
-    con = lambda c: ref("CON", 8 * consts.index(int(c)), 8 * consts.index(int(c)) + 8)
-    ts(full("BO613"), full("BOh"), 613.0, A.mult)
-    for nm, c in (("In", float(n)), ("I2n", float(2 * n)), ("I8k", 8192.0), ("Im100", -100.0), ("Ip100", 100.0), ("I8kn", -8192.0), ("Imh", -0.5), ("I7h", 7.5)):
-        act(full(nm), full("If"), F.Copy, 0.0, c)
-    act(full("G0"), full("If"), F.Copy, 0.0, sg)
-    act(full("Gn"), full("If"), F.Copy, 0.0, sgn)
-    act(full("BP"), ref("BO", 0, 128, 16), F.Copy, 0.0, -1048576.0)
-    act(ref("Sb", 0, 128, 2), ref("If", 1, 128, 2), F.Copy)
-    act(ref("Sb", 1, 128, 2), ref("If", 0, 128, 2), F.Copy)
+    ts(full("MP"), full("BO"), 524288.0, A.mult)
+    tt(full("MP"), full("MP"), full("Ibig"), A.add)
+    ts(ref("CM", 0, 8), ref("CMI", 0, 8), pm, A.add)
+    ts(ref("CM", 8, 16), ref("CMI", 0, 8), pm, A.add)
+    act(ref("Sb", 0, 128, 2), ref("Ib", 1, 128, 2), F.Copy)
+    act(ref("Sb", 1, 128, 2), ref("Ib", 0, 128, 2), F.Copy)
     act(full("Sb100"), full("Sb"), F.Copy, 0.0, 100.0)
-    act(full("I4k"), full("If"), F.Copy, 0.0, 4096.0)
-    fill(full("ON"), 1.0)
-    fill(full("CQ"), -0.25 / 128)
-    iota(full("MK"), [[0, 16 * n]], 1, 0, True)
-    sel(full("MK"), full("MK"), [[0, n], [1, 16]], A.not_equal, 0.0, 0, 0)
-    iota(full("MF"), [[0, n]], 1, 0, True)
-    sel(full("MF"), full("MF"), [[0, n // 16], [1, 16]], A.not_equal, 0.0, 0, 0)
-    iota(full("RST"), [[0, 128]], 0, 0, True)
-    sel(full("RST"), full("RST"), [[0, 8], [1, 16]], A.not_equal, 1048576.0, 0, 0)
     fill(full("QS"), 0.0)
-    fill(full("C256"), 256.0)
-    iota(full("VS"), [[0, 2 * n]], 0, 0, True)
-    iota(full("SP"), [[0, 2 * n]], 0, 0, True)
-    for k in range(8):
-        iota0(ref("ZB", k * (32 + n) + 24, k * (32 + n) + 32))
+    fill(ref("VI", 4096, 4096 + 32), 0.0)
+    fill(ref("OHW", 0, 16), 0.0)
+    ts(ref("OHW", 16, 32), full("IJ"), pm, A.is_equal)
+    w = 16
+    while w < 4096:
+        for a in range(0, w, 1024):
+            act(ref("OHW", 16 + w + a, 16 + w + min(w, a + 1024)), ref("OHW", 16 + a, 16 + min(w, a + 1024)), F.Copy)
+        w *= 2
+    fill(ref("D0", 16, 32), 1.0)
+    ts(ref("D0", 0, 16), full("IJ"), pm, A.is_equal, 262144.0, A.mult)
+    ts(ref("D0", 0, 16), ref("D0", 0, 16), 1.0, A.max)
+    cp(ref("D0", 32, 48), ref("D0", 0, 16))
+    fill(ref("D0", 0, 32, 16), 0.0)
+    for w in (48, 96, 192):
+        act(ref("D0", w, 2 * w), ref("D0", 0, w), F.Copy)
 
-    def ots(out, tile, base="Bh", first=(), last=()):
+    def ots(out, tile, first=(), last=()):
         prs = list(first)
         for j in range(16):
-            prs.append((ref(base, 15 - j, 143 - j), ref(tile[0], tile[1] + j, tile[2], 16)))
+            prs.append((ref("Bh", 15 - j, 143 - j), ref(tile[0], tile[1] + j, tile[2], 16)))
         return acc(out, *(prs + list(last)))
 
-    def spread(out, src):
-        return [(ref(out[0], out[1] + j, out[2], 16), ref("SJ", 128 * j, 128 * j + 128), src, True, True) for j in range(16)]
-
-    ts(ref("VZi", 0, 256), ref("VZ", 0, 256), 4032, A.bitwise_and)
-    cp(ref("VZh", 0, 256), ref("VZi", 0, 256))
-    ts(ref("VZi", 256, 512), ref("VZ", 0, 256), 63, A.bitwise_and)
-    cp(ref("VZh", 256, 512), ref("VZi", 256, 512))
-    cp(ref("VZh", 512, 768), ref("VZ", 256, 512))
-
-    def s16(c0):
-        return [(ref("Bh", 15 - j, 143 - j), ref("VZh", c0 + j, c0 + 256, 16)) for j in range(16)]
-    b6, b5 = bank(0), bank(0)
-    pe(acc(ref(b6, 0, 16), *(s16(0) + s16(256))))
-    pe(acc(ref(b5, 0, 16), *s16(512)))
+    ts(ref("VZh", 0, 512, 1, 0, 8), ref("VZ", 0, 512, 1, 0, 8), -2048.0, A.add)
+    b6 = bank()
+    pe(acc(ref(b6, 0, 32), *[(ref("B8", 15 - j, 143 - j, 1, 0, 8), ref("VZh", j, 512, 16, 0, 8)) for j in range(16)]))
+    ts(ref("VH", 0, 16), ref(b6, 0, 16), 2048.0, A.add)
     for h in (1, 0):
-        ts(ref("VH", 8 * h, 8 * h + 8), ref(b6, 8 * h, 8 * h + 8), -2048.0, A.add)
-        fill(ref("XZ", h * XW, h * XW + 16), 0.0)
-        ts(ref("XZ", h * XW + 16, h * XW + 24), ref(b5, 8 * h, 8 * h + 8), 1.0, A.add)
-        cp(ref("W", h * WW + n, h * WW + 2 * n), ref("FI", h * n, h * n + n))
+        ts(ref("XZ", h * XW, h * XW + 8), ref(b6, 16 + 8 * h, 24 + 8 * h), 2048.0, A.add)
+        fill(ref("XZ", h * XW + 8, h * XW + 24), 0.0)
+        ts(ref("W", h * WW + n, h * WW + 2 * n), ref("FI", h * n, h * n + n), -OFS, A.add)
+    M12 = 1.5 * 2.0 ** 35
     for c in range(2):
         x = ref("VW", 1024 * c, 1024 * c + 1024)
-        it = ref("IT", 1024 * c, 1024 * c + 1024)
+        it, yt = ref("IT", 1024 * c, 1024 * c + 1024), ref("YT", 1024 * c, 1024 * c + 1024)
+        ts(yt, x, -(2047 * 4096 + 2047.5), A.add, M12, A.add)
+        act(ref("VI", 2048 + 1024 * c, 3072 + 1024 * c), yt, F.Identity, 2047.0 - OFS - MAGIC, 2.0 ** -12)
         ts(it, x, 4095, A.bitwise_and)
-        cp(ref("VI", 1024 * c, 1024 * c + 1024), it)
-        ts(x, x, 12, A.arith_shift_right)
-        cp(ref("VI", 2048 + 1024 * c, 3072 + 1024 * c), x)
+        ts(ref("VI", 1024 * c, 1024 * c + 1024), it, -OFS, A.add)
 
     def tiles(t, h):
         k = 2 * t + h
-        x0, w0 = k * XW, k * WW
-        return {"cnt": lambda j: ref("XZ", x0 + 8 * j, x0 + 8 * j + 8), "z": ref("XZ", x0 + 32, x0 + 32 + n), "x": ref("XZ", x0 + 32 + n, x0 + 32 + 2 * n),
-                "hz": ref("XZ", x0 + 32 + 2 * n, x0 + 32 + 3 * n), "xz": ref("XZ", x0 + 32, x0 + 32 + 2 * n), "xzh": ref("XZ", x0 + 32, x0 + 32 + 3 * n),
-                "hd": ref("W", w0, w0 + n), "f": ref("W", w0 + n, w0 + 2 * n), "e": ref("W", w0 + 2 * n, w0 + 3 * n), "c": ref("W", w0 + 3 * n, w0 + 4 * n),
-                "w2": ref("W", w0, w0 + 2 * n), "w3": ref("W", w0, w0 + 3 * n), "w4": ref("W", w0, w0 + 4 * n), "vh": ref("VH", 8 * k, 8 * k + 8),
-                "land": ref("XZ", x0, x0 + 32 + n), "zb": ref("ZB", k * (32 + n), (k + 1) * (32 + n)), "zf": ref("ZB", k * (32 + n) + 32, (k + 1) * (32 + n)),
-                "zc": ref("ZB", k * (32 + n), k * (32 + n) + 24), "fb": ref("FB", k * n, k * n + n), "vb": ref("VB", 8 * k, 8 * k + 8)}
+        x0, w0, z0 = k * XW, k * WW, k * (32 + n)
+        d = {"st": lambda j, w=1: ref("XZ", x0 + 8 * j, x0 + 8 * (j + w)), "z": ref("XZ", x0 + 32, x0 + 32 + n), "x": ref("XZ", x0 + 32 + n, x0 + 32 + 2 * n),
+             "hz": ref("XZ", x0 + 32 + 2 * n, x0 + 32 + 3 * n), "xz": ref("XZ", x0 + 32, x0 + 32 + 2 * n), "xzh": ref("XZ", x0 + 32, x0 + 32 + 3 * n),
+             "hd": ref("W", w0, w0 + n), "f": ref("W", w0 + n, w0 + 2 * n), "c": ref("W", w0 + 2 * n, w0 + 3 * n),
+             "w2": ref("W", w0, w0 + 2 * n), "w3": ref("W", w0, w0 + 3 * n), "vh": ref("VH", 8 * k, 8 * k + 8),
+             "land": ref("XZ", x0, x0 + 32 + n), "fb": ref("FB", k * n, k * n + n), "vb": ref("VB", 8 * k, 8 * k + 8)}
+        if t < NT - 1:
+            d.update({"zb": ref("ZB", z0, z0 + 32 + n), "zf": ref("ZB", z0 + 32, z0 + 32 + n), "zc": ref("ZB", z0, z0 + 24)})
+        else:
+            d["zf"] = tl("ZL", h)
+        return d
 
     px, views = full("PX"), ref("VI", 0, 4096)
-    vks = {}
+    banks = {}
 
     def mark(name, h):
         pg["st"] = name + str(h)
 
     def front(t, h):
-        mark("fr", h)
         L = tiles(t, h)
-        otl = sm("OTL", h)
-        ts(otl, L["vh"], 2048.0, A.add)
-        act(L["x"], ("ind", px, otl), F.Copy)
-        act(L["e"], ("ind", views, otl), F.Copy)
-        bk = bank(h)
-        vk = ref(bank(h), 0, n)
-        vks[h] = vk
-        dx = ref(bk, 0, n)
-        pe(acc(dx, (full("Ib"), L["x"]), (full("Inb"), L["z"])))
-        y = ref(bank(h), 0, n)
-        pe(acc(y, (full("WBs"), L["z"]), (full("CH"), full("ON"))))
-        act(tl("AB", h), dx, F.Abs)
-        ts(tl("IND", h), tl("AB", h), 72.0, A.is_le)
-        pe([(vk, full("BO613"), full("C256"), True, False)]
-           + [(ref(vk[0], j, n, 16), ref("SJ", 128 * j, 128 * j + 128), L["vh"], False, j == 15) for j in range(16)])
-        ct = ref(bank(h), 0, 8)
-        pe(ots(ct, tl("IND", h), "Bh", [(full("Ib"), con(-9.0))], [(full("Inb"), L["cnt"](1))]))
-        lk = sm("LK", h)
-        ts(lk, ct, -0.5, A.is_ge)
-        b = bank(h)
-        pe([(ref(b, 0, 16), full("Ih"), ref("CM", 0, 16), True, False), (ref(b, 0, 8), full("In"), lk, False, False), (ref(b, 8, 16), full("I2n"), lk, False, True)]
-           + acc(ref(b, 16, 24), (full("Ih"), L["vh"]), (full("Ib"), con(-4096.0)), (full("I8k"), lk)))
-        cp(sm("LSL", h, 16, 0, 16), ref(b, 0, 16))
-        act(ref("VS", h * n, h * n + n, 16), ref(b, 16, 24), F.Relu, 0.0, 613.0)
-        q0 = h * 16 * n
-        mark("qx", h)
-        ts(ref("QS", 0, 16 * n, 16), ("ind", L["xz"], sm("LSL", h, 16)), -512.0, A.add)
-        scan(ref("QX", q0, q0 + 16 * n), full("MK"), full("QS"), 0.0, A.mult, A.add)
+        vh = L["vh"]
+        mark("hp", h)
         a, c = tl("HI1", h), tl("HI2", h)
+        y = ref(bank(), 0, n)
+        pe(acc(y, (full("WB"), L["z"])))
+        ts(tl("FL", h), y, 2.0 ** -12, A.mult, 1535.5 + 2.0 ** -13, A.add)
+        pe(acc(y, (full("CH"), on), (full("WB"), L["z"]), (full("I4kn"), tl("FL", h))))
+        ts(a, y, kcol, A.mult, -(HC + 31.0 / 64), A.add)
         mark("ha", h)
-        act(tl("T2", h), y, F.Identity, MAGIC)
-        act(tl("FL", h), tl("T2", h), F.Identity, -MAGIC)
-        um = ref(y[0], n, 2 * n)
-        pe(acc(um, (full("WB"), L["z"]), (full("I4kn"), tl("FL", h))))
-        act(tl("T2", h), um, F.Identity, HB, kcol)
-        cp(a, tl("T2", h))
-        ts(c, a, 5, A.arith_shift_right)
-        tt(a, c, vk, A.add)
-        ts(c, a, 4095, A.bitwise_and)
-        cp(L["hd"], c)
-        mark("dd", h)
-        scan(tl("VR", h), full("MF"), tl("VS", h), 0.0, A.mult, A.add)
-        tt(tl("EQ", h), tl("VR", h), vk, A.is_equal)
-        tt(ref("EQ2", h * n + 16, h * n + n), ref("VR", h * n, h * n + n - 16), ref(vk[0], 16, n), A.is_equal)
-        for i in range(2):
-            mark("he"[i], h)
-            he = ref("HE", (2 * h + i) * n, (2 * h + i + 1) * n)
-            act(he, ("ind", L["w2"] if i == 0 else L["w3"], sm("LSL", h, 16, 8 * i)), F.Copy)
-            cp(ref("HEL", (2 * h + i) * n, (2 * h + i + 1) * n), he)
-
-    def dedupe(t, h):
-        mark("dd", h)
-        L = tiles(t, h)
+        tt(c, ("ind", full("W613"), vh), a, A.add)
+        ts(a, c, 4095, A.bitwise_and)
+        ts(L["hd"], a, -OFS, A.add)
+        mark("fr", h)
+        flex("x", L["x"], ("ind", px, vh))
+        bk = bank()
+        dx, hz = ref(bk, 0, n), ref(bk, n, 2 * n)
+        pe(acc(dx, (full("Icn"), L["z"]), (full("Ic"), L["x"])))
+        ts(tl("IND", h), dx, MAGIC, A.add, MAGIC, A.is_equal)
+        mark("hz", h)
+        pe(acc(hz, (full("Ihz"), L["z"]), (full("Ihz"), L["x"])))
+        ts(L["hz"], hz, MAGIC, A.add, -MAGIC, A.add)
+        mark("fr", h)
+        ct = ref(bank(), 0, 8)
+        pe(ots(ct, tl("IND", h), [(full("In"), L["st"](1)), (full("I2"), L["st"](2))]))
         lk = sm("LK", h)
-        du = ref(bank(h), 0, 8)
-        m3 = acc(du, *([(full("Ib"), con(100.0)), (full("Im100"), lk)] + [(ref("LTJ", 128 * j, 128 * j + 128), ref("EQ", h * n + j, h * n + n, 16)) for j in range(16)]))
-        m3[-1] = m3[-1][:4] + (False,)
-        pe(m3 + [(ref(du[0], 1, 8, 2), ref("Bh", 15 - j, 143 - j), ref("EQ2", h * n + 16 + j, h * n + n, 32), False, j == 15) for j in range(16)])
-        ts(sm("W0", h), du, 0.5, A.is_lt)
-        vd = ref(bank(h), 0, 8)
-        pe(acc(vd, (full("Ib"), con(2048.0)), (full("Ih"), sm("CMm", h)), (full("I8kn"), sm("W0", h))))
-        tt(sm("O2", h), L["vh"], vd, A.max)
-        ts(sm("OFF", h), sm("O2", h), 2048.0, A.add)
+        ts(lk, ct, 8.5, A.is_ge)
+        b = ref(bank(), 0, 8)
+        pe(acc(b, (Ib, ref("CM", 0, 8)), (full("I128"), lk)))
+        cp(sm("LSL", h), b)
+        mark("h", h)
+        ts(ref("HEL", 2 * h * n, 2 * h * n + n), ("ind", L["w2"], sm("LSL", h)), OFS, A.add)
+        mark("qx", h)
+        q0 = h * 16 * n
+        cp(ref("QS", 0, 16 * n, 16), ("ind", L["xz"], sm("LSL", h)))
+        banks[h] = (bank(), bank())
+        scan(ref("QX", q0, q0 + 16 * n), full("MK"), full("QS"), 0.0, A.min, A.add)
+        mark("e", h)
+        act(tl("E", h), ("ind", views, vh), F.Copy)
+        ts(ref("HEL", (2 * h + 1) * n, (2 * h + 2) * n), tl("E", h), OFS, A.add)
+        mark("hm", h)
+        scan(tl("HME", h), L["f"], tl("E", h), 0.0, A.min, A.subtract)
+
+    def dedupe(t):
+        mark("dd", 0)
+        vh = ref("VH", 16 * t, 16 * t + 16)
+        ts(full("VF"), vh, -2048.0, A.add)
+        ts(full("VN"), vh, 613.0, A.mult, float(HC), A.add)
+        b = bank()
+        mm = []
+        for j, c in enumerate((0, 0, 1)):
+            mm += acc(ref(b, j, 24, 3), (Ib, ref("VF", c, 16, 2)), (full("I8kn"), ref("LK", c, 16, 2)))
+        pe(mm)
+        ts(full("DL"), ref(b, 0, 24), 10240.0, A.add, 4096.0, A.min)
+        act(full("G1"), ("ind", full("W613"), full("DL")), F.Copy)
+        tt(full("EQ"), ("ind", full("VN"), ref("CL", 8, 32)), full("G1"), A.is_equal)
+        scan(full("DS"), full("D0"), full("EQ"), 0.0, A.mult, A.add)
+        b = bank()
+        pe(grp((ref(b, 0, 16), Ib, full("VF")), (ref(b, 0, 16), full("I8kn"), full("LK")),
+               (ref(b, 0, 16, 2), full("DG"), ref("DS", 14, 384, 48)), (ref(b, 1, 16, 2), full("DG"), ref("DS", 46, 384, 48))))
+        ts(ref("OFF", 0, 16, 2), ref(b, 0, 16, 2), 10240.0, A.add, sp0, A.min)
+        ts(ref("OFF", 1, 16, 2), ref(b, 1, 16, 2), 10240.0, A.add, sp1, A.min)
 
     def early(t, h):
         mark("ea", h)
         L = tiles(t, h)
-        lk, d1, ov = sm("LK", h), sm("D1", h), sm("OV", h)
-        Ih, Ib, Sb, Ip, Im = full("Ih"), full("Ib"), full("Sb"), full("Ip100"), full("Im100")
-        hz = ref(bank(h), 0, n)
-        pe(acc(hz, (full("Ihalf"), L["x"]), (full("Ihalf"), L["z"]), (full("CQ"), full("ON"))))
-        act(tl("T1", h), hz, F.Identity, MAGIC)
-        act(L["hz"], tl("T1", h), F.Identity, -MAGIC)
-        dp = ref(bank(h), 0, 8)
-        pe(acc(dp, (Ib, L["cnt"](2)), (Im, lk)))
-        act(d1, dp, F.Relu)
-        po = ref(bank(h), 0, 8)
-        pe(acc(po, (Ib, d1), (full("Sb100"), lk)))
-        ts(ov, po, 101.5, A.is_ge)
-        b = bank(h)
-        pe([(ref(b, 0, 24), Ih, ref("CM", 8, 32), True, False)]
-           + [(ref(b, c, c + 8), full(m), v, False, c == 16) for c, m, v in ((0, "I2n", lk), (0, "I2n", ov), (0, "G0", ov), (8, "In", lk), (8, "Gn", ov), (16, "G0", ov))])
-        cp(sm("TLL", h, 24, 0, 24), ref(b, 0, 24))
-        act(L["zf"], ("ind", L["xzh"], sm("TLL", h, 24)), F.Copy)
-        b = bank(h)
-        pe([(ref(b, 0, 16), Ib, ref(L["cnt"](0)[0], L["cnt"](0)[1], L["cnt"](1)[2]), True, False), (ref(b, 0, 8), Ib, lk, False, False), (ref(b, 8, 16), full("Inb"), lk, False, True)])
-        ap_ = sm("P1", h, 16, 0, 16)
-        act(ap_, ref(b, 0, 16), F.Abs)
-        act(sm("O2V", h, 16), ov, F.Copy)
-        act(sm("O2V", h, 16, 8), ov, F.Copy)
-        oo = sm("O2V", h, 16, 0, 16)
-        b = bank(h)
-        pe(acc(ref(b, 0, 16), (Ib, ap_), (Im, oo)) + acc(ref(b, 16, 32), (Sb, ap_), (Ip, oo), (Ib, ref("CON", 56, 72))) + acc(ref(b, 32, 40), (Ib, d1), (Im, ov)))
-        ra = lambda j: sm("RA", h, 40, 8 * j)
-        ra2 = lambda j: sm("RA", h, 40, 16 * j, 16)
-        act(sm("RA", h, 40, 0, 40), ref(b, 0, 40), F.Relu)
-        b = bank(h)
+        lk, ov = sm("LK", h), sm("OV", h)
+        Sb, Ip, Im = full("Sb"), full("Ip100"), full("Im100")
+        po = ref(bank(), 0, 8)
+        pe(acc(po, (Ib, L["st"](0)), (full("Sb100"), lk), (Im, lk)))
+        ts(ov, po, 100.5, A.is_ge)
+        b = bank()
+        pe(grp((ref(b, 0, 16), Ib, full("CM")), (ref(b, 0, 8), full("I256"), lk), (ref(b, 0, 8), full("G256"), ov), (ref(b, 8, 16), full("G0"), ov)))
+        cp(sm("TLL", h, 16, 0, 16), ref(b, 0, 16))
+        flex("zf", L["zf"], ("ind", L["xzh"], sm("TLL", h, 16)))
+        mark("st", h)
+        b = bank()
+        blk = lambda j, w=1: ref(b, 8 * j, 8 * (j + w))
+        pe(grp((blk(0, 3), Ib, full("CS")), (blk(0, 2), Ib, L["st"](0, 2)), (blk(2), Sb, L["st"](1)), (blk(0), Im, lk), (blk(1), Ib, lk),
+               (blk(0), Im, ov), (blk(1), Im, ov), (blk(2), Ip, ov)))
+        ra = lambda j, w=1: sm("RA", h, 24, 8 * j, 8 * w)
+        act(ra(0, 3), blk(0, 3), F.Relu)
+        b = bank()
         if t < NT - 1:
-            pe(acc(ref(b, 0, 16), (Ib, ra2(0)), (Ib, ra2(1))) + acc(ref(b, 16, 24), (Ib, ra(4)), (Ib, con(1.0))))
-            act(L["zc"], ref(b, 0, 24), F.Copy)
+            pe(grp((blk(0, 2), Ib, ra(0, 2)), (blk(1), Ib, ra(2))) + acc(blk(2), (full("Ifl"), ra(1)), (full("Ifl"), ra(2))))
+            ts(L["zc"], blk(0, 3), MAGIC, A.add, -MAGIC, A.add)
             send("z", t + 1, h, tiles(t + 1, h)["land"], L["zb"])
         else:
-            i16 = full("I16b")
-            pe(acc(ref(b, 0, 8), (i16, ra(0)), (i16, ra(2)), (Ib, ra(4))))
-            act(sm("YC", h), ref(b, 0, 8), F.Copy)
-            b = ref(bank(h), 0, n)
-            pe([(ref(b[0], j, n, 16), ref("SJb", 128 * j, 128 * j + 128), sm("YC", h), True, True) for j in range(16)])
-            act(ref("YU", h * n, h * n + n), b, F.Copy)
-            store(T.yc[:, h * n:h * n + n], ref("YU", h * n, h * n + n, 1, 0, 128, 16))
+            pe(acc(blk(0), (full("I16"), ra(1)), (full("I16"), ra(2)), (Ib, ra(0))))
+            act(sm("YC", h), blk(0), F.Copy)
+            if h == 0:
+                b = ref(bank(), 0, n, 1, 0, 16)
+                pe([(b, full("YC"), Ib, True, True)])
+                act(ref("YU", 0, n, 1, 0, 16), b, F.Copy)
+                for g_ in range(8):
+                    store(T.yc[g_, :], ref("YU", 16 * g_, 16 * g_ + 16, 1, 0, 16))
             act(ref("YU", 1024 + h * n, 1024 + h * n + n), L["zf"], F.Copy)
             store(T.yz[:, h * n:h * n + n], ref("YU", 1024 + h * n, 1024 + h * n + n))
         mark("kk", h)
-        cb = ref(bank(h), 0, 8)
-        pe(acc(cb, (full("Imh"), lk), (full("I7h"), ov)))
-        act(sm("CB", h), cb, F.Identity, t - 7.0)
-        y = ref(bank(h), 0, n)
-        pe([(y, full("BO"), L["zf"], True, False)]
-           + [(ref(y[0], j, n, 16), ref("SJb", 128 * j, 128 * j + 128), sm("CB", h), False, j == 15) for j in range(16)])
-        act(tl("KT", h), y, F.Identity, MAGIC, 1.0 / 16)
-        act(tl("KU", h), tl("KT", h), F.Identity, -MAGIC)
-        act(tl("KT", h), tl("KU", h), F.Identity, pmh, 16.0)
-        tt(tl("OHL", h), tl("KT", h), y, A.is_equal)
+        y = ref(bank(), 0, 8)
+        pe(ots(y, L["zf"], [(full("I8k"), lk), (full("I8200"), ov)]))
+        ts(sm("KL", h), y, t + 16.0 - 8192.0, A.add)
+        flex("oh", tl("OHL", h), ("ind", full("OHW"), sm("KL", h)))
 
-    def bulk(t, h):
-        mark("hb", h)
-        L = tiles(t, h)
-        q0, e0 = h * 16 * n, h * 2 * n
-        key = tl("KEY", h)
-        bh_, be_ = bank(h), bank(h)
-
-        def part(G, D, R, l0, a, b, fused):
-            g_, d_, r_ = ref(G, q0 + 16 * a, q0 + 16 * b), ref(D, q0 + 16 * a, q0 + 16 * b), ref(R, q0 + 16 * a, q0 + 16 * b)
-            off = ref("HEL", l0 + a, l0 + b)
-            qx = ref("QX", q0 + 16 * a, q0 + 16 * b)
-            if fused:
-                tt(d_, ("ind", px, off), qx, A.subtract)
-            else:
+    def bulk(t, h, w):
+        mark("he"[w] + "b", h)
+        q0, l0 = h * 16 * n, (2 * h + w) * n
+        G, M = ("GH", "MH") if w == 0 else ("GE", "ME")
+        b = banks[h][w]
+        for a, e_, q in PARTS[w]:
+            g_, off = ref(G, q0 + 16 * a, q0 + 16 * e_), ref("HEL", l0 + a, l0 + e_)
+            if q == "S":
                 act(g_, ("ind", px, off), F.Copy)
-                scan(d_, g_, qx, 600.0, A.min, A.subtract)
-            ts(r_, d_, 512.0, A.max)
-
-        def sums(out, D, R, first):
-            mm = []
-            if first:
-                mm.append((out, full("Ib"), full("KC"), True, False))
-            for k in range(16):
-                o = ref(out[0], out[1] + k, out[2], 16)
-                mm.append((o, ref(R, q0 + k, q0 + 16 * n, 16), full("B32"), not first, False))
-                mm.append((o, ref(D, q0 + k, q0 + 16 * n, 16), full("Bm16"), False, (not first) or k == 15))
-            if len(mm) > 30:
-                pe(mm[:17])
-                pe(mm[17:])
             else:
-                pe(mm)
-        ph, pd = ref(bh_, 0, n), ref(be_, 0, n)
-        part("GH", "DH", "RH", e0, 0, n // 2, False)
-        part("GH", "DH", "RH", e0, n // 2, n, False)
-        sums(ph, "DH", "RH", True)
-        act(key, ph, F.Copy)
-        he1, he2 = ref("HE", e0, e0 + n), ref("HE", e0 + n, e0 + 2 * n)
-        mark("hm", h)
-        tt(tl("HME", h), he1, he2, A.subtract)
+                cp(g_, ("ind", px, off))
+        for a, e_ in CHUNKS[w]:
+            lo, hi = q0 + 16 * a, q0 + 16 * e_
+            g0 = ref(G, lo, hi, 16)
+            first = [(ref(b, 0, n), Ib, full("KC"), True, False) if w == 0 else (ref(b, 0, n), on, full("CP"), True, False)] if a == 0 else []
+            pe(first + [(ref(b, 0, n, 16, a, e_), g0, full("Bm16"), False, False)], sub=True)
+            if e_ == n:
+                for k0 in range(0, 16, SPLIT):
+                    pe([(ref(b, k, n, 16), ref(G, q0 + k, q0 + 16 * n, 16), full("Bm16"), False, False) for k in range(max(1, k0), k0 + SPLIT)], sub=True)
+            tt(g0, g0, ref("QX", lo, hi, 16), A.max)
+            scan(ref(M, lo, hi), ref("QX", lo, hi), ref(G, lo, hi), 0.0, A.min, A.max)
+        pe([(ref(b, 0, n), tl("OHL", h), full("Ibig" if w == 0 else "MP"), False, False)])
+        for k0 in range(0, 16, SPLIT):
+            pe([(ref(b, k, n, 16), ref(M, q0 + k, q0 + 16 * n, 16), full("B32"), False, k == 15) for k in range(k0, k0 + SPLIT)])
+
+    def tail(t, h):
+        L = tiles(t, h)
+        key = tl("KEY", h)
+        ph, pd = ref(banks[h][0], 0, n), ref(banks[h][1], 0, n)
+        bulk(t, h, 0)
         mark("km", h)
+        flex("key", key, ph)
         scan(tl("PM", h), full("RST"), key, 0.0, A.add, A.min)
-        mx = ref(bank(h), 0, 8)
-        pe([(mx, tl("OHL", h), full("BP"), True, True)])
-        tt(ref("SP", h * n, h * n + n, 16), ref("PM", h * n + 15, h * n + n, 16), mx, A.add)
-        scan(tl("MN", h), full("MF"), tl("SP", h), 0.0, A.mult, A.add)
-        tt(tl("OHT", h), tl("MN", h), ph, A.is_equal)
-        mark("eb", h)
-        if NE > 0:
-            part("GE", "DE", "RE", e0 + n, 0, NE, False)
-        if NE < n:
-            part("GE", "DE", "RE", e0 + n, NE, n, True)
-        sums(pd, "DE", "RE", False)
+        tt(tl("OHT", h), ("ind", tl("PM", h), ref("CL", 0, 8)), key, A.is_equal)
+        oc = ref(bank(), 0, n)
+        pe([(oc, tl("OHT", h), Ib, True, True)])
+        bulk(t, h, 1)
         mark("cc", h)
         tt(tl("MT", h), key, pd, A.is_lt)
-        mk = ref(bank(h), 0, n)
-        pe([(mk, tl("MT", h), full("Ib"), True, True)])
+        mk = ref(bank(), 0, n)
+        pe([(mk, tl("MT", h), Ib, True, True)])
         tt(tl("MM", h), tl("HME", h), mk, A.mult)
-        tt(L["c"], tl("MM", h), he2, A.add)
-        act(tl("CF", h), ("ind", L["w4"], sm("TLL", h, 24, 16)), F.Identity, -2048.0)
-        oc = ref(bank(h), 0, n)
-        pe([(oc, tl("OHT", h), full("Ib"), True, False), (oc, full("Ib"), tl("OHL", h), False, True)])
+        scan(L["c"], tl("MM", h), tl("E", h), -OFS, A.max, A.add)
+        flex("cf", tl("CF", h), ("ind", L["w3"], sm("TLL", h, 16)), OFS - 2048.0)
         tt(tl("PP", h), tl("CF", h), oc, A.mult)
-        vo = ref(bank(h), 0, n)
+        vo = ref(bank(), 0, n)
         if t < NT - 1:
             vo = ref(vo[0], 0, 8)
             pe(ots(vo, tl("PP", h)))
-            cp(L["vb"], vo)
+            ts(L["vb"], vo, 2048.0, A.add)
             send("v", t + 1, h, tiles(t + 1, h)["vh"], L["vb"])
         else:
-            pe(acc(vo, (full("BOh"), tl("PP", h))))
+            pe(acc(vo, (full("BO"), tl("PP", h))))
             act(ref("YU", 512 + h * n, 512 + h * n + n), vo, F.Identity, 2048.0)
             store(T.yv[:, h * n:h * n + n], ref("YU", 512 + h * n, 512 + h * n + n, 1, 0, 128, 16))
         mark("ff", h)
-        act(L["fb"], ("ind", L["w4"], sm("TLL", h, 24, 8)), F.Copy)
         if t < NT - 1:
+            flex("fb", L["fb"], ("ind", L["c"], sm("TLL", h, 16, 8)))
             send("f", t + 1, h, tiles(t + 1, h)["f"], L["fb"])
         else:
+            flex("fb", L["fb"], ("ind", L["c"], sm("TLL", h, 16, 8)), OFS)
             store(T.yf[:, h * n:h * n + n], L["fb"])
 
     def scatter(t, h):
         mark("sc", h)
-        L = tiles(t, h)
-        c0 = L["c"][1]
+        c0 = tiles(t, h)["c"][1]
         for c in range(3, -1, -1):
-            add(pg, "V", 0.18, lambda e, c=c: e.tensor_copy(ap(full("VI")).indirect(ap(ref("OFF", h * 8 + 2 * c, h * 8 + 2 * c + 2))), ap(ref("W", c0 + 32 * c, c0 + 32 * c + 32))),
-                [ref("OFF", h * 8 + 2 * c, h * 8 + 2 * c + 2), ref("W", c0 + 32 * c, c0 + 32 * c + 32)], [full("VI")], tag="scatter")
+            off, src = ref("OFF", h * 8 + 2 * c, h * 8 + 2 * c + 2), ref("W", c0 + 32 * c, c0 + 32 * c + 32)
+            add(pg, "V", CO["scat"], lambda e, off=off, src=src: e.tensor_copy(ap(full("VI")).indirect(ap(off)), ap(src)), [off, src], [full("VI")], tag="scatter")
 
-    front(0, 1)
-    sel(full("BOg"), full("BO"), [[1, 128]], A.is_gt, 0.0, 0, -1)
-    iota(full("LTJ"), [[0, 2048]], 0, 0, True)
-    for j in range(16):
-        act(ref("LTJ", 128 * j + j, 128 * j + 128, 16), ref("BOg", j, 128, 16), F.Copy)
-    fill(ref("VI", 4096, 4096 + 2 * n), 0.0)
-    front(0, 0)
     for t in range(NT):
-        for h in (1, 0):
-            if t > 0 and h == 1:
-                pass
-            early(t, h)
-            dedupe(t, h)
-            bulk(t, h)
-            scatter(t, h)
-            if t < NT - 1 and h == 1:
-                pass
-        if t < NT - 1:
-            front(t + 1, 1)
-            front(t + 1, 0)
+        pg["hop"] = t
+        front(t, 1)
+        front(t, 0)
+        early(t, 1)
+        tail(t, 1)
+        dedupe(t)
+        early(t, 0)
+        tail(t, 0)
+        scatter(t, 1)
+        scatter(t, 0)
     pg["st"] = ""
-    for c in (3, 0, 1, 2):
+    for c in range(4):
         a, b = 512 * c, 512 * c + 512
-        if c == 3:
-            yb = ref(bank(0), 0, 512)
-            pe(acc(yb, (full("If"), ref("VI", a, b)), (full("I4k"), ref("VI", 2048 + a, 2048 + b))))
-            act(ref("YT", a, b), yb, F.Copy)
-            store(T.yw[:, a:b], ref("YT", a, b))
-            continue
-        act(ref("YT", a, b), ref("VI", 2048 + a, 2048 + b), F.Copy, 0.0, 4096.0)
-        tt(ref("YT", a, b), ref("YT", a, b), ref("VI", a, b), A.add)
+        act(ref("W613", a, b), ref("VI", 2048 + a, 2048 + b), F.Identity, OFS * 4097.0, 4096.0)
+        scan(ref("YT", a, b), ref("VI", a, b), ref("W613", a, b), 0.0, A.min, A.add)
         store(T.yw[:, a:b], ref("YT", a, b))
     pg["nls"], pg["nout"] = nls[0], nout[0]
     return pg
+
+
+ORDER = []
 
 
 def rank_program(g, core, T, topo):
     rank = T.rank_of(core)
     if rank is None:
         return
+    if not ORDER:
+        ORDER.append(plan(T, topo, core, rank))
     pg = build(T, topo, core, rank)
-    schedule(pg)
-    emit(pg, g, T)
+    emit(pg, ORDER[0], g, T)
     g.wait_ge(T.sem["ls"], int(pg["nls"]))
     g.wait_ge(T.sem["out"], int(pg["nout"]))

@@ -9,12 +9,15 @@ NT = 5
 XW = 32 + 3 * n
 WW = 3 * n
 MAGIC = 12582912.0
-OFS = 8192.0
+OFS = 2.0 ** 24
+QP = True
 HC = 262000
 NOH = 4112
-PARTS = (((0, 64, "S"), (64, 128, "S")), ((0, 64, "S"), (64, 128, "S")))
+OH0 = 1024
+PARTS = ((((0, 64, "S"), (64, 128, "S")), ((0, 64, "S"), (64, 128, "S"))),) * 2
 CHUNKS = (((0, 64), (64, 128)), ((0, 64), (64, 128)))
-ONV = ("cf", "key")
+ONV = ("hz0", "hz1")
+LINES = ((),) * NT
 SPLIT = 8
 f4, b2, h2, i4, u2 = "float32", "bfloat16", "float16", "int32", "uint16"
 
@@ -22,12 +25,13 @@ SCRATCH = {
     "PX": ("sbuf", [128, 4096], b2), "VI": ("sbuf", [128, 4096 + 32], f4), "VW": ("sbuf", [128, 2048], i4),
     "IT": ("sbuf", [128, 2048], i4), "YT": ("sbuf", [128, 2048], f4), "YU": ("sbuf", [128, 2048], f4),
     "W613": ("sbuf", [128, 4096 + 8], f4), "OHW": ("sbuf", [128, NOH], b2),
-    "XZ": ("sbuf", [128, 10 * XW], b2), "W": ("sbuf", [128, 10 * WW], f4), "VH": ("sbuf", [128, 10 * 8], u2),
-    "ZB": ("sbuf", [128, 8 * (32 + n)], b2), "FB": ("sbuf", [128, 10 * n], f4), "VB": ("sbuf", [128, 10 * 8], u2), "ZL": ("sbuf", [128, 2 * n], b2),
+    "XZ": ("sbuf", [128, 10 * XW], b2), "W": ("sbuf", [128, 10 * WW], i4), "VH": ("sbuf", [128, 10 * 8], u2),
+    "ZB": ("sbuf", [128, 8 * (32 + n)], b2), "FB": ("sbuf", [128, 10 * n], i4), "SPT": ("sbuf", [128, 16], f4), "CK": ("sbuf", [128, 16], b2), "VB": ("sbuf", [128, 10 * 8], u2), "ZL": ("sbuf", [128, 2 * n], b2),
     "E": ("sbuf", [128, 2 * n], f4), "HEL": ("sbuf", [128, 4 * n], u2), "QS": ("sbuf", [128, 16 * n], b2), "QX": ("sbuf", [128, 32 * n], b2),
     "GH": ("sbuf", [128, 32 * n], b2), "GE": ("sbuf", [128, 32 * n], b2), "MH": ("sbuf", [128, 32 * n], b2), "ME": ("sbuf", [128, 32 * n], b2),
     "IND": ("sbuf", [128, 2 * n], b2), "LK": ("sbuf", [128, 16], b2), "LSL": ("sbuf", [128, 16], u2),
     "HI1": ("sbuf", [128, 2 * n], i4), "HI2": ("sbuf", [128, 2 * n], i4), "FL": ("sbuf", [128, 2 * n], h2),
+    "T2": ("sbuf", [128, 2 * n], f4),
     "OV": ("sbuf", [128, 16], b2), "TLL": ("sbuf", [128, 32], u2), "RA": ("sbuf", [128, 48], b2), "KL": ("sbuf", [128, 16], u2), "OHL": ("sbuf", [128, 2 * n], b2),
     "VF": ("sbuf", [128, 16], h2), "VN": ("sbuf", [128, 16], f4), "DL": ("sbuf", [128, 24], u2), "G1": ("sbuf", [128, 384], f4), "EQ": ("sbuf", [128, 384], b2),
     "DS": ("sbuf", [128, 384], b2), "OFF": ("sbuf", [128, 16], u2),
@@ -43,20 +47,22 @@ SCRATCH = {
     "CS": ("sbuf", [128, 24], b2), "CL": ("sbuf", [128, 32], u2), "WT": ("sbuf", [128, 2], i4), "WTf": ("sbuf", [128, 8], f4),
 }
 DIAG = {"Ib": (1.0, b2), "In": (-1.0, b2), "I2": (2.0, b2), "Ic": (0.00689697265625, b2), "Icn": (-0.00689697265625, b2), "Ihz": (0.5 - 2.0 ** -11, h2),
-        "I128": (128.0, b2), "I256": (256.0, b2), "Ip100": (100.0, b2), "Im100": (-100.0, b2), "I8k": (8192.0, b2), "I8kn": (-8192.0, b2), "I8200": (8200.0, h2),
+        "I1": (1.0 / 128, b2), "Ip100": (100.0 / 128, b2), "Im100": (-100.0 / 128, b2), "I8k": (8192.0 / 128, b2), "I8kn": (-8192.0 / 128, b2), "I8200": (8200.0 / 128, h2),
         "I4kn": (-4096.0, b2), "Ibig": (-262144.0, b2), "Ifl": (0.4375, b2), "I16": (16.0, b2)}
 for _k in DIAG:
     SCRATCH[_k] = ("sbuf", [128, 128], DIAG[_k][1])
 for _b in range(8):
     SCRATCH["b%d" % _b] = ("psum", [128, 512], f4)
 LOADS = ["px0", "px1", "vw0", "vw1", "z0", "z1", "f0", "v0", "d0", "wt", "kap"]
-SEMAPHORES = ["V", "S", "P", "G", "out", "ls"] + ["ld_" + x for x in LOADS] + ["r%s_%d_%d" % (k, t, h) for k in "zfv" for t in range(1, NT) for h in range(2)]
+SEMAPHORES = ["V", "S", "P", "G", "out", "ls", "oh"] + ["ld_" + x for x in LOADS] + ["r%s_%d_%d" % (k, t, h) for k in "zfv" for t in range(1, NT) for h in range(2)]
 
-COSTS = ({"cy": 0.00083, "gather": 1.56, "wake": 0.10, "pe": 0.00055, "link": 1.9, "scat": 0.18},
-         {"cy": 0.00083, "gather": 1.1, "wake": 0.08, "pe": 0.00045, "link": 1.6, "scat": 0.12},
-         {"cy": 0.00108, "gather": 1.8, "wake": 0.15, "pe": 0.0006, "link": 2.5, "scat": 0.25})
-FIX = {"V": 0.03, "S": 0.04, "P": 0.03, "G": 0.05, "Y": 0.05}
-ROUNDS = 3000
+COSTS = tuple(dict(zip(("cy", "gather", "wake", "pe", "link", "scat", "V", "S", "P", "row", "issue", "load"), c)) for c in (
+    (0.00083, 1.56, 0.10, 0.00055, 1.4, 0.18, 0.03, 0.04, 0.03, 1.0, 0.4, 1.0),
+    (0.00083, 1.10, 0.07, 0.00042, 1.0, 0.12, 0.03, 0.04, 0.03, 0.7, 0.3, 0.9),
+    (0.00108, 1.80, 0.15, 0.00070, 2.0, 0.25, 0.04, 0.05, 0.04, 1.5, 0.8, 1.3),
+    (0.00083, 1.56, 0.12, 0.00042, 1.8, 0.14, 0.06, 0.07, 0.02, 1.2, 0.6, 1.2),
+    (0.00090, 1.40, 0.08, 0.00070, 1.1, 0.22, 0.03, 0.04, 0.05, 0.8, 0.4, 1.0)))
+ROUNDS = 6000
 STAGGER = 7.0
 
 
@@ -79,10 +85,10 @@ def touch(pg, o, r, wr):
         over = a0 < c1 and c0 < a1 and not (st == r[3] and (a0 - c0) % st)
         if p != o["i"]:
             if psum:
-                if ops[p]["q"] != o["q"]:
-                    o["dep"].add(p)
-                elif o["q"] == "P":
+                if ops[p]["q"] == o["q"] == "P":
                     o["ord"].add(p)
+                elif ops[p]["q"] != o["q"] or ops[p]["alt"] or o["alt"]:
+                    o["dep"].add(p)
             elif over and (wr or aw):
                 o["dep"].add(p)
         if wr and a0 >= c0 and a1 <= c1 and p != o["i"] and not psum and r[3] == 1 and r[6] == 1 and r[4] == 0 and r[5] == 128:
@@ -92,13 +98,14 @@ def touch(pg, o, r, wr):
     pg["acc"][name] = keep
 
 
-def add(pg, q, cost, fn, rd, wr, sem=None, val=1, lat=0.0, tag=""):
-    o = {"i": len(pg["ops"]), "q": q, "cost": cost, "fn": fn, "dep": set(), "ord": set(), "sem": sem, "val": val, "lat": lat, "send": None, "tag": tag, "st": pg["st"], "hop": pg["hop"]}
+def add(pg, q, cost, fn, rd, wr, sem=None, val=1, lat=0.0, tag="", alt=None):
+    o = {"i": len(pg["ops"]), "q": q, "alt": alt, "cost": cost, "fn": fn, "dep": set(), "ord": set(), "sem": sem, "val": val, "lat": lat, "send": None, "tag": tag, "st": pg["st"], "hop": pg["hop"]}
     pg["ops"].append(o)
     for r in rd:
         touch(pg, o, r, False)
     for r in wr:
         touch(pg, o, r, True)
+    o["near"] = o["dep"]
     o["tiles"] = sorted(set(r[0] for r in list(rd) + list(wr) if is_psum(r[0])))
     return o["i"]
 
@@ -107,11 +114,10 @@ def place(key, pred, succ, q, cost, head):
     cnt = [len(p) for p in pred]
     ready = [(key[i], i) for i in range(len(key)) if cnt[i] == 0]
     st = [0.0] * len(key)
-    S, E = {}, {}
+    S, E = {x: [] for x in set(q)}, {x: [] for x in set(q)}
     while ready:
-        x = min(ready)
-        ready.remove(x)
-        i = x[1]
+        ready.sort(reverse=True)
+        i = ready.pop()[1]
         t = head[i]
         for d, w in pred[i]:
             x = st[d] + cost[d] + w
@@ -119,7 +125,7 @@ def place(key, pred, succ, q, cost, head):
                 t = x
         c = cost[i]
         if c > 0:
-            s, e = S.setdefault(q[i], []), E.setdefault(q[i], [])
+            s, e = S[q[i]], E[q[i]]
             m = k = len(s)
             while k > 0 and e[k - 1] > t:
                 k -= 1
@@ -136,25 +142,30 @@ def place(key, pred, succ, q, cost, head):
     return st
 
 
-def replay(ops, seq, c, dyn, uses=None):
+def priced(ops, qs):
+    return [o["alt"][q][0] if o["alt"] else o["cost"] for o, q in zip(ops, qs)]
+
+
+def replay(ops, qs, seq, c, dyn, uses=None):
     cost, lat, wake = c
     fin = [0.0] * len(ops)
-    free, bmap, held = {}, {}, {}
+    free, bmap, held = {q: 0.0 for q in set(qs)}, {}, {}
     bfree = {b: (0.0, []) for b in range(8)}
     for i in seq:
         o = ops[i]
-        q = o["q"]
-        st = free.get(q, 0.0)
-        for d in o["dep"]:
-            if fin[d] + wake > st:
-                st = fin[d] + wake
+        q = qs[i]
+        st = free[q] - wake
+        for d in o["near"]:
+            if fin[d] > st:
+                st = fin[d]
+        if uses is None and i in dyn:
+            for d in dyn[i]:
+                if fin[d] > st:
+                    st = fin[d]
+        st += wake
         if o["send"] is not None:
             st = max(st, fin[o["send"]])
-        if uses is None:
-            for d in dyn.get(i, ()):
-                if fin[d] + wake > st:
-                    st = fin[d] + wake
-        else:
+        if uses is not None:
             for t in o["tiles"]:
                 if t not in bmap:
                     if not bfree:
@@ -177,22 +188,47 @@ def replay(ops, seq, c, dyn, uses=None):
     return max(fin), bmap
 
 
-def schedule(pg, cs, rounds, seed):
-    ops = pg["ops"]
+def schedule(pgs, wakes, rounds, seed):
+    ops = pgs[0]["ops"]
     N_ = len(ops)
+    q = [o["q"] for o in ops]
+    prices = lambda qs: [(priced(p["ops"], qs), [o["lat"] for o in p["ops"]], w) for p, w in zip(pgs, wakes)]
+    cs = prices(q)
     cost, lat, wake = cs[0]
     pred, succ = [[] for _ in ops], [[] for _ in ops]
     uses, phase, seen, slot = {}, {}, {}, {}
-    for o in ops:
-        i = o["i"]
+    topo_, state, above = [], [0] * N_, [0] * N_
+    for root in range(N_):
+        stack = [root]
+        while stack:
+            i = stack[-1]
+            o = ops[i]
+            if state[i] == 0:
+                state[i] = 1
+                stack.extend(d for d in o["dep"] | o["ord"] | {o["send"]} if d is not None and state[d] == 0)
+            else:
+                stack.pop()
+                if state[i] == 1:
+                    state[i] = 2
+                    topo_.append(i)
+    for i in topo_:
+        o = ops[i]
         e = {d: wake + lat[d] for d in o["dep"]}
         for d in o["ord"]:
             e.setdefault(d, 0.0)
         if o["send"] is not None:
             e[o["send"]] = lat[o["send"]]
+        for d in o["dep"]:
+            above[i] |= above[d]
+        o["near"] = [d for d in sorted(o["dep"]) if lat[d] or not above[i] >> d & 1]
         for d in sorted(e):
-            pred[i].append((d, e[d]))
-            succ[d].append((i, e[d]))
+            if d in o["near"] or d not in o["dep"]:
+                pred[i].append((d, e[d]))
+                succ[d].append((i, e[d]))
+        for d in o["dep"]:
+            above[i] |= 1 << d
+    for o in ops:
+        i = o["i"]
         for t in o["tiles"]:
             uses[t] = uses.get(t, 0) + 1
         phase.setdefault(o["st"], []).append(i)
@@ -201,32 +237,43 @@ def schedule(pg, cs, rounds, seed):
             seen[k] = seen.get(k, 0) + 1
             slot.setdefault((o["st"], o["tag"], seen[k]), []).append(i)
     phases, slots = list(phase.values()), list(slot.values())
-    q = [o["q"] for o in ops]
+    either = [sl for sl in slots if ops[sl[0]]["alt"]] + [[o["i"]] for o in ops if o["alt"] and not o["st"]]
     zero = [0.0] * N_
     way = [0.0] * N_
-    for i in range(N_ - 1, -1, -1):
+    for i in reversed(topo_):
         way[i] = max([way[j] + w for j, w in succ[i]] + [lat[i]]) + cost[i]
     first = []
 
-    def judge(st):
+    def judge(st, q, cs):
         seq = sorted(range(N_), key=lambda i: (st[i], i))
         dyn = {}
-        f, bmap = replay(ops, seq, cs[0], dyn, dict(uses))
+        f, bmap = replay(ops, q, seq, cs[0], dyn, dict(uses))
         if f is None:
             return 1e9, None
-        r = [f] + [replay(ops, seq, c, dyn)[0] for c in cs[1:]]
+        if keep and f > keep[3][0] * 1.015:
+            return 1e9, None
+        r = [f] + [replay(ops, q, seq, c, dyn)[0] for c in cs[1:]]
         if not first:
             first.extend(r)
-        return sum(x / y for x, y in zip(r, first)) / len(r), (seq, dyn, bmap, r, st)
+        return sum(x / y for x, y in zip(r, first)) / len(r), (seq, dyn, bmap, r, st, q)
 
     rng = np.random.default_rng(seed)
     cur = [-way[o["i"]] + (STAGGER if o["st"][-1:] == "0" else 0.0) for o in ops]
     now, best, keep = 1e9, 1e9, None
     for it in range(rounds):
-        key = list(cur)
-        mode, d, a = int(rng.integers(5)), float(rng.normal()), float(rng.uniform(min(cur), max(cur)))
+        key, q2, cs2 = list(cur), q, cs
+        mode, d, a = int(rng.integers(7)), float(rng.normal()), float(rng.uniform(min(cur), max(cur)))
         if it == 0:
             pass
+        elif mode >= 5:
+            sl = either[int(rng.integers(len(either)))]
+            q2 = list(q)
+            to = "V" if q[sl[int(rng.integers(len(sl)))]] == "S" else "S"
+            cs2 = [(list(c[0]), c[1], c[2]) for c in cs]
+            for i in (sl if mode == 5 else [sl[int(rng.integers(len(sl)))]]):
+                q2[i] = to
+                for c, p in zip(cs2, pgs):
+                    c[0][i] = p["ops"][i]["alt"][to][0]
         elif mode == 0:
             for t in rng.integers(len(phases), size=int(rng.integers(1, 4))):
                 d = float(rng.normal(0, rng.choice([0.5, 1.5, 4.0])))
@@ -251,21 +298,20 @@ def schedule(pg, cs, rounds, seed):
                         d = float(rng.normal(0, 0.7))
                     for i in sl:
                         key[i] += d
-        st = place(key, pred, succ, q, cost, zero)
-        back = place([-(st[i] + cost[i]) for i in range(N_)], succ, pred, q, cost, lat)
-        for x in (st, place([-(back[i] + cost[i]) for i in range(N_)], pred, succ, q, cost, zero)):
-            f, info = judge(x)
+        cost = cs2[0][0]
+        st = place(key, pred, succ, q2, cost, zero)
+        back = place([-(st[i] + cost[i]) for i in range(N_)], succ, pred, q2, cost, lat)
+        for x in (st, place([-(back[i] + cost[i]) for i in range(N_)], pred, succ, q2, cost, zero)):
+            f, info = judge(x, q2, cs2)
             if f <= now + 0.002 * (1 - it / rounds) * float(rng.exponential()):
-                now, cur = f, x
+                now, cur, q, cs = f, x, q2, cs2
             if f < best:
                 best, keep = f, info
     return keep
 
 
 def plan(T, topo, core, rank, rounds=None, seed=1):
-    pgs = [build(T, topo, core, rank, c) for c in COSTS]
-    cs = [([o["cost"] for o in p["ops"]], [o["lat"] for o in p["ops"]], c["wake"]) for p, c in zip(pgs, COSTS)]
-    return schedule(pgs[0], cs, rounds or ROUNDS, seed)
+    return schedule([build(T, topo, core, rank, c) for c in COSTS], [c["wake"] for c in COSTS], rounds or ROUNDS, seed)
 
 
 def emit(pg, keep, g, T):
@@ -276,7 +322,7 @@ def emit(pg, keep, g, T):
     pos, key, know, count, qk = {}, {}, {}, {}, {}
     for i in seq:
         o = ops[i]
-        q = o["q"]
+        q = keep[5][i]
         if o["sem"] is None:
             count[q] = count.get(q, 0) + 1
             key[i], pos[i] = q, count[q]
@@ -300,7 +346,7 @@ def emit(pg, keep, g, T):
                 for kk, v in know[d].items():
                     if kn.get(kk, 0) < v:
                         kn[kk] = v
-            ins = o["fn"](eng[q])
+            ins = (o["alt"][q][1] if o["alt"] else o["fn"])(eng[q])
             if o["sem"] is None:
                 ins.then_inc(T.sem[q], 1)
         me = dict(kn) if o["send"] is None else {}
@@ -312,7 +358,7 @@ def emit(pg, keep, g, T):
 
 def build(T, topo, core, rank, CO=COSTS[0]):
     pg = {"ops": [], "acc": {}, "rr": [0], "st": "", "hop": 0, "bmap": {}}
-    CY, GC, PEC = CO["cy"], CO["gather"], CO["pe"]
+    CY, GC, PEC, FIX = CO["cy"], CO["gather"], CO["pe"], CO
 
     def ap(r):
         name, c0, c1, step, p0, p1, ps = r
@@ -372,10 +418,19 @@ def build(T, topo, core, rank, CO=COSTS[0]):
         return add(pg, "S", FIX["S"] + CY * max(64, cnt(out) * (GC if ind else 1)) + (0.04 if ind else 0),
                    lambda e: e.activation(ap(out), inap(in_), func, bias=dcol(bias), scale=dcol(scale)), regs(in_) + sc, [out], tag="act " + out[0])
 
-    def flex(name, out, in_, bias=0.0):
-        if name in ONV:
-            return ts(out, in_, bias, A.add) if bias else cp(out, in_)
-        return act(out, in_, F.Identity if bias else F.Copy, bias)
+    def flex(q, out, in_, bias=0.0, scale=1.0, relu=False):
+        ind = in_[0] == "ind"
+        sc = [scale] if isinstance(scale, tuple) else []
+        if scale == 1.0:
+            fv = (lambda e: e.tensor_scalar(ap(out), inap(in_), bias, None, A.add)) if bias else (lambda e: e.tensor_copy(ap(out), inap(in_)))
+        else:
+            fv = lambda e: e.tensor_scalar(ap(out), inap(in_), dcol(scale), bias, A.mult, A.add)
+        fs = lambda e: e.activation(ap(out), inap(in_), F.Relu if relu else F.Identity if bias else F.Copy, bias=bias, scale=dcol(scale))
+        if relu:
+            fv = lambda e: e.tensor_scalar(ap(out), inap(in_), 0.0, None, A.max)
+        alt = {"V": (vcost(cnt(out), 0.5 if (not ind and two(out, in_)) else 1, ind), fv),
+               "S": (FIX["S"] + CY * max(64, cnt(out) * (GC if ind else 1)) + (0.04 if ind else 0), fs)}
+        return add(pg, q, alt[q][0], None, regs(in_) + sc, [out], tag="flex " + out[0], alt=alt)
 
     def pe(mms, sub=False):
         cost = 0.0
@@ -411,7 +466,7 @@ def build(T, topo, core, rank, CO=COSTS[0]):
 
     def load(name, out, src, lat, q="Y"):
         s = "ld_" + name
-        return add(pg, q, 0.1, lambda e: e.dma_start(ap(out), src).then_inc(T.sem[s], 16), [], [out], sem=s, val=16, lat=lat, tag="load " + name)
+        return add(pg, q, 0.1, lambda e: e.dma_start(ap(out), src).then_inc(T.sem[s], 16), [], [out], sem=s, val=16, lat=lat * CO["load"], tag="load " + name)
 
     nout = [0]
 
@@ -423,14 +478,18 @@ def build(T, topo, core, rank, CO=COSTS[0]):
     rid, pid, _se = topo.addr(dst)
     mask = sum(1 << e for e in topo.engines(core, dst))
     neng = len(topo.engines(core, dst))
-    nls = [0]
+    nls, sent = [0], [None]
 
     def send(kind, t, h, out, in_):
         s = "r%s_%d_%d" % (kind, t, h)
         nls[0] += neng
-        i = add(pg, "G", 0.4, lambda e: e.remote_dma(ap(out), ap(in_), T.sem[s], T.sem["ls"], pid, rid, mask), [in_], [], sem="ls", val=nls[0], lat=CO["link"], tag="send " + kind)
+        i = add(pg, "G", CO["issue"] * (1 if sent[0] else 8), lambda e: e.remote_dma(ap(out), ap(in_), T.sem[s], T.sem["ls"], pid, rid, mask), [in_], [], sem="ls", val=nls[0], tag="send " + kind)
+        d = add(pg, "RD", CO["row"] * {"v": 0.8, "z": 1.3, "f": 1.6}[kind], None, [], [], sem="-", lat=CO["link"], tag="rows " + kind)
         j = add(pg, "R" + s, 0.0, None, [], [out], sem=s, val=neng)
-        pg["ops"][j]["send"] = i
+        pg["ops"][d]["send"], pg["ops"][j]["send"] = i, d
+        if kind == "f":
+            pg["ops"][i]["ord"].add(sent[0])
+        sent[0] = i
 
     sm = lambda name, h, w=8, x=0, k=8: ref(name, h * w + x, h * w + x + k)
     tl = lambda name, h: ref(name, h * n, h * n + n)
@@ -469,11 +528,12 @@ def build(T, topo, core, rank, CO=COSTS[0]):
     iota(ref("PI", 0, 1), [[0, 1]], 0, 1, False)
     iota(full("IJ"), [[1, 16]], 0, 0)
     iota(ref("CMI", 0, 8), [[16, 8]], 0, 0)
-    iota(ref("W613", 0, 1024), [[613, 1024]], HC, 0)
-    act(ref("W613", 1024, 2048), ref("W613", 0, 1024), F.Identity, 613.0 * 1024)
-    act(ref("W613", 2048, 4096), ref("W613", 0, 2048), F.Identity, 613.0 * 2048)
-    fill(ref("W613", 4096, 4104), -1.0)
-    iota(full("MK"), [[0, n], [256, 16]], 0, 0)
+    fill(ref("W613", 0, 8), -1.0)
+    iota(ref("W613", 8, 1032), [[613, 1024]], HC - 2 ** 23, 0)
+    act(ref("W613", 1032, 2056), ref("W613", 8, 1032), F.Identity, 613.0 * 1024)
+    act(ref("W613", 2056, 4104), ref("W613", 8, 2056), F.Identity, 613.0 * 2048)
+    fill(full("MK"), 256.0)
+    fill(ref("MK", 0, 16 * n, 16), 0.0)
     iota(full("KC"), [[0, 8], [1, 16]], 0, 0)
     for j, b in enumerate((0, 1, 1)):
         iota(ref("CMI", 8 + j, 32, 3), [[2, 8]], b, 0)
@@ -487,7 +547,7 @@ def build(T, topo, core, rank, CO=COSTS[0]):
         iota(ref("ZB", k * (32 + n) + 24, k * (32 + n) + 32), [[0, 8]], 0, 0)
     iota(full("ZE"), [[0, 128]], 0, 0)
     for nm in DIAG:
-        if nm in ("Ibig", "Ifl", "I16", "I8k", "I256", "Ip100", "I8kn"):
+        if nm in ("Ibig", "Ifl", "I16", "I8k", "I1", "Ip100", "I8kn"):
             sel(full(nm), full("ZE"), [[-1, 128]], A.not_equal, DIAG[nm][0], 0, 1)
         elif DIAG[nm][1] == h2:
             ts(full(nm), Ib, DIAG[nm][0], A.mult)
@@ -497,12 +557,13 @@ def build(T, topo, core, rank, CO=COSTS[0]):
     ts(ref("PI", 24, 25), ref("PI", 0, 1), 1, A.bitwise_and)
     pm, sg, sg256, dg, sp0, sp1 = [ref("PC", 4 * i, 4 * i + 1) for i in range(6)]
     cp(pm, ref("PI", 16, 17))
-    ts(sg, ref("PI", 24, 25), -2.0, A.mult, 1.0, A.add)
-    ts(sg256, ref("PI", 24, 25), -2.0, A.mult, 257.0, A.add)
+    ts(sg, ref("PI", 24, 25), -2.0 / 128, A.mult, 1.0 / 128, A.add)
+    ts(sg256, ref("PI", 24, 25), -2.0 / 128, A.mult, 257.0 / 128, A.add)
     ts(dg, pm, 15.0, A.is_equal, 8192.0 - 2.0 ** -5, A.mult)
     ts(dg, dg, 2.0 ** -5, A.add)
-    ts(sp0, pm, 4096.0, A.add)
-    ts(sp1, pm, 4112.0, A.add)
+    iota(full("SPT"), [[0, 8], [16, 2]], 4096, 0)
+    ts(full("SPT"), full("SPT"), pm, A.add)
+    iota(full("CK"), [[0, 16]], 10240, 0)
     ts(full("G0"), Ib, sg, A.mult)
     ts(full("G256"), Ib, sg256, A.mult)
     ts(full("DG"), Ib, dg, A.mult)
@@ -522,23 +583,26 @@ def build(T, topo, core, rank, CO=COSTS[0]):
     ts(ref("CM", 8, 16), ref("CMI", 0, 8), pm, A.add)
     act(ref("Sb", 0, 128, 2), ref("Ib", 1, 128, 2), F.Copy)
     act(ref("Sb", 1, 128, 2), ref("Ib", 0, 128, 2), F.Copy)
-    act(full("Sb100"), full("Sb"), F.Copy, 0.0, 100.0)
+    act(full("Sb100"), full("Sb"), F.Copy, 0.0, 100.0 / 128)
     fill(full("QS"), 0.0)
     fill(ref("VI", 4096, 4096 + 32), 0.0)
     fill(ref("OHW", 0, 16), 0.0)
     ts(ref("OHW", 16, 32), full("IJ"), pm, A.is_equal)
     w = 16
-    while w < 4096:
-        for a in range(0, w, 1024):
-            act(ref("OHW", 16 + w + a, 16 + w + min(w, a + 1024)), ref("OHW", 16 + a, 16 + min(w, a + 1024)), F.Copy)
+    while w < OH0:
+        cp(ref("OHW", 16 + w, 16 + 2 * w), ref("OHW", 16, 16 + w))
         w *= 2
+    for a in range(w, 4096, w):
+        i = add(pg, "Y", 0.1, lambda e, a=a: e.dma_start(ap(ref("OHW", 16 + a, 16 + a + w)), ap(ref("OHW", 16, 16 + w))).then_inc(T.sem["oh"], 16),
+                [ref("OHW", 16, 16 + w)], [ref("OHW", 16 + a, 16 + a + w)], sem="oh", val=16 * (4096 // w - 1), lat=9.5, tag="copy")
+        pg["ops"][i]["ord"].add(loads[-1])
     fill(ref("D0", 16, 32), 1.0)
     ts(ref("D0", 0, 16), full("IJ"), pm, A.is_equal, 262144.0, A.mult)
     ts(ref("D0", 0, 16), ref("D0", 0, 16), 1.0, A.max)
     cp(ref("D0", 32, 48), ref("D0", 0, 16))
     fill(ref("D0", 0, 32, 16), 0.0)
-    for w in (48, 96, 192):
-        act(ref("D0", w, 2 * w), ref("D0", 0, w), F.Copy)
+    for a in (48, 96, 192):
+        act(ref("D0", a, 2 * a), ref("D0", 0, a), F.Copy)
 
     def ots(out, tile, first=(), last=()):
         prs = list(first)
@@ -546,22 +610,20 @@ def build(T, topo, core, rank, CO=COSTS[0]):
             prs.append((ref("Bh", 15 - j, 143 - j), ref(tile[0], tile[1] + j, tile[2], 16)))
         return acc(out, *(prs + list(last)))
 
-    ts(ref("VZh", 0, 512, 1, 0, 8), ref("VZ", 0, 512, 1, 0, 8), -2048.0, A.add)
+    flex("V", ref("VZh", 0, 512, 1, 0, 8), ref("VZ", 0, 512, 1, 0, 8), -2048.0)
     b6 = bank()
     pe(acc(ref(b6, 0, 32), *[(ref("B8", 15 - j, 143 - j, 1, 0, 8), ref("VZh", j, 512, 16, 0, 8)) for j in range(16)]))
-    ts(ref("VH", 0, 16), ref(b6, 0, 16), 2048.0, A.add)
+    flex("V", ref("VH", 0, 16), ref(b6, 0, 16), 2048.0)
     for h in (1, 0):
-        ts(ref("XZ", h * XW, h * XW + 8), ref(b6, 16 + 8 * h, 24 + 8 * h), 2048.0, A.add)
+        flex("S", ref("XZ", h * XW, h * XW + 8), ref(b6, 16 + 8 * h, 24 + 8 * h), 2048.0)
         fill(ref("XZ", h * XW + 8, h * XW + 24), 0.0)
-        ts(ref("W", h * WW + n, h * WW + 2 * n), ref("FI", h * n, h * n + n), -OFS, A.add)
-    M12 = 1.5 * 2.0 ** 35
+        flex("S", ref("W", h * WW + n, h * WW + 2 * n), ref("FI", h * n, h * n + n), -OFS)
     for c in range(2):
-        x = ref("VW", 1024 * c, 1024 * c + 1024)
-        it, yt = ref("IT", 1024 * c, 1024 * c + 1024), ref("YT", 1024 * c, 1024 * c + 1024)
-        ts(yt, x, -(2047 * 4096 + 2047.5), A.add, M12, A.add)
-        act(ref("VI", 2048 + 1024 * c, 3072 + 1024 * c), yt, F.Identity, 2047.0 - OFS - MAGIC, 2.0 ** -12)
+        x, it = ref("VW", 1024 * c, 1024 * c + 1024), ref("IT", 1024 * c, 1024 * c + 1024)
         ts(it, x, 4095, A.bitwise_and)
-        ts(ref("VI", 1024 * c, 1024 * c + 1024), it, -OFS, A.add)
+        flex("S", ref("VI", 1024 * c, 1024 * c + 1024), it, -OFS)
+        ts(x, x, 12, A.arith_shift_right)
+        flex("S", ref("VI", 2048 + 1024 * c, 3072 + 1024 * c), x, -OFS)
 
     def tiles(t, h):
         k = 2 * t + h
@@ -590,62 +652,64 @@ def build(T, topo, core, rank, CO=COSTS[0]):
         a, c = tl("HI1", h), tl("HI2", h)
         y = ref(bank(), 0, n)
         pe(acc(y, (full("WB"), L["z"])))
-        ts(tl("FL", h), y, 2.0 ** -12, A.mult, 1535.5 + 2.0 ** -13, A.add)
+        flex("V", tl("FL", h), y, 1535.5 + 2.0 ** -13, 2.0 ** -12)
         pe(acc(y, (full("CH"), on), (full("WB"), L["z"]), (full("I4kn"), tl("FL", h))))
-        ts(a, y, kcol, A.mult, -(HC + 31.0 / 64), A.add)
+        flex("V", a, y, -(HC + 31.0 / 64), kcol)
         mark("ha", h)
-        tt(c, ("ind", full("W613"), vh), a, A.add)
-        ts(a, c, 4095, A.bitwise_and)
-        ts(L["hd"], a, -OFS, A.add)
+        tt(c, ("ind", ref("W613", 8, 4104), vh), a, A.add)
+        ts(L["hd"], c, 4095 - int(OFS), A.bitwise_and)
         mark("fr", h)
-        flex("x", L["x"], ("ind", px, vh))
+        flex("S", L["x"], ("ind", px, vh))
         bk = bank()
         dx, hz = ref(bk, 0, n), ref(bk, n, 2 * n)
         pe(acc(dx, (full("Icn"), L["z"]), (full("Ic"), L["x"])))
         ts(tl("IND", h), dx, MAGIC, A.add, MAGIC, A.is_equal)
         mark("hz", h)
         pe(acc(hz, (full("Ihz"), L["z"]), (full("Ihz"), L["x"])))
-        ts(L["hz"], hz, MAGIC, A.add, -MAGIC, A.add)
+        if "hz%d" % h in ONV:
+            ts(L["hz"], hz, MAGIC, A.add, -MAGIC, A.add)
+        else:
+            act(tl("T2", h), hz, F.Identity, MAGIC)
+            act(L["hz"], tl("T2", h), F.Identity, -MAGIC)
         mark("fr", h)
         ct = ref(bank(), 0, 8)
         pe(ots(ct, tl("IND", h), [(full("In"), L["st"](1)), (full("I2"), L["st"](2))]))
         lk = sm("LK", h)
-        ts(lk, ct, 8.5, A.is_ge)
-        b = ref(bank(), 0, 8)
-        pe(acc(b, (Ib, ref("CM", 0, 8)), (full("I128"), lk)))
-        cp(sm("LSL", h), b)
+        ts(lk, ct, 8.5, A.is_ge, 128.0, A.mult)
+        tt(sm("LSL", h), lk, ref("CM", 0, 8), A.add)
         mark("h", h)
-        ts(ref("HEL", 2 * h * n, 2 * h * n + n), ("ind", L["w2"], sm("LSL", h)), OFS, A.add)
+        flex("V", ref("HEL", 2 * h * n, 2 * h * n + n), ("ind", L["w2"], sm("LSL", h)), OFS)
         mark("qx", h)
         q0 = h * 16 * n
-        cp(ref("QS", 0, 16 * n, 16), ("ind", L["xz"], sm("LSL", h)))
-        banks[h] = (bank(), bank())
+        flex("V", ref("QS", 0, 16 * n, 16), ("ind", L["xz"], sm("LSL", h)))
+        banks[h] = (bank(), bank(), bank())
+        if QP:
+            pe([(ref(banks[h][2], 0, n), Ib, ref("QS", 0, 16 * n, 16), True, True)])
         scan(ref("QX", q0, q0 + 16 * n), full("MK"), full("QS"), 0.0, A.min, A.add)
         mark("e", h)
-        act(tl("E", h), ("ind", views, vh), F.Copy)
-        ts(ref("HEL", (2 * h + 1) * n, (2 * h + 2) * n), tl("E", h), OFS, A.add)
+        flex("S", tl("E", h), ("ind", views, vh))
+        flex("V", ref("HEL", (2 * h + 1) * n, (2 * h + 2) * n), tl("E", h), OFS)
         mark("hm", h)
         scan(tl("HME", h), L["f"], tl("E", h), 0.0, A.min, A.subtract)
 
     def dedupe(t):
         mark("dd", 0)
         vh = ref("VH", 16 * t, 16 * t + 16)
-        ts(full("VF"), vh, -2048.0, A.add)
-        ts(full("VN"), vh, 613.0, A.mult, float(HC), A.add)
+        flex("V", full("VF"), vh, -2048.0)
+        flex("V", full("VN"), vh, HC - 2.0 ** 23, 613.0)
         b = bank()
         mm = []
         for j, c in enumerate((0, 0, 1)):
-            mm += acc(ref(b, j, 24, 3), (Ib, ref("VF", c, 16, 2)), (full("I8kn"), ref("LK", c, 16, 2)))
+            mm += acc(ref(b, j, 24, 3), (Ib, ref("VF", c, 16, 2)), (full("I8k"), ref("LK", c, 16, 2)))
         pe(mm)
-        ts(full("DL"), ref(b, 0, 24), 10240.0, A.add, 4096.0, A.min)
-        act(full("G1"), ("ind", full("W613"), full("DL")), F.Copy)
+        flex("V", full("DL"), ref(b, 0, 24), 2056.0 - 8192.0)
+        flex("S", full("G1"), ("ind", full("W613"), full("DL")))
         tt(full("EQ"), ("ind", full("VN"), ref("CL", 8, 32)), full("G1"), A.is_equal)
         scan(full("DS"), full("D0"), full("EQ"), 0.0, A.mult, A.add)
         b = bank()
-        pe(grp((ref(b, 0, 16), Ib, full("VF")), (ref(b, 0, 16), full("I8kn"), full("LK")),
+        pe(grp((ref(b, 0, 16), Ib, full("CK")), (ref(b, 0, 16), Ib, full("VF")), (ref(b, 0, 16), full("I8kn"), full("LK")),
                (ref(b, 0, 16, 2), full("DG"), ref("DS", 14, 384, 48)), (ref(b, 1, 16, 2), full("DG"), ref("DS", 46, 384, 48))))
-        ts(ref("OFF", 0, 16, 2), ref(b, 0, 16, 2), 10240.0, A.add, sp0, A.min)
-        ts(ref("OFF", 1, 16, 2), ref(b, 1, 16, 2), 10240.0, A.add, sp1, A.min)
+        tt(full("OFF"), ref(b, 0, 16), full("SPT"), A.min)
 
     def early(t, h):
         mark("ea", h)
@@ -654,18 +718,18 @@ def build(T, topo, core, rank, CO=COSTS[0]):
         Sb, Ip, Im = full("Sb"), full("Ip100"), full("Im100")
         po = ref(bank(), 0, 8)
         pe(acc(po, (Ib, L["st"](0)), (full("Sb100"), lk), (Im, lk)))
-        ts(ov, po, 100.5, A.is_ge)
+        ts(ov, po, 100.5, A.is_ge, 128.0, A.mult)
         b = bank()
-        pe(grp((ref(b, 0, 16), Ib, full("CM")), (ref(b, 0, 8), full("I256"), lk), (ref(b, 0, 8), full("G256"), ov), (ref(b, 8, 16), full("G0"), ov)))
-        cp(sm("TLL", h, 16, 0, 16), ref(b, 0, 16))
-        flex("zf", L["zf"], ("ind", L["xzh"], sm("TLL", h, 16)))
+        pe(grp((ref(b, 0, 16), Ib, full("CM")), (ref(b, 0, 8), full("I2"), lk), (ref(b, 0, 8), full("G256"), ov), (ref(b, 8, 16), full("G0"), ov)))
+        flex("V", sm("TLL", h, 16, 0, 16), ref(b, 0, 16))
+        flex("S", L["zf"], ("ind", L["xzh"], sm("TLL", h, 16)))
         mark("st", h)
         b = bank()
         blk = lambda j, w=1: ref(b, 8 * j, 8 * (j + w))
-        pe(grp((blk(0, 3), Ib, full("CS")), (blk(0, 2), Ib, L["st"](0, 2)), (blk(2), Sb, L["st"](1)), (blk(0), Im, lk), (blk(1), Ib, lk),
+        pe(grp((blk(0, 3), Ib, full("CS")), (blk(0, 2), Ib, L["st"](0, 2)), (blk(2), Sb, L["st"](1)), (blk(0), Im, lk), (blk(1), full("I1"), lk),
                (blk(0), Im, ov), (blk(1), Im, ov), (blk(2), Ip, ov)))
         ra = lambda j, w=1: sm("RA", h, 24, 8 * j, 8 * w)
-        act(ra(0, 3), blk(0, 3), F.Relu)
+        flex("S", ra(0, 3), blk(0, 3), relu=True)
         b = bank()
         if t < NT - 1:
             pe(grp((blk(0, 2), Ib, ra(0, 2)), (blk(1), Ib, ra(2))) + acc(blk(2), (full("Ifl"), ra(1)), (full("Ifl"), ra(2))))
@@ -685,20 +749,17 @@ def build(T, topo, core, rank, CO=COSTS[0]):
         mark("kk", h)
         y = ref(bank(), 0, 8)
         pe(ots(y, L["zf"], [(full("I8k"), lk), (full("I8200"), ov)]))
-        ts(sm("KL", h), y, t + 16.0 - 8192.0, A.add)
-        flex("oh", tl("OHL", h), ("ind", full("OHW"), sm("KL", h)))
+        flex("V", sm("KL", h), y, t + 16.0 - 8192.0)
+        flex("S", tl("OHL", h), ("ind", full("OHW"), sm("KL", h)))
 
     def bulk(t, h, w):
         mark("he"[w] + "b", h)
         q0, l0 = h * 16 * n, (2 * h + w) * n
         G, M = ("GH", "MH") if w == 0 else ("GE", "ME")
         b = banks[h][w]
-        for a, e_, q in PARTS[w]:
+        for a, e_, q in PARTS[h][w]:
             g_, off = ref(G, q0 + 16 * a, q0 + 16 * e_), ref("HEL", l0 + a, l0 + e_)
-            if q == "S":
-                act(g_, ("ind", px, off), F.Copy)
-            else:
-                cp(g_, ("ind", px, off))
+            flex(q, g_, ("ind", px, off))
         for a, e_ in CHUNKS[w]:
             lo, hi = q0 + 16 * a, q0 + 16 * e_
             g0 = ref(G, lo, hi, 16)
@@ -707,7 +768,7 @@ def build(T, topo, core, rank, CO=COSTS[0]):
             if e_ == n:
                 for k0 in range(0, 16, SPLIT):
                     pe([(ref(b, k, n, 16), ref(G, q0 + k, q0 + 16 * n, 16), full("Bm16"), False, False) for k in range(max(1, k0), k0 + SPLIT)], sub=True)
-            tt(g0, g0, ref("QX", lo, hi, 16), A.max)
+            tt(g0, g0, ref(banks[h][2], a, e_) if QP else ref("QX", lo, hi, 16), A.max)
             scan(ref(M, lo, hi), ref("QX", lo, hi), ref(G, lo, hi), 0.0, A.min, A.max)
         pe([(ref(b, 0, n), tl("OHL", h), full("Ibig" if w == 0 else "MP"), False, False)])
         for k0 in range(0, 16, SPLIT):
@@ -719,7 +780,7 @@ def build(T, topo, core, rank, CO=COSTS[0]):
         ph, pd = ref(banks[h][0], 0, n), ref(banks[h][1], 0, n)
         bulk(t, h, 0)
         mark("km", h)
-        flex("key", key, ph)
+        flex("S", key, ph)
         scan(tl("PM", h), full("RST"), key, 0.0, A.add, A.min)
         tt(tl("OHT", h), ("ind", tl("PM", h), ref("CL", 0, 8)), key, A.is_equal)
         oc = ref(bank(), 0, n)
@@ -731,13 +792,13 @@ def build(T, topo, core, rank, CO=COSTS[0]):
         pe([(mk, tl("MT", h), Ib, True, True)])
         tt(tl("MM", h), tl("HME", h), mk, A.mult)
         scan(L["c"], tl("MM", h), tl("E", h), -OFS, A.max, A.add)
-        flex("cf", tl("CF", h), ("ind", L["w3"], sm("TLL", h, 16)), OFS - 2048.0)
+        flex("V", tl("CF", h), ("ind", L["w3"], sm("TLL", h, 16)), OFS - 2048.0)
         tt(tl("PP", h), tl("CF", h), oc, A.mult)
         vo = ref(bank(), 0, n)
         if t < NT - 1:
             vo = ref(vo[0], 0, 8)
             pe(ots(vo, tl("PP", h)))
-            ts(L["vb"], vo, 2048.0, A.add)
+            flex("V", L["vb"], vo, 2048.0)
             send("v", t + 1, h, tiles(t + 1, h)["vh"], L["vb"])
         else:
             pe(acc(vo, (full("BO"), tl("PP", h))))
@@ -745,11 +806,11 @@ def build(T, topo, core, rank, CO=COSTS[0]):
             store(T.yv[:, h * n:h * n + n], ref("YU", 512 + h * n, 512 + h * n + n, 1, 0, 128, 16))
         mark("ff", h)
         if t < NT - 1:
-            flex("fb", L["fb"], ("ind", L["c"], sm("TLL", h, 16, 8)))
+            flex("S", L["fb"], ("ind", L["c"], sm("TLL", h, 16, 8)))
             send("f", t + 1, h, tiles(t + 1, h)["f"], L["fb"])
         else:
-            flex("fb", L["fb"], ("ind", L["c"], sm("TLL", h, 16, 8)), OFS)
-            store(T.yf[:, h * n:h * n + n], L["fb"])
+            flex("S", ref("YU", 1536 + h * n, 1536 + h * n + n), ("ind", L["c"], sm("TLL", h, 16, 8)), OFS)
+            store(T.yf[:, h * n:h * n + n], ref("YU", 1536 + h * n, 1536 + h * n + n))
 
     def scatter(t, h):
         mark("sc", h)
@@ -772,9 +833,23 @@ def build(T, topo, core, rank, CO=COSTS[0]):
     pg["st"] = ""
     for c in range(4):
         a, b = 512 * c, 512 * c + 512
-        act(ref("W613", a, b), ref("VI", 2048 + a, 2048 + b), F.Identity, OFS * 4097.0, 4096.0)
+        flex("S", ref("W613", a, b), ref("VI", 2048 + a, 2048 + b), OFS * 4097.0, 4096.0)
         scan(ref("YT", a, b), ref("VI", a, b), ref("W613", a, b), 0.0, A.min, A.add)
         store(T.yw[:, a:b], ref("YT", a, b))
+    named, seen = {}, {}
+    for o in pg["ops"]:
+        if o["q"] == "S":
+            k = (o["hop"], o["st"] + " " + o["tag"][4:])
+            seen[k] = seen.get(k, 0) + 1
+            named[(k[0], k[1] + " %d" % seen[k])] = o["i"]
+    line = []
+    for t in range(NT):
+        for nm in LINES[t]:
+            k = (t - 1, nm[1:]) if nm[0] == "-" else (t, nm)
+            if k in named:
+                line.append(named[k])
+    for a, b in zip(line, line[1:]):
+        pg["ops"][b]["ord"].add(a)
     pg["nls"], pg["nout"] = nls[0], nout[0]
     return pg
 

@@ -9,8 +9,8 @@ NT = 5
 XW = 32 + 3 * n
 WW = 3 * n
 MAGIC = 12582912.0
-OFS = 2.0 ** 24
-QP = True
+NB = 8
+M35 = 1.5 * 2.0 ** 35
 HC = 262000
 NOH = 4112
 OH0 = 1024
@@ -18,51 +18,55 @@ PARTS = ((((0, 64, "S"), (64, 128, "S")), ((0, 64, "S"), (64, 128, "S"))),) * 2
 CHUNKS = (((0, 64), (64, 128)), ((0, 64), (64, 128)))
 ONV = ("hz0", "hz1")
 LINES = ((),) * NT
+XT = "cv"
 SPLIT = 8
 f4, b2, h2, i4, u2 = "float32", "bfloat16", "float16", "int32", "uint16"
 
 SCRATCH = {
-    "PX": ("sbuf", [128, 4096], b2), "VI": ("sbuf", [128, 4096 + 32], f4), "VW": ("sbuf", [128, 2048], i4),
-    "IT": ("sbuf", [128, 2048], i4), "YT": ("sbuf", [128, 2048], f4), "YU": ("sbuf", [128, 2048], f4),
+    "PX": ("sbuf", [128, 4096], b2), "VI": ("sbuf", [128, 4096 + 32], i4), "VW": ("sbuf", [128, 2048], i4),
+    "YT": ("sbuf", [128, 2048], f4), "YU": ("sbuf", [128, 2048], f4),
     "W613": ("sbuf", [128, 4096 + 8], f4), "OHW": ("sbuf", [128, NOH], b2),
     "XZ": ("sbuf", [128, 10 * XW], b2), "W": ("sbuf", [128, 10 * WW], i4), "VH": ("sbuf", [128, 10 * 8], u2),
-    "ZB": ("sbuf", [128, 8 * (32 + n)], b2), "FB": ("sbuf", [128, 10 * n], i4), "SPT": ("sbuf", [128, 16], f4), "CK": ("sbuf", [128, 16], b2), "VB": ("sbuf", [128, 10 * 8], u2), "ZL": ("sbuf", [128, 2 * n], b2),
-    "E": ("sbuf", [128, 2 * n], f4), "HEL": ("sbuf", [128, 4 * n], u2), "QS": ("sbuf", [128, 16 * n], b2), "QX": ("sbuf", [128, 32 * n], b2),
+    "ZB": ("sbuf", [128, 8 * (32 + n)], b2), "FB": ("sbuf", [128, 10 * n], i4), "SPT": ("sbuf", [128, 16], f4), "CK": ("sbuf", [128, 24], b2), "VB": ("sbuf", [128, 10 * 8], u2), "ZL": ("sbuf", [128, 2 * n], b2),
+    "HEL": ("sbuf", [128, 4 * n], u2), "QS": ("sbuf", [128, 16 * n], b2), "QX": ("sbuf", [128, 32 * n], b2), "MK": ("sbuf", [128, 16 * n], b2), "H16": ("sbuf", [128, 2 * n], h2),
     "GH": ("sbuf", [128, 32 * n], b2), "GE": ("sbuf", [128, 32 * n], b2), "MH": ("sbuf", [128, 32 * n], b2), "ME": ("sbuf", [128, 32 * n], b2),
     "IND": ("sbuf", [128, 2 * n], b2), "LK": ("sbuf", [128, 16], b2), "LSL": ("sbuf", [128, 16], u2),
-    "HI1": ("sbuf", [128, 2 * n], i4), "HI2": ("sbuf", [128, 2 * n], i4), "FL": ("sbuf", [128, 2 * n], h2),
+    "HI1": ("sbuf", [128, 2 * n], i4), "HI2": ("sbuf", [128, 2 * n], i4),
     "T2": ("sbuf", [128, 2 * n], f4),
     "OV": ("sbuf", [128, 16], b2), "TLL": ("sbuf", [128, 32], u2), "RA": ("sbuf", [128, 48], b2), "KL": ("sbuf", [128, 16], u2), "OHL": ("sbuf", [128, 2 * n], b2),
-    "VF": ("sbuf", [128, 16], h2), "VN": ("sbuf", [128, 16], f4), "DL": ("sbuf", [128, 24], u2), "G1": ("sbuf", [128, 384], f4), "EQ": ("sbuf", [128, 384], b2),
+    "VF": ("sbuf", [128, 16], h2), "WD": ("sbuf", [128, 48], h2), "SEL": ("sbuf", [128, 16 * 128], b2), "EQ": ("sbuf", [128, 384], b2),
     "DS": ("sbuf", [128, 384], b2), "OFF": ("sbuf", [128, 16], u2),
-    "HME": ("sbuf", [128, 2 * n], f4), "KEY": ("sbuf", [128, 2 * n], f4), "MT": ("sbuf", [128, 2 * n], b2), "MM": ("sbuf", [128, 2 * n], f4),
-    "PM": ("sbuf", [128, 2 * n], f4), "OHT": ("sbuf", [128, 2 * n], b2), "CF": ("sbuf", [128, 2 * n], f4), "PP": ("sbuf", [128, 2 * n], h2),
-    "YC": ("sbuf", [128, 16], b2), "VZ": ("sbuf", [128, 512], i4), "VZh": ("sbuf", [128, 512], h2), "FI": ("sbuf", [128, 256], i4),
+    "KEY": ("sbuf", [128, 2 * n], f4), "MT": ("sbuf", [128, 2 * n], b2), "MM": ("sbuf", [128, 2 * n], i4),
+    "PM": ("sbuf", [128, 2 * n], f4), "OHT": ("sbuf", [128, 2 * n], b2), "CF": ("sbuf", [128, 2 * n], h2), "PP": ("sbuf", [128, 2 * n], h2),
+    "YC": ("sbuf", [128, 16], b2), "VZ": ("sbuf", [128, 512], i4), "VZh": ("sbuf", [128, 512], h2),
+    "WBn": ("sbuf", [128, 128], b2), "C1": ("sbuf", [128, 128], b2), "CHn": ("sbuf", [128, 128], b2), "CN": ("sbuf", [128, 128], b2),
+    "XL": ("sbuf", [128, 2 * n], b2), "XK": ("sbuf", [128, 2 * n], h2), "XV": ("sbuf", [128, 2 * n], h2),
     "ON": ("sbuf", [128, 144], b2), "BO": ("sbuf", [128, 128], b2), "B8": ("sbuf", [128, 144], b2), "Bh": ("sbuf", [128, 144], b2),
     "B32": ("sbuf", [128, 8], b2), "Bm16": ("sbuf", [128, 8], b2), "WB": ("sbuf", [128, 128], b2), "CH": ("sbuf", [128, 128], b2), "CP": ("sbuf", [128, 128], b2),
     "Sb": ("sbuf", [128, 128], b2), "Sb100": ("sbuf", [128, 128], b2), "MP": ("sbuf", [128, 128], b2), "DG": ("sbuf", [128, 128], b2), "G0": ("sbuf", [128, 128], b2),
     "G256": ("sbuf", [128, 128], h2), "ZE": ("sbuf", [128, 128], b2),
-    "KC": ("sbuf", [128, 128], b2), "RST": ("sbuf", [128, 128], f4), "MK": ("sbuf", [128, 16 * n], b2), "D0": ("sbuf", [128, 384], b2),
+    "KC": ("sbuf", [128, 128], b2), "RST": ("sbuf", [128, 128], f4), "D0": ("sbuf", [128, 384], b2),
     "PI": ("sbuf", [128, 32], i4), "PC": ("sbuf", [128, 32], f4), "IJ": ("sbuf", [128, 16], f4), "CMI": ("sbuf", [128, 32], f4), "CM": ("sbuf", [128, 16], b2),
     "CS": ("sbuf", [128, 24], b2), "CL": ("sbuf", [128, 32], u2), "WT": ("sbuf", [128, 2], i4), "WTf": ("sbuf", [128, 8], f4),
 }
 DIAG = {"Ib": (1.0, b2), "In": (-1.0, b2), "I2": (2.0, b2), "Ic": (0.00689697265625, b2), "Icn": (-0.00689697265625, b2), "Ihz": (0.5 - 2.0 ** -11, h2),
         "I1": (1.0 / 128, b2), "Ip100": (100.0 / 128, b2), "Im100": (-100.0 / 128, b2), "I8k": (8192.0 / 128, b2), "I8kn": (-8192.0 / 128, b2), "I8200": (8200.0 / 128, h2),
-        "I4kn": (-4096.0, b2), "Ibig": (-262144.0, b2), "Ifl": (0.4375, b2), "I16": (16.0, b2)}
+        "I8192": (8192.0, b2), "Ibig": (-262144.0, b2), "Ifl": (0.4375, b2), "I16": (16.0, b2)}
 for _k in DIAG:
     SCRATCH[_k] = ("sbuf", [128, 128], DIAG[_k][1])
 for _b in range(8):
-    SCRATCH["b%d" % _b] = ("psum", [128, 512], f4)
-LOADS = ["px0", "px1", "vw0", "vw1", "z0", "z1", "f0", "v0", "d0", "wt", "kap"]
+    SCRATCH["bank%d" % _b] = ("psum", [128, 512], f4) if _b < NB else ("psum", [128, 1024], b2)
+LOADS = ["v0", "d0", "px0", "px1", "z1", "z0", "wt", "kap", "f1", "f0", "vw0", "vw1"]
 SEMAPHORES = ["V", "S", "P", "G", "out", "ls", "oh"] + ["ld_" + x for x in LOADS] + ["r%s_%d_%d" % (k, t, h) for k in "zfv" for t in range(1, NT) for h in range(2)]
 
 COSTS = tuple(dict(zip(("cy", "gather", "wake", "pe", "link", "scat", "V", "S", "P", "row", "issue", "load"), c)) for c in (
-    (0.00083, 1.56, 0.10, 0.00055, 1.4, 0.18, 0.03, 0.04, 0.03, 1.0, 0.4, 1.0),
+    (0.00083, 1.56, 0.10, 0.00046, 1.4, 0.18, 0.03, 0.04, 0.03, 1.0, 0.4, 1.0),
     (0.00083, 1.10, 0.07, 0.00042, 1.0, 0.12, 0.03, 0.04, 0.03, 0.7, 0.3, 0.9),
-    (0.00108, 1.80, 0.15, 0.00070, 2.0, 0.25, 0.04, 0.05, 0.04, 1.5, 0.8, 1.3),
+    (0.00108, 1.80, 0.15, 0.00056, 2.0, 0.25, 0.04, 0.05, 0.04, 1.5, 0.8, 1.3),
     (0.00083, 1.56, 0.12, 0.00042, 1.8, 0.14, 0.06, 0.07, 0.02, 1.2, 0.6, 1.2),
-    (0.00090, 1.40, 0.08, 0.00070, 1.1, 0.22, 0.03, 0.04, 0.05, 0.8, 0.4, 1.0)))
-ROUNDS = 6000
+    (0.00090, 1.40, 0.08, 0.00052, 1.1, 0.22, 0.03, 0.04, 0.05, 0.8, 0.4, 1.0)))
+ROUNDS = 1500
+MOVES = 70000
 STAGGER = 7.0
 
 
@@ -71,7 +75,7 @@ def ref(name, c0, c1, step=1, p0=0, p1=128, pstep=1):
 
 
 def is_psum(name):
-    return name[0] == "b" and name[1:].isdigit()
+    return name[0] in "bc" and name[1:].isdigit()
 
 
 def touch(pg, o, r, wr):
@@ -106,7 +110,7 @@ def add(pg, q, cost, fn, rd, wr, sem=None, val=1, lat=0.0, tag="", alt=None):
     for r in wr:
         touch(pg, o, r, True)
     o["near"] = o["dep"]
-    o["tiles"] = sorted(set(r[0] for r in list(rd) + list(wr) if is_psum(r[0])))
+    o["tiles"] = sorted(set(r[0] for r in list(rd) + list(wr) if is_psum(r[0]) and r[0][0] == "b"))
     return o["i"]
 
 
@@ -150,7 +154,7 @@ def replay(ops, qs, seq, c, dyn, uses=None):
     cost, lat, wake = c
     fin = [0.0] * len(ops)
     free, bmap, held = {q: 0.0 for q in set(qs)}, {}, {}
-    bfree = {b: (0.0, []) for b in range(8)}
+    bfree = {b: (0.0, []) for b in range(NB)}
     for i in seq:
         o = ops[i]
         q = qs[i]
@@ -310,8 +314,165 @@ def schedule(pgs, wakes, rounds, seed):
     return keep
 
 
-def plan(T, topo, core, rank, rounds=None, seed=1):
-    return schedule([build(T, topo, core, rank, c) for c in COSTS], [c["wake"] for c in COSTS], rounds or ROUNDS, seed)
+def polish(pgs, wakes, keep, moves, seed, temp=0.0004):
+    ops = pgs[0]["ops"]
+    N_, M = len(ops), len(pgs)
+    seq, dyn, bmap, r0, _, q = keep
+    seq, q = list(seq), list(q)
+    dep = [sorted(set(o["near"]) | set(dyn.get(o["i"], ()))) for o in ops]
+    snd = [o["send"] for o in ops]
+    before = [set(dep[i]) | ops[i]["ord"] | ({snd[i]} if snd[i] is not None else set()) for i in range(N_)]
+    sends = [i for i in seq if ops[i]["sem"] == "ls"]
+    for a, b in zip(sends, sends[1:]):
+        before[b].add(a)
+    after = [[] for _ in ops]
+    for i in range(N_):
+        for d in before[i]:
+            after[d].append(i)
+    cost = [priced(p["ops"], q) for p in pgs]
+    lat = [[o["lat"] for o in p["ops"]] for p in pgs]
+    Z = N_
+
+    def links(seq):
+        prev, last = [Z] * N_, {}
+        for i in seq:
+            prev[i] = last.get(q[i], Z)
+            last[q[i]] = i
+        return prev
+
+    def run(m, p0, prev, end, fin):
+        c, l, w = cost[m], lat[m], wakes[m]
+        for i in seq[p0:]:
+            t = -w
+            for d in dep[i]:
+                if fin[d] > t:
+                    t = fin[d]
+            t += w
+            d = snd[i]
+            if d is not None and fin[d] > t:
+                t = fin[d]
+            d = end[prev[i]]
+            if d > t:
+                t = d
+            t += c[i]
+            end[i] = t
+            fin[i] = t + l[i]
+        return max(fin)
+
+    def path(m):
+        end, fin, c, w = E[m], Fi[m], cost[m], wakes[m]
+        i = fin.index(max(fin))
+        out = []
+        while i != Z:
+            t = end[i] - c[i]
+            p = prev[i]
+            if p != Z and end[p] > t - 1e-9:
+                if q[i] != "RD":
+                    out.append((p, i))
+                i = p
+                continue
+            nx = Z
+            for d in dep[i]:
+                if fin[d] + w > t - 1e-9:
+                    nx = d
+            if snd[i] is not None and fin[snd[i]] > t - 1e-9:
+                nx = snd[i]
+            i = nx
+        return out
+
+    prev = links(seq)
+    E, Fi = [[0.0] * (N_ + 1) for _ in pgs], [[0.0] * (N_ + 1) for _ in pgs]
+    r = [run(m, 0, prev, E[m], Fi[m]) for m in range(M)]
+    first = list(r)
+    now = best = 1.0
+    kept = (list(seq), list(q), list(r))
+    rng = np.random.default_rng(seed)
+    pos = [0] * N_
+    fresh, paths = True, None
+    for it in range(moves):
+        if fresh:
+            st = [E[0][i] - cost[0][i] for i in range(N_)]
+            seq.sort(key=lambda i: st[i])
+            for k, i in enumerate(seq):
+                pos[i] = k
+            paths = [path(m) for m in range(M)]
+            fresh = False
+        u = rng.random(5)
+        pt = paths[int(u[0] * M)]
+        if not pt:
+            continue
+        a, b = pt[int(u[1] * len(pt))]
+        undo = None
+        if u[2] < 0.15:
+            i = a if u[3] < 0.5 else b
+            if not ops[i]["alt"]:
+                continue
+            to = "V" if q[i] == "S" else "S"
+            undo = (i, q[i], [cost[m][i] for m in range(M)])
+            q[i] = to
+            for m in range(M):
+                cost[m][i] = pgs[m]["ops"][i]["alt"][to][0]
+            p0 = p1 = pos[i]
+            if u[2] < 0.08:
+                lo = max([pos[d] for d in before[i]] + [-1]) + 1
+                p0 = lo + int((p1 - lo) * (u[3] * 7 % 1) ** 2)
+            old = seq[p0:p1 + 1]
+            seq[p0:p1 + 1] = [i] + old[:-1]
+        elif u[2] < 0.58:
+            for _ in range(int(u[3] * u[3] * 5)):
+                if prev[a] != Z:
+                    a = prev[a]
+            lo = max([pos[d] for d in before[b]] + [-1])
+            while a != b and pos[a] <= lo:
+                a = [j for j in seq[pos[a] + 1:pos[b] + 1] if q[j] == q[b]][0]
+            if a == b:
+                continue
+            p0, p1 = pos[a], pos[b]
+            old = seq[p0:p1 + 1]
+            seq[p0:p1 + 1] = [b] + old[:-1]
+        else:
+            hi = min([pos[d] for d in after[a]] + [N_])
+            if hi <= pos[b]:
+                continue
+            k = int(u[3] * u[3] * 5)
+            for j in seq[pos[b] + 1:hi]:
+                if k == 0:
+                    break
+                if q[j] == q[a]:
+                    b = j
+                    k -= 1
+            p0, p1 = pos[a], pos[b]
+            old = seq[p0:p1 + 1]
+            seq[p0:p1 + 1] = old[1:] + [a]
+        pv = links(seq)
+        lim = now - temp * (1 - it / moves) * float(np.log(u[4] + 1e-12))
+        E2, F2, r2, f = [], [], [], 0.0
+        for m in range(M):
+            e, fi = list(E[m]), list(Fi[m])
+            x = run(m, p0, pv, e, fi)
+            E2.append(e)
+            F2.append(fi)
+            r2.append(x)
+            f += (x - r[m]) / first[m] / M
+            if m == 0 and x > r[0] + 0.4:
+                f = 1.0
+                break
+        if now + f <= lim:
+            now, E, Fi, r, prev, fresh = now + f, E2, F2, r2, pv, True
+            if now < best - 1e-9:
+                best, kept = now, (list(seq), list(q), list(r))
+        else:
+            seq[p0:p0 + len(old)] = old
+            if undo:
+                i, q[i] = undo[0], undo[1]
+                for m in range(M):
+                    cost[m][i] = undo[2][m]
+    return kept[0], dyn, bmap, kept[2], None, kept[1]
+
+
+def plan(T, topo, core, rank):
+    pgs, wakes = [build(T, topo, core, rank, c) for c in COSTS], [c["wake"] for c in COSTS]
+    return polish(pgs, wakes, schedule(pgs, wakes, ROUNDS, 1), MOVES, 1)
 
 
 def emit(pg, keep, g, T):
@@ -357,12 +518,12 @@ def emit(pg, keep, g, T):
 
 
 def build(T, topo, core, rank, CO=COSTS[0]):
-    pg = {"ops": [], "acc": {}, "rr": [0], "st": "", "hop": 0, "bmap": {}}
+    pg = {"ops": [], "acc": {}, "rr": [0], "st": "", "hop": 0, "bmap": {"c0": NB, "c1": NB + 1}}
     CY, GC, PEC, FIX = CO["cy"], CO["gather"], CO["pe"], CO
 
     def ap(r):
         name, c0, c1, step, p0, p1, ps = r
-        t = T["b%d" % pg["bmap"][name]] if name in pg["bmap"] else T[name]
+        t = T["bank%d" % pg["bmap"][name]] if name in pg["bmap"] else T[name]
         rows = slice(p0, p1) if ps == 1 else slice(p0, p1, ps)
         cols = slice(c0, c1) if step == 1 else slice(c0, c1, step)
         return t[rows, cols]
@@ -371,7 +532,7 @@ def build(T, topo, core, rank, CO=COSTS[0]):
         return (r[2] - r[1] + r[3] - 1) // r[3]
 
     def two(*rs):
-        return all(r[0] in SCRATCH and SCRATCH[r[0]][2] in (b2, h2, u2) for r in rs)
+        return all(r[0][0] == "c" if is_psum(r[0]) else SCRATCH[r[0]][2] in (b2, h2, u2) for r in rs)
 
     def inap(x):
         if x[0] == "ind":
@@ -450,7 +611,7 @@ def build(T, topo, core, rank, CO=COSTS[0]):
         def fn(e):
             ins = None
             for out, l, r, s, e_ in mms:
-                ins = e.matmul(ap(out), ap(l), ap(r), s, e_)
+                ins = e.transpose(ap(out), ap(l), ap(r)) if out[0][0] == "c" else e.matmul(ap(out), ap(l), ap(r), s, e_)
             return ins
         return add(pg, "P", cost + FIX["P"], fn, list(rd.values()), list(wr.values()), tag="pe " + mms[0][1][0] + " " + mms[0][2][0])
 
@@ -460,9 +621,9 @@ def build(T, topo, core, rank, CO=COSTS[0]):
     def grp(*mms):
         return [(o, l, r, i == 0, i == len(mms) - 1) for i, (o, l, r) in enumerate(mms)]
 
-    def bank():
+    def bank(kind="b"):
         pg["rr"][0] += 1
-        return "b%d" % (99 + pg["rr"][0])
+        return kind + "%d" % (99 + pg["rr"][0])
 
     def load(name, out, src, lat, q="Y"):
         s = "ld_" + name
@@ -495,17 +656,17 @@ def build(T, topo, core, rank, CO=COSTS[0]):
     tl = lambda name, h: ref(name, h * n, h * n + n)
     full = lambda name: ref(name, 0, SCRATCH[name][1][1])
 
-    loads = [load("v0", ref("VZ", 0, 256, 1, 0, 8), T.v0[:, :], 2.2),
-             load("d0", ref("VZ", 256, 512, 1, 0, 8), T.d0[:, :], 2.2),
-             load("px0", ref("PX", 0, 2048), T.px[:, 0:2048], 3.8),
-             load("px1", ref("PX", 2048, 4096), T.px[:, 2048:4096], 5.3)]
-    for h in (1, 0):
-        loads.append(load("z%d" % h, ref("XZ", h * XW + 32, h * XW + 32 + n), T.z0[:, h * n:h * n + n], 5.3))
-    loads += [load("wt", ref("WT", 0, 1), T.wt[:, :], 5.3),
-              load("kap", ref("WT", 1, 2), T.kap[:, :], 5.3),
-              load("f0", full("FI"), T.f0[:, :], 5.6),
-              load("vw0", ref("VW", 0, 1024), T.vw[:, 0:1024], 7.0),
-              load("vw1", ref("VW", 1024, 2048), T.vw[:, 1024:2048], 8.5)]
+    what = {"v0": (ref("VZ", 0, 256, 1, 0, 8), T.v0[:, :], 0.02), "d0": (ref("VZ", 256, 512, 1, 0, 8), T.d0[:, :], 0.02),
+            "wt": (ref("WT", 0, 1), T.wt[:, :], 0.15), "kap": (ref("WT", 1, 2), T.kap[:, :], 0.15)}
+    for h in range(2):
+        what["px%d" % h] = (ref("PX", 2048 * h, 2048 * h + 2048), T.px[:, 2048 * h:2048 * h + 2048], 1.5)
+        what["vw%d" % h] = (ref("VW", 1024 * h, 1024 * h + 1024), T.vw[:, 1024 * h:1024 * h + 1024], 1.5)
+        what["z%d" % h] = (ref("XZ", h * XW + 32, h * XW + 32 + n), T.z0[:, h * n:h * n + n], 0.2)
+        what["f%d" % h] = (ref("W", h * WW + n, h * WW + 2 * n), T.f0[:, h * n:h * n + n], 0.25)
+    loads, at = [], 2.0
+    for k, nm in enumerate(LOADS):
+        at = max(at, 2.0 + 0.1 * k) + what[nm][2]
+        loads.append(load(nm, what[nm][0], what[nm][1], at - 0.1 * k))
     for a, b in zip(loads, loads[1:]):
         pg["ops"][b]["ord"].add(a)
 
@@ -534,11 +695,11 @@ def build(T, topo, core, rank, CO=COSTS[0]):
     act(ref("W613", 2056, 4104), ref("W613", 8, 2056), F.Identity, 613.0 * 2048)
     fill(full("MK"), 256.0)
     fill(ref("MK", 0, 16 * n, 16), 0.0)
+    fill(full("QS"), 0.0)
     iota(full("KC"), [[0, 8], [1, 16]], 0, 0)
-    for j, b in enumerate((0, 1, 1)):
-        iota(ref("CMI", 8 + j, 32, 3), [[2, 8]], b, 0)
+    for j in range(16):
+        sel(ref("SEL", 128 * j, 128 * j + 128), on, [[-16, 8], [0, 16]], A.is_equal, 0.0, -j, 1)
     ts(ref("CL", 0, 8), ref("CMI", 0, 8), 15.0, A.add)
-    cp(ref("CL", 8, 32), ref("CMI", 8, 32))
     iota(full("RST"), [[0, 128]], 0, 0)
     sel(full("RST"), full("RST"), [[0, 8], [1, 16]], A.not_equal, 1048576.0, 0, 0)
     for i, c in enumerate((1, 0, -99)):
@@ -547,7 +708,7 @@ def build(T, topo, core, rank, CO=COSTS[0]):
         iota(ref("ZB", k * (32 + n) + 24, k * (32 + n) + 32), [[0, 8]], 0, 0)
     iota(full("ZE"), [[0, 128]], 0, 0)
     for nm in DIAG:
-        if nm in ("Ibig", "Ifl", "I16", "I8k", "I1", "Ip100", "I8kn"):
+        if nm in ("Ibig", "Ifl", "I16", "I8k", "I1", "Ip100", "I8kn", "I8192"):
             sel(full(nm), full("ZE"), [[-1, 128]], A.not_equal, DIAG[nm][0], 0, 1)
         elif DIAG[nm][1] == h2:
             ts(full(nm), Ib, DIAG[nm][0], A.mult)
@@ -563,7 +724,8 @@ def build(T, topo, core, rank, CO=COSTS[0]):
     ts(dg, dg, 2.0 ** -5, A.add)
     iota(full("SPT"), [[0, 8], [16, 2]], 4096, 0)
     ts(full("SPT"), full("SPT"), pm, A.add)
-    iota(full("CK"), [[0, 16]], 10240, 0)
+    iota(ref("CK", 0, 16), [[0, 16]], 10240, 0)
+    iota(ref("CK", 16, 24), [[0, 8]], 8192, 0)
     ts(full("G0"), Ib, sg, A.mult)
     ts(full("G256"), Ib, sg256, A.mult)
     ts(full("DG"), Ib, dg, A.mult)
@@ -573,7 +735,12 @@ def build(T, topo, core, rank, CO=COSTS[0]):
     ts(full("WB"), full("BO"), wcol, A.mult)
     fill(full("Bh"), 0.0)
     cp(ref("Bh", 15, 143, 16), ref("BO", 0, 128, 16))
-    fill(full("CH"), 49152.0)
+    act(full("WBn"), full("WB"), F.Copy, 0.0, -1.0)
+    fill(full("CH"), M35 / 128)
+    fill(full("CHn"), -M35 / 128)
+    fill(full("C1"), 16.0)
+    fill(ref("C1", 0, 128, 1, 0, 1), 15.5)
+    fill(full("CN"), -16.0)
     fill(full("CP"), -4096.0)
     ts(full("B32"), ref("BO", 0, 128, 16), 32.0, A.mult)
     ts(full("Bm16"), ref("BO", 0, 128, 16), -16.0, A.mult)
@@ -584,8 +751,7 @@ def build(T, topo, core, rank, CO=COSTS[0]):
     act(ref("Sb", 0, 128, 2), ref("Ib", 1, 128, 2), F.Copy)
     act(ref("Sb", 1, 128, 2), ref("Ib", 0, 128, 2), F.Copy)
     act(full("Sb100"), full("Sb"), F.Copy, 0.0, 100.0 / 128)
-    fill(full("QS"), 0.0)
-    fill(ref("VI", 4096, 4096 + 32), 0.0)
+    fill(ref("VI", 4096, 4096 + 32), 0)
     fill(ref("OHW", 0, 16), 0.0)
     ts(ref("OHW", 16, 32), full("IJ"), pm, A.is_equal)
     w = 16
@@ -610,6 +776,13 @@ def build(T, topo, core, rank, CO=COSTS[0]):
             prs.append((ref("Bh", 15 - j, 143 - j), ref(tile[0], tile[1] + j, tile[2], 16)))
         return acc(out, *(prs + list(last)))
 
+    def xts(b, tile, first=()):
+        mm = [(ref(b, 0, n, 1, 0, 8), l, r, i == 0, False) for i, (l, r) in enumerate(first)]
+        return mm + [(ref(b, j, n, 16, 0, 8), ref(tile[0], tile[1] + j, tile[2], 16), ref("BO", 0, n, 16), not first, j == 15 or not first) for j in range(16)]
+
+    I8 = ref("Ib", 0, 8, 1, 0, 8)
+    xl = lambda name, h: ref(name, h * n, h * n + n, 1, 0, 8)
+
     flex("V", ref("VZh", 0, 512, 1, 0, 8), ref("VZ", 0, 512, 1, 0, 8), -2048.0)
     b6 = bank()
     pe(acc(ref(b6, 0, 32), *[(ref("B8", 15 - j, 143 - j, 1, 0, 8), ref("VZh", j, 512, 16, 0, 8)) for j in range(16)]))
@@ -617,13 +790,10 @@ def build(T, topo, core, rank, CO=COSTS[0]):
     for h in (1, 0):
         flex("S", ref("XZ", h * XW, h * XW + 8), ref(b6, 16 + 8 * h, 24 + 8 * h), 2048.0)
         fill(ref("XZ", h * XW + 8, h * XW + 24), 0.0)
-        flex("S", ref("W", h * WW + n, h * WW + 2 * n), ref("FI", h * n, h * n + n), -OFS)
-    for c in range(2):
-        x, it = ref("VW", 1024 * c, 1024 * c + 1024), ref("IT", 1024 * c, 1024 * c + 1024)
-        ts(it, x, 4095, A.bitwise_and)
-        flex("S", ref("VI", 1024 * c, 1024 * c + 1024), it, -OFS)
-        ts(x, x, 12, A.arith_shift_right)
-        flex("S", ref("VI", 2048 + 1024 * c, 3072 + 1024 * c), x, -OFS)
+    for c in range(0, 2048, 512):
+        x = ref("VW", c, c + 512)
+        ts(ref("VI", c, c + 512), x, 4095, A.bitwise_and)
+        ts(ref("VI", 2048 + c, 2560 + c), x, 12, A.arith_shift_right)
 
     def tiles(t, h):
         k = 2 * t + h
@@ -651,13 +821,11 @@ def build(T, topo, core, rank, CO=COSTS[0]):
         mark("hp", h)
         a, c = tl("HI1", h), tl("HI2", h)
         y = ref(bank(), 0, n)
-        pe(acc(y, (full("WB"), L["z"])))
-        flex("V", tl("FL", h), y, 1535.5 + 2.0 ** -13, 2.0 ** -12)
-        pe(acc(y, (full("CH"), on), (full("WB"), L["z"]), (full("I4kn"), tl("FL", h))))
+        pe(acc(y, (full("C1"), on), (full("WBn"), L["z"]), (full("CH"), on), (full("CHn"), on), (full("WB"), L["z"])))
         flex("V", a, y, -(HC + 31.0 / 64), kcol)
         mark("ha", h)
         tt(c, ("ind", ref("W613", 8, 4104), vh), a, A.add)
-        ts(L["hd"], c, 4095 - int(OFS), A.bitwise_and)
+        ts(L["hd"], c, 4095, A.bitwise_and)
         mark("fr", h)
         flex("S", L["x"], ("ind", px, vh))
         bk = bank()
@@ -672,42 +840,56 @@ def build(T, topo, core, rank, CO=COSTS[0]):
             act(tl("T2", h), hz, F.Identity, MAGIC)
             act(L["hz"], tl("T2", h), F.Identity, -MAGIC)
         mark("fr", h)
-        ct = ref(bank(), 0, 8)
-        pe(ots(ct, tl("IND", h), [(full("In"), L["st"](1)), (full("I2"), L["st"](2))]))
         lk = sm("LK", h)
-        ts(lk, ct, 8.5, A.is_ge, 128.0, A.mult)
-        tt(sm("LSL", h), lk, ref("CM", 0, 8), A.add)
+        if "c" in XT:
+            b = bank()
+            mm = xts(b, tl("IND", h), [(L["st"](1), full("In")), (L["st"](2), full("I2"))])
+            pe(mm[:2])
+            pe(mm[2:])
+            ts(xl("XL", h), ref(b, 0, n, 1, 0, 8), 8.5, A.is_ge, 128.0, A.mult)
+            b = bank()
+            pe(acc(ref(b, 0, 8), (Ib, ref("CM", 0, 8)), (xl("XL", h), I8)) + acc(ref(b, 8, 16), (xl("XL", h), I8)))
+            flex("V", sm("LSL", h), ref(b, 0, 8))
+            flex("V", lk, ref(b, 8, 16))
+        else:
+            ct = ref(bank(), 0, 8)
+            pe(ots(ct, tl("IND", h), [(full("In"), L["st"](1)), (full("I2"), L["st"](2))]))
+            ts(lk, ct, 8.5, A.is_ge, 128.0, A.mult)
+            tt(sm("LSL", h), lk, ref("CM", 0, 8), A.add)
         mark("h", h)
-        flex("V", ref("HEL", 2 * h * n, 2 * h * n + n), ("ind", L["w2"], sm("LSL", h)), OFS)
+        flex("V", ref("HEL", 2 * h * n, 2 * h * n + n), ("ind", L["w2"], sm("LSL", h)))
+        mark("hm", h)
+        flex("V", tl("H16", h), ref("HEL", 2 * h * n, 2 * h * n + n), -2048.0)
         mark("qx", h)
         q0 = h * 16 * n
         flex("V", ref("QS", 0, 16 * n, 16), ("ind", L["xz"], sm("LSL", h)))
         banks[h] = (bank(), bank(), bank())
-        if QP:
-            pe([(ref(banks[h][2], 0, n), Ib, ref("QS", 0, 16 * n, 16), True, True)])
+        pe([(ref(banks[h][2], 0, n), Ib, ref("QS", 0, 16 * n, 16), True, True)])
         scan(ref("QX", q0, q0 + 16 * n), full("MK"), full("QS"), 0.0, A.min, A.add)
         mark("e", h)
-        flex("S", tl("E", h), ("ind", views, vh))
-        flex("V", ref("HEL", (2 * h + 1) * n, (2 * h + 2) * n), tl("E", h), OFS)
-        mark("hm", h)
-        scan(tl("HME", h), L["f"], tl("E", h), 0.0, A.min, A.subtract)
+        flex("S", ref("HEL", (2 * h + 1) * n, (2 * h + 2) * n), ("ind", views, vh))
 
     def dedupe(t):
         mark("dd", 0)
         vh = ref("VH", 16 * t, 16 * t + 16)
         flex("V", full("VF"), vh, -2048.0)
-        flex("V", full("VN"), vh, HC - 2.0 ** 23, 613.0)
         b = bank()
         mm = []
-        for j, c in enumerate((0, 0, 1)):
+        for j, (c, d) in enumerate(((0, 0), (0, 1), (1, 1))):
             mm += acc(ref(b, j, 24, 3), (Ib, ref("VF", c, 16, 2)), (full("I8k"), ref("LK", c, 16, 2)))
+            mm += acc(ref(b, 24 + j, 48, 3), (Ib, ref("VF", d, 16, 2)), (Ib, ref("CK", 16, 24)))
         pe(mm)
-        flex("V", full("DL"), ref(b, 0, 24), 2056.0 - 8192.0)
-        flex("S", full("G1"), ("ind", full("W613"), full("DL")))
-        tt(full("EQ"), ("ind", full("VN"), ref("CL", 8, 32)), full("G1"), A.is_equal)
+        flex("V", full("WD"), ref(b, 0, 48), -8192.0)
+        b = bank()
+        for j0 in (0, 8):
+            mm = []
+            for j in range(j0, j0 + 8):
+                mm += acc(ref(b, j, 384, 16), (ref("SEL", 128 * j, 128 * j + 128), ref("WD", 0, 24)), (full("In"), ref("WD", 24, 48)))
+            pe(mm)
+        ts(full("EQ"), ref(b, 0, 384), 0.0, A.is_equal)
         scan(full("DS"), full("D0"), full("EQ"), 0.0, A.mult, A.add)
         b = bank()
-        pe(grp((ref(b, 0, 16), Ib, full("CK")), (ref(b, 0, 16), Ib, full("VF")), (ref(b, 0, 16), full("I8kn"), full("LK")),
+        pe(grp((ref(b, 0, 16), Ib, ref("CK", 0, 16)), (ref(b, 0, 16), Ib, full("VF")), (ref(b, 0, 16), full("I8kn"), full("LK")),
                (ref(b, 0, 16, 2), full("DG"), ref("DS", 14, 384, 48)), (ref(b, 1, 16, 2), full("DG"), ref("DS", 46, 384, 48))))
         tt(full("OFF"), ref(b, 0, 16), full("SPT"), A.min)
 
@@ -748,8 +930,14 @@ def build(T, topo, core, rank, CO=COSTS[0]):
             store(T.yz[:, h * n:h * n + n], ref("YU", 1024 + h * n, 1024 + h * n + n))
         mark("kk", h)
         y = ref(bank(), 0, 8)
-        pe(ots(y, L["zf"], [(full("I8k"), lk), (full("I8200"), ov)]))
-        flex("V", sm("KL", h), y, t + 16.0 - 8192.0)
+        if "k" in XT:
+            b = bank()
+            pe(xts(b, L["zf"]))
+            flex("S", xl("XK", h), ref(b, 0, n, 1, 0, 8), -2048.0)
+            pe(acc(y, (full("I8k"), lk), (full("I8200"), ov), (xl("XK", h), I8)))
+        else:
+            pe(ots(y, L["zf"], [(full("I8k"), lk), (full("I8200"), ov)]))
+        flex("V", sm("KL", h), y, t + 16.0 - 8192.0 + (2048.0 if "k" in XT else 0.0))
         flex("S", tl("OHL", h), ("ind", full("OHW"), sm("KL", h)))
 
     def bulk(t, h, w):
@@ -768,7 +956,7 @@ def build(T, topo, core, rank, CO=COSTS[0]):
             if e_ == n:
                 for k0 in range(0, 16, SPLIT):
                     pe([(ref(b, k, n, 16), ref(G, q0 + k, q0 + 16 * n, 16), full("Bm16"), False, False) for k in range(max(1, k0), k0 + SPLIT)], sub=True)
-            tt(g0, g0, ref(banks[h][2], a, e_) if QP else ref("QX", lo, hi, 16), A.max)
+            tt(g0, g0, ref(banks[h][2], a, e_), A.max)
             scan(ref(M, lo, hi), ref("QX", lo, hi), ref(G, lo, hi), 0.0, A.min, A.max)
         pe([(ref(b, 0, n), tl("OHL", h), full("Ibig" if w == 0 else "MP"), False, False)])
         for k0 in range(0, 16, SPLIT):
@@ -789,15 +977,22 @@ def build(T, topo, core, rank, CO=COSTS[0]):
         mark("cc", h)
         tt(tl("MT", h), key, pd, A.is_lt)
         mk = ref(bank(), 0, n)
-        pe([(mk, tl("MT", h), Ib, True, True)])
-        tt(tl("MM", h), tl("HME", h), mk, A.mult)
-        scan(L["c"], tl("MM", h), tl("E", h), -OFS, A.max, A.add)
-        flex("V", tl("CF", h), ("ind", L["w3"], sm("TLL", h, 16)), OFS - 2048.0)
+        pe([(mk, full("CN"), on, True, False), (mk, Ib, tl("H16", h), False, False)])
+        pe([(mk, tl("MT", h), full("I8192"), False, True)])
+        tt(tl("MM", h), ref("HEL", (2 * h + 1) * n, (2 * h + 2) * n), mk, A.max)
+        ts(L["c"], tl("MM", h), 4095, A.bitwise_and)
+        flex("V", tl("CF", h), ("ind", L["w3"], sm("TLL", h, 16)), -2048.0)
         tt(tl("PP", h), tl("CF", h), oc, A.mult)
         vo = ref(bank(), 0, n)
         if t < NT - 1:
             vo = ref(vo[0], 0, 8)
-            pe(ots(vo, tl("PP", h)))
+            if "v" in XT:
+                b = bank()
+                pe(xts(b, tl("PP", h)))
+                flex("V", xl("XV", h), ref(b, 0, n, 1, 0, 8))
+                pe([(vo, xl("XV", h), I8, True, True)])
+            else:
+                pe(ots(vo, tl("PP", h)))
             flex("V", L["vb"], vo, 2048.0)
             send("v", t + 1, h, tiles(t + 1, h)["vh"], L["vb"])
         else:
@@ -809,7 +1004,7 @@ def build(T, topo, core, rank, CO=COSTS[0]):
             flex("S", L["fb"], ("ind", L["c"], sm("TLL", h, 16, 8)))
             send("f", t + 1, h, tiles(t + 1, h)["f"], L["fb"])
         else:
-            flex("S", ref("YU", 1536 + h * n, 1536 + h * n + n), ("ind", L["c"], sm("TLL", h, 16, 8)), OFS)
+            flex("S", ref("YU", 1536 + h * n, 1536 + h * n + n), ("ind", L["c"], sm("TLL", h, 16, 8)))
             store(T.yf[:, h * n:h * n + n], ref("YU", 1536 + h * n, 1536 + h * n + n))
 
     def scatter(t, h):
@@ -833,8 +1028,9 @@ def build(T, topo, core, rank, CO=COSTS[0]):
     pg["st"] = ""
     for c in range(4):
         a, b = 512 * c, 512 * c + 512
-        flex("S", ref("W613", a, b), ref("VI", 2048 + a, 2048 + b), OFS * 4097.0, 4096.0)
-        scan(ref("YT", a, b), ref("VI", a, b), ref("W613", a, b), 0.0, A.min, A.add)
+        y = ref(bank(), 0, 512)
+        flex("S", y, ref("VI", 2048 + a, 2048 + b), 0.0, 4096.0)
+        tt(ref("YT", a, b), ref("VI", a, b), y, A.add)
         store(T.yw[:, a:b], ref("YT", a, b))
     named, seen = {}, {}
     for o in pg["ops"]:

@@ -15,22 +15,26 @@ HC = 262000
 NOH = 4112
 OH0 = 1024
 PARTS = ((((0, 64, "S"), (64, 128, "S")), ((0, 64, "S"), (64, 128, "S"))),) * 2
-CHUNKS = (((0, 64), (64, 128)), ((0, 64), (64, 128)))
+CHUNKS = ((((0, 64), (64, 128)), ((0, 128),)), (((0, 128),), ((0, 64), (64, 128))))
 ONV = ("hz0", "hz1")
-LINES = ((),) * NT
-XT = "cv"
+LINES = [tuple("%sb%s  G%s %d" % (x[0], x[1], x[0].upper(), k) for x in ("h1 e1 e0 h0" if t else "h1 e1 h0 e0").split() for k in ()) for t in range(NT)]
+WAW = False
+XT = "ckv"
+PACK = (0, 192, 576, 1088, 1600, 2048)
+JOIN = 0
+SELP = 4
 SPLIT = 8
 f4, b2, h2, i4, u2 = "float32", "bfloat16", "float16", "int32", "uint16"
 
 SCRATCH = {
-    "PX": ("sbuf", [128, 4096], b2), "VI": ("sbuf", [128, 4096 + 32], i4), "VW": ("sbuf", [128, 2048], i4),
+    "PX": ("sbuf", [128, NOH + 4096], b2), "VI": ("sbuf", [128, 4096 + 32], i4), "VW": ("sbuf", [128, 2048], i4),
     "YT": ("sbuf", [128, 2048], f4), "YU": ("sbuf", [128, 2048], f4),
-    "W613": ("sbuf", [128, 4096 + 8], f4), "OHW": ("sbuf", [128, NOH], b2),
+    "W613": ("sbuf", [128, 4096 + 8], f4), "TRI": ("sbuf", [128, 384], b2),
     "XZ": ("sbuf", [128, 10 * XW], b2), "W": ("sbuf", [128, 10 * WW], i4), "VH": ("sbuf", [128, 10 * 8], u2),
     "ZB": ("sbuf", [128, 8 * (32 + n)], b2), "FB": ("sbuf", [128, 10 * n], i4), "SPT": ("sbuf", [128, 16], f4), "CK": ("sbuf", [128, 24], b2), "VB": ("sbuf", [128, 10 * 8], u2), "ZL": ("sbuf", [128, 2 * n], b2),
     "HEL": ("sbuf", [128, 4 * n], u2), "QS": ("sbuf", [128, 16 * n], b2), "QX": ("sbuf", [128, 32 * n], b2), "MK": ("sbuf", [128, 16 * n], b2), "H16": ("sbuf", [128, 2 * n], h2),
     "GH": ("sbuf", [128, 32 * n], b2), "GE": ("sbuf", [128, 32 * n], b2), "MH": ("sbuf", [128, 32 * n], b2), "ME": ("sbuf", [128, 32 * n], b2),
-    "IND": ("sbuf", [128, 2 * n], b2), "LK": ("sbuf", [128, 16], b2), "LSL": ("sbuf", [128, 16], u2),
+    "IND": ("sbuf", [128, 2 * n], b2), "LK": ("sbuf", [128, 16], b2), "LSL": ("sbuf", [128, 16], u2), "LSF": ("sbuf", [128, 32], u2), "CMF": ("sbuf", [128, 16], b2),
     "HI1": ("sbuf", [128, 2 * n], i4), "HI2": ("sbuf", [128, 2 * n], i4),
     "T2": ("sbuf", [128, 2 * n], f4),
     "OV": ("sbuf", [128, 16], b2), "TLL": ("sbuf", [128, 32], u2), "RA": ("sbuf", [128, 48], b2), "KL": ("sbuf", [128, 16], u2), "OHL": ("sbuf", [128, 2 * n], b2),
@@ -51,22 +55,28 @@ SCRATCH = {
 }
 DIAG = {"Ib": (1.0, b2), "In": (-1.0, b2), "I2": (2.0, b2), "Ic": (0.00689697265625, b2), "Icn": (-0.00689697265625, b2), "Ihz": (0.5 - 2.0 ** -11, h2),
         "I1": (1.0 / 128, b2), "Ip100": (100.0 / 128, b2), "Im100": (-100.0 / 128, b2), "I8k": (8192.0 / 128, b2), "I8kn": (-8192.0 / 128, b2), "I8200": (8200.0 / 128, h2),
-        "I8192": (8192.0, b2), "Ibig": (-262144.0, b2), "Ifl": (0.4375, b2), "I16": (16.0, b2)}
+        "I10240": (10240.0, b2), "In8192": (-8192.0, b2), "Ibig": (-262144.0, b2), "Ifl": (0.8125, b2), "I16": (16.0, b2)}
 for _k in DIAG:
     SCRATCH[_k] = ("sbuf", [128, 128], DIAG[_k][1])
 for _b in range(8):
     SCRATCH["bank%d" % _b] = ("psum", [128, 512], f4) if _b < NB else ("psum", [128, 1024], b2)
-LOADS = ["v0", "d0", "px0", "px1", "z1", "z0", "wt", "kap", "f1", "f0", "vw0", "vw1"]
-SEMAPHORES = ["V", "S", "P", "G", "out", "ls", "oh"] + ["ld_" + x for x in LOADS] + ["r%s_%d_%d" % (k, t, h) for k in "zfv" for t in range(1, NT) for h in range(2)]
+LOADS = ["v0", "d0", "wt", "kap", "z1", "px0", "px1", "z0", "f1", "f0", "vw0", "vw1"]
+SEMAPHORES = ["V", "S", "P", "G", "out", "ls", "oh", "sl"] + ["ld_" + x for x in LOADS] + ["r%s_%d_%d" % (k, t, h) for k in "zfv" for t in range(1, NT) for h in range(2)]
 
 COSTS = tuple(dict(zip(("cy", "gather", "wake", "pe", "link", "scat", "V", "S", "P", "row", "issue", "load"), c)) for c in (
     (0.00083, 1.56, 0.10, 0.00046, 1.4, 0.18, 0.03, 0.04, 0.03, 1.0, 0.4, 1.0),
     (0.00083, 1.10, 0.07, 0.00042, 1.0, 0.12, 0.03, 0.04, 0.03, 0.7, 0.3, 0.9),
-    (0.00108, 1.80, 0.15, 0.00056, 2.0, 0.25, 0.04, 0.05, 0.04, 1.5, 0.8, 1.3),
-    (0.00083, 1.56, 0.12, 0.00042, 1.8, 0.14, 0.06, 0.07, 0.02, 1.2, 0.6, 1.2),
+    (0.00112, 1.95, 0.15, 0.00056, 2.0, 0.25, 0.04, 0.05, 0.04, 1.5, 0.8, 1.3),
+    (0.00102, 1.70, 0.12, 0.00050, 1.8, 0.14, 0.06, 0.07, 0.02, 1.2, 0.6, 1.2),
     (0.00090, 1.40, 0.08, 0.00052, 1.1, 0.22, 0.03, 0.04, 0.05, 0.8, 0.4, 1.0)))
-ROUNDS = 1500
-MOVES = 70000
+ROUGH = 0.0
+SEEDS = (1, 2, 3)
+ROUNDS = 600
+MOVES = (8000, 55000)
+LOADW = 0.0
+FIRST = {}
+ALIKE = 0.0
+EVERY = 0.9
 STAGGER = 7.0
 
 
@@ -311,7 +321,22 @@ def schedule(pgs, wakes, rounds, seed):
                 now, cur, q, cs = f, x, q2, cs2
             if f < best:
                 best, keep = f, info
-    return keep
+    st, q, tries = keep[4], keep[5], []
+    keep = None
+    for t0 in (1, 2, 3) if ALIKE else ():
+        step = sorted(st[sl[3]] - st[sl[1]] for sl in slots if len(sl) == NT)
+        step = step[len(step) // 2] / 2
+        key, q2 = list(st), list(q)
+        for sl in slots:
+            by = {ops[i]["hop"]: i for i in sl}
+            for t in by:
+                if t and t0 in by:
+                    key[by[t]], q2[by[t]] = st[by[t0]] + (t - t0) * step, q[by[t0]]
+        cs2 = prices(q2)
+        f, info = judge(place(key, pred, succ, q2, cs2[0][0], zero), q2, cs2)
+        if info:
+            tries.append((f, t0, info))
+    return min(tries)[2] if tries else judge(st, q, prices(q))[1]
 
 
 def polish(pgs, wakes, keep, moves, seed, temp=0.0004):
@@ -380,6 +405,64 @@ def polish(pgs, wakes, keep, moves, seed, temp=0.0004):
             i = nx
         return out
 
+    def tails(m):
+        c, l, w = cost[m], lat[m], wakes[m]
+        tl = [0.0] * (N_ + 1)
+        for i in reversed(seq):
+            t = tl[i]
+            if t < l[i]:
+                t = l[i]
+            t += c[i]
+            tl[i] = t
+            if tl[prev[i]] < t:
+                tl[prev[i]] = t
+            for d in dep[i]:
+                if tl[d] < t + l[d] + w:
+                    tl[d] = t + l[d] + w
+            d = snd[i]
+            if d is not None and tl[d] < t + l[d]:
+                tl[d] = t + l[d]
+        return tl
+
+    def least(m, p0, p1):
+        c, l, w, end, fin, tl = cost[m], lat[m], wakes[m], E[m], Fi[m], rest[m]
+        new, last, x = {}, {}, 0.0
+        for i in seq[p0:p1]:
+            if pos[prev[i]] < p0 and prev[i] != Z and q[prev[i]] not in last:
+                last[q[prev[i]]] = end[prev[i]]
+        for i in seq[p0:p1]:
+            t = last.get(q[i], 0.0)
+            for d in dep[i]:
+                y = new.get(d, fin[d]) + w
+                if y > t:
+                    t = y
+            d = snd[i]
+            if d is not None and new.get(d, fin[d]) > t:
+                t = new.get(d, fin[d])
+            t += c[i]
+            last[q[i]] = t
+            new[i] = t = t + l[i]
+            for j in waits[i]:
+                if pos[j] >= p1 and t + w + tl[j] > x:
+                    x = t + w + tl[j]
+        for j in seq[p1:p1 + 40]:
+            t = last.pop(q[j], None)
+            if t is not None and t + tl[j] > x:
+                x = t + tl[j]
+        return x
+
+    either = [o["i"] for o in ops if o["alt"]]
+    twin, seen, slot = {}, {}, {}
+    for o in ops:
+        if o["st"]:
+            k = (o["hop"], o["st"], o["tag"])
+            seen[k] = seen.get(k, 0) + 1
+            twin[o["i"]] = slot.setdefault((o["st"], o["tag"], seen[k]), {})
+            twin[o["i"]][o["hop"]] = o["i"]
+    waits = [[] for _ in ops]
+    for i in range(N_):
+        for d in dep[i]:
+            waits[d].append(i)
     prev = links(seq)
     E, Fi = [[0.0] * (N_ + 1) for _ in pgs], [[0.0] * (N_ + 1) for _ in pgs]
     r = [run(m, 0, prev, E[m], Fi[m]) for m in range(M)]
@@ -387,34 +470,72 @@ def polish(pgs, wakes, keep, moves, seed, temp=0.0004):
     now = best = 1.0
     kept = (list(seq), list(q), list(r))
     rng = np.random.default_rng(seed)
-    pos = [0] * N_
-    fresh, paths = True, None
+    pos = [0] * (N_ + 1)
+    fresh, paths, rest = True, None, None
     for it in range(moves):
         if fresh:
             st = [E[0][i] - cost[0][i] for i in range(N_)]
             seq.sort(key=lambda i: st[i])
             for k, i in enumerate(seq):
                 pos[i] = k
-            paths = [path(m) for m in range(M)]
+            paths, rest = {}, {}
             fresh = False
         u = rng.random(5)
-        pt = paths[int(u[0] * M)]
+        if not paths or u[0] < 0.05:
+            m0 = int(rng.integers(M))
+        if m0 not in paths:
+            paths[m0], rest[m0] = path(m0), tails(m0)
+        pt = paths[m0]
         if not pt:
             continue
         a, b = pt[int(u[1] * len(pt))]
-        undo = None
-        if u[2] < 0.15:
+        undo, gain, quick = None, 0.0, True
+        if rng.random() < (EVERY if it < moves * ALIKE else 0.05) and (a in twin and b in twin):
+            p0, old, done, quick = None, list(seq), 0, False
+            kind = int(u[2] * 5)
             i = a if u[3] < 0.5 else b
+            if kind == 0:
+                if not ops[i]["alt"]:
+                    continue
+                to = "V" if q[i] == "S" else "S"
+                undo = [(j, q[j], [cost[m][j] for m in range(M)]) for j in twin[i].values()]
+                for j in twin[i].values():
+                    q[j] = to
+                    for m in range(M):
+                        cost[m][j] = pgs[m]["ops"][j]["alt"][to][0]
+                p0 = min(pos[j] for j in twin[i].values())
+            else:
+                for _ in range(int(u[3] * u[3] * 4) if kind < 3 else 0):
+                    if prev[a] in twin:
+                        a = prev[a]
+                for t in range(NT):
+                    a2, b2_ = twin[a].get(t), twin[b].get(t + ops[b]["hop"] - ops[a]["hop"])
+                    if a2 is None or b2_ is None or q[a2] != q[b2_] or not done <= pos[a2] < pos[b2_]:
+                        continue
+                    x, y = pos[a2], pos[b2_]
+                    if kind < 3 and all(pos[d] < x for d in before[b2_]):
+                        seq[x:y + 1] = [b2_] + old[x:y]
+                    elif kind >= 3 and all(pos[d] > y for d in after[a2]):
+                        seq[x:y + 1] = old[x + 1:y + 1] + [a2]
+                    else:
+                        continue
+                    p0, done = x if p0 is None else p0, y + 1
+                if p0 is None:
+                    continue
+            old = old[p0:]
+        elif u[2] < 0.15:
+            i = a if u[3] < 0.3 else b if u[3] < 0.6 else either[int(rng.integers(len(either)))]
             if not ops[i]["alt"]:
                 continue
             to = "V" if q[i] == "S" else "S"
-            undo = (i, q[i], [cost[m][i] for m in range(M)])
+            gain = LOADW * ops[i]["alt"]["V"][0] * (1 if to == "S" else -1) / first[0]
+            undo = [(i, q[i], [cost[m][i] for m in range(M)])]
             q[i] = to
             for m in range(M):
                 cost[m][i] = pgs[m]["ops"][i]["alt"][to][0]
             p0 = p1 = pos[i]
             if u[2] < 0.08:
-                lo = max([pos[d] for d in before[i]] + [-1]) + 1
+                lo = min(p1, max([pos[d] for d in before[i]] + [-1]) + 1)
                 p0 = lo + int((p1 - lo) * (u[3] * 7 % 1) ** 2)
             old = seq[p0:p1 + 1]
             seq[p0:p1 + 1] = [i] + old[:-1]
@@ -444,10 +565,12 @@ def polish(pgs, wakes, keep, moves, seed, temp=0.0004):
             p0, p1 = pos[a], pos[b]
             old = seq[p0:p1 + 1]
             seq[p0:p1 + 1] = old[1:] + [a]
-        pv = links(seq)
-        lim = now - temp * (1 - it / moves) * float(np.log(u[4] + 1e-12))
+        lim = now - temp * (1 - it / moves) * float(np.log(u[4] + 1e-12)) + gain
         E2, F2, r2, f = [], [], [], 0.0
-        for m in range(M):
+        if quick and least(m0, p0, p0 + len(old)) > r[m0] + (lim - now) * first[m0] * 2 + 0.05:
+            f = 1.0
+        pv = links(seq) if f == 0.0 else None
+        for m in range(M if f == 0.0 else 0):
             e, fi = list(E[m]), list(Fi[m])
             x = run(m, p0, pv, e, fi)
             E2.append(e)
@@ -463,16 +586,27 @@ def polish(pgs, wakes, keep, moves, seed, temp=0.0004):
                 best, kept = now, (list(seq), list(q), list(r))
         else:
             seq[p0:p0 + len(old)] = old
-            if undo:
-                i, q[i] = undo[0], undo[1]
+            for i, x, cs in undo or ():
+                q[i] = x
                 for m in range(M):
-                    cost[m][i] = undo[2][m]
+                    cost[m][i] = cs[m]
     return kept[0], dyn, bmap, kept[2], None, kept[1]
 
 
 def plan(T, topo, core, rank):
-    pgs, wakes = [build(T, topo, core, rank, c) for c in COSTS], [c["wake"] for c in COSTS]
-    return polish(pgs, wakes, schedule(pgs, wakes, ROUNDS, 1), MOVES, 1)
+    pgs, wakes = [build(T, topo, core, rank, c) for c in COSTS], [c["wake"] * 2.6 for c in COSTS]
+    rng = np.random.default_rng(5)
+    for p in pgs:
+        by = {}
+        for o in p["ops"]:
+            for x in o["alt"] or (o["q"],):
+                f = by.setdefault((x, o["tag"]), float(np.exp(rng.normal(0, ROUGH))))
+                if o["alt"]:
+                    o["alt"][x] = (o["alt"][x][0] * f, o["alt"][x][1])
+                if x == o["q"]:
+                    o["cost"] *= f
+    starts = [polish(pgs, wakes, schedule(pgs, wakes, ROUNDS, s), MOVES[0], s) for s in SEEDS]
+    return polish(pgs, wakes, min(starts, key=lambda k: sum(x / y for x, y in zip(k[3], starts[0][3]))), MOVES[1], 1, 0.0003)
 
 
 def emit(pg, keep, g, T):
@@ -579,7 +713,7 @@ def build(T, topo, core, rank, CO=COSTS[0]):
         return add(pg, "S", FIX["S"] + CY * max(64, cnt(out) * (GC if ind else 1)) + (0.04 if ind else 0),
                    lambda e: e.activation(ap(out), inap(in_), func, bias=dcol(bias), scale=dcol(scale)), regs(in_) + sc, [out], tag="act " + out[0])
 
-    def flex(q, out, in_, bias=0.0, scale=1.0, relu=False):
+    def flex(q, out, in_, bias=0.0, scale=1.0, relu=False, size=False):
         ind = in_[0] == "ind"
         sc = [scale] if isinstance(scale, tuple) else []
         if scale == 1.0:
@@ -589,8 +723,12 @@ def build(T, topo, core, rank, CO=COSTS[0]):
         fs = lambda e: e.activation(ap(out), inap(in_), F.Relu if relu else F.Identity if bias else F.Copy, bias=bias, scale=dcol(scale))
         if relu:
             fv = lambda e: e.tensor_scalar(ap(out), inap(in_), 0.0, None, A.max)
+        if size:
+            fv = lambda e: e.tensor_scalar(ap(out), inap(in_), 0.0, None, A.not_equal)
+            fs = lambda e: e.activation(ap(out), inap(in_), F.Abs)
         alt = {"V": (vcost(cnt(out), 0.5 if (not ind and two(out, in_)) else 1, ind), fv),
                "S": (FIX["S"] + CY * max(64, cnt(out) * (GC if ind else 1)) + (0.04 if ind else 0), fs)}
+        q = FIRST.get(pg["st"], q)
         return add(pg, q, alt[q][0], None, regs(in_) + sc, [out], tag="flex " + out[0], alt=alt)
 
     def pe(mms, sub=False):
@@ -613,7 +751,7 @@ def build(T, topo, core, rank, CO=COSTS[0]):
             for out, l, r, s, e_ in mms:
                 ins = e.transpose(ap(out), ap(l), ap(r)) if out[0][0] == "c" else e.matmul(ap(out), ap(l), ap(r), s, e_)
             return ins
-        return add(pg, "P", cost + FIX["P"], fn, list(rd.values()), list(wr.values()), tag="pe " + mms[0][1][0] + " " + mms[0][2][0])
+        return add(pg, "P", cost + FIX["P"] / 2, fn, list(rd.values()), list(wr.values()), tag="pe " + mms[0][1][0] + " " + mms[0][2][0])
 
     def acc(out, *pairs):
         return [(out, l, r, i == 0, i == len(pairs) - 1) for i, (l, r) in enumerate(pairs)]
@@ -645,7 +783,7 @@ def build(T, topo, core, rank, CO=COSTS[0]):
         s = "r%s_%d_%d" % (kind, t, h)
         nls[0] += neng
         i = add(pg, "G", CO["issue"] * (1 if sent[0] else 8), lambda e: e.remote_dma(ap(out), ap(in_), T.sem[s], T.sem["ls"], pid, rid, mask), [in_], [], sem="ls", val=nls[0], tag="send " + kind)
-        d = add(pg, "RD", CO["row"] * {"v": 0.8, "z": 1.3, "f": 1.6}[kind], None, [], [], sem="-", lat=CO["link"], tag="rows " + kind)
+        d = add(pg, "RD", CO["row"] * {"v": 0.8, "z": 1.3, "f": 1.6}[kind], None, [], [], sem="-", lat=CO["link"] - 0.3, tag="rows " + kind)
         j = add(pg, "R" + s, 0.0, None, [], [out], sem=s, val=neng)
         pg["ops"][d]["send"], pg["ops"][j]["send"] = i, d
         if kind == "f":
@@ -659,7 +797,7 @@ def build(T, topo, core, rank, CO=COSTS[0]):
     what = {"v0": (ref("VZ", 0, 256, 1, 0, 8), T.v0[:, :], 0.02), "d0": (ref("VZ", 256, 512, 1, 0, 8), T.d0[:, :], 0.02),
             "wt": (ref("WT", 0, 1), T.wt[:, :], 0.15), "kap": (ref("WT", 1, 2), T.kap[:, :], 0.15)}
     for h in range(2):
-        what["px%d" % h] = (ref("PX", 2048 * h, 2048 * h + 2048), T.px[:, 2048 * h:2048 * h + 2048], 1.5)
+        what["px%d" % h] = (ref("PX", NOH + 2048 * h, NOH + 2048 * h + 2048), T.px[:, 2048 * h:2048 * h + 2048], 1.5)
         what["vw%d" % h] = (ref("VW", 1024 * h, 1024 * h + 1024), T.vw[:, 1024 * h:1024 * h + 1024], 1.5)
         what["z%d" % h] = (ref("XZ", h * XW + 32, h * XW + 32 + n), T.z0[:, h * n:h * n + n], 0.2)
         what["f%d" % h] = (ref("W", h * WW + n, h * WW + 2 * n), T.f0[:, h * n:h * n + n], 0.25)
@@ -693,22 +831,18 @@ def build(T, topo, core, rank, CO=COSTS[0]):
     iota(ref("W613", 8, 1032), [[613, 1024]], HC - 2 ** 23, 0)
     act(ref("W613", 1032, 2056), ref("W613", 8, 1032), F.Identity, 613.0 * 1024)
     act(ref("W613", 2056, 4104), ref("W613", 8, 2056), F.Identity, 613.0 * 2048)
-    fill(full("MK"), 256.0)
-    fill(ref("MK", 0, 16 * n, 16), 0.0)
+    iota(full("MK"), [[0, n], [256, 16]], 0, 0)
     fill(full("QS"), 0.0)
     iota(full("KC"), [[0, 8], [1, 16]], 0, 0)
-    for j in range(16):
-        sel(ref("SEL", 128 * j, 128 * j + 128), on, [[-16, 8], [0, 16]], A.is_equal, 0.0, -j, 1)
+    sel(ref("SEL", 0, 128), on, [[-16, 8], [0, 16]], A.is_equal, 0.0, 0, 1)
     ts(ref("CL", 0, 8), ref("CMI", 0, 8), 15.0, A.add)
     iota(full("RST"), [[0, 128]], 0, 0)
     sel(full("RST"), full("RST"), [[0, 8], [1, 16]], A.not_equal, 1048576.0, 0, 0)
     for i, c in enumerate((1, 0, -99)):
         iota(ref("CS", 8 * i, 8 * i + 8), [[0, 8]], c, 0)
-    for k in range(8):
-        iota(ref("ZB", k * (32 + n) + 24, k * (32 + n) + 32), [[0, 8]], 0, 0)
     iota(full("ZE"), [[0, 128]], 0, 0)
     for nm in DIAG:
-        if nm in ("Ibig", "Ifl", "I16", "I8k", "I1", "Ip100", "I8kn", "I8192"):
+        if nm in ("Ibig", "Ifl", "I16", "I8k", "I1", "Ip100", "I8kn", "I10240", "In8192"):
             sel(full(nm), full("ZE"), [[-1, 128]], A.not_equal, DIAG[nm][0], 0, 1)
         elif DIAG[nm][1] == h2:
             ts(full(nm), Ib, DIAG[nm][0], A.mult)
@@ -720,55 +854,65 @@ def build(T, topo, core, rank, CO=COSTS[0]):
     cp(pm, ref("PI", 16, 17))
     ts(sg, ref("PI", 24, 25), -2.0 / 128, A.mult, 1.0 / 128, A.add)
     ts(sg256, ref("PI", 24, 25), -2.0 / 128, A.mult, 257.0 / 128, A.add)
-    ts(dg, pm, 15.0, A.is_equal, 8192.0 - 2.0 ** -5, A.mult)
-    ts(dg, dg, 2.0 ** -5, A.add)
     iota(full("SPT"), [[0, 8], [16, 2]], 4096, 0)
     ts(full("SPT"), full("SPT"), pm, A.add)
-    iota(ref("CK", 0, 16), [[0, 16]], 10240, 0)
+    iota(ref("CK", 0, 16), [[0, 16]], 18432, 0)
     iota(ref("CK", 16, 24), [[0, 8]], 8192, 0)
     ts(full("G0"), Ib, sg, A.mult)
     ts(full("G256"), Ib, sg256, A.mult)
-    ts(full("DG"), Ib, dg, A.mult)
     cp(ref("WTf", 0, 2), full("WT"))
     ts(ref("WTf", 4, 5), ref("WTf", 1, 2), 1.0 / 32, A.mult)
     wcol, kcol = ref("WTf", 0, 1), ref("WTf", 4, 5)
     ts(full("WB"), full("BO"), wcol, A.mult)
-    fill(full("Bh"), 0.0)
-    cp(ref("Bh", 15, 143, 16), ref("BO", 0, 128, 16))
+    if len(XT) < 3:
+        fill(full("Bh"), 0.0)
+        cp(ref("Bh", 15, 143, 16), ref("BO", 0, 128, 16))
     act(full("WBn"), full("WB"), F.Copy, 0.0, -1.0)
     fill(full("CH"), M35 / 128)
     fill(full("CHn"), -M35 / 128)
     fill(full("C1"), 16.0)
     fill(ref("C1", 0, 128, 1, 0, 1), 15.5)
-    fill(full("CN"), -16.0)
-    fill(full("CP"), -4096.0)
+    iota(full("CN"), [[0, 128]], -32, 0)
+    iota(full("CP"), [[0, 128]], -4096, 0)
     ts(full("B32"), ref("BO", 0, 128, 16), 32.0, A.mult)
     ts(full("Bm16"), ref("BO", 0, 128, 16), -16.0, A.mult)
     ts(full("MP"), full("BO"), 524288.0, A.mult)
     tt(full("MP"), full("MP"), full("Ibig"), A.add)
     ts(ref("CM", 0, 8), ref("CMI", 0, 8), pm, A.add)
     ts(ref("CM", 8, 16), ref("CMI", 0, 8), pm, A.add)
+    iota(ref("CMF", 0, 8), [[0, 8]], 256, 0)
+    ts(ref("CMF", 8, 16), ref("CMI", 0, 8), pm, A.add, 128.0, A.add)
     act(ref("Sb", 0, 128, 2), ref("Ib", 1, 128, 2), F.Copy)
     act(ref("Sb", 1, 128, 2), ref("Ib", 0, 128, 2), F.Copy)
     act(full("Sb100"), full("Sb"), F.Copy, 0.0, 100.0 / 128)
     fill(ref("VI", 4096, 4096 + 32), 0)
-    fill(ref("OHW", 0, 16), 0.0)
-    ts(ref("OHW", 16, 32), full("IJ"), pm, A.is_equal)
+    fill(ref("PX", 0, 16), 0.0)
+    ts(ref("PX", 16, 32), full("IJ"), pm, A.is_equal)
     w = 16
     while w < OH0:
-        cp(ref("OHW", 16 + w, 16 + 2 * w), ref("OHW", 16, 16 + w))
+        cp(ref("PX", 16 + w, 16 + 2 * w), ref("PX", 16, 16 + w))
         w *= 2
     for a in range(w, 4096, w):
-        i = add(pg, "Y", 0.1, lambda e, a=a: e.dma_start(ap(ref("OHW", 16 + a, 16 + a + w)), ap(ref("OHW", 16, 16 + w))).then_inc(T.sem["oh"], 16),
-                [ref("OHW", 16, 16 + w)], [ref("OHW", 16 + a, 16 + a + w)], sem="oh", val=16 * (4096 // w - 1), lat=9.5, tag="copy")
+        i = add(pg, "Y", 0.1, lambda e, a=a: e.dma_start(ap(ref("PX", 16 + a, 16 + a + w)), ap(ref("PX", 16, 16 + w))).then_inc(T.sem["oh"], 16),
+                [ref("PX", 16, 16 + w)], [ref("PX", 16 + a, 16 + a + w)], sem="oh", val=16 * (4096 // w - 1), lat=9.5, tag="copy")
         pg["ops"][i]["ord"].add(loads[-1])
-    fill(ref("D0", 16, 32), 1.0)
-    ts(ref("D0", 0, 16), full("IJ"), pm, A.is_equal, 262144.0, A.mult)
-    ts(ref("D0", 0, 16), ref("D0", 0, 16), 1.0, A.max)
-    cp(ref("D0", 32, 48), ref("D0", 0, 16))
-    fill(ref("D0", 0, 32, 16), 0.0)
+    for step, k in enumerate((1, 2, 4, 8)):
+        for p0, p1, s0 in ((k, 128, 0), (0, k, k)):
+            out, src = ref("SEL", 128 * k, 256 * k, 1, p0, p1), ref("SEL", 0, 128 * k, 1, s0, s0 + p1 - p0)
+            j = add(pg, "Y", 0.1, lambda e, out=out, src=src: e.dma_start(ap(out), ap(src)).then_inc(T.sem["sl"], 16), [src], [] if s0 else [out],
+                    sem="sl", val=32 * step + 32, lat=7.0 if step == 0 else 2.5, tag="copy")
+            pg["ops"][j]["ord"].add(i)
+            if s0:
+                pg["acc"]["SEL"].append((j, 128 * k, 256 * k, True, 1))
+            i = j
+    fill(full("D0"), 0.0)
+    fill(ref("D0", 0, 384, 48), 1.0)
+    fill(ref("D0", 16, 384, 48), 1.0)
+    ts(ref("TRI", 0, 16), full("IJ"), pm, A.is_ge, 16384.0, A.mult)
+    fill(ref("TRI", 16, 32), 0.0)
+    cp(ref("TRI", 32, 48), ref("TRI", 0, 16))
     for a in (48, 96, 192):
-        act(ref("D0", a, 2 * a), ref("D0", 0, a), F.Copy)
+        flex("S", ref("TRI", a, 2 * a), ref("TRI", 0, a))
 
     def ots(out, tile, first=(), last=()):
         prs = list(first)
@@ -789,7 +933,8 @@ def build(T, topo, core, rank, CO=COSTS[0]):
     flex("V", ref("VH", 0, 16), ref(b6, 0, 16), 2048.0)
     for h in (1, 0):
         flex("S", ref("XZ", h * XW, h * XW + 8), ref(b6, 16 + 8 * h, 24 + 8 * h), 2048.0)
-        fill(ref("XZ", h * XW + 8, h * XW + 24), 0.0)
+        fill(ref("XZ", h * XW + 8, h * XW + 16), 0.0)
+        flex("S", ref("XZ", h * XW + 16, h * XW + 32), full("CMF"))
     for c in range(0, 2048, 512):
         x = ref("VW", c, c + 512)
         ts(ref("VI", c, c + 512), x, 4095, A.bitwise_and)
@@ -804,12 +949,13 @@ def build(T, topo, core, rank, CO=COSTS[0]):
              "w2": ref("W", w0, w0 + 2 * n), "w3": ref("W", w0, w0 + 3 * n), "vh": ref("VH", 8 * k, 8 * k + 8),
              "land": ref("XZ", x0, x0 + 32 + n), "fb": ref("FB", k * n, k * n + n), "vb": ref("VB", 8 * k, 8 * k + 8)}
         if t < NT - 1:
-            d.update({"zb": ref("ZB", z0, z0 + 32 + n), "zf": ref("ZB", z0 + 32, z0 + 32 + n), "zc": ref("ZB", z0, z0 + 24)})
+            d.update({"zb": ref("ZB", z0, z0 + 32 + n), "zf": ref("ZB", z0 + 32, z0 + 32 + n), "zc": ref("ZB", z0, z0 + 32)})
         else:
             d["zf"] = tl("ZL", h)
         return d
 
-    px, views = full("PX"), ref("VI", 0, 4096)
+    px, views = ref("PX", NOH, NOH + 4096), ref("VI", 0, 4096)
+    pxe = ref("PX", NOH - 4096, NOH + 4096)
     banks = {}
 
     def mark(name, h):
@@ -821,8 +967,10 @@ def build(T, topo, core, rank, CO=COSTS[0]):
         mark("hp", h)
         a, c = tl("HI1", h), tl("HI2", h)
         y = ref(bank(), 0, n)
-        pe(acc(y, (full("C1"), on), (full("WBn"), L["z"]), (full("CH"), on), (full("CHn"), on), (full("WB"), L["z"])))
-        flex("V", a, y, -(HC + 31.0 / 64), kcol)
+        mm = acc(y, (full("WBn"), L["z"]), (full("C1"), on), (full("CH"), on), (full("CHn"), on), (full("WB"), L["z"]))
+        pe(mm[:3])
+        pe(mm[3:])
+        flex("S", a, y, -(HC + 31.0 / 64), kcol)
         mark("ha", h)
         tt(c, ("ind", ref("W613", 8, 4104), vh), a, A.add)
         ts(L["hd"], c, 4095, A.bitwise_and)
@@ -830,7 +978,7 @@ def build(T, topo, core, rank, CO=COSTS[0]):
         flex("S", L["x"], ("ind", px, vh))
         bk = bank()
         dx, hz = ref(bk, 0, n), ref(bk, n, 2 * n)
-        pe(acc(dx, (full("Icn"), L["z"]), (full("Ic"), L["x"])))
+        idx = pe(acc(dx, (full("Icn"), L["z"]), (full("Ic"), L["x"])))
         ts(tl("IND", h), dx, MAGIC, A.add, MAGIC, A.is_equal)
         mark("hz", h)
         pe(acc(hz, (full("Ihz"), L["z"]), (full("Ihz"), L["x"])))
@@ -843,54 +991,55 @@ def build(T, topo, core, rank, CO=COSTS[0]):
         lk = sm("LK", h)
         if "c" in XT:
             b = bank()
-            mm = xts(b, tl("IND", h), [(L["st"](1), full("In")), (L["st"](2), full("I2"))])
-            pe(mm[:2])
-            pe(mm[2:])
-            ts(xl("XL", h), ref(b, 0, n, 1, 0, 8), 8.5, A.is_ge, 128.0, A.mult)
+            mm = xts(b, tl("IND", h), [(L["st"](1), full("In")), (L["st"](2), Ib)] if t else [])
+            if t:
+                pg["ops"][pe(mm[:2])]["ord"].add(idx)
+            pe(mm[-16:])
+            ts(xl("XL", h), ref(b, 0, n, 1, 0, 8), 264.5 if t else 8.5, A.is_ge, 128.0, A.mult)
             b = bank()
-            pe(acc(ref(b, 0, 8), (Ib, ref("CM", 0, 8)), (xl("XL", h), I8)) + acc(ref(b, 8, 16), (xl("XL", h), I8)))
-            flex("V", sm("LSL", h), ref(b, 0, 8))
-            flex("V", lk, ref(b, 8, 16))
+            pe(grp((ref(b, 0, 16), Ib, full("CM")), (ref(b, 0, 8), xl("XL", h), I8), (ref(b, 8, 16), xl("XL", h), ref("I2", 0, 8, 1, 0, 8)))
+               + [(ref(b, 16, 24), xl("XL", h), I8, True, True)])
+            tt(sm("LSF", h, 16, 0, 16), ref(b, 0, 16), L["st"](2, 2), A.min)
+            flex("V", lk, ref(b, 16, 24))
         else:
             ct = ref(bank(), 0, 8)
             pe(ots(ct, tl("IND", h), [(full("In"), L["st"](1)), (full("I2"), L["st"](2))]))
             ts(lk, ct, 8.5, A.is_ge, 128.0, A.mult)
             tt(sm("LSL", h), lk, ref("CM", 0, 8), A.add)
         mark("h", h)
-        flex("V", ref("HEL", 2 * h * n, 2 * h * n + n), ("ind", L["w2"], sm("LSL", h)))
+        flex("V", ref("HEL", 2 * h * n, 2 * h * n + n), ("ind", L["w2"], sm("LSF", h, 16, 8)))
         mark("hm", h)
-        flex("V", tl("H16", h), ref("HEL", 2 * h * n, 2 * h * n + n), -2048.0)
+        flex("S", tl("H16", h), ref("HEL", 2 * h * n, 2 * h * n + n), -2048.0)
         mark("qx", h)
         q0 = h * 16 * n
-        flex("V", ref("QS", 0, 16 * n, 16), ("ind", L["xz"], sm("LSL", h)))
+        flex("V", ref("QS", 0, 16 * n, 16), ("ind", L["xz"], sm("LSF", h, 16)))
         banks[h] = (bank(), bank(), bank())
         pe([(ref(banks[h][2], 0, n), Ib, ref("QS", 0, 16 * n, 16), True, True)])
         scan(ref("QX", q0, q0 + 16 * n), full("MK"), full("QS"), 0.0, A.min, A.add)
         mark("e", h)
-        flex("S", ref("HEL", (2 * h + 1) * n, (2 * h + 2) * n), ("ind", views, vh))
+        flex("S", ref("HEL", (2 * h + 1) * n, (2 * h + 2) * n), ("ind", views, vh), 4096.0 if t else 0.0)
 
     def dedupe(t):
         mark("dd", 0)
         vh = ref("VH", 16 * t, 16 * t + 16)
-        flex("V", full("VF"), vh, -2048.0)
+        flex("S", full("VF"), vh, -2048.0)
         b = bank()
         mm = []
         for j, (c, d) in enumerate(((0, 0), (0, 1), (1, 1))):
             mm += acc(ref(b, j, 24, 3), (Ib, ref("VF", c, 16, 2)), (full("I8k"), ref("LK", c, 16, 2)))
             mm += acc(ref(b, 24 + j, 48, 3), (Ib, ref("VF", d, 16, 2)), (Ib, ref("CK", 16, 24)))
-        pe(mm)
-        flex("V", full("WD"), ref(b, 0, 48), -8192.0)
+        pe(mm[:6])
+        pe(mm[6:])
+        flex("S", full("WD"), ref(b, 0, 48), -8192.0)
         b = bank()
-        for j0 in (0, 8):
-            mm = []
-            for j in range(j0, j0 + 8):
-                mm += acc(ref(b, j, 384, 16), (ref("SEL", 128 * j, 128 * j + 128), ref("WD", 0, 24)), (full("In"), ref("WD", 24, 48)))
-            pe(mm)
-        ts(full("EQ"), ref(b, 0, 384), 0.0, A.is_equal)
-        scan(full("DS"), full("D0"), full("EQ"), 0.0, A.mult, A.add)
+        for j0 in range(0, 16, SELP):
+            pe([(ref(b, 0, 384), Ib, full("TRI"), True, False)][j0:] + [(ref(b, j, 384, 16), l, r, False, j == 15 and r[1] == 24) for j in range(j0, j0 + SELP)
+                for l, r in ((ref("SEL", 128 * j, 128 * j + 128), ref("WD", 0, 24)), (full("In"), ref("WD", 24, 48)))])
+        flex("S", full("EQ"), ref(b, 0, 384), size=True)
+        scan(full("DS"), full("D0"), full("EQ"), 0.0, A.max, A.min)
         b = bank()
         pe(grp((ref(b, 0, 16), Ib, ref("CK", 0, 16)), (ref(b, 0, 16), Ib, full("VF")), (ref(b, 0, 16), full("I8kn"), full("LK")),
-               (ref(b, 0, 16, 2), full("DG"), ref("DS", 14, 384, 48)), (ref(b, 1, 16, 2), full("DG"), ref("DS", 46, 384, 48))))
+               (ref(b, 0, 16, 2), full("In8192"), ref("DS", 15, 384, 48)), (ref(b, 1, 16, 2), full("In8192"), ref("DS", 47, 384, 48))))
         tt(full("OFF"), ref(b, 0, 16), full("SPT"), A.min)
 
     def early(t, h):
@@ -902,8 +1051,9 @@ def build(T, topo, core, rank, CO=COSTS[0]):
         pe(acc(po, (Ib, L["st"](0)), (full("Sb100"), lk), (Im, lk)))
         ts(ov, po, 100.5, A.is_ge, 128.0, A.mult)
         b = bank()
-        pe(grp((ref(b, 0, 16), Ib, full("CM")), (ref(b, 0, 8), full("I2"), lk), (ref(b, 0, 8), full("G256"), ov), (ref(b, 8, 16), full("G0"), ov)))
-        flex("V", sm("TLL", h, 16, 0, 16), ref(b, 0, 16))
+        w = 8 if t < NT - 1 else 16
+        idx = pe(grp(*[(ref(b, 0, w), Ib, ref("CM", 0, w)), (ref(b, 0, 8), full("I2"), lk), (ref(b, 0, 8), full("G256"), ov), (ref(b, 8, 16), full("G0"), ov)][:3 + w // 16]))
+        flex("V", sm("TLL", h, 16, 0, w), ref(b, 0, w))
         flex("S", L["zf"], ("ind", L["xzh"], sm("TLL", h, 16)))
         mark("st", h)
         b = bank()
@@ -914,8 +1064,9 @@ def build(T, topo, core, rank, CO=COSTS[0]):
         flex("S", ra(0, 3), blk(0, 3), relu=True)
         b = bank()
         if t < NT - 1:
-            pe(grp((blk(0, 2), Ib, ra(0, 2)), (blk(1), Ib, ra(2))) + acc(blk(2), (full("Ifl"), ra(1)), (full("Ifl"), ra(2))))
-            ts(L["zc"], blk(0, 3), MAGIC, A.add, -MAGIC, A.add)
+            pe(grp((blk(0, 2), Ib, ra(0, 2)), (blk(1), Ib, ra(2)))
+               + grp((blk(2, 2), Ib, full("CMF")), (blk(2), full("Ifl"), ra(1)), (blk(2), full("Ifl"), ra(2)), (blk(3), full("G0"), ov)))
+            ts(L["zc"], blk(0, 4), MAGIC, A.add, -MAGIC, A.add)
             send("z", t + 1, h, tiles(t + 1, h)["land"], L["zb"])
         else:
             pe(acc(blk(0), (full("I16"), ra(1)), (full("I16"), ra(2)), (Ib, ra(0))))
@@ -937,8 +1088,8 @@ def build(T, topo, core, rank, CO=COSTS[0]):
             pe(acc(y, (full("I8k"), lk), (full("I8200"), ov), (xl("XK", h), I8)))
         else:
             pe(ots(y, L["zf"], [(full("I8k"), lk), (full("I8200"), ov)]))
-        flex("V", sm("KL", h), y, t + 16.0 - 8192.0 + (2048.0 if "k" in XT else 0.0))
-        flex("S", tl("OHL", h), ("ind", full("OHW"), sm("KL", h)))
+        flex("S", sm("KL", h), y, t + 16.0 - 8192.0 + (2048.0 if "k" in XT else 0.0))
+        flex("S", tl("OHL", h), ("ind", ref("PX", 0, NOH), sm("KL", h)))
 
     def bulk(t, h, w):
         mark("he"[w] + "b", h)
@@ -947,8 +1098,8 @@ def build(T, topo, core, rank, CO=COSTS[0]):
         b = banks[h][w]
         for a, e_, q in PARTS[h][w]:
             g_, off = ref(G, q0 + 16 * a, q0 + 16 * e_), ref("HEL", l0 + a, l0 + e_)
-            flex(q, g_, ("ind", px, off))
-        for a, e_ in CHUNKS[w]:
+            flex(q, g_, ("ind", pxe if w and t else px, off))
+        for a, e_ in CHUNKS[h][w]:
             lo, hi = q0 + 16 * a, q0 + 16 * e_
             g0 = ref(G, lo, hi, 16)
             first = [(ref(b, 0, n), Ib, full("KC"), True, False) if w == 0 else (ref(b, 0, n), on, full("CP"), True, False)] if a == 0 else []
@@ -958,9 +1109,12 @@ def build(T, topo, core, rank, CO=COSTS[0]):
                     pe([(ref(b, k, n, 16), ref(G, q0 + k, q0 + 16 * n, 16), full("Bm16"), False, False) for k in range(max(1, k0), k0 + SPLIT)], sub=True)
             tt(g0, g0, ref(banks[h][2], a, e_), A.max)
             scan(ref(M, lo, hi), ref("QX", lo, hi), ref(G, lo, hi), 0.0, A.min, A.max)
-        pe([(ref(b, 0, n), tl("OHL", h), full("Ibig" if w == 0 else "MP"), False, False)])
+        oh = [(ref(b, 0, n), tl("OHL", h), full("Ibig" if w == 0 else "MP"), False, False)]
+        if not JOIN:
+            pe(oh)
         for k0 in range(0, 16, SPLIT):
-            pe([(ref(b, k, n, 16), ref(M, q0 + k, q0 + 16 * n, 16), full("B32"), False, k == 15) for k in range(k0, k0 + SPLIT)])
+            i = pe(oh[k0:JOIN] + [(ref(b, k, n, 16), ref(M, q0 + k, q0 + 16 * n, 16), full("B32"), False, k == 15) for k in range(k0, k0 + SPLIT)])
+        return i
 
     def tail(t, h):
         L = tiles(t, h)
@@ -973,12 +1127,13 @@ def build(T, topo, core, rank, CO=COSTS[0]):
         tt(tl("OHT", h), ("ind", tl("PM", h), ref("CL", 0, 8)), key, A.is_equal)
         oc = ref(bank(), 0, n)
         pe([(oc, tl("OHT", h), Ib, True, True)])
-        bulk(t, h, 1)
+        last = bulk(t, h, 1)
         mark("cc", h)
         tt(tl("MT", h), key, pd, A.is_lt)
         mk = ref(bank(), 0, n)
-        pe([(mk, full("CN"), on, True, False), (mk, Ib, tl("H16", h), False, False)])
-        pe([(mk, tl("MT", h), full("I8192"), False, True)])
+        i = pe([(mk, Ib, tl("H16", h), True, False)] + [(mk, full("CN"), on, False, False)][t:])
+        pg["ops"][i]["ord"].add(last)
+        pe([(mk, tl("MT", h), full("I10240"), False, True)])
         tt(tl("MM", h), ref("HEL", (2 * h + 1) * n, (2 * h + 2) * n), mk, A.max)
         ts(L["c"], tl("MM", h), 4095, A.bitwise_and)
         flex("V", tl("CF", h), ("ind", L["w3"], sm("TLL", h, 16)), -2048.0)
@@ -1001,8 +1156,7 @@ def build(T, topo, core, rank, CO=COSTS[0]):
             store(T.yv[:, h * n:h * n + n], ref("YU", 512 + h * n, 512 + h * n + n, 1, 0, 128, 16))
         mark("ff", h)
         if t < NT - 1:
-            flex("S", L["fb"], ("ind", L["c"], sm("TLL", h, 16, 8)))
-            send("f", t + 1, h, tiles(t + 1, h)["f"], L["fb"])
+            send("f", t + 1, h, tiles(t + 1, h)["f"], L["c"])
         else:
             flex("S", ref("YU", 1536 + h * n, 1536 + h * n + n), ("ind", L["c"], sm("TLL", h, 16, 8)))
             store(T.yf[:, h * n:h * n + n], ref("YU", 1536 + h * n, 1536 + h * n + n))
@@ -1012,7 +1166,12 @@ def build(T, topo, core, rank, CO=COSTS[0]):
         c0 = tiles(t, h)["c"][1]
         for c in range(3, -1, -1):
             off, src = ref("OFF", h * 8 + 2 * c, h * 8 + 2 * c + 2), ref("W", c0 + 32 * c, c0 + 32 * c + 32)
-            add(pg, "V", CO["scat"], lambda e, off=off, src=src: e.tensor_copy(ap(full("VI")).indirect(ap(off)), ap(src)), [off, src], [full("VI")], tag="scatter")
+            i = add(pg, "V", CO["scat"], lambda e, off=off, src=src: e.tensor_copy(ap(full("VI")).indirect(ap(off)), ap(src)), [off, src], [full("VI")], tag="scatter")
+            o = pg["ops"][i]
+            for d in [d for d in o["dep"] if WAW and pg["ops"][d]["tag"] == "scatter" and pg["ops"][d]["hop"] == t]:
+                o["dep"].discard(d)
+                o["dep"] |= pg["ops"][d]["dep"]
+                o["ord"].add(d)
 
     for t in range(NT):
         pg["hop"] = t
@@ -1026,9 +1185,8 @@ def build(T, topo, core, rank, CO=COSTS[0]):
         scatter(t, 1)
         scatter(t, 0)
     pg["st"] = ""
-    for c in range(4):
-        a, b = 512 * c, 512 * c + 512
-        y = ref(bank(), 0, 512)
+    for a, b in zip(PACK, PACK[1:]):
+        y = ref(bank(), 0, b - a)
         flex("S", y, ref("VI", 2048 + a, 2048 + b), 0.0, 4096.0)
         tt(ref("YT", a, b), ref("VI", a, b), y, A.add)
         store(T.yw[:, a:b], ref("YT", a, b))

@@ -7,15 +7,20 @@ F = ActivationFunctionType
 n = 128
 NT = 5
 XW = 32 + 3 * n
-WW = 3 * n
+WW = 4 * n
+WIDE = False
+BIG = ()
+LATE = (0,)
 MAGIC = 12582912.0
 NB = 8
 M35 = 1.5 * 2.0 ** 35
 HC = 262000
 NOH = 4112
 OH0 = 1024
-PARTS = ((((0, 64, "S"), (64, 128, "S")), ((0, 64, "S"), (64, 128, "S"))),) * 2
-CHUNKS = ((((0, 64), (64, 128)), ((0, 128),)), (((0, 128),), ((0, 64), (64, 128))))
+PARTS = ((((0, 48, "S"), (48, 96, "S"), (96, 128, "V")), ((0, 48, "S"), (48, 96, "S"), (96, 128, "S"))),
+         (((0, 48, "S"), (48, 96, "S"), (96, 128, "S")), ((0, 48, "S"), (48, 96, "S"), (96, 128, "V"))))
+CHUNKS = ((((0, 48), (48, 96), (96, 128)),) * 2,) * 2
+SUMS = ((((0, 128),), ((0, 128),)),) * 2
 ONV = ("hz0", "hz1")
 LINES = [tuple("%sb%s  G%s %d" % (x[0], x[1], x[0].upper(), k) for x in ("h1 e1 e0 h0" if t else "h1 e1 h0 e0").split() for k in ()) for t in range(NT)]
 WAW = False
@@ -24,55 +29,65 @@ PACK = (0, 192, 576, 1088, 1600, 2048)
 JOIN = 0
 SELP = 4
 SPLIT = 8
+LOWP = 1024
+QST = 2
+QSCAN = ((0, 48), (48, 128))
+QG = ((2, ((0, 48), (48, 96), (96, 128))),) * 2
+QV = (0, 0)
 f4, b2, h2, i4, u2 = "float32", "bfloat16", "float16", "int32", "uint16"
 
 SCRATCH = {
-    "PX": ("sbuf", [128, NOH + 4096], b2), "VI": ("sbuf", [128, 4096 + 32], i4), "VW": ("sbuf", [128, 2048], i4),
+    "PX": ("sbuf", [128, NOH + 8192], b2), "ML": ("sbuf", [128, 4 * n], b2), "Cm2": ("sbuf", [128, 128], b2), "VI": ("sbuf", [128, 4096 + 64], i4), "SPU": ("sbuf", [128, 16], f4), "VW": ("sbuf", [128, 2048], i4),
     "YT": ("sbuf", [128, 2048], f4), "YU": ("sbuf", [128, 2048], f4),
-    "W613": ("sbuf", [128, 4096 + 8], f4), "TRI": ("sbuf", [128, 384], b2),
+    "W613": ("sbuf", [128, 4096 + 8], f4), "TRI": ("sbuf", [128, 512], b2),
     "XZ": ("sbuf", [128, 10 * XW], b2), "W": ("sbuf", [128, 10 * WW], i4), "VH": ("sbuf", [128, 10 * 8], u2),
     "ZB": ("sbuf", [128, 8 * (32 + n)], b2), "FB": ("sbuf", [128, 10 * n], i4), "SPT": ("sbuf", [128, 16], f4), "CK": ("sbuf", [128, 24], b2), "VB": ("sbuf", [128, 10 * 8], u2), "ZL": ("sbuf", [128, 2 * n], b2),
-    "HEL": ("sbuf", [128, 4 * n], u2), "QS": ("sbuf", [128, 16 * n], b2), "QX": ("sbuf", [128, 32 * n], b2), "MK": ("sbuf", [128, 16 * n], b2), "H16": ("sbuf", [128, 2 * n], h2),
+    "HEL": ("sbuf", [128, 4 * n], u2), "QS": ("sbuf", [128, 16 // QST * n], b2), "QX": ("sbuf", [128, 32 * n], b2), "MK": ("sbuf", [128, 16 // QST * n], b2), "H16": ("sbuf", [128, 2 * n], h2),
     "GH": ("sbuf", [128, 32 * n], b2), "GE": ("sbuf", [128, 32 * n], b2), "MH": ("sbuf", [128, 32 * n], b2), "ME": ("sbuf", [128, 32 * n], b2),
     "IND": ("sbuf", [128, 2 * n], b2), "LK": ("sbuf", [128, 16], b2), "LSL": ("sbuf", [128, 16], u2), "LSF": ("sbuf", [128, 32], u2), "CMF": ("sbuf", [128, 16], b2),
     "HI1": ("sbuf", [128, 2 * n], i4), "HI2": ("sbuf", [128, 2 * n], i4),
     "T2": ("sbuf", [128, 2 * n], f4),
     "OV": ("sbuf", [128, 16], b2), "TLL": ("sbuf", [128, 32], u2), "RA": ("sbuf", [128, 48], b2), "KL": ("sbuf", [128, 16], u2), "OHL": ("sbuf", [128, 2 * n], b2),
-    "VF": ("sbuf", [128, 16], h2), "WD": ("sbuf", [128, 48], h2), "SEL": ("sbuf", [128, 16 * 128], b2), "EQ": ("sbuf", [128, 384], b2),
-    "DS": ("sbuf", [128, 384], b2), "OFF": ("sbuf", [128, 16], u2),
-    "KEY": ("sbuf", [128, 2 * n], f4), "MT": ("sbuf", [128, 2 * n], b2), "MM": ("sbuf", [128, 2 * n], i4),
+    "VF": ("sbuf", [128, 16], h2), "WD": ("sbuf", [128, 64], h2), "SEL": ("sbuf", [128, 16 * 128], b2), "EQ": ("sbuf", [128, 512], b2),
+    "DS": ("sbuf", [128, 512], b2), "OFF": ("sbuf", [128, 16], u2),
+    "KEY": ("sbuf", [128, 2 * n], f4), "MT": ("sbuf", [128, 2 * n], b2), "CI": ("sbuf", [128, 2 * n], i4),
+    "PF": ("sbuf", [128, 2 * n], f4), "RB": ("sbuf", [128, 2 * n], f4), "Bf": ("sbuf", [128, 8], f4),
     "PM": ("sbuf", [128, 2 * n], f4), "OHT": ("sbuf", [128, 2 * n], b2), "CF": ("sbuf", [128, 2 * n], h2), "PP": ("sbuf", [128, 2 * n], h2),
     "YC": ("sbuf", [128, 16], b2), "VZ": ("sbuf", [128, 512], i4), "VZh": ("sbuf", [128, 512], h2),
     "WBn": ("sbuf", [128, 128], b2), "C1": ("sbuf", [128, 128], b2), "CHn": ("sbuf", [128, 128], b2), "CN": ("sbuf", [128, 128], b2),
+    "CQ": ("sbuf", [128, 128], b2), "CQn": ("sbuf", [128, 128], b2),
     "XL": ("sbuf", [128, 2 * n], b2), "XK": ("sbuf", [128, 2 * n], h2), "XV": ("sbuf", [128, 2 * n], h2),
     "ON": ("sbuf", [128, 144], b2), "BO": ("sbuf", [128, 128], b2), "B8": ("sbuf", [128, 144], b2), "Bh": ("sbuf", [128, 144], b2),
-    "B32": ("sbuf", [128, 8], b2), "Bm16": ("sbuf", [128, 8], b2), "WB": ("sbuf", [128, 128], b2), "CH": ("sbuf", [128, 128], b2), "CP": ("sbuf", [128, 128], b2),
+    "Bm32": ("sbuf", [128, 8], b2), "B16": ("sbuf", [128, 8], b2), "WB": ("sbuf", [128, 128], b2), "CH": ("sbuf", [128, 128], b2), "CP": ("sbuf", [128, 128], b2),
     "Sb": ("sbuf", [128, 128], b2), "Sb100": ("sbuf", [128, 128], b2), "MP": ("sbuf", [128, 128], b2), "DG": ("sbuf", [128, 128], b2), "G0": ("sbuf", [128, 128], b2),
     "G256": ("sbuf", [128, 128], h2), "ZE": ("sbuf", [128, 128], b2),
-    "KC": ("sbuf", [128, 128], b2), "RST": ("sbuf", [128, 128], f4), "D0": ("sbuf", [128, 384], b2),
+    "KC": ("sbuf", [128, 128], b2), "RST": ("sbuf", [128, 128], f4), "D0": ("sbuf", [128, 512], b2),
     "PI": ("sbuf", [128, 32], i4), "PC": ("sbuf", [128, 32], f4), "IJ": ("sbuf", [128, 16], f4), "CMI": ("sbuf", [128, 32], f4), "CM": ("sbuf", [128, 16], b2),
     "CS": ("sbuf", [128, 24], b2), "CL": ("sbuf", [128, 32], u2), "WT": ("sbuf", [128, 2], i4), "WTf": ("sbuf", [128, 8], f4),
 }
 DIAG = {"Ib": (1.0, b2), "In": (-1.0, b2), "I2": (2.0, b2), "Ic": (0.00689697265625, b2), "Icn": (-0.00689697265625, b2), "Ihz": (0.5 - 2.0 ** -11, h2),
         "I1": (1.0 / 128, b2), "Ip100": (100.0 / 128, b2), "Im100": (-100.0 / 128, b2), "I8k": (8192.0 / 128, b2), "I8kn": (-8192.0 / 128, b2), "I8200": (8200.0 / 128, h2),
-        "I10240": (10240.0, b2), "In8192": (-8192.0, b2), "Ibig": (-262144.0, b2), "Ifl": (0.8125, b2), "I16": (16.0, b2)}
+        "Iwin": (14336.0, b2), "In8192": (-8192.0, b2), "Ibig": (-262144.0, b2), "Ifl": (0.8125, b2), "I16": (16.0, b2)}
 for _k in DIAG:
     SCRATCH[_k] = ("sbuf", [128, 128], DIAG[_k][1])
 for _b in range(8):
     SCRATCH["bank%d" % _b] = ("psum", [128, 512], f4) if _b < NB else ("psum", [128, 1024], b2)
-LOADS = ["v0", "d0", "wt", "kap", "z1", "px0", "px1", "z0", "f1", "f0", "vw0", "vw1"]
-SEMAPHORES = ["V", "S", "P", "G", "out", "ls", "oh", "sl"] + ["ld_" + x for x in LOADS] + ["r%s_%d_%d" % (k, t, h) for k in "zfv" for t in range(1, NT) for h in range(2)]
+SMALL = []
+LOADS = SMALL + ["v0", "d0", "wt", "kap", "z1", "px0", "px1", "z0", "vw0", "f1", "vw1", "f0"]
+SEMAPHORES = ["V", "S", "P", "G", "out", "ls", "oh"] + ["ld_" + x for x in LOADS] + ["r%s_%d_%d" % (k, t, h) for k in "zfv" for t in range(1, NT) for h in range(2)]
 
 COSTS = tuple(dict(zip(("cy", "gather", "wake", "pe", "link", "scat", "V", "S", "P", "row", "issue", "load"), c)) for c in (
-    (0.00083, 1.56, 0.10, 0.00046, 1.4, 0.18, 0.03, 0.04, 0.03, 1.0, 0.4, 1.0),
-    (0.00083, 1.10, 0.07, 0.00042, 1.0, 0.12, 0.03, 0.04, 0.03, 0.7, 0.3, 0.9),
-    (0.00112, 1.95, 0.15, 0.00056, 2.0, 0.25, 0.04, 0.05, 0.04, 1.5, 0.8, 1.3),
-    (0.00102, 1.70, 0.12, 0.00050, 1.8, 0.14, 0.06, 0.07, 0.02, 1.2, 0.6, 1.2),
-    (0.00090, 1.40, 0.08, 0.00052, 1.1, 0.22, 0.03, 0.04, 0.05, 0.8, 0.4, 1.0)))
+    (0.00083, 1.56, 0.10, 0.00042, 1.2, 0.15, 0.005, 0.02, 0.01, 0.8, 0.5, 0.9),
+    (0.00087, 1.15, 0.09, 0.00044, 1.0, 0.12, 0.005, 0.02, 0.01, 0.7, 0.4, 0.9),
+    (0.00118, 1.95, 0.12, 0.00059, 1.8, 0.25, 0.01, 0.03, 0.02, 1.3, 0.8, 1.2),
+    (0.00104, 1.65, 0.13, 0.00052, 1.6, 0.16, 0.01, 0.04, 0.01, 1.1, 0.7, 1.1),
+    (0.00100, 1.30, 0.08, 0.00050, 1.1, 0.24, 0.005, 0.02, 0.02, 0.8, 0.5, 1.0),
+    (0.00085, 1.08, 0.045, 0.00042, 0.9, 0.15, 0.015, 0.02, 0.01, 0.6, 0.3, 0.8)))
+WEIGHT = (1.2, 1.1, 1.0, 1.0, 1.1, 0.6)
 ROUGH = 0.0
 SEEDS = (1, 2, 3)
-ROUNDS = 600
-MOVES = (8000, 55000)
+ROUNDS = 100
+MOVES = (15000, 160000)
 LOADW = 0.0
 FIRST = {}
 ALIKE = 0.0
@@ -100,7 +115,8 @@ def touch(pg, o, r, wr):
         if p != o["i"]:
             if psum:
                 if ops[p]["q"] == o["q"] == "P":
-                    o["ord"].add(p)
+                    if not (o["free"] and ops[p]["free"]):
+                        o["ord"].add(p)
                 elif ops[p]["q"] != o["q"] or ops[p]["alt"] or o["alt"]:
                     o["dep"].add(p)
             elif over and (wr or aw):
@@ -112,8 +128,8 @@ def touch(pg, o, r, wr):
     pg["acc"][name] = keep
 
 
-def add(pg, q, cost, fn, rd, wr, sem=None, val=1, lat=0.0, tag="", alt=None):
-    o = {"i": len(pg["ops"]), "q": q, "alt": alt, "cost": cost, "fn": fn, "dep": set(), "ord": set(), "sem": sem, "val": val, "lat": lat, "send": None, "tag": tag, "st": pg["st"], "hop": pg["hop"]}
+def add(pg, q, cost, fn, rd, wr, sem=None, val=1, lat=0.0, tag="", alt=None, free=False):
+    o = {"free": free, "i": len(pg["ops"]), "q": q, "alt": alt, "cost": cost, "fn": fn, "dep": set(), "ord": set(), "sem": sem, "val": val, "lat": lat, "send": None, "tag": tag, "st": pg["st"], "hop": pg["hop"]}
     pg["ops"].append(o)
     for r in rd:
         touch(pg, o, r, False)
@@ -365,6 +381,56 @@ def polish(pgs, wakes, keep, moves, seed, temp=0.0004):
             last[q[i]] = i
         return prev
 
+    def relink(p0, p1):
+        pv, last = list(prev), {}
+        for i in seq[p0:p1]:
+            d = prev[i]
+            if d == Z:
+                last[was.get(i, q[i])] = Z
+            elif pos[d] < p0:
+                last[q[d]] = d
+        for i in seq[p0:p1]:
+            x = q[i]
+            if x not in last:
+                k = p0 - 1
+                while k >= 0 and q[seq[k]] != x:
+                    k -= 1
+                last[x] = seq[k] if k >= 0 else Z
+            pv[i] = last[x]
+            last[x] = i
+        k = p1
+        while last and k < N_:
+            i = seq[k]
+            if q[i] in last:
+                pv[i] = last.pop(q[i])
+            k += 1
+        return pv, k
+
+    def rerun(m, p0, p1, prev, end, fin):
+        c, l, w = cost[m], lat[m], wakes[m]
+        k = p0
+        while k < p1:
+            for i in seq[k:p1]:
+                t = -w
+                for d in dep[i]:
+                    if fin[d] > t:
+                        t = fin[d]
+                t += w
+                d = snd[i]
+                if d is not None and fin[d] > t:
+                    t = fin[d]
+                d = end[prev[i]]
+                if d > t:
+                    t = d
+                t += c[i]
+                if t != end[i]:
+                    end[i] = t
+                    fin[i] = t + l[i]
+                    if far[i] > k:
+                        k = far[i]
+            k, p1 = p1, (k + 1 if k >= p1 else p1)
+        return max(fin[i] for i in ends)
+
     def run(m, p0, prev, end, fin):
         c, l, w = cost[m], lat[m], wakes[m]
         for i in seq[p0:]:
@@ -463,28 +529,50 @@ def polish(pgs, wakes, keep, moves, seed, temp=0.0004):
     for i in range(N_):
         for d in dep[i]:
             waits[d].append(i)
+    ahead = [dep[i] + ([snd[i]] if snd[i] is not None else []) for i in range(N_)]
+    waited = set(d for a in ahead for d in a)
+    ends = [i for i in range(N_) if i not in waited]
+    far, was = None, {}
     prev = links(seq)
     E, Fi = [[0.0] * (N_ + 1) for _ in pgs], [[0.0] * (N_ + 1) for _ in pgs]
     r = [run(m, 0, prev, E[m], Fi[m]) for m in range(M)]
-    first = list(r)
+    first = [x / w for x, w in zip(r, WEIGHT)]
     now = best = 1.0
     kept = (list(seq), list(q), list(r))
     rng = np.random.default_rng(seed)
     pos = [0] * (N_ + 1)
-    fresh, paths, rest = True, None, None
+    fresh, taken, paths, rest, m0 = 8, 0, None, None, 0
     for it in range(moves):
-        if fresh:
-            st = [E[0][i] - cost[0][i] for i in range(N_)]
+        if fresh and fresh % 8:
+            for k in range(p0, p1):
+                i = seq[k]
+                pos[i] = k
+                for d in ahead[i]:
+                    if far[d] < k:
+                        far[d] = k
+                if far[prev[i]] < k:
+                    far[prev[i]] = k
+            paths = {}
+            taken, fresh = fresh, 0
+        elif fresh:
+            st = [a - b for a, b in zip(E[0], cost[0])]
             seq.sort(key=lambda i: st[i])
             for k, i in enumerate(seq):
                 pos[i] = k
+            far = [0] * (N_ + 1)
+            for k, i in enumerate(seq):
+                far[prev[i]] = k
+                for d in ahead[i]:
+                    far[d] = k
             paths, rest = {}, {}
-            fresh = False
+            taken, fresh = fresh, 0
         u = rng.random(5)
-        if not paths or u[0] < 0.05:
+        if (not paths and taken % 8 == 0) or u[0] < 0.05:
             m0 = int(rng.integers(M))
         if m0 not in paths:
-            paths[m0], rest[m0] = path(m0), tails(m0)
+            paths[m0] = path(m0)
+        if m0 not in rest:
+            rest[m0] = tails(m0)
         pt = paths[m0]
         if not pt:
             continue
@@ -569,10 +657,12 @@ def polish(pgs, wakes, keep, moves, seed, temp=0.0004):
         E2, F2, r2, f = [], [], [], 0.0
         if quick and least(m0, p0, p0 + len(old)) > r[m0] + (lim - now) * first[m0] * 2 + 0.05:
             f = 1.0
-        pv = links(seq) if f == 0.0 else None
+        if f == 0.0:
+            was = {x[0]: x[1] for x in undo or ()}
+            pv, p1 = relink(p0, p0 + len(old)) if quick else (links(seq), N_)
         for m in range(M if f == 0.0 else 0):
             e, fi = list(E[m]), list(Fi[m])
-            x = run(m, p0, pv, e, fi)
+            x = rerun(m, p0, p1, pv, e, fi)
             E2.append(e)
             F2.append(fi)
             r2.append(x)
@@ -581,7 +671,7 @@ def polish(pgs, wakes, keep, moves, seed, temp=0.0004):
                 f = 1.0
                 break
         if now + f <= lim:
-            now, E, Fi, r, prev, fresh = now + f, E2, F2, r2, pv, True
+            now, E, Fi, r, prev, fresh = now + f, E2, F2, r2, pv, taken + 1
             if now < best - 1e-9:
                 best, kept = now, (list(seq), list(q), list(r))
         else:
@@ -594,7 +684,7 @@ def polish(pgs, wakes, keep, moves, seed, temp=0.0004):
 
 
 def plan(T, topo, core, rank):
-    pgs, wakes = [build(T, topo, core, rank, c) for c in COSTS], [c["wake"] * 2.6 for c in COSTS]
+    pgs, wakes = [build(T, topo, core, rank, c) for c in COSTS], [c["wake"] * 3.0 for c in COSTS]
     rng = np.random.default_rng(5)
     for p in pgs:
         by = {}
@@ -605,14 +695,15 @@ def plan(T, topo, core, rank):
                     o["alt"][x] = (o["alt"][x][0] * f, o["alt"][x][1])
                 if x == o["q"]:
                     o["cost"] *= f
-    starts = [polish(pgs, wakes, schedule(pgs, wakes, ROUNDS, s), MOVES[0], s) for s in SEEDS]
-    return polish(pgs, wakes, min(starts, key=lambda k: sum(x / y for x, y in zip(k[3], starts[0][3]))), MOVES[1], 1, 0.0003)
+    starts = [polish(pgs, wakes, schedule(pgs, wakes, ROUNDS, s), MOVES[0], s, 0.001) for s in SEEDS]
+    return polish(pgs, wakes, min(starts, key=lambda k: sum(x / y for x, y in zip(k[3], starts[0][3]))), MOVES[1], 1, 0.0008)
 
 
 def emit(pg, keep, g, T):
     ops = pg["ops"]
     seq, dyn, bmap = keep[:3]
     pg["bmap"].update(bmap)
+    pg["last"].update({ops[i]["tiles"][0]: i for i in seq if ops[i]["free"]}.values())
     eng = {"V": g.vector, "S": g.scalar, "P": g.tensor, "G": g, "Y": g.sync}
     pos, key, know, count, qk = {}, {}, {}, {}, {}
     for i in seq:
@@ -652,18 +743,18 @@ def emit(pg, keep, g, T):
 
 
 def build(T, topo, core, rank, CO=COSTS[0]):
-    pg = {"ops": [], "acc": {}, "rr": [0], "st": "", "hop": 0, "bmap": {"c0": NB, "c1": NB + 1}}
+    pg = {"ops": [], "acc": {}, "rr": [0], "st": "", "hop": 0, "last": set(), "bmap": {"c0": NB, "c1": NB + 1}}
     CY, GC, PEC, FIX = CO["cy"], CO["gather"], CO["pe"], CO
 
     def ap(r):
         name, c0, c1, step, p0, p1, ps = r
         t = T["bank%d" % pg["bmap"][name]] if name in pg["bmap"] else T[name]
         rows = slice(p0, p1) if ps == 1 else slice(p0, p1, ps)
-        cols = slice(c0, c1) if step == 1 else slice(c0, c1, step)
+        cols = slice(c0, c1) if step == 1 else slice(c0, c1, step) if step > 0 else slice(c1 - 1, c0 - 1 if c0 else None, step)
         return t[rows, cols]
 
     def cnt(r):
-        return (r[2] - r[1] + r[3] - 1) // r[3]
+        return (r[2] - r[1] + abs(r[3]) - 1) // abs(r[3])
 
     def two(*rs):
         return all(r[0][0] == "c" if is_psum(r[0]) else SCRATCH[r[0]][2] in (b2, h2, u2) for r in rs)
@@ -680,7 +771,7 @@ def build(T, topo, core, rank, CO=COSTS[0]):
         return ap(s) if isinstance(s, tuple) else s
 
     def vcost(e, c, ind):
-        return FIX["V"] + CY * max(64, e * (GC if ind else c)) + (0.03 if ind else 0)
+        return FIX["V"] + CY * max(64, e * (GC if ind else c)) + (0.04 if ind else 0)
 
     def ts(out, in0, s1, op0, s2=None, op1=None):
         ind = in0[0] == "ind"
@@ -715,12 +806,12 @@ def build(T, topo, core, rank, CO=COSTS[0]):
 
     def flex(q, out, in_, bias=0.0, scale=1.0, relu=False, size=False):
         ind = in_[0] == "ind"
-        sc = [scale] if isinstance(scale, tuple) else []
+        sc = [s for s in (bias, scale) if isinstance(s, tuple)]
         if scale == 1.0:
-            fv = (lambda e: e.tensor_scalar(ap(out), inap(in_), bias, None, A.add)) if bias else (lambda e: e.tensor_copy(ap(out), inap(in_)))
+            fv = (lambda e: e.tensor_scalar(ap(out), inap(in_), dcol(bias), None, A.add)) if bias else (lambda e: e.tensor_copy(ap(out), inap(in_)))
         else:
-            fv = lambda e: e.tensor_scalar(ap(out), inap(in_), dcol(scale), bias, A.mult, A.add)
-        fs = lambda e: e.activation(ap(out), inap(in_), F.Relu if relu else F.Identity if bias else F.Copy, bias=bias, scale=dcol(scale))
+            fv = lambda e: e.tensor_scalar(ap(out), inap(in_), dcol(scale), dcol(bias), A.mult, A.add)
+        fs = lambda e: e.activation(ap(out), inap(in_), F.Relu if relu else F.Identity if bias else F.Copy, bias=dcol(bias), scale=dcol(scale))
         if relu:
             fv = lambda e: e.tensor_scalar(ap(out), inap(in_), 0.0, None, A.max)
         if size:
@@ -728,10 +819,11 @@ def build(T, topo, core, rank, CO=COSTS[0]):
             fs = lambda e: e.activation(ap(out), inap(in_), F.Abs)
         alt = {"V": (vcost(cnt(out), 0.5 if (not ind and two(out, in_)) else 1, ind), fv),
                "S": (FIX["S"] + CY * max(64, cnt(out) * (GC if ind else 1)) + (0.04 if ind else 0), fs)}
-        q = FIRST.get(pg["st"], q)
+        if pg["st"] and cnt(out) <= 384:
+            q = "V" if ind else "S"
         return add(pg, q, alt[q][0], None, regs(in_) + sc, [out], tag="flex " + out[0], alt=alt)
 
-    def pe(mms, sub=False):
+    def pe(mms, sub=False, free=False):
         cost = 0.0
         rd, wr = {}, {}
         for out, l, r, s, e_ in mms:
@@ -746,12 +838,14 @@ def build(T, topo, core, rank, CO=COSTS[0]):
             y = wr.get(out[0])
             wr[out[0]] = (out[0], min(out[1], y[1]) if y else out[1], max(out[2], y[2]) if y else out[2], 1, 0, 128, 1)
 
+        me = len(pg["ops"])
+
         def fn(e):
             ins = None
-            for out, l, r, s, e_ in mms:
-                ins = e.transpose(ap(out), ap(l), ap(r)) if out[0][0] == "c" else e.matmul(ap(out), ap(l), ap(r), s, e_)
+            for j, (out, l, r, s, e_) in enumerate(mms):
+                ins = e.matmul(ap(out), ap(l), ap(r), s, e_ or (j == len(mms) - 1 and me in pg["last"]))
             return ins
-        return add(pg, "P", cost + FIX["P"] / 2, fn, list(rd.values()), list(wr.values()), tag="pe " + mms[0][1][0] + " " + mms[0][2][0])
+        return add(pg, "P", cost + FIX["P"] / 2, fn, list(rd.values()), list(wr.values()), tag="pe " + mms[0][1][0] + " " + mms[0][2][0], free=free)
 
     def acc(out, *pairs):
         return [(out, l, r, i == 0, i == len(pairs) - 1) for i, (l, r) in enumerate(pairs)]
@@ -801,12 +895,15 @@ def build(T, topo, core, rank, CO=COSTS[0]):
         what["vw%d" % h] = (ref("VW", 1024 * h, 1024 * h + 1024), T.vw[:, 1024 * h:1024 * h + 1024], 1.5)
         what["z%d" % h] = (ref("XZ", h * XW + 32, h * XW + 32 + n), T.z0[:, h * n:h * n + n], 0.2)
         what["f%d" % h] = (ref("W", h * WW + n, h * WW + 2 * n), T.f0[:, h * n:h * n + n], 0.25)
-    loads, at = [], 2.0
-    for k, nm in enumerate(LOADS):
-        at = max(at, 2.0 + 0.1 * k) + what[nm][2]
+    loads, small, at = [], [], 2.0
+    for k, nm in enumerate(SMALL):
+        small.append(load(nm, what[nm][0], what[nm][1], 2.2 + 0.1 * k, "S"))
+    for k, nm in enumerate(LOADS[len(SMALL):]):
+        at = max(at, 2.0 + 0.1 * k) + what[nm][2] + (0.1 * len(SMALL) if k == 0 else 0.0)
         loads.append(load(nm, what[nm][0], what[nm][1], at - 0.1 * k))
-    for a, b in zip(loads, loads[1:]):
-        pg["ops"][b]["ord"].add(a)
+    for x in (loads, small):
+        for a, b in zip(x, x[1:]):
+            pg["ops"][b]["ord"].add(a)
 
     def sel(out, in_, pat, cmp, fillv, base, cm):
         return add(pg, "G", 0.2 + 2 * CY * cnt(out), lambda e: e.affine_select(ap(out), ap(in_), pat, cmp, fillv, base, cm), [in_], [out], tag="sel " + out[0])
@@ -819,6 +916,7 @@ def build(T, topo, core, rank, CO=COSTS[0]):
         return add(pg, "G", 0.15 + 2 * CY * cnt(out), fn, [], [out], tag="iota " + out[0])
 
     Ib, on = full("Ib"), ref("ON", 0, 128)
+    const = lambda out, c: flex("S", out, ref("ON", 0, cnt(out)), 0.0, float(c))
     fill(full("ON"), 1.0)
     sel(Ib, on, [[-1, 128]], A.is_equal, 0.0, 0, 1)
     sel(ref("B8", 0, 144, 1, 0, 8), ref("ON", 0, 144, 1, 0, 8), [[1, 144]], A.is_equal, 0.0, -15, -16)
@@ -831,33 +929,38 @@ def build(T, topo, core, rank, CO=COSTS[0]):
     iota(ref("W613", 8, 1032), [[613, 1024]], HC - 2 ** 23, 0)
     act(ref("W613", 1032, 2056), ref("W613", 8, 1032), F.Identity, 613.0 * 1024)
     act(ref("W613", 2056, 4104), ref("W613", 8, 2056), F.Identity, 613.0 * 2048)
-    iota(full("MK"), [[0, n], [256, 16]], 0, 0)
+    iota(full("MK"), [[0, n], [256, 16 // QST]], 0, 0)
     fill(full("QS"), 0.0)
-    iota(full("KC"), [[0, 8], [1, 16]], 0, 0)
-    sel(ref("SEL", 0, 128), on, [[-16, 8], [0, 16]], A.is_equal, 0.0, 0, 1)
+    fill(full("KC"), 0.0)
+    iota(ref("KC", 0, 128, 1, 0, 1), [[0, 8], [1, 16]], 0, 0)
+    fill(ref("KC", 15, 128, 16, 32, 33), -65536.0)
+    fill(full("SEL"), 0.0)
+    for a in range(0, 16, 4):
+        x = ref("SEL", 128 * a, 128 * a + 512)
+        sel(x, x, [[-1, 4], [-16, 8], [0, 16]], A.not_equal, 1.0, -a, 1)
     ts(ref("CL", 0, 8), ref("CMI", 0, 8), 15.0, A.add)
     iota(full("RST"), [[0, 128]], 0, 0)
     sel(full("RST"), full("RST"), [[0, 8], [1, 16]], A.not_equal, 1048576.0, 0, 0)
     for i, c in enumerate((1, 0, -99)):
-        iota(ref("CS", 8 * i, 8 * i + 8), [[0, 8]], c, 0)
-    iota(full("ZE"), [[0, 128]], 0, 0)
+        const(ref("CS", 8 * i, 8 * i + 8), c)
     for nm in DIAG:
-        if nm in ("Ibig", "Ifl", "I16", "I8k", "I1", "Ip100", "I8kn", "I10240", "In8192"):
-            sel(full(nm), full("ZE"), [[-1, 128]], A.not_equal, DIAG[nm][0], 0, 1)
-        elif DIAG[nm][1] == h2:
-            ts(full(nm), Ib, DIAG[nm][0], A.mult)
-        elif nm != "Ib":
-            act(full(nm), Ib, F.Copy, 0.0, DIAG[nm][0])
+        if nm != "Ib":
+            flex("S", full(nm), Ib, 0.0, DIAG[nm][0])
     ts(ref("PI", 16, 17), ref("PI", 0, 1), 15, A.bitwise_and)
     ts(ref("PI", 24, 25), ref("PI", 0, 1), 1, A.bitwise_and)
-    pm, sg, sg256, dg, sp0, sp1 = [ref("PC", 4 * i, 4 * i + 1) for i in range(6)]
+    pm, sg, sg256, low, lowe, lowh = [ref("PC", 4 * i, 4 * i + 1) for i in range(6)]
     cp(pm, ref("PI", 16, 17))
+    ts(low, pm, 15.0, A.is_equal, 4096.0, A.mult)
+    flex("S", lowe, low, 4096.0)
+    flex("S", lowh, low, -2048.0, -1.0)
     ts(sg, ref("PI", 24, 25), -2.0 / 128, A.mult, 1.0 / 128, A.add)
     ts(sg256, ref("PI", 24, 25), -2.0 / 128, A.mult, 257.0 / 128, A.add)
     iota(full("SPT"), [[0, 8], [16, 2]], 4096, 0)
-    ts(full("SPT"), full("SPT"), pm, A.add)
-    iota(ref("CK", 0, 16), [[0, 16]], 18432, 0)
-    iota(ref("CK", 16, 24), [[0, 8]], 8192, 0)
+    iota(full("SPU"), [[0, 4], [16, 4]], 4096, 0)
+    flex("S", full("SPU"), full("SPU"), pm)
+    flex("S", full("SPT"), full("SPT"), pm)
+    const(ref("CK", 0, 16), 18432)
+    const(ref("CK", 16, 24), 8192)
     ts(full("G0"), Ib, sg, A.mult)
     ts(full("G256"), Ib, sg256, A.mult)
     cp(ref("WTf", 0, 2), full("WT"))
@@ -867,25 +970,29 @@ def build(T, topo, core, rank, CO=COSTS[0]):
     if len(XT) < 3:
         fill(full("Bh"), 0.0)
         cp(ref("Bh", 15, 143, 16), ref("BO", 0, 128, 16))
-    act(full("WBn"), full("WB"), F.Copy, 0.0, -1.0)
+    flex("S", full("WBn"), full("WB"), 0.0, -1.0)
     fill(full("CH"), M35 / 128)
     fill(full("CHn"), -M35 / 128)
+    const(full("CQ"), 16 * MAGIC / 128)
+    const(full("CQn"), -16 * MAGIC / 128)
     fill(full("C1"), 16.0)
     fill(ref("C1", 0, 128, 1, 0, 1), 15.5)
-    iota(full("CN"), [[0, 128]], -32, 0)
-    iota(full("CP"), [[0, 128]], -4096, 0)
-    ts(full("B32"), ref("BO", 0, 128, 16), 32.0, A.mult)
-    ts(full("Bm16"), ref("BO", 0, 128, 16), -16.0, A.mult)
-    ts(full("MP"), full("BO"), 524288.0, A.mult)
+    const(full("CN"), -32)
+    const(full("CP"), -4096)
+    flex("V", full("Bm32"), ref("BO", 0, 128, 16), 0.0, -32.0)
+    flex("V", full("B16"), ref("BO", 0, 128, 16), 0.0, 16.0)
+    const(ref("CP", 15, 128, 16), -4096 - 512)
+    const(full("Cm2"), -2)
+    flex("V", full("MP"), full("BO"), 0.0, 524288.0)
     tt(full("MP"), full("MP"), full("Ibig"), A.add)
     ts(ref("CM", 0, 8), ref("CMI", 0, 8), pm, A.add)
     ts(ref("CM", 8, 16), ref("CMI", 0, 8), pm, A.add)
-    iota(ref("CMF", 0, 8), [[0, 8]], 256, 0)
+    const(ref("CMF", 0, 8), 256)
     ts(ref("CMF", 8, 16), ref("CMI", 0, 8), pm, A.add, 128.0, A.add)
-    act(ref("Sb", 0, 128, 2), ref("Ib", 1, 128, 2), F.Copy)
-    act(ref("Sb", 1, 128, 2), ref("Ib", 0, 128, 2), F.Copy)
-    act(full("Sb100"), full("Sb"), F.Copy, 0.0, 100.0 / 128)
-    fill(ref("VI", 4096, 4096 + 32), 0)
+    flex("S", ref("Sb", 0, 128, 2), ref("Ib", 1, 128, 2))
+    flex("S", ref("Sb", 1, 128, 2), ref("Ib", 0, 128, 2))
+    flex("S", full("Sb100"), full("Sb"), 0.0, 100.0 / 128)
+    fill(ref("VI", 4096, 4096 + 64), 0)
     fill(ref("PX", 0, 16), 0.0)
     ts(ref("PX", 16, 32), full("IJ"), pm, A.is_equal)
     w = 16
@@ -896,18 +1003,11 @@ def build(T, topo, core, rank, CO=COSTS[0]):
         i = add(pg, "Y", 0.1, lambda e, a=a: e.dma_start(ap(ref("PX", 16 + a, 16 + a + w)), ap(ref("PX", 16, 16 + w))).then_inc(T.sem["oh"], 16),
                 [ref("PX", 16, 16 + w)], [ref("PX", 16 + a, 16 + a + w)], sem="oh", val=16 * (4096 // w - 1), lat=9.5, tag="copy")
         pg["ops"][i]["ord"].add(loads[-1])
-    for step, k in enumerate((1, 2, 4, 8)):
-        for p0, p1, s0 in ((k, 128, 0), (0, k, k)):
-            out, src = ref("SEL", 128 * k, 256 * k, 1, p0, p1), ref("SEL", 0, 128 * k, 1, s0, s0 + p1 - p0)
-            j = add(pg, "Y", 0.1, lambda e, out=out, src=src: e.dma_start(ap(out), ap(src)).then_inc(T.sem["sl"], 16), [src], [] if s0 else [out],
-                    sem="sl", val=32 * step + 32, lat=7.0 if step == 0 else 2.5, tag="copy")
-            pg["ops"][j]["ord"].add(i)
-            if s0:
-                pg["acc"]["SEL"].append((j, 128 * k, 256 * k, True, 1))
-            i = j
     fill(full("D0"), 0.0)
     fill(ref("D0", 0, 384, 48), 1.0)
     fill(ref("D0", 16, 384, 48), 1.0)
+    fill(ref("D0", 384, 512, 32), 1.0)
+    const(ref("TRI", 384, 512), 0)
     ts(ref("TRI", 0, 16), full("IJ"), pm, A.is_ge, 16384.0, A.mult)
     fill(ref("TRI", 16, 32), 0.0)
     cp(ref("TRI", 32, 48), ref("TRI", 0, 16))
@@ -920,9 +1020,11 @@ def build(T, topo, core, rank, CO=COSTS[0]):
             prs.append((ref("Bh", 15 - j, 143 - j), ref(tile[0], tile[1] + j, tile[2], 16)))
         return acc(out, *(prs + list(last)))
 
-    def xts(b, tile, first=()):
+    cp(full("Bf"), ref("BO", 0, n, 16))
+
+    def xts(b, tile, first=(), ones=ref("BO", 0, n, 16)):
         mm = [(ref(b, 0, n, 1, 0, 8), l, r, i == 0, False) for i, (l, r) in enumerate(first)]
-        return mm + [(ref(b, j, n, 16, 0, 8), ref(tile[0], tile[1] + j, tile[2], 16), ref("BO", 0, n, 16), not first, j == 15 or not first) for j in range(16)]
+        return mm + [(ref(b, j, n, 16, 0, 8), ref(tile[0], tile[1] + j, tile[2], 16), ones, not first, j == 15 or not first) for j in range(16)]
 
     I8 = ref("Ib", 0, 8, 1, 0, 8)
     xl = lambda name, h: ref(name, h * n, h * n + n, 1, 0, 8)
@@ -943,9 +1045,10 @@ def build(T, topo, core, rank, CO=COSTS[0]):
     def tiles(t, h):
         k = 2 * t + h
         x0, w0, z0 = k * XW, k * WW, k * (32 + n)
+        cm = (3, 2) if WIDE and t < NT - 1 else (2, 3)
         d = {"st": lambda j, w=1: ref("XZ", x0 + 8 * j, x0 + 8 * (j + w)), "z": ref("XZ", x0 + 32, x0 + 32 + n), "x": ref("XZ", x0 + 32 + n, x0 + 32 + 2 * n),
              "hz": ref("XZ", x0 + 32 + 2 * n, x0 + 32 + 3 * n), "xz": ref("XZ", x0 + 32, x0 + 32 + 2 * n), "xzh": ref("XZ", x0 + 32, x0 + 32 + 3 * n),
-             "hd": ref("W", w0, w0 + n), "f": ref("W", w0 + n, w0 + 2 * n), "c": ref("W", w0 + 2 * n, w0 + 3 * n),
+             "hd": ref("W", w0, w0 + n), "f": ref("W", w0 + n, w0 + 2 * n), "c": ref("W", w0 + cm[0] * n, w0 + cm[0] * n + n), "mm": ref("W", w0 + cm[1] * n, w0 + cm[1] * n + n),
              "w2": ref("W", w0, w0 + 2 * n), "w3": ref("W", w0, w0 + 3 * n), "vh": ref("VH", 8 * k, 8 * k + 8),
              "land": ref("XZ", x0, x0 + 32 + n), "fb": ref("FB", k * n, k * n + n), "vb": ref("VB", 8 * k, 8 * k + 8)}
         if t < NT - 1:
@@ -955,7 +1058,10 @@ def build(T, topo, core, rank, CO=COSTS[0]):
         return d
 
     px, views = ref("PX", NOH, NOH + 4096), ref("VI", 0, 4096)
-    pxe = ref("PX", NOH - 4096, NOH + 4096)
+    px2 = ref("PX", NOH, NOH + 8192)
+    pxe = ref("PX", NOH - 4096, NOH + 8192)
+    for c in range(0, 4096, LOWP):
+        flex("S", ref("PX", NOH + 4096 + c, NOH + 4096 + c + LOWP), ref("PX", NOH + c, NOH + c + LOWP), -256.0)
     banks = {}
 
     def mark(name, h):
@@ -1007,40 +1113,56 @@ def build(T, topo, core, rank, CO=COSTS[0]):
             ts(lk, ct, 8.5, A.is_ge, 128.0, A.mult)
             tt(sm("LSL", h), lk, ref("CM", 0, 8), A.add)
         mark("h", h)
-        flex("V", ref("HEL", 2 * h * n, 2 * h * n + n), ("ind", L["w2"], sm("LSF", h, 16, 8)))
+        flex("V", ref("HEL", 2 * h * n, 2 * h * n + n), ("ind", L["w2"], sm("LSF", h, 16, 8)), low)
         mark("hm", h)
-        flex("S", tl("H16", h), ref("HEL", 2 * h * n, 2 * h * n + n), -2048.0)
+        flex("S", tl("H16", h), ref("HEL", 2 * h * n, 2 * h * n + n), lowh)
         mark("qx", h)
         q0 = h * 16 * n
-        flex("V", ref("QS", 0, 16 * n, 16), ("ind", L["xz"], sm("LSF", h, 16)))
+        st, cuts = QG[h]
+        w = 16 // st
+        qs = ref("QS", 0, 8 * n, 8)
+        flex("V", qs, ("ind", L["xz"], sm("LSF", h, 16)))
         banks[h] = (bank(), bank(), bank())
-        pe([(ref(banks[h][2], 0, n), Ib, ref("QS", 0, 16 * n, 16), True, True)])
-        scan(ref("QX", q0, q0 + 16 * n), full("MK"), full("QS"), 0.0, A.min, A.add)
+        pe(acc(ref(banks[h][2], 0, n), (full("Cm2"), on), (Ib, qs)))
+        for a, e_ in QSCAN:
+            scan(ref("QX", q0 + 16 * a, q0 + 16 * e_, st), ref("MK", 8 * a, 8 * e_, st // 2), ref("QS", 8 * a, 8 * e_, st // 2), 0.0, A.min, A.add)
+        for a, e_ in cuts:
+            for r in range(1, st):
+                out, src = ref("QX", q0 + 16 * a + r, q0 + 16 * e_, st), ref("QX", q0 + 16 * a, q0 + 16 * e_, st)
+                if a < QV[h]:
+                    flex("V", out, src)
+                else:
+                    sel(out, src, [[0, w * (e_ - a)]], A.is_ge, 0.0, 0, 0)
         mark("e", h)
-        flex("S", ref("HEL", (2 * h + 1) * n, (2 * h + 2) * n), ("ind", views, vh), 4096.0 if t else 0.0)
+        flex("S", ref("HEL", (2 * h + 1) * n, (2 * h + 2) * n), ("ind", views, vh), lowe if t else low)
 
     def dedupe(t):
         mark("dd", 0)
         vh = ref("VH", 16 * t, 16 * t + 16)
         flex("S", full("VF"), vh, -2048.0)
         b = bank()
-        mm = []
+        mm, ns = [], 32 if t in BIG else 24
         for j, (c, d) in enumerate(((0, 0), (0, 1), (1, 1))):
             mm += acc(ref(b, j, 24, 3), (Ib, ref("VF", c, 16, 2)), (full("I8k"), ref("LK", c, 16, 2)))
-            mm += acc(ref(b, 24 + j, 48, 3), (Ib, ref("VF", d, 16, 2)), (Ib, ref("CK", 16, 24)))
-        pe(mm[:6])
-        pe(mm[6:])
-        flex("S", full("WD"), ref(b, 0, 48), -8192.0)
+            mm += acc(ref(b, ns + j, ns + 24, 3), (Ib, ref("VF", d, 16, 2)), (Ib, ref("CK", 16, 24)))
+        big = t in BIG
+        for j, (c, d) in enumerate(((0, 2), (1, 2), (0, 3), (1, 3)) if big else ()):
+            mm += acc(ref(b, 24 + j, 32, 4), (Ib, ref("VF", c, 8, 4)), (full("I8k"), ref("LK", c, 8, 4)))
+            mm += acc(ref(b, 56 + j, 64, 4), (Ib, ref("VF", d, 8, 4)), (Ib, ref("CK", 16, 18)))
+        for j in range(0, len(mm), 6):
+            pe(mm[j:j + 6])
+        flex("S", ref("WD", 0, 2 * ns), ref(b, 0, 2 * ns), -8192.0)
         b = bank()
         for j0 in range(0, 16, SELP):
-            pe([(ref(b, 0, 384), Ib, full("TRI"), True, False)][j0:] + [(ref(b, j, 384, 16), l, r, False, j == 15 and r[1] == 24) for j in range(j0, j0 + SELP)
-                for l, r in ((ref("SEL", 128 * j, 128 * j + 128), ref("WD", 0, 24)), (full("In"), ref("WD", 24, 48)))])
-        flex("S", full("EQ"), ref(b, 0, 384), size=True)
-        scan(full("DS"), full("D0"), full("EQ"), 0.0, A.max, A.min)
+            pe([(ref(b, 0, 16 * ns), Ib, ref("TRI", 0, 16 * ns), True, False)][j0:] + [(ref(b, j, 16 * ns, 16), l, r, False, j == 15 and r[1] == ns) for j in range(j0, j0 + SELP)
+                for l, r in ((ref("SEL", 128 * j, 128 * j + 128), ref("WD", 0, ns)), (full("In"), ref("WD", ns, 2 * ns)))])
+        flex("S", ref("EQ", 0, 16 * ns), ref(b, 0, 16 * ns), size=True)
+        scan(ref("DS", 0, 16 * ns), ref("D0", 0, 16 * ns), ref("EQ", 0, 16 * ns), 0.0, A.max, A.min)
         b = bank()
-        pe(grp((ref(b, 0, 16), Ib, ref("CK", 0, 16)), (ref(b, 0, 16), Ib, full("VF")), (ref(b, 0, 16), full("I8kn"), full("LK")),
+        more = [x for d in (2, 3) for x in ((ref(b, d, 8, 4), Ib, ref("CK", 16, 18)), (ref(b, d, 8, 4), full("In8192"), ref("DS", 351 + 32 * d, 512, 64)))] if big else []
+        pe(grp((ref(b, 0, 16), Ib, ref("CK", 0, 16)), (ref(b, 0, 16), Ib, full("VF")), (ref(b, 0, 16), full("I8kn"), full("LK")), *more,
                (ref(b, 0, 16, 2), full("In8192"), ref("DS", 15, 384, 48)), (ref(b, 1, 16, 2), full("In8192"), ref("DS", 47, 384, 48))))
-        tt(full("OFF"), ref(b, 0, 16), full("SPT"), A.min)
+        tt(full("OFF"), ref(b, 0, 16), full("SPU" if big else "SPT"), A.min)
 
     def early(t, h):
         mark("ea", h)
@@ -1081,15 +1203,18 @@ def build(T, topo, core, rank, CO=COSTS[0]):
             store(T.yz[:, h * n:h * n + n], ref("YU", 1024 + h * n, 1024 + h * n + n))
         mark("kk", h)
         y = ref(bank(), 0, 8)
-        if "k" in XT:
+        if "k" in XT or t == 0:
             b = bank()
             pe(xts(b, L["zf"]))
             flex("S", xl("XK", h), ref(b, 0, n, 1, 0, 8), -2048.0)
-            pe(acc(y, (full("I8k"), lk), (full("I8200"), ov), (xl("XK", h), I8)))
+            off = [(xl("XK", h), ref("In", 0, 8, 1, 0, 8)), (full("CQ"), ref("ON", 0, 8)), (full("CQn"), ref("ON", 0, 8))] if t == 0 else []
+            pe(acc(y, *off, (full("I8k"), lk), (full("I8200"), ov), (xl("XK", h), I8)))
         else:
-            pe(ots(y, L["zf"], [(full("I8k"), lk), (full("I8200"), ov)]))
-        flex("S", sm("KL", h), y, t + 16.0 - 8192.0 + (2048.0 if "k" in XT else 0.0))
-        flex("S", tl("OHL", h), ("ind", ref("PX", 0, NOH), sm("KL", h)))
+            mm = ots(y, L["zf"], [(full("I8k"), lk), (full("I8200"), ov)])
+            pe(mm[:10])
+            pe(mm[10:])
+        flex("S", sm("KL", h), y, t + 16.0 - 8192.0 + (16.0 if t == 0 else 2048.0 if "k" in XT else 0.0))
+        flex("S", tl("OHL", h), ("ind", ref("PX", 0, NOH if t else 80), sm("KL", h)))
 
     def bulk(t, h, w):
         mark("he"[w] + "b", h)
@@ -1098,53 +1223,67 @@ def build(T, topo, core, rank, CO=COSTS[0]):
         b = banks[h][w]
         for a, e_, q in PARTS[h][w]:
             g_, off = ref(G, q0 + 16 * a, q0 + 16 * e_), ref("HEL", l0 + a, l0 + e_)
-            flex(q, g_, ("ind", pxe if w and t else px, off))
+            flex(q, g_, ("ind", pxe if w and t else px2, off))
+        first = [(ref(b, 0, n), on, full("CP" if w else "KC"), True, False)]
+        for k0 in range(0, 16, SPLIT):
+            pe(first[k0:] + [(ref(b, k, n, 16), ref(G, q0 + k, q0 + 16 * n, 16), full("B16"), False, False) for k in range(k0, k0 + SPLIT)], free=k0 > 0)
         for a, e_ in CHUNKS[h][w]:
             lo, hi = q0 + 16 * a, q0 + 16 * e_
-            g0 = ref(G, lo, hi, 16)
-            first = [(ref(b, 0, n), Ib, full("KC"), True, False) if w == 0 else (ref(b, 0, n), on, full("CP"), True, False)] if a == 0 else []
-            pe(first + [(ref(b, 0, n, 16, a, e_), g0, full("Bm16"), False, False)], sub=True)
-            if e_ == n:
-                for k0 in range(0, 16, SPLIT):
-                    pe([(ref(b, k, n, 16), ref(G, q0 + k, q0 + 16 * n, 16), full("Bm16"), False, False) for k in range(max(1, k0), k0 + SPLIT)], sub=True)
-            tt(g0, g0, ref(banks[h][2], a, e_), A.max)
-            scan(ref(M, lo, hi), ref("QX", lo, hi), ref(G, lo, hi), 0.0, A.min, A.max)
-        oh = [(ref(b, 0, n), tl("OHL", h), full("Ibig" if w == 0 else "MP"), False, False)]
-        if not JOIN:
-            pe(oh)
-        for k0 in range(0, 16, SPLIT):
-            i = pe(oh[k0:JOIN] + [(ref(b, k, n, 16), ref(M, q0 + k, q0 + 16 * n, 16), full("B32"), False, k == 15) for k in range(k0, k0 + SPLIT)])
+            scan(ref(M, lo, hi), ref("QX", lo, hi), ref(G, lo, hi), 0.0, A.max, A.min)
+        pe([(ref(b, 0, n), tl("OHL", h), full("Ibig" if w == 0 else "MP"), False, False)], free=True)
+        for a, e_ in SUMS[h][w]:
+            tt(ref("ML", l0 + a, l0 + e_), ref(G, q0 + 16 * a + 15, q0 + 16 * e_, 16), ref(banks[h][2], a, e_), A.min)
+            step = SPLIT if e_ - a > 32 else 16
+            for k0 in range(0, 16, step):
+                i = pe([(ref(b, k, n, 16, a, e_), ref(M, q0 + 16 * a + k, q0 + 16 * e_, 16) if k < 15 else ref("ML", l0 + a, l0 + e_), full("Bm32"), False, False)
+                        for k in range(k0, k0 + step)], free=True)
         return i
 
     def tail(t, h):
         L = tiles(t, h)
         key = tl("KEY", h)
         ph, pd = ref(banks[h][0], 0, n), ref(banks[h][1], 0, n)
-        bulk(t, h, 0)
+        last = bulk(t, h, 0)
         mark("km", h)
-        flex("S", key, ph)
-        scan(tl("PM", h), full("RST"), key, 0.0, A.add, A.min)
-        tt(tl("OHT", h), ("ind", tl("PM", h), ref("CL", 0, 8)), key, A.is_equal)
+        if h in LATE:
+            scan(tl("PM", h), full("RST"), ph, 0.0, A.add, A.min)
+            back = lambda x: ref(x, h * n, h * n + n, -1)
+            scan(back("RB"), full("RST"), back("PM"), 0.0, A.add, A.min)
+            tt(tl("OHT", h), tl("RB", h), ph, A.is_equal)
+        else:
+            flex("S", key, ph)
+            scan(tl("PM", h), full("RST"), key, 0.0, A.add, A.min)
+            tt(tl("OHT", h), ("ind", tl("PM", h), ref("CL", 0, 8)), key, A.is_equal)
         oc = ref(bank(), 0, n)
         pe([(oc, tl("OHT", h), Ib, True, True)])
-        last = bulk(t, h, 1)
+        i = bulk(t, h, 1)
         mark("cc", h)
-        tt(tl("MT", h), key, pd, A.is_lt)
+        if h in LATE:
+            flex("S", key, pd)
+            tt(tl("MT", h), key, ph, A.is_gt)
+        else:
+            last = i
+            tt(tl("MT", h), key, pd, A.is_lt)
         mk = ref(bank(), 0, n)
         i = pe([(mk, Ib, tl("H16", h), True, False)] + [(mk, full("CN"), on, False, False)][t:])
         pg["ops"][i]["ord"].add(last)
-        pe([(mk, tl("MT", h), full("I10240"), False, True)])
-        tt(tl("MM", h), ref("HEL", (2 * h + 1) * n, (2 * h + 2) * n), mk, A.max)
-        ts(L["c"], tl("MM", h), 4095, A.bitwise_and)
-        flex("V", tl("CF", h), ("ind", L["w3"], sm("TLL", h, 16)), -2048.0)
-        tt(tl("PP", h), tl("CF", h), oc, A.mult)
+        pe([(mk, tl("MT", h), full("Iwin"), False, True)])
+        tt(L["mm"], ref("HEL", (2 * h + 1) * n, (2 * h + 2) * n), mk, A.max)
+        ts(L["c"], L["mm"], 4095, A.bitwise_and)
+        wide = WIDE and t < NT - 1
+        if wide:
+            ts(tl("CI", h), ("ind", L["w3"], sm("TLL", h, 16)), 4095, A.bitwise_and)
+            tt(tl("PF", h), tl("CI", h), oc, A.mult)
+        else:
+            flex("V", tl("CF", h), ("ind", L["w3"], sm("TLL", h, 16)), -2048.0)
+            tt(tl("PP", h), tl("CF", h), oc, A.mult)
         vo = ref(bank(), 0, n)
         if t < NT - 1:
             vo = ref(vo[0], 0, 8)
             if "v" in XT:
                 b = bank()
-                pe(xts(b, tl("PP", h)))
-                flex("V", xl("XV", h), ref(b, 0, n, 1, 0, 8))
+                pe(xts(b, tl("PF", h), ones=full("Bf")) if wide else xts(b, tl("PP", h)))
+                flex("V", xl("XV", h), ref(b, 0, n, 1, 0, 8), -2048.0 if wide else 0.0)
                 pe([(vo, xl("XV", h), I8, True, True)])
             else:
                 pe(ots(vo, tl("PP", h)))
@@ -1164,9 +1303,10 @@ def build(T, topo, core, rank, CO=COSTS[0]):
     def scatter(t, h):
         mark("sc", h)
         c0 = tiles(t, h)["c"][1]
-        for c in range(3, -1, -1):
-            off, src = ref("OFF", h * 8 + 2 * c, h * 8 + 2 * c + 2), ref("W", c0 + 32 * c, c0 + 32 * c + 32)
-            i = add(pg, "V", CO["scat"], lambda e, off=off, src=src: e.tensor_copy(ap(full("VI")).indirect(ap(off)), ap(src)), [off, src], [full("VI")], tag="scatter")
+        w = 4 if t in BIG and h == 0 else 2
+        for c in range(8 - w, -1, -w):
+            off, src = ref("OFF", h * 8 + c, h * 8 + c + w), ref("W", c0 + 16 * c, c0 + 16 * (c + w))
+            i = add(pg, "V", CO["scat"] * (1.7 if w > 2 else 1.0), lambda e, off=off, src=src: e.tensor_copy(ap(full("VI")).indirect(ap(off)), ap(src)), [off, src], [full("VI")], tag="scatter")
             o = pg["ops"][i]
             for d in [d for d in o["dep"] if WAW and pg["ops"][d]["tag"] == "scatter" and pg["ops"][d]["hop"] == t]:
                 o["dep"].discard(d)

import numpy as np
from concourse.bass import DstId, RemoteDMATransfer
from concourse.mybir import dt, AluOpType, AxisListType, ActivationFunctionType

A = AluOpType
F = ActivationFunctionType
n = 128
NT = 5
XW = 32 + 3 * n
WW = 4 * n
WIDE = False
BIG = ()
LATE = (0,)
MAGIC = 12582912.0
NB = 8
M35 = 1.5 * 2.0 ** 35
HC = 262000
NOH = 4112
OH0 = 1024
PARTS = ((((0, 48, "S"), (48, 96, "S"), (96, 128, "V")), ((0, 48, "S"), (48, 96, "S"), (96, 128, "S"))),
         (((0, 48, "S"), (48, 96, "S"), (96, 128, "S")), ((0, 48, "S"), (48, 96, "S"), (96, 128, "V"))))
CHUNKS = ((((0, 48), (48, 96), (96, 128)),) * 2,) * 2
SUMS = ((((0, 128),), ((0, 128),)),) * 2
ONV = ("hz0", "hz1")
LINES = [tuple("%sb%s  G%s %d" % (x[0], x[1], x[0].upper(), k) for x in ("h1 e1 e0 h0" if t else "h1 e1 h0 e0").split() for k in ()) for t in range(NT)]
WAW = False
XT = "ckv"
PACK = (0, 192, 576, 1088, 1600, 2048)
JOIN = 0
SELP = 4
SPLIT = 8
LOWP = 1024
QST = 2
QSCAN = ((0, 48), (48, 128))
QG = ((2, ((0, 48), (48, 96), (96, 128))),) * 2
QV = (0, 0)
f4, b2, h2, i4, u2 = "float32", "bfloat16", "float16", "int32", "uint16"

SCRATCH = {
    "PX": ("sbuf", [128, NOH + 8192], b2), "ML": ("sbuf", [128, 4 * n], b2), "Cm2": ("sbuf", [128, 128], b2), "VI": ("sbuf", [128, 4096 + 64], i4), "SPU": ("sbuf", [128, 16], f4), "VW": ("sbuf", [128, 2048], i4),
    "YT": ("sbuf", [128, 2048], f4), "YU": ("sbuf", [128, 2048], f4),
    "W613": ("sbuf", [128, 4096 + 8], f4), "TRI": ("sbuf", [128, 512], b2),
    "XZ": ("sbuf", [128, 10 * XW], b2), "W": ("sbuf", [128, 10 * WW], i4), "VH": ("sbuf", [128, 10 * 8], u2),
    "ZB": ("sbuf", [128, 8 * (32 + n)], b2), "FB": ("sbuf", [128, 10 * n], i4), "SPT": ("sbuf", [128, 16], f4), "CK": ("sbuf", [128, 24], b2), "VB": ("sbuf", [128, 10 * 8], u2), "ZL": ("sbuf", [128, 2 * n], b2),
    "HEL": ("sbuf", [128, 4 * n], u2), "QS": ("sbuf", [128, 16 // QST * n], b2), "QX": ("sbuf", [128, 32 * n], b2), "MK": ("sbuf", [128, 16 // QST * n], b2), "H16": ("sbuf", [128, 2 * n], h2),
    "GH": ("sbuf", [128, 32 * n], b2), "GE": ("sbuf", [128, 32 * n], b2), "MH": ("sbuf", [128, 32 * n], b2), "ME": ("sbuf", [128, 32 * n], b2),
    "IND": ("sbuf", [128, 2 * n], b2), "LK": ("sbuf", [128, 16], b2), "LSL": ("sbuf", [128, 16], u2), "LSF": ("sbuf", [128, 32], u2), "CMF": ("sbuf", [128, 16], b2),
    "HI1": ("sbuf", [128, 2 * n], i4), "HI2": ("sbuf", [128, 2 * n], i4),
    "T2": ("sbuf", [128, 2 * n], f4),
    "OV": ("sbuf", [128, 16], b2), "TLL": ("sbuf", [128, 32], u2), "RA": ("sbuf", [128, 48], b2), "KL": ("sbuf", [128, 16], u2), "OHL": ("sbuf", [128, 2 * n], b2),
    "VF": ("sbuf", [128, 16], h2), "WD": ("sbuf", [128, 64], h2), "SEL": ("sbuf", [128, 16 * 128], b2), "EQ": ("sbuf", [128, 512], b2),
    "DS": ("sbuf", [128, 512], b2), "OFF": ("sbuf", [128, 16], u2),
    "KEY": ("sbuf", [128, 2 * n], f4), "MT": ("sbuf", [128, 2 * n], b2), "CI": ("sbuf", [128, 2 * n], i4),
    "PF": ("sbuf", [128, 2 * n], f4), "RB": ("sbuf", [128, 2 * n], f4), "Bf": ("sbuf", [128, 8], f4),
    "PM": ("sbuf", [128, 2 * n], f4), "OHT": ("sbuf", [128, 2 * n], b2), "CF": ("sbuf", [128, 2 * n], h2), "PP": ("sbuf", [128, 2 * n], h2),
    "YC": ("sbuf", [128, 16], b2), "VZ": ("sbuf", [128, 512], i4), "VZh": ("sbuf", [128, 512], h2),
    "WBn": ("sbuf", [128, 128], b2), "C1": ("sbuf", [128, 128], b2), "CHn": ("sbuf", [128, 128], b2), "CN": ("sbuf", [128, 128], b2),
    "CQ": ("sbuf", [128, 128], b2), "CQn": ("sbuf", [128, 128], b2),
    "XL": ("sbuf", [128, 2 * n], b2), "XK": ("sbuf", [128, 2 * n], h2), "XV": ("sbuf", [128, 2 * n], h2),
    "ON": ("sbuf", [128, 144], b2), "BO": ("sbuf", [128, 128], b2), "B8": ("sbuf", [128, 144], b2), "Bh": ("sbuf", [128, 144], b2),
    "Bm32": ("sbuf", [128, 8], b2), "B16": ("sbuf", [128, 8], b2), "WB": ("sbuf", [128, 128], b2), "CH": ("sbuf", [128, 128], b2), "CP": ("sbuf", [128, 128], b2),
    "Sb": ("sbuf", [128, 128], b2), "Sb100": ("sbuf", [128, 128], b2), "MP": ("sbuf", [128, 128], b2), "DG": ("sbuf", [128, 128], b2), "G0": ("sbuf", [128, 128], b2),
    "G256": ("sbuf", [128, 128], h2), "ZE": ("sbuf", [128, 128], b2),
    "KC": ("sbuf", [128, 128], b2), "RST": ("sbuf", [128, 128], f4), "D0": ("sbuf", [128, 512], b2),
    "PI": ("sbuf", [128, 32], i4), "PC": ("sbuf", [128, 32], f4), "IJ": ("sbuf", [128, 16], f4), "CMI": ("sbuf", [128, 32], f4), "CM": ("sbuf", [128, 16], b2),
    "CS": ("sbuf", [128, 24], b2), "CL": ("sbuf", [128, 32], u2), "WT": ("sbuf", [128, 2], i4), "WTf": ("sbuf", [128, 8], f4),
}
DIAG = {"Ib": (1.0, b2), "In": (-1.0, b2), "I2": (2.0, b2), "Ic": (0.00689697265625, b2), "Icn": (-0.00689697265625, b2), "Ihz": (0.5 - 2.0 ** -11, h2),
        "I1": (1.0 / 128, b2), "Ip100": (100.0 / 128, b2), "Im100": (-100.0 / 128, b2), "I8k": (8192.0 / 128, b2), "I8kn": (-8192.0 / 128, b2), "I8200": (8200.0 / 128, h2),
        "Iwin": (14336.0, b2), "In8192": (-8192.0, b2), "Ibig": (-262144.0, b2), "Ifl": (0.8125, b2), "I16": (16.0, b2)}
for _k in DIAG:
    SCRATCH[_k] = ("sbuf", [128, 128], DIAG[_k][1])
for _b in range(8):
    SCRATCH["bank%d" % _b] = ("psum", [128, 512], f4) if _b < NB else ("psum", [128, 1024], b2)
SMALL = []
LOADS = SMALL + ["v0", "d0", "wt", "kap", "z1", "px0", "px1", "z0", "vw0", "f1", "vw1", "f0"]
SEMAPHORES = ["V", "S", "P", "G", "out", "ls", "oh"] + ["ld_" + x for x in LOADS] + ["r%s_%d_%d" % (k, t, h) for k in "zfv" for t in range(1, NT) for h in range(2)]

COSTS = tuple(dict(zip(("cy", "gather", "wake", "pe", "link", "scat", "V", "S", "P", "row", "issue", "load"), c)) for c in (
    (0.00083, 1.56, 0.10, 0.00042, 1.2, 0.15, 0.005, 0.02, 0.01, 0.8, 0.5, 0.9),
    (0.00087, 1.15, 0.09, 0.00044, 1.0, 0.12, 0.005, 0.02, 0.01, 0.7, 0.4, 0.9),
    (0.00118, 1.95, 0.12, 0.00059, 1.8, 0.25, 0.01, 0.03, 0.02, 1.3, 0.8, 1.2),
    (0.00104, 1.65, 0.13, 0.00052, 1.6, 0.16, 0.01, 0.04, 0.01, 1.1, 0.7, 1.1),
    (0.00100, 1.30, 0.08, 0.00050, 1.1, 0.24, 0.005, 0.02, 0.02, 0.8, 0.5, 1.0),
    (0.00085, 1.08, 0.045, 0.00042, 0.9, 0.15, 0.015, 0.02, 0.01, 0.6, 0.3, 0.8)))
WEIGHT = (1.2, 1.1, 1.0, 1.0, 1.1, 0.6)
ROUGH = 0.0
SEEDS = (1, 2, 3)
ROUNDS = 100
MOVES = (15000, 160000)
LOADW = 0.0
FIRST = {}
ALIKE = 0.0
EVERY = 0.9
STAGGER = 7.0


def ref(name, c0, c1, step=1, p0=0, p1=128, pstep=1):
    return (name, c0, c1, step, p0, p1, pstep)


def is_psum(name):
    return name[0] in "bc" and name[1:].isdigit()


def touch(pg, o, r, wr):
    name, c0, c1 = r[0], r[1], r[2]
    lst = pg["acc"].setdefault(name, [])
    psum = is_psum(name)
    ops = pg["ops"]
    keep = []
    for a in lst:
        p, a0, a1, aw, st = a
        over = a0 < c1 and c0 < a1 and not (st == r[3] and (a0 - c0) % st)
        if p != o["i"]:
            if psum:
                if ops[p]["q"] == o["q"] == "P":
                    if not (o["free"] and ops[p]["free"]):
                        o["ord"].add(p)
                elif ops[p]["q"] != o["q"] or ops[p]["alt"] or o["alt"]:
                    o["dep"].add(p)
            elif over and (wr or aw):
                o["dep"].add(p)
        if wr and a0 >= c0 and a1 <= c1 and p != o["i"] and not psum and r[3] == 1 and r[6] == 1 and r[4] == 0 and r[5] == 128:
            continue
        keep.append(a)
    keep.append((o["i"], c0, c1, wr, r[3]))
    pg["acc"][name] = keep


def add(pg, q, cost, fn, rd, wr, sem=None, val=1, lat=0.0, tag="", alt=None, free=False):
    o = {"free": free, "i": len(pg["ops"]), "q": q, "alt": alt, "cost": cost, "fn": fn, "dep": set(), "ord": set(), "sem": sem, "val": val, "lat": lat, "send": None, "tag": tag, "st": pg["st"], "hop": pg["hop"]}
    pg["ops"].append(o)
    for r in rd:
        touch(pg, o, r, False)
    for r in wr:
        touch(pg, o, r, True)
    o["near"] = o["dep"]
    o["tiles"] = sorted(set(r[0] for r in list(rd) + list(wr) if is_psum(r[0]) and r[0][0] == "b"))
    return o["i"]


def place(key, pred, succ, q, cost, head):
    cnt = [len(p) for p in pred]
    ready = [(key[i], i) for i in range(len(key)) if cnt[i] == 0]
    st = [0.0] * len(key)
    S, E = {x: [] for x in set(q)}, {x: [] for x in set(q)}
    while ready:
        ready.sort(reverse=True)
        i = ready.pop()[1]
        t = head[i]
        for d, w in pred[i]:
            x = st[d] + cost[d] + w
            if x > t:
                t = x
        c = cost[i]
        if c > 0:
            s, e = S[q[i]], E[q[i]]
            m = k = len(s)
            while k > 0 and e[k - 1] > t:
                k -= 1
            while k < m and s[k] < t + c - 1e-9:
                t = e[k]
                k += 1
            s.insert(k, t)
            e.insert(k, t + c)
        st[i] = t
        for j, w in succ[i]:
            cnt[j] -= 1
            if cnt[j] == 0:
                ready.append((key[j], j))
    return st


def priced(ops, qs):
    return [o["alt"][q][0] if o["alt"] else o["cost"] for o, q in zip(ops, qs)]


def replay(ops, qs, seq, c, dyn, uses=None):
    cost, lat, wake = c
    fin = [0.0] * len(ops)
    free, bmap, held = {q: 0.0 for q in set(qs)}, {}, {}
    bfree = {b: (0.0, []) for b in range(NB)}
    for i in seq:
        o = ops[i]
        q = qs[i]
        st = free[q] - wake
        for d in o["near"]:
            if fin[d] > st:
                st = fin[d]
        if uses is None and i in dyn:
            for d in dyn[i]:
                if fin[d] > st:
                    st = fin[d]
        st += wake
        if o["send"] is not None:
            st = max(st, fin[o["send"]])
        if uses is not None:
            for t in o["tiles"]:
                if t not in bmap:
                    if not bfree:
                        return None, None
                    bmap[t] = min(bfree, key=lambda b: bfree[b][0])
                    x, l = bfree.pop(bmap[t])
                    st = max(st, x)
                    dyn.setdefault(i, []).extend(l)
                    held[t] = [0.0, []]
        free[q] = st + cost[i]
        fin[i] = free[q] + lat[i]
        if uses is not None:
            for t in o["tiles"]:
                if q != "P":
                    held[t][0] = max(held[t][0], free[q] + wake)
                    held[t][1].append(i)
                uses[t] -= 1
                if uses[t] == 0:
                    bfree[bmap[t]] = held[t]
    return max(fin), bmap


def schedule(pgs, wakes, rounds, seed):
    ops = pgs[0]["ops"]
    N_ = len(ops)
    q = [o["q"] for o in ops]
    prices = lambda qs: [(priced(p["ops"], qs), [o["lat"] for o in p["ops"]], w) for p, w in zip(pgs, wakes)]
    cs = prices(q)
    cost, lat, wake = cs[0]
    pred, succ = [[] for _ in ops], [[] for _ in ops]
    uses, phase, seen, slot = {}, {}, {}, {}
    topo_, state, above = [], [0] * N_, [0] * N_
    for root in range(N_):
        stack = [root]
        while stack:
            i = stack[-1]
            o = ops[i]
            if state[i] == 0:
                state[i] = 1
                stack.extend(d for d in o["dep"] | o["ord"] | {o["send"]} if d is not None and state[d] == 0)
            else:
                stack.pop()
                if state[i] == 1:
                    state[i] = 2
                    topo_.append(i)
    for i in topo_:
        o = ops[i]
        e = {d: wake + lat[d] for d in o["dep"]}
        for d in o["ord"]:
            e.setdefault(d, 0.0)
        if o["send"] is not None:
            e[o["send"]] = lat[o["send"]]
        for d in o["dep"]:
            above[i] |= above[d]
        o["near"] = [d for d in sorted(o["dep"]) if lat[d] or not above[i] >> d & 1]
        for d in sorted(e):
            if d in o["near"] or d not in o["dep"]:
                pred[i].append((d, e[d]))
                succ[d].append((i, e[d]))
        for d in o["dep"]:
            above[i] |= 1 << d
    for o in ops:
        i = o["i"]
        for t in o["tiles"]:
            uses[t] = uses.get(t, 0) + 1
        phase.setdefault(o["st"], []).append(i)
        if o["st"]:
            k = (o["hop"], o["st"], o["tag"])
            seen[k] = seen.get(k, 0) + 1
            slot.setdefault((o["st"], o["tag"], seen[k]), []).append(i)
    phases, slots = list(phase.values()), list(slot.values())
    either = [sl for sl in slots if ops[sl[0]]["alt"]] + [[o["i"]] for o in ops if o["alt"] and not o["st"]]
    zero = [0.0] * N_
    way = [0.0] * N_
    for i in reversed(topo_):
        way[i] = max([way[j] + w for j, w in succ[i]] + [lat[i]]) + cost[i]
    first = []

    def judge(st, q, cs):
        seq = sorted(range(N_), key=lambda i: (st[i], i))
        dyn = {}
        f, bmap = replay(ops, q, seq, cs[0], dyn, dict(uses))
        if f is None:
            return 1e9, None
        if keep and f > keep[3][0] * 1.015:
            return 1e9, None
        r = [f] + [replay(ops, q, seq, c, dyn)[0] for c in cs[1:]]
        if not first:
            first.extend(r)
        return sum(x / y for x, y in zip(r, first)) / len(r), (seq, dyn, bmap, r, st, q)

    rng = np.random.default_rng(seed)
    cur = [-way[o["i"]] + (STAGGER if o["st"][-1:] == "0" else 0.0) for o in ops]
    now, best, keep = 1e9, 1e9, None
    for it in range(rounds):
        key, q2, cs2 = list(cur), q, cs
        mode, d, a = int(rng.integers(7)), float(rng.normal()), float(rng.uniform(min(cur), max(cur)))
        if it == 0:
            pass
        elif mode >= 5:
            sl = either[int(rng.integers(len(either)))]
            q2 = list(q)
            to = "V" if q[sl[int(rng.integers(len(sl)))]] == "S" else "S"
            cs2 = [(list(c[0]), c[1], c[2]) for c in cs]
            for i in (sl if mode == 5 else [sl[int(rng.integers(len(sl)))]]):
                q2[i] = to
                for c, p in zip(cs2, pgs):
                    c[0][i] = p["ops"][i]["alt"][to][0]
        elif mode == 0:
            for t in rng.integers(len(phases), size=int(rng.integers(1, 4))):
                d = float(rng.normal(0, rng.choice([0.5, 1.5, 4.0])))
                for i in phases[t]:
                    key[i] += d
        elif mode == 1:
            wd, sg = float(rng.uniform(2, 15)), float(rng.choice([0.2, 0.6, 1.5]))
            for i in range(N_):
                if a <= key[i] <= a + wd:
                    key[i] += float(rng.normal(0, sg))
        elif mode == 2:
            for i in phases[int(rng.integers(len(phases)))]:
                if a <= key[i] <= a + 18:
                    key[i] += 3 * d
        else:
            s0 = slots[int(rng.integers(len(slots)))]
            at = lambda sl: cur[sl[min(1, len(sl) - 1)]]
            wd, d = float(rng.choice([0.0, 0.5, 2.0])), d * float(rng.choice([0.3, 1.0, 3.0]))
            for sl in slots:
                if at(s0) <= at(sl) <= at(s0) + wd and (mode == 3 or q[sl[0]] == q[s0[0]]):
                    if mode == 4:
                        d = float(rng.normal(0, 0.7))
                    for i in sl:
                        key[i] += d
        cost = cs2[0][0]
        st = place(key, pred, succ, q2, cost, zero)
        back = place([-(st[i] + cost[i]) for i in range(N_)], succ, pred, q2, cost, lat)
        for x in (st, place([-(back[i] + cost[i]) for i in range(N_)], pred, succ, q2, cost, zero)):
            f, info = judge(x, q2, cs2)
            if f <= now + 0.002 * (1 - it / rounds) * float(rng.exponential()):
                now, cur, q, cs = f, x, q2, cs2
            if f < best:
                best, keep = f, info
    st, q, tries = keep[4], keep[5], []
    keep = None
    for t0 in (1, 2, 3) if ALIKE else ():
        step = sorted(st[sl[3]] - st[sl[1]] for sl in slots if len(sl) == NT)
        step = step[len(step) // 2] / 2
        key, q2 = list(st), list(q)
        for sl in slots:
            by = {ops[i]["hop"]: i for i in sl}
            for t in by:
                if t and t0 in by:
                    key[by[t]], q2[by[t]] = st[by[t0]] + (t - t0) * step, q[by[t0]]
        cs2 = prices(q2)
        f, info = judge(place(key, pred, succ, q2, cs2[0][0], zero), q2, cs2)
        if info:
            tries.append((f, t0, info))
    return min(tries)[2] if tries else judge(st, q, prices(q))[1]


def polish(pgs, wakes, keep, moves, seed, temp=0.0004):
    ops = pgs[0]["ops"]
    N_, M = len(ops), len(pgs)
    seq, dyn, bmap, r0, _, q = keep
    seq, q = list(seq), list(q)
    dep = [sorted(set(o["near"]) | set(dyn.get(o["i"], ()))) for o in ops]
    snd = [o["send"] for o in ops]
    before = [set(dep[i]) | ops[i]["ord"] | ({snd[i]} if snd[i] is not None else set()) for i in range(N_)]
    sends = [i for i in seq if ops[i]["sem"] == "ls"]
    for a, b in zip(sends, sends[1:]):
        before[b].add(a)
    after = [[] for _ in ops]
    for i in range(N_):
        for d in before[i]:
            after[d].append(i)
    cost = [priced(p["ops"], q) for p in pgs]
    lat = [[o["lat"] for o in p["ops"]] for p in pgs]
    Z = N_

    def links(seq):
        prev, last = [Z] * N_, {}
        for i in seq:
            prev[i] = last.get(q[i], Z)
            last[q[i]] = i
        return prev

    def relink(p0, p1):
        pv, last = list(prev), {}
        for i in seq[p0:p1]:
            d = prev[i]
            if d == Z:
                last[was.get(i, q[i])] = Z
            elif pos[d] < p0:
                last[q[d]] = d
        for i in seq[p0:p1]:
            x = q[i]
            if x not in last:
                k = p0 - 1
                while k >= 0 and q[seq[k]] != x:
                    k -= 1
                last[x] = seq[k] if k >= 0 else Z
            pv[i] = last[x]
            last[x] = i
        k = p1
        while last and k < N_:
            i = seq[k]
            if q[i] in last:
                pv[i] = last.pop(q[i])
            k += 1
        return pv, k

    def rerun(m, p0, p1, prev, end, fin):
        c, l, w = cost[m], lat[m], wakes[m]
        k = p0
        while k < p1:
            for i in seq[k:p1]:
                t = -w
                for d in dep[i]:
                    if fin[d] > t:
                        t = fin[d]
                t += w
                d = snd[i]
                if d is not None and fin[d] > t:
                    t = fin[d]
                d = end[prev[i]]
                if d > t:
                    t = d
                t += c[i]
                if t != end[i]:
                    end[i] = t
                    fin[i] = t + l[i]
                    if far[i] > k:
                        k = far[i]
            k, p1 = p1, (k + 1 if k >= p1 else p1)
        return max(fin[i] for i in ends)

    def run(m, p0, prev, end, fin):
        c, l, w = cost[m], lat[m], wakes[m]
        for i in seq[p0:]:
            t = -w
            for d in dep[i]:
                if fin[d] > t:
                    t = fin[d]
            t += w
            d = snd[i]
            if d is not None and fin[d] > t:
                t = fin[d]
            d = end[prev[i]]
            if d > t:
                t = d
            t += c[i]
            end[i] = t
            fin[i] = t + l[i]
        return max(fin)

    def path(m):
        end, fin, c, w = E[m], Fi[m], cost[m], wakes[m]
        i = fin.index(max(fin))
        out = []
        while i != Z:
            t = end[i] - c[i]
            p = prev[i]
            if p != Z and end[p] > t - 1e-9:
                if q[i] != "RD":
                    out.append((p, i))
                i = p
                continue
            nx = Z
            for d in dep[i]:
                if fin[d] + w > t - 1e-9:
                    nx = d
            if snd[i] is not None and fin[snd[i]] > t - 1e-9:
                nx = snd[i]
            i = nx
        return out

    def tails(m):
        c, l, w = cost[m], lat[m], wakes[m]
        tl = [0.0] * (N_ + 1)
        for i in reversed(seq):
            t = tl[i]
            if t < l[i]:
                t = l[i]
            t += c[i]
            tl[i] = t
            if tl[prev[i]] < t:
                tl[prev[i]] = t
            for d in dep[i]:
                if tl[d] < t + l[d] + w:
                    tl[d] = t + l[d] + w
            d = snd[i]
            if d is not None and tl[d] < t + l[d]:
                tl[d] = t + l[d]
        return tl

    def least(m, p0, p1):
        c, l, w, end, fin, tl = cost[m], lat[m], wakes[m], E[m], Fi[m], rest[m]
        new, last, x = {}, {}, 0.0
        for i in seq[p0:p1]:
            if pos[prev[i]] < p0 and prev[i] != Z and q[prev[i]] not in last:
                last[q[prev[i]]] = end[prev[i]]
        for i in seq[p0:p1]:
            t = last.get(q[i], 0.0)
            for d in dep[i]:
                y = new.get(d, fin[d]) + w
                if y > t:
                    t = y
            d = snd[i]
            if d is not None and new.get(d, fin[d]) > t:
                t = new.get(d, fin[d])
            t += c[i]
            last[q[i]] = t
            new[i] = t = t + l[i]
            for j in waits[i]:
                if pos[j] >= p1 and t + w + tl[j] > x:
                    x = t + w + tl[j]
        for j in seq[p1:p1 + 40]:
            t = last.pop(q[j], None)
            if t is not None and t + tl[j] > x:
                x = t + tl[j]
        return x

    either = [o["i"] for o in ops if o["alt"]]
    twin, seen, slot = {}, {}, {}
    for o in ops:
        if o["st"]:
            k = (o["hop"], o["st"], o["tag"])
            seen[k] = seen.get(k, 0) + 1
            twin[o["i"]] = slot.setdefault((o["st"], o["tag"], seen[k]), {})
            twin[o["i"]][o["hop"]] = o["i"]
    waits = [[] for _ in ops]
    for i in range(N_):
        for d in dep[i]:
            waits[d].append(i)
    ahead = [dep[i] + ([snd[i]] if snd[i] is not None else []) for i in range(N_)]
    waited = set(d for a in ahead for d in a)
    ends = [i for i in range(N_) if i not in waited]
    far, was = None, {}
    prev = links(seq)
    E, Fi = [[0.0] * (N_ + 1) for _ in pgs], [[0.0] * (N_ + 1) for _ in pgs]
    r = [run(m, 0, prev, E[m], Fi[m]) for m in range(M)]
    first = [x / w for x, w in zip(r, WEIGHT)]
    now = best = 1.0
    kept = (list(seq), list(q), list(r))
    rng = np.random.default_rng(seed)
    pos = [0] * (N_ + 1)
    fresh, taken, paths, rest, m0 = 8, 0, None, None, 0
    for it in range(moves):
        if fresh and fresh % 8:
            for k in range(p0, p1):
                i = seq[k]
                pos[i] = k
                for d in ahead[i]:
                    if far[d] < k:
                        far[d] = k
                if far[prev[i]] < k:
                    far[prev[i]] = k
            paths = {}
            taken, fresh = fresh, 0
        elif fresh:
            st = [a - b for a, b in zip(E[0], cost[0])]
            seq.sort(key=lambda i: st[i])
            for k, i in enumerate(seq):
                pos[i] = k
            far = [0] * (N_ + 1)
            for k, i in enumerate(seq):
                far[prev[i]] = k
                for d in ahead[i]:
                    far[d] = k
            paths, rest = {}, {}
            taken, fresh = fresh, 0
        u = rng.random(5)
        if (not paths and taken % 8 == 0) or u[0] < 0.05:
            m0 = int(rng.integers(M))
        if m0 not in paths:
            paths[m0] = path(m0)
        if m0 not in rest:
            rest[m0] = tails(m0)
        pt = paths[m0]
        if not pt:
            continue
        a, b = pt[int(u[1] * len(pt))]
        undo, gain, quick = None, 0.0, True
        if rng.random() < (EVERY if it < moves * ALIKE else 0.05) and (a in twin and b in twin):
            p0, old, done, quick = None, list(seq), 0, False
            kind = int(u[2] * 5)
            i = a if u[3] < 0.5 else b
            if kind == 0:
                if not ops[i]["alt"]:
                    continue
                to = "V" if q[i] == "S" else "S"
                undo = [(j, q[j], [cost[m][j] for m in range(M)]) for j in twin[i].values()]
                for j in twin[i].values():
                    q[j] = to
                    for m in range(M):
                        cost[m][j] = pgs[m]["ops"][j]["alt"][to][0]
                p0 = min(pos[j] for j in twin[i].values())
            else:
                for _ in range(int(u[3] * u[3] * 4) if kind < 3 else 0):
                    if prev[a] in twin:
                        a = prev[a]
                for t in range(NT):
                    a2, b2_ = twin[a].get(t), twin[b].get(t + ops[b]["hop"] - ops[a]["hop"])
                    if a2 is None or b2_ is None or q[a2] != q[b2_] or not done <= pos[a2] < pos[b2_]:
                        continue
                    x, y = pos[a2], pos[b2_]
                    if kind < 3 and all(pos[d] < x for d in before[b2_]):
                        seq[x:y + 1] = [b2_] + old[x:y]
                    elif kind >= 3 and all(pos[d] > y for d in after[a2]):
                        seq[x:y + 1] = old[x + 1:y + 1] + [a2]
                    else:
                        continue
                    p0, done = x if p0 is None else p0, y + 1
                if p0 is None:
                    continue
            old = old[p0:]
        elif u[2] < 0.15:
            i = a if u[3] < 0.3 else b if u[3] < 0.6 else either[int(rng.integers(len(either)))]
            if not ops[i]["alt"]:
                continue
            to = "V" if q[i] == "S" else "S"
            gain = LOADW * ops[i]["alt"]["V"][0] * (1 if to == "S" else -1) / first[0]
            undo = [(i, q[i], [cost[m][i] for m in range(M)])]
            q[i] = to
            for m in range(M):
                cost[m][i] = pgs[m]["ops"][i]["alt"][to][0]
            p0 = p1 = pos[i]
            if u[2] < 0.08:
                lo = min(p1, max([pos[d] for d in before[i]] + [-1]) + 1)
                p0 = lo + int((p1 - lo) * (u[3] * 7 % 1) ** 2)
            old = seq[p0:p1 + 1]
            seq[p0:p1 + 1] = [i] + old[:-1]
        elif u[2] < 0.58:
            for _ in range(int(u[3] * u[3] * 5)):
                if prev[a] != Z:
                    a = prev[a]
            lo = max([pos[d] for d in before[b]] + [-1])
            while a != b and pos[a] <= lo:
                a = [j for j in seq[pos[a] + 1:pos[b] + 1] if q[j] == q[b]][0]
            if a == b:
                continue
            p0, p1 = pos[a], pos[b]
            old = seq[p0:p1 + 1]
            seq[p0:p1 + 1] = [b] + old[:-1]
        else:
            hi = min([pos[d] for d in after[a]] + [N_])
            if hi <= pos[b]:
                continue
            k = int(u[3] * u[3] * 5)
            for j in seq[pos[b] + 1:hi]:
                if k == 0:
                    break
                if q[j] == q[a]:
                    b = j
                    k -= 1
            p0, p1 = pos[a], pos[b]
            old = seq[p0:p1 + 1]
            seq[p0:p1 + 1] = old[1:] + [a]
        lim = now - temp * (1 - it / moves) * float(np.log(u[4] + 1e-12)) + gain
        E2, F2, r2, f = [], [], [], 0.0
        if quick and least(m0, p0, p0 + len(old)) > r[m0] + (lim - now) * first[m0] * 2 + 0.05:
            f = 1.0
        if f == 0.0:
            was = {x[0]: x[1] for x in undo or ()}
            pv, p1 = relink(p0, p0 + len(old)) if quick else (links(seq), N_)
        for m in range(M if f == 0.0 else 0):
            e, fi = list(E[m]), list(Fi[m])
            x = rerun(m, p0, p1, pv, e, fi)
            E2.append(e)
            F2.append(fi)
            r2.append(x)
            f += (x - r[m]) / first[m] / M
            if m == 0 and x > r[0] + 0.4:
                f = 1.0
                break
        if now + f <= lim:
            now, E, Fi, r, prev, fresh = now + f, E2, F2, r2, pv, taken + 1
            if now < best - 1e-9:
                best, kept = now, (list(seq), list(q), list(r))
        else:
            seq[p0:p0 + len(old)] = old
            for i, x, cs in undo or ():
                q[i] = x
                for m in range(M):
                    cost[m][i] = cs[m]
    return kept[0], dyn, bmap, kept[2], None, kept[1]


def plan(T, topo, core, rank):
    pgs, wakes = [build(T, topo, core, rank, c) for c in COSTS], [c["wake"] * 3.0 for c in COSTS]
    rng = np.random.default_rng(5)
    for p in pgs:
        by = {}
        for o in p["ops"]:
            for x in o["alt"] or (o["q"],):
                f = by.setdefault((x, o["tag"]), float(np.exp(rng.normal(0, ROUGH))))
                if o["alt"]:
                    o["alt"][x] = (o["alt"][x][0] * f, o["alt"][x][1])
                if x == o["q"]:
                    o["cost"] *= f
    starts = [polish(pgs, wakes, schedule(pgs, wakes, ROUNDS, s), MOVES[0], s, 0.001) for s in SEEDS]
    return polish(pgs, wakes, min(starts, key=lambda k: sum(x / y for x, y in zip(k[3], starts[0][3]))), MOVES[1], 1, 0.0008)


def emit(pg, keep, g, T):
    ops = pg["ops"]
    seq, dyn, bmap = keep[:3]
    pg["bmap"].update(bmap)
    pg["last"].update({ops[i]["tiles"][0]: i for i in seq if ops[i]["free"]}.values())
    eng = {"V": g.vector, "S": g.scalar, "P": g.tensor, "G": g, "Y": g.sync}
    pos, key, know, count, qk = {}, {}, {}, {}, {}
    for i in seq:
        o = ops[i]
        q = keep[5][i]
        if o["sem"] is None:
            count[q] = count.get(q, 0) + 1
            key[i], pos[i] = q, count[q]
        else:
            key[i], pos[i] = o["sem"], o["val"]
        dep = sorted(o["dep"] | set(dyn.get(i, ())))
        kn = qk.setdefault(q, {})
        if q[0] != "R":
            need = {}
            for d in dep:
                if kn.get(key[d], 0) < pos[d] and need.get(key[d], 0) < pos[d]:
                    need[key[d]] = pos[d]
            ds = [d for d in dep if need.get(key[d], 0) == pos[d]]
            for d in ds:
                for d2 in ds:
                    if key[d] != key[d2] and key[d] in need and key[d2] in need and know[d2].get(key[d], 0) >= pos[d]:
                        need.pop(key[d])
            for kk in sorted(need):
                eng[q].wait_ge(T.sem[kk], int(need[kk]))
            for d in dep:
                for kk, v in know[d].items():
                    if kn.get(kk, 0) < v:
                        kn[kk] = v
            ins = (o["alt"][q][1] if o["alt"] else o["fn"])(eng[q])
            if o["sem"] is None:
                ins.then_inc(T.sem[q], 1)
        me = dict(kn) if o["send"] is None else {}
        me[key[i]] = max(me.get(key[i], 0), pos[i])
        know[i] = me
    for q in "VSPG":
        g.wait_ge(T.sem[q], int(count[q]))


def build(T, topo, core, rank, CO=COSTS[0]):
    pg = {"ops": [], "acc": {}, "rr": [0], "st": "", "hop": 0, "last": set(), "bmap": {"c0": NB, "c1": NB + 1}}
    CY, GC, PEC, FIX = CO["cy"], CO["gather"], CO["pe"], CO

    def ap(r):
        name, c0, c1, step, p0, p1, ps = r
        t = T["bank%d" % pg["bmap"][name]] if name in pg["bmap"] else T[name]
        rows = slice(p0, p1) if ps == 1 else slice(p0, p1, ps)
        cols = slice(c0, c1) if step == 1 else slice(c0, c1, step) if step > 0 else slice(c1 - 1, c0 - 1 if c0 else None, step)
        return t[rows, cols]

    def cnt(r):
        return (r[2] - r[1] + abs(r[3]) - 1) // abs(r[3])

    def two(*rs):
        return all(r[0][0] == "c" if is_psum(r[0]) else SCRATCH[r[0]][2] in (b2, h2, u2) for r in rs)

    def inap(x):
        if x[0] == "ind":
            return ap(x[1]).indirect(ap(x[2]))
        return ap(x)

    def regs(x):
        return [x[1], x[2]] if x[0] == "ind" else [x]

    def dcol(s):
        return ap(s) if isinstance(s, tuple) else s

    def vcost(e, c, ind):
        return FIX["V"] + CY * max(64, e * (GC if ind else c)) + (0.04 if ind else 0)

    def ts(out, in0, s1, op0, s2=None, op1=None):
        ind = in0[0] == "ind"
        sc = [s for s in (s1, s2) if isinstance(s, tuple)]
        c = 0.5 if (not ind and two(out, in0)) else 1
        if op1 is None:
            fn = lambda e: e.tensor_scalar(ap(out), inap(in0), dcol(s1), None, op0)
        else:
            fn = lambda e: e.tensor_scalar(ap(out), inap(in0), dcol(s1), dcol(s2), op0, op1)
        return add(pg, "V", vcost(cnt(out), c, ind), fn, regs(in0) + sc, [out], tag="ts " + out[0])

    def tt(out, a, b, op):
        ind = a[0] == "ind"
        ps = any(is_psum(r[0]) for r in (a, b) if r[0] != "ind")
        return add(pg, "V", vcost(cnt(out), 1 if ps else 2, ind), lambda e: e.tensor_tensor(ap(out), inap(a), ap(b), op), regs(a) + [b], [out], tag="tt " + out[0])

    def cp(out, a):
        ind = a[0] == "ind"
        return add(pg, "V", vcost(cnt(out), 0.5 if (not ind and two(out, a)) else 1, ind), lambda e: e.tensor_copy(ap(out), inap(a)), regs(a), [out], tag="cp " + out[0])

    def scan(out, d0, d1, init, op0, op1):
        return add(pg, "V", vcost(cnt(out), 0.5 if two(out, d0, d1) else 1, False), lambda e: e.tensor_tensor_scan(ap(out), ap(d0), ap(d1), init, op0, op1), [d0, d1], [out], tag="scan " + out[0])

    def fill(out, c):
        return add(pg, "V", vcost(cnt(out), 0.5 if two(out) else 1, False), lambda e: e.memset(ap(out), c), [], [out], tag="fill " + out[0])

    def act(out, in_, func, bias=0.0, scale=1.0):
        ind = in_[0] == "ind"
        sc = [s for s in (bias, scale) if isinstance(s, tuple)]
        return add(pg, "S", FIX["S"] + CY * max(64, cnt(out) * (GC if ind else 1)) + (0.04 if ind else 0),
                   lambda e: e.activation(ap(out), inap(in_), func, bias=dcol(bias), scale=dcol(scale)), regs(in_) + sc, [out], tag="act " + out[0])

    def flex(q, out, in_, bias=0.0, scale=1.0, relu=False, size=False):
        ind = in_[0] == "ind"
        sc = [s for s in (bias, scale) if isinstance(s, tuple)]
        if scale == 1.0:
            fv = (lambda e: e.tensor_scalar(ap(out), inap(in_), dcol(bias), None, A.add)) if bias else (lambda e: e.tensor_copy(ap(out), inap(in_)))
        else:
            fv = lambda e: e.tensor_scalar(ap(out), inap(in_), dcol(scale), dcol(bias), A.mult, A.add)
        fs = lambda e: e.activation(ap(out), inap(in_), F.Relu if relu else F.Identity if bias else F.Copy, bias=dcol(bias), scale=dcol(scale))
        if relu:
            fv = lambda e: e.tensor_scalar(ap(out), inap(in_), 0.0, None, A.max)
        if size:
            fv = lambda e: e.tensor_scalar(ap(out), inap(in_), 0.0, None, A.not_equal)
            fs = lambda e: e.activation(ap(out), inap(in_), F.Abs)
        alt = {"V": (vcost(cnt(out), 0.5 if (not ind and two(out, in_)) else 1, ind), fv),
               "S": (FIX["S"] + CY * max(64, cnt(out) * (GC if ind else 1)) + (0.04 if ind else 0), fs)}
        if pg["st"] and cnt(out) <= 384:
            q = "V" if ind else "S"
        return add(pg, q, alt[q][0], None, regs(in_) + sc, [out], tag="flex " + out[0], alt=alt)

    def pe(mms, sub=False, free=False):
        cost = 0.0
        rd, wr = {}, {}
        for out, l, r, s, e_ in mms:
            k = 4 if SCRATCH[l[0]][2] == f4 else 1
            cost += PEC * k * max(min(64, cnt(l)), cnt(r)) + 0.006
            for x in (l, r):
                if sub:
                    rd[x] = x
                    continue
                y = rd.get(x[0])
                rd[x[0]] = (x[0], min(x[1], y[1]) if y else x[1], max(x[2], y[2]) if y else x[2], 1, 0, 128, 1)
            y = wr.get(out[0])
            wr[out[0]] = (out[0], min(out[1], y[1]) if y else out[1], max(out[2], y[2]) if y else out[2], 1, 0, 128, 1)

        me = len(pg["ops"])

        def fn(e):
            ins = None
            for j, (out, l, r, s, e_) in enumerate(mms):
                ins = e.matmul(ap(out), ap(l), ap(r), s, e_ or (j == len(mms) - 1 and me in pg["last"]))
            return ins
        return add(pg, "P", cost + FIX["P"] / 2, fn, list(rd.values()), list(wr.values()), tag="pe " + mms[0][1][0] + " " + mms[0][2][0], free=free)

    def acc(out, *pairs):
        return [(out, l, r, i == 0, i == len(pairs) - 1) for i, (l, r) in enumerate(pairs)]

    def grp(*mms):
        return [(o, l, r, i == 0, i == len(mms) - 1) for i, (o, l, r) in enumerate(mms)]

    def bank(kind="b"):
        pg["rr"][0] += 1
        return kind + "%d" % (99 + pg["rr"][0])

    def load(name, out, src, lat, q="Y"):
        s = "ld_" + name
        return add(pg, q, 0.1, lambda e: e.dma_start(ap(out), src).then_inc(T.sem[s], 16), [], [out], sem=s, val=16, lat=lat * CO["load"], tag="load " + name)

    nout = [0]

    def store(dst, in_, q="Y"):
        nout[0] += 16
        return add(pg, q, 0.1, lambda e: e.dma_start(dst, ap(in_)).then_inc(T.sem["out"], 16), [in_], [], sem="out", val=nout[0], lat=2.5, tag="store")

    dst = T.cores[(rank + 1) % 4]
    rid, pid, _se = topo.addr(dst)
    mask = sum(1 << e for e in topo.engines(core, dst))
    neng = len(topo.engines(core, dst))
    nls, sent = [0], [None]

    def send(kind, t, h, out, in_):
        s = "r%s_%d_%d" % (kind, t, h)
        nls[0] += neng
        i = add(pg, "G", CO["issue"] * (1 if sent[0] else 8), lambda e: e.remote_dma(ap(out), ap(in_), T.sem[s], T.sem["ls"], pid, rid, mask), [in_], [], sem="ls", val=nls[0], tag="send " + kind)
        d = add(pg, "RD", CO["row"] * {"v": 0.8, "z": 1.3, "f": 1.6}[kind], None, [], [], sem="-", lat=CO["link"] - 0.3, tag="rows " + kind)
        j = add(pg, "R" + s, 0.0, None, [], [out], sem=s, val=neng)
        pg["ops"][d]["send"], pg["ops"][j]["send"] = i, d
        if kind == "f":
            pg["ops"][i]["ord"].add(sent[0])
        sent[0] = i

    sm = lambda name, h, w=8, x=0, k=8: ref(name, h * w + x, h * w + x + k)
    tl = lambda name, h: ref(name, h * n, h * n + n)
    full = lambda name: ref(name, 0, SCRATCH[name][1][1])

    what = {"v0": (ref("VZ", 0, 256, 1, 0, 8), T.v0[:, :], 0.02), "d0": (ref("VZ", 256, 512, 1, 0, 8), T.d0[:, :], 0.02),
            "wt": (ref("WT", 0, 1), T.wt[:, :], 0.15), "kap": (ref("WT", 1, 2), T.kap[:, :], 0.15)}
    for h in range(2):
        what["px%d" % h] = (ref("PX", NOH + 2048 * h, NOH + 2048 * h + 2048), T.px[:, 2048 * h:2048 * h + 2048], 1.5)
        what["vw%d" % h] = (ref("VW", 1024 * h, 1024 * h + 1024), T.vw[:, 1024 * h:1024 * h + 1024], 1.5)
        what["z%d" % h] = (ref("XZ", h * XW + 32, h * XW + 32 + n), T.z0[:, h * n:h * n + n], 0.2)
        what["f%d" % h] = (ref("W", h * WW + n, h * WW + 2 * n), T.f0[:, h * n:h * n + n], 0.25)
    loads, small, at = [], [], 2.0
    for k, nm in enumerate(SMALL):
        small.append(load(nm, what[nm][0], what[nm][1], 2.2 + 0.1 * k, "S"))
    for k, nm in enumerate(LOADS[len(SMALL):]):
        at = max(at, 2.0 + 0.1 * k) + what[nm][2] + (0.1 * len(SMALL) if k == 0 else 0.0)
        loads.append(load(nm, what[nm][0], what[nm][1], at - 0.1 * k))
    for x in (loads, small):
        for a, b in zip(x, x[1:]):
            pg["ops"][b]["ord"].add(a)

    def sel(out, in_, pat, cmp, fillv, base, cm):
        return add(pg, "G", 0.2 + 2 * CY * cnt(out), lambda e: e.affine_select(ap(out), ap(in_), pat, cmp, fillv, base, cm), [in_], [out], tag="sel " + out[0])

    def iota(out, pat, base, cm, small=True):
        if small:
            fn = lambda e: e.iota(ap(out), pat, base, cm, allow_small_or_imprecise_dtypes=True)
        else:
            fn = lambda e: e.iota(ap(out), pat, base, cm)
        return add(pg, "G", 0.15 + 2 * CY * cnt(out), fn, [], [out], tag="iota " + out[0])

    Ib, on = full("Ib"), ref("ON", 0, 128)
    const = lambda out, c: flex("S", out, ref("ON", 0, cnt(out)), 0.0, float(c))
    fill(full("ON"), 1.0)
    sel(Ib, on, [[-1, 128]], A.is_equal, 0.0, 0, 1)
    sel(ref("B8", 0, 144, 1, 0, 8), ref("ON", 0, 144, 1, 0, 8), [[1, 144]], A.is_equal, 0.0, -15, -16)
    sel(full("BO"), on, [[-16, 8], [0, 16]], A.is_ge, 0.0, 0, 1)
    sel(full("BO"), full("BO"), [[16, 8], [0, 16]], A.is_ge, 0.0, 15, -1)
    iota(ref("PI", 0, 1), [[0, 1]], 0, 1, False)
    iota(full("IJ"), [[1, 16]], 0, 0)
    iota(ref("CMI", 0, 8), [[16, 8]], 0, 0)
    fill(ref("W613", 0, 8), -1.0)
    iota(ref("W613", 8, 1032), [[613, 1024]], HC - 2 ** 23, 0)
    act(ref("W613", 1032, 2056), ref("W613", 8, 1032), F.Identity, 613.0 * 1024)
    act(ref("W613", 2056, 4104), ref("W613", 8, 2056), F.Identity, 613.0 * 2048)
    iota(full("MK"), [[0, n], [256, 16 // QST]], 0, 0)
    fill(full("QS"), 0.0)
    fill(full("KC"), 0.0)
    iota(ref("KC", 0, 128, 1, 0, 1), [[0, 8], [1, 16]], 0, 0)
    fill(ref("KC", 15, 128, 16, 32, 33), -65536.0)
    fill(full("SEL"), 0.0)
    for a in range(0, 16, 4):
        x = ref("SEL", 128 * a, 128 * a + 512)
        sel(x, x, [[-1, 4], [-16, 8], [0, 16]], A.not_equal, 1.0, -a, 1)
    ts(ref("CL", 0, 8), ref("CMI", 0, 8), 15.0, A.add)
    iota(full("RST"), [[0, 128]], 0, 0)
    sel(full("RST"), full("RST"), [[0, 8], [1, 16]], A.not_equal, 1048576.0, 0, 0)
    for i, c in enumerate((1, 0, -99)):
        const(ref("CS", 8 * i, 8 * i + 8), c)
    for nm in DIAG:
        if nm != "Ib":
            flex("S", full(nm), Ib, 0.0, DIAG[nm][0])
    ts(ref("PI", 16, 17), ref("PI", 0, 1), 15, A.bitwise_and)
    ts(ref("PI", 24, 25), ref("PI", 0, 1), 1, A.bitwise_and)
    pm, sg, sg256, low, lowe, lowh = [ref("PC", 4 * i, 4 * i + 1) for i in range(6)]
    cp(pm, ref("PI", 16, 17))
    ts(low, pm, 15.0, A.is_equal, 4096.0, A.mult)
    flex("S", lowe, low, 4096.0)
    flex("S", lowh, low, -2048.0, -1.0)
    ts(sg, ref("PI", 24, 25), -2.0 / 128, A.mult, 1.0 / 128, A.add)
    ts(sg256, ref("PI", 24, 25), -2.0 / 128, A.mult, 257.0 / 128, A.add)
    iota(full("SPT"), [[0, 8], [16, 2]], 4096, 0)
    iota(full("SPU"), [[0, 4], [16, 4]], 4096, 0)
    flex("S", full("SPU"), full("SPU"), pm)
    flex("S", full("SPT"), full("SPT"), pm)
    const(ref("CK", 0, 16), 18432)
    const(ref("CK", 16, 24), 8192)
    ts(full("G0"), Ib, sg, A.mult)
    ts(full("G256"), Ib, sg256, A.mult)
    cp(ref("WTf", 0, 2), full("WT"))
    ts(ref("WTf", 4, 5), ref("WTf", 1, 2), 1.0 / 32, A.mult)
    wcol, kcol = ref("WTf", 0, 1), ref("WTf", 4, 5)
    ts(full("WB"), full("BO"), wcol, A.mult)
    if len(XT) < 3:
        fill(full("Bh"), 0.0)
        cp(ref("Bh", 15, 143, 16), ref("BO", 0, 128, 16))
    flex("S", full("WBn"), full("WB"), 0.0, -1.0)
    fill(full("CH"), M35 / 128)
    fill(full("CHn"), -M35 / 128)
    const(full("CQ"), 16 * MAGIC / 128)
    const(full("CQn"), -16 * MAGIC / 128)
    fill(full("C1"), 16.0)
    fill(ref("C1", 0, 128, 1, 0, 1), 15.5)
    const(full("CN"), -32)
    const(full("CP"), -4096)
    flex("V", full("Bm32"), ref("BO", 0, 128, 16), 0.0, -32.0)
    flex("V", full("B16"), ref("BO", 0, 128, 16), 0.0, 16.0)
    const(ref("CP", 15, 128, 16), -4096 - 512)
    const(full("Cm2"), -2)
    flex("V", full("MP"), full("BO"), 0.0, 524288.0)
    tt(full("MP"), full("MP"), full("Ibig"), A.add)
    ts(ref("CM", 0, 8), ref("CMI", 0, 8), pm, A.add)
    ts(ref("CM", 8, 16), ref("CMI", 0, 8), pm, A.add)
    const(ref("CMF", 0, 8), 256)
    ts(ref("CMF", 8, 16), ref("CMI", 0, 8), pm, A.add, 128.0, A.add)
    flex("S", ref("Sb", 0, 128, 2), ref("Ib", 1, 128, 2))
    flex("S", ref("Sb", 1, 128, 2), ref("Ib", 0, 128, 2))
    flex("S", full("Sb100"), full("Sb"), 0.0, 100.0 / 128)
    fill(ref("VI", 4096, 4096 + 64), 0)
    fill(ref("PX", 0, 16), 0.0)
    ts(ref("PX", 16, 32), full("IJ"), pm, A.is_equal)
    w = 16
    while w < OH0:
        cp(ref("PX", 16 + w, 16 + 2 * w), ref("PX", 16, 16 + w))
        w *= 2
    for a in range(w, 4096, w):
        i = add(pg, "Y", 0.1, lambda e, a=a: e.dma_start(ap(ref("PX", 16 + a, 16 + a + w)), ap(ref("PX", 16, 16 + w))).then_inc(T.sem["oh"], 16),
                [ref("PX", 16, 16 + w)], [ref("PX", 16 + a, 16 + a + w)], sem="oh", val=16 * (4096 // w - 1), lat=9.5, tag="copy")
        pg["ops"][i]["ord"].add(loads[-1])
    fill(full("D0"), 0.0)
    fill(ref("D0", 0, 384, 48), 1.0)
    fill(ref("D0", 16, 384, 48), 1.0)
    fill(ref("D0", 384, 512, 32), 1.0)
    const(ref("TRI", 384, 512), 0)
    ts(ref("TRI", 0, 16), full("IJ"), pm, A.is_ge, 16384.0, A.mult)
    fill(ref("TRI", 16, 32), 0.0)
    cp(ref("TRI", 32, 48), ref("TRI", 0, 16))
    for a in (48, 96, 192):
        flex("S", ref("TRI", a, 2 * a), ref("TRI", 0, a))

    def ots(out, tile, first=(), last=()):
        prs = list(first)
        for j in range(16):
            prs.append((ref("Bh", 15 - j, 143 - j), ref(tile[0], tile[1] + j, tile[2], 16)))
        return acc(out, *(prs + list(last)))

    cp(full("Bf"), ref("BO", 0, n, 16))

    def xts(b, tile, first=(), ones=ref("BO", 0, n, 16)):
        mm = [(ref(b, 0, n, 1, 0, 8), l, r, i == 0, False) for i, (l, r) in enumerate(first)]
        return mm + [(ref(b, j, n, 16, 0, 8), ref(tile[0], tile[1] + j, tile[2], 16), ones, not first, j == 15 or not first) for j in range(16)]

    I8 = ref("Ib", 0, 8, 1, 0, 8)
    xl = lambda name, h: ref(name, h * n, h * n + n, 1, 0, 8)

    flex("V", ref("VZh", 0, 512, 1, 0, 8), ref("VZ", 0, 512, 1, 0, 8), -2048.0)
    b6 = bank()
    pe(acc(ref(b6, 0, 32), *[(ref("B8", 15 - j, 143 - j, 1, 0, 8), ref("VZh", j, 512, 16, 0, 8)) for j in range(16)]))
    flex("V", ref("VH", 0, 16), ref(b6, 0, 16), 2048.0)
    for h in (1, 0):
        flex("S", ref("XZ", h * XW, h * XW + 8), ref(b6, 16 + 8 * h, 24 + 8 * h), 2048.0)
        fill(ref("XZ", h * XW + 8, h * XW + 16), 0.0)
        flex("S", ref("XZ", h * XW + 16, h * XW + 32), full("CMF"))
    for c in range(0, 2048, 512):
        x = ref("VW", c, c + 512)
        ts(ref("VI", c, c + 512), x, 4095, A.bitwise_and)
        ts(ref("VI", 2048 + c, 2560 + c), x, 12, A.arith_shift_right)

    def tiles(t, h):
        k = 2 * t + h
        x0, w0, z0 = k * XW, k * WW, k * (32 + n)
        cm = (3, 2) if WIDE and t < NT - 1 else (2, 3)
        d = {"st": lambda j, w=1: ref("XZ", x0 + 8 * j, x0 + 8 * (j + w)), "z": ref("XZ", x0 + 32, x0 + 32 + n), "x": ref("XZ", x0 + 32 + n, x0 + 32 + 2 * n),
             "hz": ref("XZ", x0 + 32 + 2 * n, x0 + 32 + 3 * n), "xz": ref("XZ", x0 + 32, x0 + 32 + 2 * n), "xzh": ref("XZ", x0 + 32, x0 + 32 + 3 * n),
             "hd": ref("W", w0, w0 + n), "f": ref("W", w0 + n, w0 + 2 * n), "c": ref("W", w0 + cm[0] * n, w0 + cm[0] * n + n), "mm": ref("W", w0 + cm[1] * n, w0 + cm[1] * n + n),
             "w2": ref("W", w0, w0 + 2 * n), "w3": ref("W", w0, w0 + 3 * n), "vh": ref("VH", 8 * k, 8 * k + 8),
             "land": ref("XZ", x0, x0 + 32 + n), "fb": ref("FB", k * n, k * n + n), "vb": ref("VB", 8 * k, 8 * k + 8)}
        if t < NT - 1:
            d.update({"zb": ref("ZB", z0, z0 + 32 + n), "zf": ref("ZB", z0 + 32, z0 + 32 + n), "zc": ref("ZB", z0, z0 + 32)})
        else:
            d["zf"] = tl("ZL", h)
        return d

    px, views = ref("PX", NOH, NOH + 4096), ref("VI", 0, 4096)
    px2 = ref("PX", NOH, NOH + 8192)
    pxe = ref("PX", NOH - 4096, NOH + 8192)
    for c in range(0, 4096, LOWP):
        flex("S", ref("PX", NOH + 4096 + c, NOH + 4096 + c + LOWP), ref("PX", NOH + c, NOH + c + LOWP), -256.0)
    banks = {}

    def mark(name, h):
        pg["st"] = name + str(h)

    def front(t, h):
        L = tiles(t, h)
        vh = L["vh"]
        mark("hp", h)
        a, c = tl("HI1", h), tl("HI2", h)
        y = ref(bank(), 0, n)
        mm = acc(y, (full("WBn"), L["z"]), (full("C1"), on), (full("CH"), on), (full("CHn"), on), (full("WB"), L["z"]))
        pe(mm[:3])
        pe(mm[3:])
        flex("S", a, y, -(HC + 31.0 / 64), kcol)
        mark("ha", h)
        tt(c, ("ind", ref("W613", 8, 4104), vh), a, A.add)
        ts(L["hd"], c, 4095, A.bitwise_and)
        mark("fr", h)
        flex("S", L["x"], ("ind", px, vh))
        bk = bank()
        dx, hz = ref(bk, 0, n), ref(bk, n, 2 * n)
        idx = pe(acc(dx, (full("Icn"), L["z"]), (full("Ic"), L["x"])))
        ts(tl("IND", h), dx, MAGIC, A.add, MAGIC, A.is_equal)
        mark("hz", h)
        pe(acc(hz, (full("Ihz"), L["z"]), (full("Ihz"), L["x"])))
        if "hz%d" % h in ONV:
            ts(L["hz"], hz, MAGIC, A.add, -MAGIC, A.add)
        else:
            act(tl("T2", h), hz, F.Identity, MAGIC)
            act(L["hz"], tl("T2", h), F.Identity, -MAGIC)
        mark("fr", h)
        lk = sm("LK", h)
        if "c" in XT:
            b = bank()
            mm = xts(b, tl("IND", h), [(L["st"](1), full("In")), (L["st"](2), Ib)] if t else [])
            if t:
                pg["ops"][pe(mm[:2])]["ord"].add(idx)
            pe(mm[-16:])
            ts(xl("XL", h), ref(b, 0, n, 1, 0, 8), 264.5 if t else 8.5, A.is_ge, 128.0, A.mult)
            b = bank()
            pe(grp((ref(b, 0, 16), Ib, full("CM")), (ref(b, 0, 8), xl("XL", h), I8), (ref(b, 8, 16), xl("XL", h), ref("I2", 0, 8, 1, 0, 8)))
               + [(ref(b, 16, 24), xl("XL", h), I8, True, True)])
            tt(sm("LSF", h, 16, 0, 16), ref(b, 0, 16), L["st"](2, 2), A.min)
            flex("V", lk, ref(b, 16, 24))
        else:
            ct = ref(bank(), 0, 8)
            pe(ots(ct, tl("IND", h), [(full("In"), L["st"](1)), (full("I2"), L["st"](2))]))
            ts(lk, ct, 8.5, A.is_ge, 128.0, A.mult)
            tt(sm("LSL", h), lk, ref("CM", 0, 8), A.add)
        mark("h", h)
        flex("V", ref("HEL", 2 * h * n, 2 * h * n + n), ("ind", L["w2"], sm("LSF", h, 16, 8)), low)
        mark("hm", h)
        flex("S", tl("H16", h), ref("HEL", 2 * h * n, 2 * h * n + n), lowh)
        mark("qx", h)
        q0 = h * 16 * n
        st, cuts = QG[h]
        w = 16 // st
        qs = ref("QS", 0, 8 * n, 8)
        flex("V", qs, ("ind", L["xz"], sm("LSF", h, 16)))
        banks[h] = (bank(), bank(), bank())
        pe(acc(ref(banks[h][2], 0, n), (full("Cm2"), on), (Ib, qs)))
        for a, e_ in QSCAN:
            scan(ref("QX", q0 + 16 * a, q0 + 16 * e_, st), ref("MK", 8 * a, 8 * e_, st // 2), ref("QS", 8 * a, 8 * e_, st // 2), 0.0, A.min, A.add)
        for a, e_ in cuts:
            for r in range(1, st):
                out, src = ref("QX", q0 + 16 * a + r, q0 + 16 * e_, st), ref("QX", q0 + 16 * a, q0 + 16 * e_, st)
                if a < QV[h]:
                    flex("V", out, src)
                else:
                    sel(out, src, [[0, w * (e_ - a)]], A.is_ge, 0.0, 0, 0)
        mark("e", h)
        flex("S", ref("HEL", (2 * h + 1) * n, (2 * h + 2) * n), ("ind", views, vh), lowe if t else low)

    def dedupe(t):
        mark("dd", 0)
        vh = ref("VH", 16 * t, 16 * t + 16)
        flex("S", full("VF"), vh, -2048.0)
        b = bank()
        mm, ns = [], 32 if t in BIG else 24
        for j, (c, d) in enumerate(((0, 0), (0, 1), (1, 1))):
            mm += acc(ref(b, j, 24, 3), (Ib, ref("VF", c, 16, 2)), (full("I8k"), ref("LK", c, 16, 2)))
            mm += acc(ref(b, ns + j, ns + 24, 3), (Ib, ref("VF", d, 16, 2)), (Ib, ref("CK", 16, 24)))
        big = t in BIG
        for j, (c, d) in enumerate(((0, 2), (1, 2), (0, 3), (1, 3)) if big else ()):
            mm += acc(ref(b, 24 + j, 32, 4), (Ib, ref("VF", c, 8, 4)), (full("I8k"), ref("LK", c, 8, 4)))
            mm += acc(ref(b, 56 + j, 64, 4), (Ib, ref("VF", d, 8, 4)), (Ib, ref("CK", 16, 18)))
        for j in range(0, len(mm), 6):
            pe(mm[j:j + 6])
        flex("S", ref("WD", 0, 2 * ns), ref(b, 0, 2 * ns), -8192.0)
        b = bank()
        for j0 in range(0, 16, SELP):
            pe([(ref(b, 0, 16 * ns), Ib, ref("TRI", 0, 16 * ns), True, False)][j0:] + [(ref(b, j, 16 * ns, 16), l, r, False, j == 15 and r[1] == ns) for j in range(j0, j0 + SELP)
                for l, r in ((ref("SEL", 128 * j, 128 * j + 128), ref("WD", 0, ns)), (full("In"), ref("WD", ns, 2 * ns)))])
        flex("S", ref("EQ", 0, 16 * ns), ref(b, 0, 16 * ns), size=True)
        scan(ref("DS", 0, 16 * ns), ref("D0", 0, 16 * ns), ref("EQ", 0, 16 * ns), 0.0, A.max, A.min)
        b = bank()
        more = [x for d in (2, 3) for x in ((ref(b, d, 8, 4), Ib, ref("CK", 16, 18)), (ref(b, d, 8, 4), full("In8192"), ref("DS", 351 + 32 * d, 512, 64)))] if big else []
        pe(grp((ref(b, 0, 16), Ib, ref("CK", 0, 16)), (ref(b, 0, 16), Ib, full("VF")), (ref(b, 0, 16), full("I8kn"), full("LK")), *more,
               (ref(b, 0, 16, 2), full("In8192"), ref("DS", 15, 384, 48)), (ref(b, 1, 16, 2), full("In8192"), ref("DS", 47, 384, 48))))
        tt(full("OFF"), ref(b, 0, 16), full("SPU" if big else "SPT"), A.min)

    def early(t, h):
        mark("ea", h)
        L = tiles(t, h)
        lk, ov = sm("LK", h), sm("OV", h)
        Sb, Ip, Im = full("Sb"), full("Ip100"), full("Im100")
        po = ref(bank(), 0, 8)
        pe(acc(po, (Ib, L["st"](0)), (full("Sb100"), lk), (Im, lk)))
        ts(ov, po, 100.5, A.is_ge, 128.0, A.mult)
        b = bank()
        w = 8 if t < NT - 1 else 16
        idx = pe(grp(*[(ref(b, 0, w), Ib, ref("CM", 0, w)), (ref(b, 0, 8), full("I2"), lk), (ref(b, 0, 8), full("G256"), ov), (ref(b, 8, 16), full("G0"), ov)][:3 + w // 16]))
        flex("V", sm("TLL", h, 16, 0, w), ref(b, 0, w))
        flex("S", L["zf"], ("ind", L["xzh"], sm("TLL", h, 16)))
        mark("st", h)
        b = bank()
        blk = lambda j, w=1: ref(b, 8 * j, 8 * (j + w))
        pe(grp((blk(0, 3), Ib, full("CS")), (blk(0, 2), Ib, L["st"](0, 2)), (blk(2), Sb, L["st"](1)), (blk(0), Im, lk), (blk(1), full("I1"), lk),
               (blk(0), Im, ov), (blk(1), Im, ov), (blk(2), Ip, ov)))
        ra = lambda j, w=1: sm("RA", h, 24, 8 * j, 8 * w)
        flex("S", ra(0, 3), blk(0, 3), relu=True)
        b = bank()
        if t < NT - 1:
            pe(grp((blk(0, 2), Ib, ra(0, 2)), (blk(1), Ib, ra(2)))
               + grp((blk(2, 2), Ib, full("CMF")), (blk(2), full("Ifl"), ra(1)), (blk(2), full("Ifl"), ra(2)), (blk(3), full("G0"), ov)))
            ts(L["zc"], blk(0, 4), MAGIC, A.add, -MAGIC, A.add)
            send("z", t + 1, h, tiles(t + 1, h)["land"], L["zb"])
        else:
            pe(acc(blk(0), (full("I16"), ra(1)), (full("I16"), ra(2)), (Ib, ra(0))))
            act(sm("YC", h), blk(0), F.Copy)
            if h == 0:
                b = ref(bank(), 0, n, 1, 0, 16)
                pe([(b, full("YC"), Ib, True, True)])
                act(ref("YU", 0, n, 1, 0, 16), b, F.Copy)
                for g_ in range(8):
                    store(T.yc[g_, :], ref("YU", 16 * g_, 16 * g_ + 16, 1, 0, 16))
            act(ref("YU", 1024 + h * n, 1024 + h * n + n), L["zf"], F.Copy)
            store(T.yz[:, h * n:h * n + n], ref("YU", 1024 + h * n, 1024 + h * n + n))
        mark("kk", h)
        y = ref(bank(), 0, 8)
        if "k" in XT or t == 0:
            b = bank()
            pe(xts(b, L["zf"]))
            flex("S", xl("XK", h), ref(b, 0, n, 1, 0, 8), -2048.0)
            off = [(xl("XK", h), ref("In", 0, 8, 1, 0, 8)), (full("CQ"), ref("ON", 0, 8)), (full("CQn"), ref("ON", 0, 8))] if t == 0 else []
            pe(acc(y, *off, (full("I8k"), lk), (full("I8200"), ov), (xl("XK", h), I8)))
        else:
            mm = ots(y, L["zf"], [(full("I8k"), lk), (full("I8200"), ov)])
            pe(mm[:10])
            pe(mm[10:])
        flex("S", sm("KL", h), y, t + 16.0 - 8192.0 + (16.0 if t == 0 else 2048.0 if "k" in XT else 0.0))
        flex("S", tl("OHL", h), ("ind", ref("PX", 0, NOH if t else 80), sm("KL", h)))

    def bulk(t, h, w):
        mark("he"[w] + "b", h)
        q0, l0 = h * 16 * n, (2 * h + w) * n
        G, M = ("GH", "MH") if w == 0 else ("GE", "ME")
        b = banks[h][w]
        for a, e_, q in PARTS[h][w]:
            g_, off = ref(G, q0 + 16 * a, q0 + 16 * e_), ref("HEL", l0 + a, l0 + e_)
            flex(q, g_, ("ind", pxe if w and t else px2, off))
        first = [(ref(b, 0, n), on, full("CP" if w else "KC"), True, False)]
        for k0 in range(0, 16, SPLIT):
            pe(first[k0:] + [(ref(b, k, n, 16), ref(G, q0 + k, q0 + 16 * n, 16), full("B16"), False, False) for k in range(k0, k0 + SPLIT)], free=k0 > 0)
        for a, e_ in CHUNKS[h][w]:
            lo, hi = q0 + 16 * a, q0 + 16 * e_
            scan(ref(M, lo, hi), ref("QX", lo, hi), ref(G, lo, hi), 0.0, A.max, A.min)
        pe([(ref(b, 0, n), tl("OHL", h), full("Ibig" if w == 0 else "MP"), False, False)], free=True)
        for a, e_ in SUMS[h][w]:
            tt(ref("ML", l0 + a, l0 + e_), ref(G, q0 + 16 * a + 15, q0 + 16 * e_, 16), ref(banks[h][2], a, e_), A.min)
            step = SPLIT if e_ - a > 32 else 16
            for k0 in range(0, 16, step):
                i = pe([(ref(b, k, n, 16, a, e_), ref(M, q0 + 16 * a + k, q0 + 16 * e_, 16) if k < 15 else ref("ML", l0 + a, l0 + e_), full("Bm32"), False, False)
                        for k in range(k0, k0 + step)], free=True)
        return i

    def tail(t, h):
        L = tiles(t, h)
        key = tl("KEY", h)
        ph, pd = ref(banks[h][0], 0, n), ref(banks[h][1], 0, n)
        last = bulk(t, h, 0)
        mark("km", h)
        if h in LATE:
            scan(tl("PM", h), full("RST"), ph, 0.0, A.add, A.min)
            back = lambda x: ref(x, h * n, h * n + n, -1)
            scan(back("RB"), full("RST"), back("PM"), 0.0, A.add, A.min)
            tt(tl("OHT", h), tl("RB", h), ph, A.is_equal)
        else:
            flex("S", key, ph)
            scan(tl("PM", h), full("RST"), key, 0.0, A.add, A.min)
            tt(tl("OHT", h), ("ind", tl("PM", h), ref("CL", 0, 8)), key, A.is_equal)
        oc = ref(bank(), 0, n)
        pe([(oc, tl("OHT", h), Ib, True, True)])
        i = bulk(t, h, 1)
        mark("cc", h)
        if h in LATE:
            flex("S", key, pd)
            tt(tl("MT", h), key, ph, A.is_gt)
        else:
            last = i
            tt(tl("MT", h), key, pd, A.is_lt)
        mk = ref(bank(), 0, n)
        i = pe([(mk, Ib, tl("H16", h), True, False)] + [(mk, full("CN"), on, False, False)][t:])
        pg["ops"][i]["ord"].add(last)
        pe([(mk, tl("MT", h), full("Iwin"), False, True)])
        tt(L["mm"], ref("HEL", (2 * h + 1) * n, (2 * h + 2) * n), mk, A.max)
        ts(L["c"], L["mm"], 4095, A.bitwise_and)
        wide = WIDE and t < NT - 1
        if wide:
            ts(tl("CI", h), ("ind", L["w3"], sm("TLL", h, 16)), 4095, A.bitwise_and)
            tt(tl("PF", h), tl("CI", h), oc, A.mult)
        else:
            flex("V", tl("CF", h), ("ind", L["w3"], sm("TLL", h, 16)), -2048.0)
            tt(tl("PP", h), tl("CF", h), oc, A.mult)
        vo = ref(bank(), 0, n)
        if t < NT - 1:
            vo = ref(vo[0], 0, 8)
            if "v" in XT:
                b = bank()
                pe(xts(b, tl("PF", h), ones=full("Bf")) if wide else xts(b, tl("PP", h)))
                flex("V", xl("XV", h), ref(b, 0, n, 1, 0, 8), -2048.0 if wide else 0.0)
                pe([(vo, xl("XV", h), I8, True, True)])
            else:
                pe(ots(vo, tl("PP", h)))
            flex("V", L["vb"], vo, 2048.0)
            send("v", t + 1, h, tiles(t + 1, h)["vh"], L["vb"])
        else:
            pe(acc(vo, (full("BO"), tl("PP", h))))
            act(ref("YU", 512 + h * n, 512 + h * n + n), vo, F.Identity, 2048.0)
            store(T.yv[:, h * n:h * n + n], ref("YU", 512 + h * n, 512 + h * n + n, 1, 0, 128, 16))
        mark("ff", h)
        if t < NT - 1:
            send("f", t + 1, h, tiles(t + 1, h)["f"], L["c"])
        else:
            flex("S", ref("YU", 1536 + h * n, 1536 + h * n + n), ("ind", L["c"], sm("TLL", h, 16, 8)))
            store(T.yf[:, h * n:h * n + n], ref("YU", 1536 + h * n, 1536 + h * n + n))

    def scatter(t, h):
        mark("sc", h)
        c0 = tiles(t, h)["c"][1]
        w = 4 if t in BIG and h == 0 else 2
        for c in range(8 - w, -1, -w):
            off, src = ref("OFF", h * 8 + c, h * 8 + c + w), ref("W", c0 + 16 * c, c0 + 16 * (c + w))
            i = add(pg, "V", CO["scat"] * (1.7 if w > 2 else 1.0), lambda e, off=off, src=src: e.tensor_copy(ap(full("VI")).indirect(ap(off)), ap(src)), [off, src], [full("VI")], tag="scatter")
            o = pg["ops"][i]
            for d in [d for d in o["dep"] if WAW and pg["ops"][d]["tag"] == "scatter" and pg["ops"][d]["hop"] == t]:
                o["dep"].discard(d)
                o["dep"] |= pg["ops"][d]["dep"]
                o["ord"].add(d)

    for t in range(NT):
        pg["hop"] = t
        front(t, 1)
        front(t, 0)
        early(t, 1)
        tail(t, 1)
        dedupe(t)
        early(t, 0)
        tail(t, 0)
        scatter(t, 1)
        scatter(t, 0)
    pg["st"] = ""
    for a, b in zip(PACK, PACK[1:]):
        y = ref(bank(), 0, b - a)
        flex("S", y, ref("VI", 2048 + a, 2048 + b), 0.0, 4096.0)
        tt(ref("YT", a, b), ref("VI", a, b), y, A.add)
        store(T.yw[:, a:b], ref("YT", a, b))
    named, seen = {}, {}
    for o in pg["ops"]:
        if o["q"] == "S":
            k = (o["hop"], o["st"] + " " + o["tag"][4:])
            seen[k] = seen.get(k, 0) + 1
            named[(k[0], k[1] + " %d" % seen[k])] = o["i"]
    line = []
    for t in range(NT):
        for nm in LINES[t]:
            k = (t - 1, nm[1:]) if nm[0] == "-" else (t, nm)
            if k in named:
                line.append(named[k])
    for a, b in zip(line, line[1:]):
        pg["ops"][b]["ord"].add(a)
    pg["nls"], pg["nout"] = nls[0], nout[0]
    return pg


ORDER = []


def rank_program(g, core, T, topo):
    rank = T.rank_of(core)
    if rank is None:
        return
    if not ORDER:
        ORDER.append(plan(T, topo, core, rank))
    pg = build(T, topo, core, rank)
    emit(pg, ORDER[0], g, T)
    g.wait_ge(T.sem["ls"], int(pg["nls"]))
    g.wait_ge(T.sem["out"], int(pg["nout"]))
